import numpy as np, ml_dtypes
CORES = [24,25,26,27,28,29,30,31]
N = 8
BF = ml_dtypes.bfloat16
def gentries(a):
    return np.ascontiguousarray(a.reshape(8, 16, -1).transpose(0, 2, 1)).reshape(8, -1)
def gtable(e):
    e = np.asarray(e); return np.ascontiguousarray(e.reshape(8, -1, 16).transpose(0, 2, 1)).reshape(128, -1).astype(np.int32)
W, K, O, TH, CAP, RO = 8192, 16, 256, 320, 16, 4
def ring(rng):
    gap = rng.integers(0, W // K, (N, 8, K, O)) + 1; gap[:, :, 0] = rng.integers(0, W, (N, 8, O))
    return np.add.accumulate(gap, axis=2) & (W - 1)
def held(c, want, pri):
    h = np.zeros(c.shape, np.int64)
    for q in range(N):
        for g in range(8):
            p = np.broadcast_to(pri[q, g], (K, O)); low = np.full(W, O); w = want[q, g]
            np.minimum.at(low, c[q, g][w], p[w]); h[q, g] = w & (low[c[q, g]] == p)
    return h
def crew(rng):
    c = ring(rng); lv = rng.choice(np.array([0, K // 2, K - 2, K - 1, K]), (8, O)); pri = np.zeros((8, O), np.int64); cls = np.zeros((8, 1, O), bool)
    nf = rng.permutation(8 + (O * 45 // 100 - 8) * np.arange(8) // 7)
    for g in range(8):
        n = int(nf[g]); o = rng.permutation(O); lv[g, o[:n]] = K; pri[g, o] = np.arange(O); cls[g, 0, o[:n]] = True
        for q in range(N):
            own = rng.permutation(W)[:n * K].reshape(K, n); c[q, g][:, o[:n]] = own
            rest = c[q, g][:, o[n:]]; t = rng.choice(own.reshape(-1), O - n); k = rng.integers(0, K, O - n)
            ok = (rng.random(O - n) < 0.3) & ~np.any(rest == t, axis=0)
            rest[k[ok], np.flatnonzero(ok)] = t[ok]; c[q, g][:, o[n:]] = rest
    want = (np.arange(K)[:, None] < lv[:, None, :]) & (cls | (rng.random((N, 8, K, O)) < 0.95))
    return c, held(c, want, np.broadcast_to(pri, (N, 8, O)))
def far(rng, m, share, over):
    k = rng.integers(0, K, (N, 8, O)); k = np.where(rng.random(k.shape) < 0.5, k, (K - 1) * rng.integers(0, 2, k.shape))
    hit = (rng.random((N, 8, 1, O)) < share) & (np.arange(K)[:, None] == k[:, :, None, :])
    return np.where(hit, TH + rng.integers(1, over + 1, m.shape), m)
def naps(rng, share):
    return np.add.reduce((rng.random((N, 8, O, RO)) < share).astype(np.int64) << np.arange(RO), axis=3)
def pack(x, c, h, m, wk, lump=None):
    ix = c.reshape(N, 8, 1, K * O); xc = np.take_along_axis(x, ix, 3); m = m.reshape(N, 8, 1, K * O)
    d = (m >> 4) + (((np.arange(16).reshape(16, 1) + ix) & 15) < (m & 15))
    if lump is not None:
        s = lump.reshape(N, 8, 1, K * O); i = (np.arange(16).reshape(16, 1) + s) & 15
        most = np.take_along_axis(np.maximum(xc, 255 - xc), i, 2).astype(np.int64); before = np.add.accumulate(most, axis=2) - most
        u = np.zeros(i.shape, np.int64); np.put_along_axis(u, i, np.minimum(np.maximum(m - before, 0), most), 2)
        d = np.where(s < 16, u, d)
    e = np.where(xc < 128, xc + d, xc - d)
    return {"x": np.ascontiguousarray(x.reshape(N, 128, W)).astype(np.float32).astype(BF), "snap": np.ascontiguousarray(e.reshape(N, 128, K * O)).astype(np.float32).astype(BF),
            "cs": np.stack([gtable(a.reshape(8, -1)) for a in c]), "hold": np.stack([gtable(a.reshape(8, -1)) for a in h]), "wake": np.stack([gtable(a) for a in wk])}
def cells(rng):
    return rng.integers(0, 256, (N, 8, 16, W), dtype=np.int32)
def setup_inputs(rng):
    x = cells(rng); c, h = crew(rng); m = far(rng, rng.integers(0, TH + 1, c.shape), 0.08, 600)
    return pack(x, c, h, m, naps(rng, rng.choice(np.array([0.5, 0.7, 0.9]), (N, 8, 1, 1))))
def setup_inputs_room(rng):
    x = cells(rng); c = np.zeros((N, 8, K, O), np.int64); h = np.ones((N, 8, K, O), np.int64); m = rng.integers(0, TH + 1, c.shape); wk = naps(rng, 0.7)
    cnt = rng.permutation(np.array([0, 1, CAP - 1, CAP, CAP + 1, 2 * CAP, O - 1, O]))
    for g in range(8):
        n = int(cnt[g]); o = rng.permutation(O)
        if n == 0: wk[:, g] = 1
        for q in range(N):
            c[q, g] = rng.permutation(W)[:K * O].reshape(K, O)
            rest = o[n:] if q & 1 else o[n:][rng.random(O - n) < 0.5]
            h[q, g][rng.integers(0, K, len(rest)), rest] = 0
            if q & 1 == 0 and n > 0: m[q, g][rng.integers(0, K), rest[rng.random(len(rest)) < 0.15]] = TH + 1
    return pack(x, c, h, m, wk)
def setup_inputs_storm(rng):
    x = cells(rng); c = ring(rng); m = rng.integers(0, TH + 1, c.shape); want = rng.random(c.shape) < 0.5; wk = naps(rng, 0.8)
    pri = np.argsort(rng.random((N, 8, O)), axis=-1); deal = rng.permutation(8); role = deal & 3
    for g in range(8):
        if deal[g] == 0:
            want[:, g] = True
            for q in range(N): c[q, g] = rng.permutation(W)[:K * O].reshape(K, O)
        if role[g] == 0: m[:, g, rng.integers(0, K)] = TH + 1 + rng.integers(0, 600, (N, O))
        if role[g] == 1: m[::2, g, 0, ::2] = TH + 1
        if role[g] == 2:
            o = int(rng.integers(0, O))
            for q in range(N):
                v = int(rng.integers(0, W)); k = rng.integers(0, K, O); ok = ~np.any(c[q, g] == v, axis=0)
                c[q, g][k[ok], np.flatnonzero(ok)] = v; x[q, g, :, v] = rng.integers(0, 16, 16) + 240 * (q & 1)
                want[q, g, :, o] = True; i = int(np.flatnonzero(pri[q, g] == 0)[0]); pri[q, g, i] = pri[q, g, o]; pri[q, g, o] = 0
        if role[g] == 3: want[:, g] = False; wk[:, g] = wk[:, g] & ~1
    p = 2 * int(rng.integers(0, N // 2)); m[p:p + 2] = far(rng, m, 1.0, 600)[p:p + 2]
    return pack(x, c, held(c, want, pri), m, wk)
def setup_inputs_crowd(rng):
    x = cells(rng); c = np.zeros((N, 8, K, O), np.int64)
    for q in range(N):
        for g in range(8):
            P = 64 if g & 1 else 256
            pool = rng.permutation(np.concatenate([np.array([0, W - 1]), 1 + rng.permutation(W - 2)[:P - 2]]))
            c[q, g] = pool[(rng.integers(0, P, O) + np.arange(K)[:, None] * (2 * rng.integers(0, P // 2, O) + 1)) & (P - 1)]
    pri = np.argsort(rng.random((8, O)), axis=-1); lv = np.where(pri < 3, K, rng.integers(0, K + 1, (8, O)))
    lv[rng.permutation(8)[:4]] = 0
    want = np.broadcast_to(np.arange(K)[:, None] < lv[:, None, :], (N, 8, K, O))
    m = far(rng, rng.integers(0, TH + 1, c.shape), 0.01, 600)
    return pack(x, c, held(c, want, np.broadcast_to(pri, (N, 8, O))), m, naps(rng, rng.choice(np.array([0.6, 1.0]), (N, 8, 1, 1))))
def setup_inputs_ties(rng):
    x = cells(rng); z = rng.random((N, 8, 1, W)); x = np.where(z < 0.06, 0, np.where(z < 0.12, 255, x)).astype(np.int32)
    c, h = crew(rng); m = far(rng, rng.choice(np.array([0, TH - 1, TH]), c.shape), 0.12, 1)
    wk = naps(rng, 0.75) & ~(1 << int(rng.integers(1, 3)))
    return pack(x, c, h, m, wk, np.minimum(rng.integers(0, 32, c.shape), 16))
def setup_inputs_spread(rng):
    x = np.minimum((np.exp2(8.01 * rng.random((N, 8, 1, W))) * rng.random((N, 8, 16, W))).astype(np.int32), 255)
    c, h = crew(rng); m = far(rng, (TH * rng.random(c.shape) ** 4).astype(np.int64), 0.1, 1000)
    share = np.ones((N, 1, 1, 1)) * rng.permutation(np.array([0.0, 0.2, 0.4, 0.6, 0.8, 0.9, 1.0, 1.0])).reshape(1, 8, 1, 1)
    return pack(x, c, h, m, naps(rng, share))
def check_inputs(d):
    bad = []
    for k in ("x", "snap"):
        v = np.asarray(d[k]).astype(np.float32)
        if not (np.all(v >= 0) and np.all(v <= 255) and np.all(v == np.floor(v))): bad.append("range of " + k)
    for k, hi in (("cs", W - 1), ("hold", 1), ("wake", 2 ** RO - 1)):
        if np.min(d[k]) < 0 or np.max(d[k]) > hi: bad.append("range of " + k)
    c = np.stack([gentries(a) for a in d["cs"]]).reshape(N, 8, K, O); h = np.stack([gentries(a) for a in d["hold"]]).reshape(N, 8, K, O)
    s = np.sort(c, axis=2)
    if np.any(s[:, :, 1:] == s[:, :, :-1]): bad.append("cells of an operation differ")
    for q in range(N):
        for g in range(8):
            v = c[q, g][h[q, g] == 1]
            if len(np.unique(v)) != len(v) and "a cell has one holder" not in bad: bad.append("a cell has one holder")
    return bad
def reference(x, snap, cs, hold, wake):
    v = np.zeros((N, 8, 16, W + 1), np.int32)
    v[..., :W] = x.astype(np.float32).astype(np.int32).reshape(N, 8, 16, W)
    e = snap.astype(np.float32).astype(np.int32).reshape(N, 8, 16, K * O)
    c = np.stack([gentries(a) for a in cs]).astype(np.int64).reshape(N, 8, K, O); h = np.stack([gentries(a) for a in hold]).reshape(N, 8, K, O)
    wk = np.stack([gentries(a) for a in wake]).astype(np.int64)
    own = np.arange(O) + 1; lane = np.broadcast_to(np.arange(O), (N, 8, O)); cur = np.array(lane)
    lock = np.zeros((N, 8, W + 1), np.int64)
    np.put_along_axis(lock, np.where(h == 1, c, W).reshape(N, 8, -1), np.broadcast_to(own, c.shape).reshape(N, 8, -1), 2)
    for t in range(RO):
        twin = np.arange(N) ^ (1 + t % (N - 1))
        got = np.take_along_axis(v, c.reshape(N, 8, 1, -1), 3)
        dist = np.add.reduce(np.abs(got - e), axis=2).reshape(N, 8, K, O)
        who = np.take_along_axis(lock, c.reshape(N, 8, -1), 2).reshape(N, 8, K, O); mine = who == own
        bad = np.any(dist > TH, axis=2); full = np.all(mine, axis=2)
        abort = bad | bad[twin]; ready = full & full[twin] & ~abort
        before = np.add.accumulate(ready.astype(np.int64), axis=2) - ready
        commit = ready & (before < CAP); done = abort | commit
        first = np.argmin(mine, axis=2)[:, :, None, :]
        cell = np.take_along_axis(np.take_along_axis(c, first, 2)[:, :, 0], cur, 2); by = np.take_along_axis(np.take_along_axis(who, first, 2)[:, :, 0], cur, 2)
        gone = np.take_along_axis(done, cur, 2); act = (((wk >> t) & 1) == 1) & ~gone & ~np.take_along_axis(full, cur, 2)
        np.put_along_axis(lock, np.where(done[:, :, None, :] & mine, c, W).reshape(N, 8, -1), 0, 2)
        for q in range(N):
            for g in range(8):
                w = np.flatnonzero(act[q, g] & (by[q, g] == 0)); low = np.full(W, O); a = cell[q, g][w]
                np.minimum.at(low, a, w); win = low[a] == w
                lock[q, g][a[win]] = cur[q, g][w[win]] + 1
        cur = np.where(gone, lane, np.where(act & (by > 0), by - 1, cur))
        cm = np.broadcast_to(commit[:, :, None, :], (N, 8, K, O)); dn = np.broadcast_to(done[:, :, None, :], (N, 8, K, O)).reshape(N, 8, 1, -1)
        d = np.where(cm.reshape(N, 8, 1, -1), got[twin], e)
        np.put_along_axis(v, np.where(cm, c, W).reshape(N, 8, 1, -1), d, 3)
        u = np.add.reduce(d.reshape(N, 8, 2, 8, K, O).astype(np.int64), axis=3); hs = (u[:, :, 0] * u[:, :, 1]) >> 3
        new = np.zeros((N, 8, K, O), np.int64); new[:, :, 0] = hs[:, :, 0] & (W - 1)
        for k in range(1, K): new[:, :, k] = (new[:, :, k - 1] + 1 + (hs[:, :, k] & (W // K - 1))) & (W - 1)
        c = np.where(done[:, :, None, :], new, c)
        e = np.where(dn, np.take_along_axis(v, c.reshape(N, 8, 1, -1), 3), e)
    lock[..., W] = 0
    mine = np.take_along_axis(lock, c.reshape(N, 8, -1), 2).reshape(N, 8, K, O) == own
    ys = np.add.reduce(v[..., :W] * np.arange(1, 17, dtype=np.int32).reshape(16, 1), axis=2)
    return {"ys": ys.astype(np.float32), "yc": np.stack([gtable(a.reshape(8, -1)) for a in c]).astype(np.float32),
            "yh": np.stack([gtable(a.reshape(8, -1)) for a in mine]).astype(np.float32), "yl": np.stack([gtable(a) for a in cur]).astype(np.float32)}

@@ -1,0 +1,683 @@
+from concourse.mybir import dt, AluOpType, ActivationFunctionType
+
+ALU = AluOpType
+ACT = ActivationFunctionType
+STEPS = 4
+NV = 8192
+EA, DUM, VO, EB = 0, 4096, 4352, 12544
+BIGW = 16640
+LW = 12416
+HELD = 262144.0
+CODE = 33
+NVC = 3
+WAKE, CY = 0.03, 0.00083
+INORDER = ("g", "y")
+URGE = {"rsf": 4.0}
+
+SCRATCH = {
+    "big": ("sbuf", [128, BIGW], "bfloat16"),
+    "snk": ("sbuf", [128, 16, 256], "bfloat16"),
+    "diff": ("sbuf", [128, 4096], "bfloat16"),
+    "absd": ("sbuf", [128, 4096], "bfloat16"),
+    "lock": ("sbuf", [128, LW], "float32"),
+    "yt": ("sbuf", [128, 256 + NV], "float32"),
+    "oh": ("sbuf", [128, 2048], "bfloat16"),
+    "eq": ("sbuf", [128, 1920], "bfloat16"),
+    "eqd": ("sbuf", [128, 256], "bfloat16"),
+    "ld_": ("sbuf", [128, 2048], "bfloat16"),
+    "lu_": ("sbuf", [128, 2048], "bfloat16"),
+    "sel_": ("sbuf", [128, 2048], "bfloat16"),
+}
+for _n in ("csk", "hok", "keyi", "ci", "ti", "tj", "ui", "th", "tl_"):
+    SCRATCH[_n] = ("sbuf", [128, 256], "int32")
+for _n in ("r16", "jt1", "jt2", "dj", "kc8", "rst", "rbig", "diag", "tri", "key", "ka", "ue", "hf", "mx", "mkt", "cg", "cs2", "clm",
+           "m1", "s1", "f1", "f2", "xab", "xcm", "xun", "xp", "xk", "xm", "pxx", "pd", "kx", "kd", "cv", "yco", "yho", "yd"):
+    SCRATCH[_n] = ("sbuf", [128, 256], "float32")
+SCRATCH["codec"] = ("sbuf", [128, 1024], "float32")
+for _n in ("iw", "pw", "ldw"):
+    SCRATCH[_n] = ("sbuf", [128, 296], "float32")
+for _n in ("qb", "blkf"):
+    SCRATCH[_n] = ("sbuf", [128, 128], "float32")
+for _n in ("blk", "mix", "iotas", "ly", "id_", "nid_"):
+    SCRATCH[_n] = ("sbuf", [128, 128], "bfloat16")
+SCRATCH["ldg"] = ("sbuf", [128, 256], "bfloat16")
+SCRATCH["chl"] = ("sbuf", [128, 512], "bfloat16")
+for _n in ("coff", "loff", "eidx", "ku"):
+    SCRATCH[_n] = ("sbuf", [128, 256], "uint16")
+for _n in ("xu", "ou", "curu", "curv", "offu", "listu"):
+    SCRATCH[_n] = ("sbuf", [128, 16], "uint16")
+FS = ["prf", "pgf", "wu", "gi", "giu", "q8", "sent", "home", "j16", "one", "thr", "fulls", "nb", "x", "dec", "decm", "val", "byc",
+      "p", "p8", "gone", "isb", "mv", "d1", "c1", "d2", "cura", "curb", "fr", "cl", "k1", "k2", "lose", "offl", "l1", "l2", "yl"]
+IS = ["mki", "xl", "cint", "o", "ep", "pint", "by", "xx", "aw0", "aw1", "aw2", "aw3", "h0", "pr", "pg", "wk"]
+SCRATCH["fs"] = ("sbuf", [128, 16 * len(FS)], "float32")
+SCRATCH["is_"] = ("sbuf", [128, 16 * len(IS)], "int32")
+for _n in ("rdy", "rs", "sfu", "lfu"):
+    SCRATCH[_n] = ("sbuf", [128, 16], "bfloat16")
+for _t in range(STEPS):
+    SCRATCH["sf%d" % _t] = ("sbuf", [128, 16], "bfloat16")
+    SCRATCH["lsf%d" % _t] = ("sbuf", [128, 16], "bfloat16")
+    SCRATCH["skg%d" % _t] = ("sbuf", [128, 256], "float32")
+    SCRATCH["lkc%d" % _t] = ("sbuf", [128, 256], "float32")
+    SCRATCH["snd%d" % _t] = ("sbuf", [128, 256], "bfloat16")
+    SCRATCH["lnd%d" % _t] = ("sbuf", [128, 256], "bfloat16")
+for _b in range(8):
+    SCRATCH["b%d" % _b] = ("psum", [128, 512], "float32")
+
+SEMAPHORES = ["c" + q for q in "vspgy"] + ["dcs", "dho", "dwk", "dsn", "dx0", "dx1", "oys", "oyc", "oyh", "oyl", "rfu", "qfu"]
+for _t in range(STEPS):
+    SEMAPHORES += [k + str(_t) for k in ("rsf", "rkc", "rdd", "qsf", "qkc", "qdd")]
+
+
+def emitter(g, T):
+    eng = {"v": g.vector, "s": g.scalar, "p": g.tensor, "g": g, "y": g.sync}
+    known = {q: {} for q in eng}
+    cnt = {q: 0 for q in eng}
+    hist, bank, final, prog = {}, {}, {}, []
+
+    def isbank(n):
+        return n[0] == "b" and n[1:].isdigit()
+
+    def before(q, rd, wr):
+        evs = []
+        for isw, regs in ((False, rd), (True, wr)):
+            for n, a, b in regs:
+                if isbank(n):
+                    evs += [e for q2, e in bank.get(n, {}).items() if q2 != q]
+                for lo, hi, w, q2, asyn, e in hist.get(n, ()):
+                    if lo < b and hi > a and (w or isw) and not (q2 == q == "p"):
+                        evs.append(e)
+        todo = {}
+        for s, v, ck in evs:
+            if known[q].get(s, 0) < v and (s not in todo or todo[s][0] < v):
+                todo[s] = (v, ck)
+        for s in sorted(todo):
+            v = todo[s][0]
+            if not any(s2 != s and c2.get(s, 0) >= v for s2, (v2, c2) in todo.items()):
+                eng[q].wait_ge(T.sem[s], v)
+        for s, (v, ck) in todo.items():
+            for s2, v2 in ck.items():
+                known[q][s2] = max(known[q].get(s2, 0), v2)
+
+    def after(q, rd, wr, sem, val, asyn):
+        ck = dict(known[q])
+        ck[sem] = val
+        e = (sem, val, ck)
+        final[sem] = val
+        for n, a, b in wr:
+            hist[n] = [x for x in hist.get(n, ()) if not (a <= x[0] and x[1] <= b)] + [(a, b, True, q, asyn, e)]
+        for n, a, b in rd:
+            hist[n] = [x for x in hist.get(n, ()) if not (not x[2] and x[3] == q and not asyn and a <= x[0] and x[1] <= b)] + [(a, b, False, q, asyn, e)]
+        for n, a, b in rd + wr:
+            if isbank(n):
+                bank.setdefault(n, {})[q] = e
+
+    def op(q, call, outs, ins, cost):
+        prog.append((q, "op", call, [x for o in ins for x in o[1]], [x for o in outs for x in o[1]], cost, cost, None))
+
+    def dma(q, out, in_, sem, lat):
+        call = lambda: eng[q].dma_start(out=out[0], in_=in_[0]).then_inc(T.sem[sem], 16)
+        prog.append((q, "dma", call, in_[1], out[1], 0.1, lat, sem))
+
+    def send(topo, core, dst, out, in_, rsem, lsem):
+        rid, pid, _s = topo.addr(dst)
+        n = len(topo.engines(core, dst))
+        call = lambda: g.remote_dma(out[0], in_[0], T.sem[rsem], T.sem[lsem], pid, rid, topo.mask(core, dst))
+        prog.append(("g", "send", call, in_[1], [], 0.6, 2.0, (lsem, n)))
+        prog.append(("net", "land", None, in_[1], out[1], 0.0, 3.0, (rsem, n)))
+
+    def order():
+        m = len(prog)
+        succ, npred, seen = [[] for _ in range(m)], [0] * m, {}
+        for i, (q, kind, call, rd, wr, occ, lat, x) in enumerate(prog):
+            pred = {}
+            for isw, regs in ((False, rd), (True, wr)):
+                for n, a, b in regs:
+                    bk = isbank(n)
+                    for k, lo, hi, w, q2 in seen.get(n, ()):
+                        if k != i and ((lo < b and hi > a and (w or isw)) or (bk and (q2 != q or q == "p"))):
+                            pred[k] = 1
+            for n, a, b in wr:
+                keep = [e for e in seen.get(n, ()) if not (a <= e[1] and e[2] <= b) or isbank(n)]
+                seen[n] = keep[-60:] + [(i, a, b, True, q)]
+            for n, a, b in rd:
+                seen.setdefault(n, []).append((i, a, b, False, q))
+            npred[i] = len(pred)
+            for k in pred:
+                succ[k].append(i)
+
+        def wake(i, k):
+            return 0.0 if prog[i][0] == prog[k][0] == "p" else WAKE
+
+        way = [0.0] * m
+        for i in range(m - 1, -1, -1):
+            way[i] = prog[i][6] + max([way[k] + wake(i, k) for k in succ[i]] + [0.0])
+            if prog[i][1] == "land":
+                way[i] += URGE.get(prog[i][7][0][:3], 0.0)
+        when, free, ready, out = [0.0] * m, {}, {}, []
+        for i in range(m):
+            if npred[i] == 0:
+                ready.setdefault(prog[i][0], []).append(i)
+        while len(out) < m:
+            best = None
+            for q in ready:
+                if not ready[q]:
+                    continue
+                if q == "net":
+                    i = min(ready[q], key=lambda i: when[i])
+                    t = when[i]
+                elif q in INORDER:
+                    i = min(ready[q])
+                    t = max(free.get(q, 0.0), when[i])
+                else:
+                    t = max(free.get(q, 0.0), min(when[i] for i in ready[q]))
+                    i = max((i for i in ready[q] if when[i] <= t + 0.001), key=lambda i: way[i])
+                if best is None or t < best[0]:
+                    best = (t, q, i)
+            t, q, i = best
+            ready[q].remove(i)
+            out.append(i)
+            if q != "net":
+                free[q] = t + prog[i][5]
+            for k in succ[i]:
+                when[k] = max(when[k], t + prog[i][6] + wake(i, k))
+                npred[k] -= 1
+                if npred[k] == 0:
+                    ready.setdefault(prog[k][0], []).append(k)
+        return out
+
+    def issue():
+        for i in order():
+            q, kind, call, rd, wr, occ, lat, x = prog[i]
+            if kind == "land":
+                final[x[0]] = x[1]
+                nm, a, b = wr[0]
+                hist[nm] = [(a, b, True, "net", True, (x[0], x[1], {x[0]: x[1]}))]
+                continue
+            before(q, rd, wr)
+            if kind == "op":
+                cnt[q] += 1
+                call().then_inc(T.sem["c" + q], 1)
+                after(q, rd, wr, "c" + q, cnt[q], False)
+            else:
+                call()
+                s, n = (x, 16) if kind == "dma" else x
+                after(q, rd, wr, s, n, True)
+        for s in sorted(final):
+            if known["g"].get(s, 0) < final[s]:
+                g.wait_ge(T.sem[s], final[s])
+
+    return op, dma, send, issue
+
+
+def rank_program(g, core, T, topo):
+    rank = T.rank_of(core)
+    if rank is None:
+        return
+    op, dma, send, issue = emitter(g, T)
+
+    def r(n, a=None, b=None, st=None):
+        a = 0 if a is None else a
+        b = T[n].shape[-1] if b is None else b
+        return (T[n][:, a:b] if st is None else T[n][:, a:b:st], [(n, a, b)], -((a - b) // (st or 1)))
+
+    def f(n, k=16):
+        i = 16 * FS.index(n)
+        return r("fs", i, i + k)
+
+    def iv(n, k=16):
+        i = 16 * IS.index(n)
+        return r("is_", i, i + k)
+
+    def ind(win, off):
+        return (win[0].indirect(off[0]), win[1] + off[1], 16 * off[2])
+
+    def hd(n):
+        return r(n, 0, 256, 16)
+
+    def tl(n):
+        return r(n, 15, 256, 16)
+
+    def ext(t):
+        return (t, [], 0)
+
+    def kind(o):
+        w, _s, d = SCRATCH[o[1][0][0]]
+        return len(o[1]) > 1, w == "psum", d in ("bfloat16", "uint16")
+
+    def cost(out, a, b=None):
+        n, ko, ka = a[2], kind(out), kind(a)
+        if ko[0]:
+            return 0.05 + n * 3.8 * CY
+        if ka[0]:
+            return 0.05 + n * 1.5 * CY
+        if b is not None:
+            return max(64, n * (1 if ka[1] or kind(b)[1] else 2)) * CY
+        return max(64, n * (0.5 if ko[2] and ka[2] else 1)) * CY
+
+    def tt(out, a, b, o):
+        op("v", lambda: g.vector.tensor_tensor(out=out[0], in0=a[0], in1=b[0], op=o), [out], [a, b], cost(out, a, b))
+
+    def ts(out, a, s1, s2, o0, o1=None):
+        ins = [a] + [s for s in (s1, s2) if isinstance(s, tuple)]
+        x1 = s1[0] if isinstance(s1, tuple) else s1
+        if o1 is None:
+            op("v", lambda: g.vector.tensor_scalar(out=out[0], in0=a[0], scalar1=x1, scalar2=None, op0=o0), [out], ins, cost(out, a))
+        else:
+            op("v", lambda: g.vector.tensor_scalar(out=out[0], in0=a[0], scalar1=x1, scalar2=s2, op0=o0, op1=o1), [out], ins, cost(out, a))
+
+    def cp(out, a):
+        op("v", lambda: g.vector.tensor_copy(out=out[0], in_=a[0]), [out], [a], cost(out, a))
+
+    def scan(out, d0, d1, o0, o1):
+        op("v", lambda: g.vector.tensor_tensor_scan(out=out[0], data0=d0[0], data1=d1[0], initial=0.0, op0=o0, op1=o1), [out], [d0, d1],
+           max(64, d1[2]) * CY)
+
+    def ms(out, v):
+        op("v", lambda: g.vector.memset(out[0], v), [out], [], cost(out, out))
+
+    def act(out, a, fn, bias=0.0, scale=1.0):
+        cs = cost(out, a) if kind(out)[0] or kind(a)[0] else max(64, a[2]) * CY
+        if bias == 0.0 and scale == 1.0:
+            op("s", lambda: g.scalar.activation(out=out[0], in_=a[0], func=fn), [out], [a], cs)
+        else:
+            op("s", lambda: g.scalar.activation(out=out[0], in_=a[0], func=fn, bias=bias, scale=scale), [out], [a], cs)
+
+    def mm(out, l, x, start, stop):
+        op("p", lambda: g.tensor.matmul(out[0], l[0], x[0], start, stop), [out], [l, x], max(64, x[2]) * CY * (1 if kind(x)[2] else 4))
+
+    def iota(out, pat, base, cm):
+        op("g", lambda: g.iota(out[0], pat, base, cm, allow_small_or_imprecise_dtypes=True), [out], [], 0.13 + 2 * CY * out[2])
+
+    def tell(t, out, in_, rsem, lsem):
+        send(topo, core, T.cores[rank ^ (1 + t)], r(out), r(in_), rsem, lsem)
+
+    add, sub, mul, mx, mn = ALU.add, ALU.subtract, ALU.mult, ALU.max, ALU.min
+    band, shr = ALU.bitwise_and, ALU.arith_shift_right
+
+    dma("s", r("csk"), ext(T.cs[:]), "dcs", 2.5)
+    dma("y", r("hok"), ext(T.hold[:]), "dho", 3.0)
+    dma("s", iv("wk"), ext(T.wake[:]), "dwk", 2.5)
+    dma("y", (T.snk[:], [("snk", 0, 256)], 256), ext(T.snap[:]), "dsn", 8.0)
+    dma("s", r("big", VO, VO + 4096), ext(T.x[:, 0:4096]), "dx0", 13.0)
+    dma("y", r("big", VO + 4096, EB), ext(T.x[:, 4096:8192]), "dx1", 14.0)
+
+    iota(iv("pr", 1), [[0, 1]], 0, 1)
+    iota(r("r16"), [[0, 16], [1, 16]], 0, 0)
+    iota(f("q8", 8), [[1, 8]], 0, 0)
+    iota(r("dj"), [[16, 256]], 8192, 1)
+    iota(r("qb"), [[1, 8], [0, 16]], 0, 0)
+    iota(f("j16"), [[16, 16]], 0, 0)
+    iota(r("kc8"), [[0, 16], [8192, 16]], 8192, 0)
+
+    def codes(a):
+        iota(r("yt", 256 + 1024 * a, 1280 + 1024 * a), [[16, 4], [0, 16], [1, 16]], CODE + 64 * a, 0)
+
+    codes(0)
+    iota(r("lock", 5120, 8192), [[0, 3072]], 0, 0)
+    codes(1)
+    iota(f("sent"), [[16, 16]], 8192, 1)
+
+    ms(r("sel_"), 0.0)
+    for a, n in ((0, 2048), (2048, 2048), (4096, 1024)):
+        act(r("lock", a, a + n), r("sel_", 0, n), ACT.Copy)
+    for n in ("xab", "xcm", "xun", "xp", "xk", "xm", "pw", "ldw"):
+        act(r(n), r("sel_", 0, T[n].shape[-1]), ACT.Copy)
+    ms(r("ld_"), 0.0)
+    ts(iv("pg", 1), iv("pr", 1), 4, None, shr)
+    cp(f("pgf", 1), iv("pg", 1))
+    ts(iv("h0", 1), iv("pr", 1), 15, None, band)
+    cp(f("prf", 1), iv("h0", 1))
+    PRF, PGF = f("prf", 1), f("pgf", 1)
+    ts(f("gi", 8), f("q8", 8), PGF, None, ALU.is_equal)
+    ms(f("one"), 1.0)
+    gi, giu = 16 * FS.index("gi"), 16 * FS.index("giu")
+    for k in range(16):
+        cp(r("ci", k, 256, 16), r("csk", 16 * k, 16 * k + 16))
+    cp(r("coff"), r("ci"))
+    UNDX, T1, T2, DG = r("b6", 0, 256), r("b6", 256, 512), r("b7", 0, 256), r("b7", 256, 512)
+
+    def chl():
+        ts(r("th"), r("ci"), 7, None, shr)
+        ts(r("tl_"), r("ci"), 127, None, band)
+        ts(r("chl", 0, 512, 2), r("th"), 128.0, 256.0, mul, add)
+        cp(r("chl", 1, 512, 2), r("tl_"))
+
+    for h in range(8):
+        ts(r("ld_", 16 * h, 2048, 129), f("one"), r("fs", gi + h, gi + h + 1), None, mul)
+    ms(r("lu_"), 0.0)
+    ts(f("wu", 1), PRF, 8.0, 4095.0, ALU.is_lt, mul)
+    ts(f("wu", 1), f("wu", 1), 1.0, None, add)
+    ts(f("giu", 8), f("gi", 8), f("wu", 1), None, mul)
+    for h in range(8):
+        ts(r("lu_", 16 * h, 2048, 129), f("one"), r("fs", giu + h, giu + h + 1), None, mul)
+    ts(r("diag"), r("r16"), PRF, None, ALU.is_equal)
+    ts(r("blk"), r("qb"), PGF, None, ALU.is_equal)
+    ts(r("blkf"), r("qb"), PGF, None, ALU.is_equal)
+    ts(r("tri"), r("r16"), PRF, None, ALU.is_gt)
+    tt(r("f1", 0, 128), r("blkf"), r("tri", 0, 128), mul)
+    tt(r("f1", 128, 256), r("blkf"), r("diag", 0, 128), mul)
+    cp(r("id_"), r("f1", 128, 256))
+    ts(r("nid_"), r("f1", 128, 256), -1.0, None, mul)
+    ts(r("f1", 128, 256), r("f1", 128, 256), -64.0, None, mul)
+    tt(r("f2", 0, 128), r("f1", 0, 128), r("f1", 128, 256), add)
+    tt(r("mix"), r("f2", 0, 128), r("blkf"), sub)
+    ts(r("f2", 128, 256), r("r16", 0, 128), 936.0, None, add)
+    tt(r("f1", 0, 128), r("f2", 128, 256), r("blkf"), mul)
+    ts(r("iotas"), r("f1", 0, 128), -1000.0, None, add)
+    ts(f("wu", 1), PRF, 1.0, None, add)
+    ts(r("ly"), r("blkf"), f("wu", 1), None, mul)
+    ts(f("j16"), f("j16"), PRF, None, add)
+    chl()
+    ms(r("big", DUM, VO), 0.0)
+
+    for k in range(16):
+        cp(r("hf", k, 256, 16), r("hok", 16 * k, 16 * k + 16))
+    tt(r("f2"), r("ci"), r("dj"), sub)
+    tt(r("f2"), r("f2"), r("hf"), mul)
+    tt(r("f2"), r("f2"), r("dj"), add)
+    cp(r("loff"), r("f2"))
+
+    def locks(a):
+        for b in (2 * a, 2 * a + 1):
+            act(ind(r("lock"), r("loff", 32 * b, 32 * b + 32)), r("yt", 256 + 512 * b, 768 + 512 * b), ACT.Silu)
+
+    def pre_a():
+        scan(r("mkt"), r("rbig"), r("key"), mx, mn)
+        ts(f("fulls"), tl("mkt"), HELD, 1.0, ALU.is_ge, add)
+        cp(iv("mki"), tl("mkt"))
+        ts(iv("xl"), iv("mki"), 8191, None, band)
+        cp(r("xu"), iv("xl"))
+
+    ts(r("rst"), r("r16"), 0.0, None, ALU.is_gt)
+    ts(r("rbig"), r("r16"), 0.0, 1048576.0, ALU.is_equal, mul)
+    tt(r("f1"), r("ci"), r("kc8"), add)
+    ts(r("f2"), r("hf"), HELD, None, mul)
+    tt(r("key"), r("f1"), r("f2"), add)
+    pre_a()
+    cp(r("sfu"), f("fulls"))
+    tell(0, "lfu", "sfu", "rfu", "qfu")
+    locks(0)
+    locks(1)
+    for oc in range(16):
+        cp(r("big", EA + 256 * oc, EA + 256 * oc + 256), (T.snk[:, :, 16 * oc:16 * oc + 16], [("snk", 0, 256)], 256))
+
+    codes(2)
+    codes(3)
+    iota(r("jt1"), [[16, 256]], EA - VO, 0)
+    iota(r("jt2"), [[16, 256]], EB - VO, 0)
+    iota(r("iw"), [[1, 296]], 0, 0)
+    iota(r("codec"), [[512, 4], [1, 256]], CODE + 512, 0)
+
+    for h in range(8):
+        ts(r("sel_", 16 * h, 2048, 129), r("diag", 0, 16), r("fs", gi + h, gi + h + 1), None, mul)
+    ts(f("home"), f("j16"), float(CODE), None, add)
+    cp(f("cura"), f("home"))
+    cp(r("curu"), f("home"))
+    cp(DG, r("diag"))
+    ms(r("ldw", 0, 8), 100.0)
+    for t in range(STEPS):
+        ts(iv("aw%d" % t), iv("wk"), t, 1, shr, band)
+
+    def constants3():
+        ts(r("jt1"), r("jt1"), PRF, None, add)
+        ts(r("jt2"), r("jt2"), PRF, None, add)
+        ts(r("f2"), r("diag"), 1000000.0, -1.0, mul, add)
+        for t in range(STEPS):
+            tt(r("codec", 256 * t, 256 * t + 256), r("codec", 256 * t, 256 * t + 256), r("f2"), mn)
+
+    V = r("big", VO, EB)
+    VD = r("big", DUM, EB)
+    esrc = [EA, EA, EB, EA]
+
+    def sums(bk, lw, src, base, a):
+        for m in range(16):
+            mm(r(bk, 64 * a, 64 * a + 64), r(lw, 128 * m, 128 * m + 128), r(src, base + 1024 * a + m, base + 1024 * a + 1024, 16), m == 0, m == 15)
+
+    def dist(a):
+        sums("b0", "ld_", "absd", 0, a)
+
+    def halves(a):
+        sums("b1", "lu_", "diff", 0, a)
+
+    def chain(out):
+        ts(r("ti"), r("ui"), 12, None, shr)
+        ts(r("tj"), r("ui"), 4095, None, band)
+        tt(r("ti"), r("ti"), r("tj"), mul)
+        ts(r("tj"), r("ti"), 3, 511, shr, band)
+        ts(iv("h0"), hd("ti"), 3, 8191, shr, band)
+        ts(r("hf"), r("tj"), 8193.0, None, add)
+        ts(hd("hf"), iv("h0"), 8192.0, None, add)
+        scan(out, r("rst"), r("hf"), mul, add)
+
+    def judge_v(a, t):
+        d = r("diff", 1024 * a, 1024 * a + 1024)
+        tt(d, ind(V, r("coff", 64 * a, 64 * a + 64)), r("big", esrc[t] + 1024 * a, esrc[t] + 1024 * a + 1024), sub)
+        act(r("absd", 1024 * a, 1024 * a + 1024), d, ACT.Abs)
+
+    def judge_s(a, t):
+        act(r("diff", 1024 * a, 1024 * a + 1024), ind(V, r("coff", 64 * a, 64 * a + 64)), ACT.Copy)
+        for h, bk in ((0, "b2"), (1, "b3")):
+            c = 1024 * a + 512 * h
+            mm(r(bk), r("id_"), r("diff", c, c + 512), True, False)
+            mm(r(bk), r("nid_"), r("big", esrc[t] + c, esrc[t] + c + 512), False, True)
+            act(r("absd", c, c + 512), r(bk), ACT.Abs)
+
+    def pre_b():
+        tt(r("cg"), ind(r("lock", 0, NV), r("xu")), r("diag"), mul)
+        scan(r("cs2"), r("rst"), r("cg"), mul, add)
+        cp(iv("cint"), tl("cs2"))
+        ts(iv("o"), iv("cint"), 511, None, band)
+        cp(r("ou"), iv("o"))
+        act(r("ldg"), ind(r("ldw"), r("ou")), ACT.Copy)
+        ts(iv("ep"), iv("cint"), 9, None, shr)
+
+    def pre_c():
+        for m in range(16):
+            mm(r("b5", 256, 272), r("sel_", 128 * m, 128 * m + 128), r("ldg", m, 256, 16), m == 0, m == 15)
+        tt(f("val"), iv("ep"), r("b5", 256, 272), ALU.is_ge)
+        tt(f("byc"), f("val"), iv("o"), mul)
+        ts(f("p8"), f("byc"), 8192.0, None, mul)
+        tt(f("p"), f("p8"), iv("xl"), add)
+
+    def lanes(t):
+        cur, curn = ("cura", "curb") if t % 2 == 0 else ("curb", "cura")
+        cu, cun = ("curu", "curv") if t % 2 == 0 else ("curv", "curu")
+        last = t == STEPS - 1
+        ts(f("decm"), f("dec"), -8388609.0, 8388608.0, mul, add)
+        tt(hd("xp"), f("p"), f("decm"), mn)
+        scan(r("pxx"), r("rst"), r("xp"), mul, add)
+        tt(r("pd"), r("pxx"), DG, mul)
+        mm(r("b4", 0, 256), r("blkf"), r("pd"), True, True)
+        act(r("pw", CODE, CODE + 256), r("b4", 0, 256), ACT.Copy)
+        if not last:
+            act(r("b4", 0, 256), r("pw", CODE, CODE + 256), ACT.Relu, scale=-float(t + 1))
+        act(r("cv"), ind(r("iw"), r(cu)), ACT.Identity, bias=float(512 * (t + 1)))
+        tt(r("cg"), ind(r("pw"), r(cu)), r("diag"), mul)
+        scan(r("cs2"), r("rst"), r("cg"), mul, add)
+        cp(iv("pint"), tl("cs2"))
+        ts(iv("by"), iv("pint"), 13, None, shr)
+        ts(iv("xx"), iv("pint"), 8191, None, band)
+        ts(f("fr"), iv("by"), 0.0, None, ALU.is_equal)
+        tt(f("k1"), iv("xx"), f("sent"), sub)
+        tt(f("cl"), f("fr"), iv("aw%d" % t), mul)
+        tt(f("k1"), f("k1"), f("cl"), mul)
+        tt(hd("xk"), f("k1"), f("sent"), add)
+        scan(r("kx"), r("rst"), r("xk"), mul, add)
+        if not last:
+            tt(r("ldw", CODE, CODE + 256), r("ldw", CODE, CODE + 256), r("b4", 0, 256), mx)
+        tt(r("kd"), r("kx"), DG, mul)
+        mm(r("b4", 256, 512), r("blkf"), r("kd"), True, True)
+        ts(f("isb"), iv("by"), 0.0, None, ALU.is_gt)
+        tt(f("d1"), iv("by"), f(cur), sub)
+        tt(f("mv"), f("isb"), iv("aw%d" % t), mul)
+        ts(f("gone"), iv("by"), 0.0, None, ALU.is_lt)
+        tt(f("d1"), f("d1"), f("mv"), mul)
+        tt(f("c1"), f(cur), f("d1"), add)
+        tt(f("d2"), f("home"), f("c1"), sub)
+        tt(f("d2"), f("d2"), f("gone"), mul)
+        tt(f(curn), f("c1"), f("d2"), add)
+        cp(r(cun), f(curn))
+        tt(T2, r("kx"), r("b4", 256, 512), ALU.is_equal)
+        cp(r("ku"), r("b4", 256, 512))
+        tt(r("eqd"), T2, r("tri"), mul)
+        mm(r("b5", 0, 256), r("blk"), r("eqd"), True, False)
+        at = 0
+        for oc in range(15):
+            n = 240 - 16 * oc
+            ts(r("eq", at, at + n), r("ku", 256 - n, 256), r("kx", 16 * oc, 16 * oc + 1), None, ALU.is_equal)
+            mm(r("b5", 256 - n, 256), r("blk"), r("eq", at, at + n), False, oc == 14)
+            at += n
+        tt(f("k2"), f("sent"), hd("xk"), sub)
+        tt(r("cg"), r("b5", 0, 256), r("diag"), mul)
+        scan(r("cs2"), r("rst"), r("cg"), mul, add)
+        ts(f("lose"), tl("cs2"), 0.0, None, ALU.is_gt)
+        tt(f("k2"), f("k2"), f("lose"), mul)
+        tt(f("offl"), hd("xk"), f("k2"), add)
+        cp(r("offu"), f("offl"))
+        cp(ind(r("lock"), r("offu")), r("cv"))
+        tt(r("clm"), ind(r("lock", 0, NV), r("xu")), r("codec", 256 * t, 256 * t + 256), ALU.is_equal)
+        scan(r("cs2"), r("rst"), r("clm"), mul, add)
+        tt(hd("xm"), tl("mkt"), tl("cs2"), mul)
+        scan(T1, r("rst"), r("xm"), mul, add)
+        tt(T2, r("keyi"), T1, ALU.is_equal)
+        if not last:
+            ts(T1, T2, HELD, None, mul)
+            tt(r("key"), r("keyi"), T1, add)
+            pre_a()
+
+    def decide(t):
+        if t == 0:
+            tt(f("l1"), f("nb"), f("fulls"), mul)
+            tt(f("l2"), f("l1"), r("lfu"), mul)
+            tt(f("x"), f("l2"), r("lsf0"), mul)
+        else:
+            tt(f("x"), r("sf%d" % t), r("lsf%d" % t), mul)
+        ts(r("rdy"), f("x"), 4.0, None, ALU.is_equal)
+        scan(r("rs"), f("one"), r("rdy"), mul, add)
+        mm(r("b2", 0, 16), r("mix"), r("rdy"), True, False)
+        mm(r("b2", 0, 16), r("blk"), r("rs"), False, True)
+        ts(hd("xab"), f("x"), 0.0, None, ALU.is_equal)
+        for oc in range(16):
+            ts(r("oh", 128 * oc, 128 * oc + 128), r("iotas"), r("b2", oc, oc + 1), None, ALU.is_equal)
+            mm(r("b3", 0, 32), r("oh", 128 * oc, 128 * oc + 128), r("chl", 32 * oc, 32 * oc + 32), oc == 0, oc == 15)
+        ts(hd("xcm"), r("b2", 0, 16), -48.0, None, ALU.is_lt)
+        tt(f("dec"), hd("xab"), hd("xcm"), add)
+        ts(f("thr"), f("dec"), 1000000.0, 320.0, mul, add)
+        ts(hd("xun"), f("dec"), -1.0, 1.0, mul, add)
+        tt(f("l1"), r("b3", 0, 32, 2), f("j16"), mx)
+        tt(f("l2"), r("b3", 1, 32, 2), f("l1"), add)
+        cp(r("listu"), f("l2"))
+        cp(r("snd%d" % t), ind(VD, r("listu")))
+        tell(t, "lnd%d" % t, "snd%d" % t, "rdd%d" % t, "qdd%d" % t)
+
+    def ysum(c):
+        bk = "b%d" % (c % 2)
+        mm(r(bk), r("ly"), r("big", VO + 512 * c, VO + 512 * c + 512), True, True)
+        act(r("yt", 256 + 512 * c, 768 + 512 * c), r(bk), ACT.Copy)
+
+    nc = 64 * NVC
+    for t in range(STEPS):
+        last = t == STEPS - 1
+        if t == 0:
+            for a in range(4):
+                sums("b4", "lu_", "big", EA, a)
+            for a in range(4):
+                judge_v(a, t)
+                dist(a)
+                if a < 2:
+                    halves(a)
+            halves(2)
+            halves(3)
+            ms(f("thr"), 320.0)
+        else:
+            chl()
+            for a in range(NVC, 4):
+                judge_s(a, t)
+            for a in range(NVC):
+                judge_v(a, t)
+                dist(a)
+            for a in range(NVC, 4):
+                dist(a)
+            for a in range(4):
+                halves(a)
+        scan(r("mx"), r("rst"), r("b0", 0, 256), mul, mx)
+        tt(f("nb"), f("thr"), tl("mx"), ALU.is_ge)
+        if t == 0:
+            cp(r("sf0"), f("nb"))
+            locks(2)
+            locks(3)
+        else:
+            tt(r("sf%d" % t), f("nb"), f("fulls"), mul)
+        tell(t, "lsf%d" % t, "sf%d" % t, "rsf%d" % t, "qsf%d" % t)
+        if t in (1, 2):
+            e0, e1 = (EA, EB) if t == 1 else (EB, EA)
+            lo, hi = (EA, EB) if t == 1 else (VO, EB + 4096)
+            tt(r("f1"), r("jt%d" % t), r("ci"), sub)
+            tt(T1, r("f1"), UNDX, mul)
+            tt(r("f1"), T1, r("ci"), add)
+            ts(r("eidx"), r("f1"), float(VO - lo), None, add)
+            for a in range(4):
+                act(r("big", e1 + 1024 * a, e1 + 1024 * a + 1024), ind(r("big", lo, hi), r("eidx", 64 * a, 64 * a + 64)), ACT.Copy)
+        if t > 0:
+            pre_b()
+        kg = r("skg%d" % t)
+        if t == 0:
+            cp(r("ue"), r("b4", 0, 256))
+            tt(r("ui"), r("b1", 0, 256), r("ue"), add)
+        else:
+            tt(r("ui", 0, nc), r("b1", 0, nc), r("ue", 0, nc), add)
+            cp(r("ui", nc, 256), r("b1", nc, 256))
+        chain(kg)
+        tell(t, "lkc%d" % t, "skg%d" % t, "rkc%d" % t, "qkc%d" % t)
+        if t == 0:
+            cp(r("ui"), r("ue"))
+            chain(r("ka"))
+            constants3()
+        else:
+            tt(r("f2"), r("ka"), kg, sub)
+            tt(T1, r("f2"), UNDX, mul)
+            tt(r("ka"), T1, kg, add)
+            pre_c()
+        if last:
+            for c in range(4):
+                ysum(c)
+        decide(t)
+        if t in (1, 2):
+            for a in range(NVC):
+                sums("b1", "lu_", "big", e1, a)
+            act(r("ue", 0, nc), r("b1", 0, nc), ACT.Copy)
+        if last:
+            for c in range(4, 11):
+                ysum(c)
+        scan(UNDX, r("rst"), r("xun"), mul, add)
+        tt(r("m1"), r("key"), UNDX, mul)
+        scan(T1, r("rst"), r("xab"), mul, add)
+        tt(T1, r("ka"), T1, mul)
+        tt(r("s1"), r("m1"), T1, add)
+        scan(T2, r("rst"), r("xcm"), mul, add)
+        tt(T2, r("lkc%d" % t), T2, mul)
+        tt(r("keyi"), r("s1"), T2, add)
+        ts(r("ci"), r("keyi"), 8191, None, band)
+        if not last:
+            cp(r("coff"), r("ci"))
+            cp(ind(VD, r("listu")), r("lnd%d" % t))
+        if t == 0:
+            pre_b()
+            pre_c()
+        lanes(t)
+    for c in range(11, 16):
+        ysum(c)
+    mm(r("b2", 0, 256), r("ly"), r("lnd3"), True, True)
+    act(r("yd"), r("b2", 0, 256), ACT.Copy)
+    cp(ind(r("yt"), r("listu")), r("yd"))
+    dma("y", ext(T.ys[:]), (T.yt[0:128:16, 256:256 + NV], [("yt", 256, 256 + NV)], 0), "oys", 4.0)
+    ts(f("yl"), f("cura"), -float(CODE), None, add)
+    dma("y", ext(T.yl[:]), f("yl"), "oyl", 2.0)
+    for k in range(16):
+        cp(r("yco", 16 * k, 16 * k + 16), r("ci", k, 256, 16))
+    dma("y", ext(T.yc[:]), r("yco"), "oyc", 2.0)
+    ts(r("f1"), r("keyi"), HELD, None, ALU.is_ge)
+    for k in range(16):
+        tt(r("yho", 16 * k, 16 * k + 16), (T.b7[:, k:256:16], T2[1], 16), r("f1", k, 256, 16), add)
+    dma("y", ext(T.yh[:]), r("yho"), "oyh", 2.0)
+    issue()

@@ -1,57 +1,73 @@
-from concourse.mybir import dt, AluOpType, ActivationFunctionType
+from concourse.mybir import AluOpType, ActivationFunctionType, AxisListType
 
 ALU = AluOpType
 ACT = ActivationFunctionType
 STEPS = 4
 NV = 8192
-EA, DUM, VO, EB = 0, 4096, 4352, 12544
-BIGW = 16640
-LW = 12416
-HELD = 262144.0
-CODE = 33
-NVC = 3
-WAKE, CY = 0.03, 0.00083
-INORDER = ("g", "y")
+FB = 16384
+DUM, VO = 0, 256
+FO = VO + FB
+BIGW = FO + NV
+LW = NV + 512
+NEW = 131072.0
+LOW, LOWER = 1048576.0, 2097152.0
+HM = 16384.0
+GONE = 8589934592.0
+FLAG = {1: 768.0, 2: 2048.0}
+FTHR = {2: 6000.0, 3: 20000.0}
+NVC = (4, 2, 2, 2)
+WAKE, CY = 0.04, 0.00095
+FIX = 0.03
+INORDER = ("y",)
 URGE = {"rsf": 4.0}
 
 SCRATCH = {
     "big": ("sbuf", [128, BIGW], "bfloat16"),
     "snk": ("sbuf", [128, 16, 256], "bfloat16"),
+    "ea": ("sbuf", [128, 4096], "bfloat16"),
     "diff": ("sbuf", [128, 4096], "bfloat16"),
     "absd": ("sbuf", [128, 4096], "bfloat16"),
     "lock": ("sbuf", [128, LW], "float32"),
-    "yt": ("sbuf", [128, 256 + NV], "float32"),
+    "zero": ("sbuf", [128, 2048], "bfloat16"),
     "oh": ("sbuf", [128, 2048], "bfloat16"),
-    "eq": ("sbuf", [128, 1920], "bfloat16"),
-    "eqd": ("sbuf", [128, 256], "bfloat16"),
-    "ld_": ("sbuf", [128, 2048], "bfloat16"),
-    "lu_": ("sbuf", [128, 2048], "bfloat16"),
-    "sel_": ("sbuf", [128, 2048], "bfloat16"),
+    "eq": ("sbuf", [128, 16, 272], "bfloat16"),
+    "res": ("sbuf", [128, 16, 16], "int32"),
+    "codes": ("sbuf", [128, 512], "float32"),
+    "yt": ("sbuf", [128, 512], "float32"),
+    "chl": ("sbuf", [128, 512], "bfloat16"),
+    "ldw": ("sbuf", [128, 272], "bfloat16"),
+    "tla": ("sbuf", [128, 80], "int32"),
+    "tlb": ("sbuf", [128, 80], "int32"),
 }
-for _n in ("csk", "hok", "keyi", "ci", "ti", "tj", "ui", "th", "tl_"):
+for _n in ("csk", "hok", "ci", "cf", "st", "ti", "tj"):
     SCRATCH[_n] = ("sbuf", [128, 256], "int32")
-for _n in ("r16", "jt1", "jt2", "dj", "kc8", "rst", "rbig", "diag", "tri", "key", "ka", "ue", "hf", "mx", "mkt", "cg", "cs2", "clm",
-           "m1", "s1", "f1", "f2", "xab", "xcm", "xun", "xp", "xk", "xm", "pxx", "pd", "kx", "kd", "cv", "yco", "yho", "yd"):
+for _n in ("r16", "dj", "rst", "diag", "thd", "ka", "ue", "mx", "cg", "cs2", "s1", "f1", "f2", "cr", "hr", "un", "qk", "q16", "xab", "pd",
+           "am", "aa", "an", "cv", "fb", "yco", "yho"):
     SCRATCH[_n] = ("sbuf", [128, 256], "float32")
-SCRATCH["codec"] = ("sbuf", [128, 1024], "float32")
-for _n in ("iw", "pw", "ldw"):
-    SCRATCH[_n] = ("sbuf", [128, 296], "float32")
-for _n in ("qb", "blkf"):
+for _n in ("iw", "pw"):
+    SCRATCH[_n] = ("sbuf", [128, 520], "float32")
+for _n in ("qb", "blkf", "idf"):
     SCRATCH[_n] = ("sbuf", [128, 128], "float32")
-for _n in ("blk", "mix", "iotas", "ly", "id_", "nid_"):
+for _n in ("blk", "blkw", "blkh", "mix", "iotas", "id_", "nid_"):
     SCRATCH[_n] = ("sbuf", [128, 128], "bfloat16")
-SCRATCH["ldg"] = ("sbuf", [128, 256], "bfloat16")
-SCRATCH["chl"] = ("sbuf", [128, 512], "bfloat16")
-for _n in ("coff", "loff", "eidx", "ku"):
+SCRATCH["qw"] = ("sbuf", [128, 144], "float32")
+for _n in ("wlu", "wcode", "wwin"):
+    SCRATCH[_n] = ("sbuf", [128, 144], "bfloat16")
+SCRATCH["lg"] = ("sbuf", [128, 512], "bfloat16")
+for _n in ("ldg", "fa", "fv", "yb", "zb", "lq", "ls", "rstb"):
+    SCRATCH[_n] = ("sbuf", [128, 256], "bfloat16")
+for _n in ("xw", "wx", "td", "rst4"):
+    SCRATCH[_n] = ("sbuf", [128, 64], "float32")
+for _n in ("coff", "loff", "ku"):
     SCRATCH[_n] = ("sbuf", [128, 256], "uint16")
-for _n in ("xu", "ou", "curu", "curv", "offu", "listu"):
-    SCRATCH[_n] = ("sbuf", [128, 16], "uint16")
-FS = ["prf", "pgf", "wu", "gi", "giu", "q8", "sent", "home", "j16", "one", "thr", "fulls", "nb", "x", "dec", "decm", "val", "byc",
-      "p", "p8", "gone", "isb", "mv", "d1", "c1", "d2", "cura", "curb", "fr", "cl", "k1", "k2", "lose", "offl", "l1", "l2", "yl"]
-IS = ["mki", "xl", "cint", "o", "ep", "pint", "by", "xx", "aw0", "aw1", "aw2", "aw3", "h0", "pr", "pg", "wk"]
+FS = ["prf", "col", "gi", "q8", "sent", "home", "j16", "one", "thr", "fulls", "nb", "x", "cm", "dec", "cls", "vs", "byc", "p", "pm", "ev1", "ev2",
+      "u", "u1", "z", "c1", "c2", "d2", "gm", "cura", "curb", "k1", "k2", "k3", "l1", "l2", "yl", "own0", "own1", "own2", "own3", "iso", "h1", "h2"]
+IS = ["oi", "hi", "hs", "pi", "by", "sl0", "sl1", "sl2", "sl3", "nw", "h0", "pr", "pg", "wk"]
+US = ["xu", "xv", "ou", "cua", "cub", "offu", "listu", "lc", "lr", "lperm", "lrev", "lq"]
 SCRATCH["fs"] = ("sbuf", [128, 16 * len(FS)], "float32")
 SCRATCH["is_"] = ("sbuf", [128, 16 * len(IS)], "int32")
-for _n in ("rdy", "rs", "sfu", "lfu"):
+SCRATCH["us"] = ("sbuf", [128, 16 * len(US)], "uint16")
+for _n in ("rdy", "rs", "wy", "gib"):
     SCRATCH[_n] = ("sbuf", [128, 16], "bfloat16")
 for _t in range(STEPS):
     SCRATCH["sf%d" % _t] = ("sbuf", [128, 16], "bfloat16")
@@ -63,7 +79,7 @@ for _t in range(STEPS):
 for _b in range(8):
     SCRATCH["b%d" % _b] = ("psum", [128, 512], "float32")
 
-SEMAPHORES = ["c" + q for q in "vspgy"] + ["dcs", "dho", "dwk", "dsn", "dx0", "dx1", "oys", "oyc", "oyh", "oyl", "rfu", "qfu"]
+SEMAPHORES = ["c" + q for q in "vspgy"] + ["dcs", "dho", "dwk", "dsn", "dx0", "dx1", "oyc", "oyh", "oyl"] + ["oys%d" % _g for _g in range(8)]
 for _t in range(STEPS):
     SEMAPHORES += [k + str(_t) for k in ("rsf", "rkc", "rdd", "qsf", "qkc", "qdd")]
 
@@ -112,7 +128,8 @@ def emitter(g, T):
                 bank.setdefault(n, {})[q] = e
 
     def op(q, call, outs, ins, cost):
-        prog.append((q, "op", call, [x for o in ins for x in o[1]], [x for o in outs for x in o[1]], cost, cost, None))
+        rd = [x for o in ins for x in o[1]] + [x for o in outs for x in o[1][1:]]
+        prog.append((q, "op", call, rd, [o[1][0] for o in outs], cost, cost, None))
 
     def dma(q, out, in_, sem, lat):
         call = lambda: eng[q].dma_start(out=out[0], in_=in_[0]).then_inc(T.sem[sem], 16)
@@ -123,11 +140,12 @@ def emitter(g, T):
         n = len(topo.engines(core, dst))
         call = lambda: g.remote_dma(out[0], in_[0], T.sem[rsem], T.sem[lsem], pid, rid, topo.mask(core, dst))
         prog.append(("g", "send", call, in_[1], [], 0.6, 2.0, (lsem, n)))
-        prog.append(("net", "land", None, in_[1], out[1], 0.0, 3.0, (rsem, n)))
+        prog.append(("net", "land", None, in_[1], out[1], 0.0, 2.8, (rsem, n)))
 
     def order():
         m = len(prog)
         succ, npred, seen = [[] for _ in range(m)], [0] * m, {}
+        lastq = {}
         for i, (q, kind, call, rd, wr, occ, lat, x) in enumerate(prog):
             pred = {}
             for isw, regs in ((False, rd), (True, wr)):
@@ -136,21 +154,27 @@ def emitter(g, T):
                     for k, lo, hi, w, q2 in seen.get(n, ()):
                         if k != i and ((lo < b and hi > a and (w or isw)) or (bk and (q2 != q or q == "p"))):
                             pred[k] = 1
+            if q in INORDER or kind == "dma":
+                if q in lastq:
+                    pred.setdefault(lastq[q], 0)
+                lastq[q] = i
             for n, a, b in wr:
                 keep = [e for e in seen.get(n, ()) if not (a <= e[1] and e[2] <= b) or isbank(n)]
-                seen[n] = keep[-60:] + [(i, a, b, True, q)]
+                seen[n] = (keep[-60:] if isbank(n) else keep) + [(i, a, b, True, q)]
             for n, a, b in rd:
                 seen.setdefault(n, []).append((i, a, b, False, q))
             npred[i] = len(pred)
-            for k in pred:
-                succ[k].append(i)
+            for k, data in pred.items():
+                succ[k].append((i, data))
 
-        def wake(i, k):
-            return 0.0 if prog[i][0] == prog[k][0] == "p" else WAKE
+        def lag(i, k, data):
+            if not data:
+                return prog[i][5]
+            return prog[i][6] + (0.0 if prog[i][0] == prog[k][0] == "p" else WAKE)
 
         way = [0.0] * m
         for i in range(m - 1, -1, -1):
-            way[i] = prog[i][6] + max([way[k] + wake(i, k) for k in succ[i]] + [0.0])
+            way[i] = max([way[k] + lag(i, k, d) for k, d in succ[i]] + [prog[i][6]])
             if prog[i][1] == "land":
                 way[i] += URGE.get(prog[i][7][0][:3], 0.0)
         when, free, ready, out = [0.0] * m, {}, {}, []
@@ -165,9 +189,6 @@ def emitter(g, T):
                 if q == "net":
                     i = min(ready[q], key=lambda i: when[i])
                     t = when[i]
-                elif q in INORDER:
-                    i = min(ready[q])
-                    t = max(free.get(q, 0.0), when[i])
                 else:
                     t = max(free.get(q, 0.0), min(when[i] for i in ready[q]))
                     i = max((i for i in ready[q] if when[i] <= t + 0.001), key=lambda i: way[i])
@@ -178,8 +199,8 @@ def emitter(g, T):
             out.append(i)
             if q != "net":
                 free[q] = t + prog[i][5]
-            for k in succ[i]:
-                when[k] = max(when[k], t + prog[i][6] + wake(i, k))
+            for k, d in succ[i]:
+                when[k] = max(when[k], t + lag(i, k, d))
                 npred[k] -= 1
                 if npred[k] == 0:
                     ready.setdefault(prog[k][0], []).append(k)
@@ -220,13 +241,10 @@ def rank_program(g, core, T, topo):
         b = T[n].shape[-1] if b is None else b
         return (T[n][:, a:b] if st is None else T[n][:, a:b:st], [(n, a, b)], -((a - b) // (st or 1)))
 
-    def f(n, k=16):
-        i = 16 * FS.index(n)
-        return r("fs", i, i + k)
+    def small(buf, names):
+        return lambda n, k=16, at=0: r(buf, 16 * names.index(n) + at, 16 * names.index(n) + at + k)
 
-    def iv(n, k=16):
-        i = 16 * IS.index(n)
-        return r("is_", i, i + k)
+    f, iv, uv = small("fs", FS), small("is_", IS), small("us", US)
 
     def ind(win, off):
         return (win[0].indirect(off[0]), win[1] + off[1], 16 * off[2])
@@ -249,10 +267,10 @@ def rank_program(g, core, T, topo):
         if ko[0]:
             return 0.05 + n * 3.8 * CY
         if ka[0]:
-            return 0.05 + n * 1.5 * CY
+            return 0.05 + n * 1.56 * CY
         if b is not None:
-            return max(64, n * (1 if ka[1] or kind(b)[1] else 2)) * CY
-        return max(64, n * (0.5 if ko[2] and ka[2] else 1)) * CY
+            return FIX + max(64, n * (1 if ka[1] or kind(b)[1] else 2)) * CY
+        return FIX + max(64, n * (0.5 if ko[2] and ka[2] else 1)) * CY
 
     def tt(out, a, b, o):
         op("v", lambda: g.vector.tensor_tensor(out=out[0], in0=a[0], in1=b[0], op=o), [out], [a, b], cost(out, a, b))
@@ -260,27 +278,28 @@ def rank_program(g, core, T, topo):
     def ts(out, a, s1, s2, o0, o1=None):
         ins = [a] + [s for s in (s1, s2) if isinstance(s, tuple)]
         x1 = s1[0] if isinstance(s1, tuple) else s1
+        x2 = s2[0] if isinstance(s2, tuple) else s2
         if o1 is None:
             op("v", lambda: g.vector.tensor_scalar(out=out[0], in0=a[0], scalar1=x1, scalar2=None, op0=o0), [out], ins, cost(out, a))
         else:
-            op("v", lambda: g.vector.tensor_scalar(out=out[0], in0=a[0], scalar1=x1, scalar2=s2, op0=o0, op1=o1), [out], ins, cost(out, a))
+            op("v", lambda: g.vector.tensor_scalar(out=out[0], in0=a[0], scalar1=x1, scalar2=x2, op0=o0, op1=o1), [out], ins, cost(out, a))
 
     def cp(out, a):
         op("v", lambda: g.vector.tensor_copy(out=out[0], in_=a[0]), [out], [a], cost(out, a))
 
     def scan(out, d0, d1, o0, o1):
+        half = kind(out)[2] and kind(d0)[2] and kind(d1)[2]
         op("v", lambda: g.vector.tensor_tensor_scan(out=out[0], data0=d0[0], data1=d1[0], initial=0.0, op0=o0, op1=o1), [out], [d0, d1],
-           max(64, d1[2]) * CY)
+           FIX + max(64, d1[2] * (0.5 if half else 1)) * CY)
 
     def ms(out, v):
         op("v", lambda: g.vector.memset(out[0], v), [out], [], cost(out, out))
 
-    def act(out, a, fn, bias=0.0, scale=1.0):
-        cs = cost(out, a) if kind(out)[0] or kind(a)[0] else max(64, a[2]) * CY
-        if bias == 0.0 and scale == 1.0:
-            op("s", lambda: g.scalar.activation(out=out[0], in_=a[0], func=fn), [out], [a], cs)
-        else:
-            op("s", lambda: g.scalar.activation(out=out[0], in_=a[0], func=fn, bias=bias, scale=scale), [out], [a], cs)
+    def act(out, a, fn, bias=None, scale=None):
+        cs = cost(out, a) if kind(out)[0] or kind(a)[0] else FIX + max(64, a[2]) * CY
+        ins = [a] + [s for s in (bias, scale) if isinstance(s, tuple)]
+        kw = {k: s[0] if isinstance(s, tuple) else s for k, s in (("bias", bias), ("scale", scale)) if s is not None}
+        op("s", lambda: g.scalar.activation(out=out[0], in_=a[0], func=fn, **kw), [out], ins, cs)
 
     def mm(out, l, x, start, stop):
         op("p", lambda: g.tensor.matmul(out[0], l[0], x[0], start, stop), [out], [l, x], max(64, x[2]) * CY * (1 if kind(x)[2] else 4))
@@ -292,392 +311,397 @@ def rank_program(g, core, T, topo):
         send(topo, core, T.cores[rank ^ (1 + t)], r(out), r(in_), rsem, lsem)
 
     add, sub, mul, mx, mn = ALU.add, ALU.subtract, ALU.mult, ALU.max, ALU.min
-    band, shr = ALU.bitwise_and, ALU.arith_shift_right
+    band, shr, eq_, ge, gt, lt = ALU.bitwise_and, ALU.arith_shift_right, ALU.is_equal, ALU.is_ge, ALU.is_gt, ALU.is_lt
+    RES, RES4 = (T.res[:], [("res", 0, 256)], 256), (T.res[:, :, 0:4], [("res", 0, 256)], 64)
+    P0, P1 = r("b6", 0, 256), r("b6", 256, 512)
+    P2 = P0
+
+    def col(i):
+        return f("col", 1, i)
 
     dma("s", r("csk"), ext(T.cs[:]), "dcs", 2.5)
     dma("y", r("hok"), ext(T.hold[:]), "dho", 3.0)
-    dma("s", iv("wk"), ext(T.wake[:]), "dwk", 2.5)
+    dma("s", iv("wk"), ext(T.wake[:]), "dwk", 3.0)
     dma("y", (T.snk[:], [("snk", 0, 256)], 256), ext(T.snap[:]), "dsn", 8.0)
-    dma("s", r("big", VO, VO + 4096), ext(T.x[:, 0:4096]), "dx0", 13.0)
-    dma("y", r("big", VO + 4096, EB), ext(T.x[:, 4096:8192]), "dx1", 14.0)
+    dma("s", r("big", VO, VO + 4096), ext(T.x[:, 0:4096]), "dx0", 14.0)
+    dma("y", r("big", VO + 4096, VO + NV), ext(T.x[:, 4096:8192]), "dx1", 17.0)
 
     iota(iv("pr", 1), [[0, 1]], 0, 1)
+    iota(r("dj"), [[0, 8], [16, 32]], NV, 0)
+    iota(r("codes"), [[0, 2], [1, 256]], 17, 0)
+    iota(r("lock", 6656, NV), [[0, 1536]], 0, 0)
+    iota(f("q8"), [[1, 16]], 0, 0)
+    iota(r("qw"), [[1, 144]], -15, 0)
     iota(r("r16"), [[0, 16], [1, 16]], 0, 0)
-    iota(f("q8", 8), [[1, 8]], 0, 0)
-    iota(r("dj"), [[16, 256]], 8192, 1)
     iota(r("qb"), [[1, 8], [0, 16]], 0, 0)
-    iota(f("j16"), [[16, 16]], 0, 0)
-    iota(r("kc8"), [[0, 16], [8192, 16]], 8192, 0)
+    iota(r("iw", 1, 513), [[0, 2], [1, 256]], 1, 0)
+    iota(r("q16"), [[-1, 16], [0, 16]], 16, 0)
 
-    def codes(a):
-        iota(r("yt", 256 + 1024 * a, 1280 + 1024 * a), [[16, 4], [0, 16], [1, 16]], CODE + 64 * a, 0)
+    def noflags(a, b):
+        for c in range(a, b):
+            lo = FO - 256 + 1056 * c
+            iota(r("big", lo, lo + 1056), [[0, 1056]], 0, 0)
 
-    codes(0)
-    iota(r("lock", 5120, 8192), [[0, 3072]], 0, 0)
-    codes(1)
-    iota(f("sent"), [[16, 16]], 8192, 1)
+    noflags(0, 4)
 
-    ms(r("sel_"), 0.0)
-    for a, n in ((0, 2048), (2048, 2048), (4096, 1024)):
-        act(r("lock", a, a + n), r("sel_", 0, n), ACT.Copy)
-    for n in ("xab", "xcm", "xun", "xp", "xk", "xm", "pw", "ldw"):
-        act(r(n), r("sel_", 0, T[n].shape[-1]), ACT.Copy)
-    ms(r("ld_"), 0.0)
+    ms(r("zero"), 0.0)
+    ms(r("lock", 0, 2560), 0.0)
+    for a in (2560, 4608):
+        act(r("lock", a, a + 2048), r("zero"), ACT.Copy)
     ts(iv("pg", 1), iv("pr", 1), 4, None, shr)
-    cp(f("pgf", 1), iv("pg", 1))
     ts(iv("h0", 1), iv("pr", 1), 15, None, band)
     cp(f("prf", 1), iv("h0", 1))
-    PRF, PGF = f("prf", 1), f("pgf", 1)
-    ts(f("gi", 8), f("q8", 8), PGF, None, ALU.is_equal)
-    ms(f("one"), 1.0)
-    gi, giu = 16 * FS.index("gi"), 16 * FS.index("giu")
-    for k in range(16):
-        cp(r("ci", k, 256, 16), r("csk", 16 * k, 16 * k + 16))
-    cp(r("coff"), r("ci"))
-    UNDX, T1, T2, DG = r("b6", 0, 256), r("b6", 256, 512), r("b7", 0, 256), r("b7", 256, 512)
+    cp(col(0), iv("pg", 1))
+    PRF, PGF = f("prf", 1), col(0)
+    ts(r("dj"), r("dj"), PRF, None, add)
+    ts(r("f1"), r("hok"), -100000.0, 100000.0, mul, add)
+    tt(r("f1"), r("f1"), r("csk"), add)
+    tt(r("f1"), r("f1"), r("dj"), mn)
+    cp(r("loff"), r("f1"))
+    for b in range(8):
+        act(ind(r("lock"), r("loff", 32 * b, 32 * b + 32)), r("codes"), ACT.Silu)
 
-    def chl():
-        ts(r("th"), r("ci"), 7, None, shr)
-        ts(r("tl_"), r("ci"), 127, None, band)
-        ts(r("chl", 0, 512, 2), r("th"), 128.0, 256.0, mul, add)
-        cp(r("chl", 1, 512, 2), r("tl_"))
-
-    for h in range(8):
-        ts(r("ld_", 16 * h, 2048, 129), f("one"), r("fs", gi + h, gi + h + 1), None, mul)
-    ms(r("lu_"), 0.0)
-    ts(f("wu", 1), PRF, 8.0, 4095.0, ALU.is_lt, mul)
-    ts(f("wu", 1), f("wu", 1), 1.0, None, add)
-    ts(f("giu", 8), f("gi", 8), f("wu", 1), None, mul)
-    for h in range(8):
-        ts(r("lu_", 16 * h, 2048, 129), f("one"), r("fs", giu + h, giu + h + 1), None, mul)
-    ts(r("diag"), r("r16"), PRF, None, ALU.is_equal)
-    ts(r("blk"), r("qb"), PGF, None, ALU.is_equal)
-    ts(r("blkf"), r("qb"), PGF, None, ALU.is_equal)
-    ts(r("tri"), r("r16"), PRF, None, ALU.is_gt)
-    tt(r("f1", 0, 128), r("blkf"), r("tri", 0, 128), mul)
-    tt(r("f1", 128, 256), r("blkf"), r("diag", 0, 128), mul)
-    cp(r("id_"), r("f1", 128, 256))
-    ts(r("nid_"), r("f1", 128, 256), -1.0, None, mul)
-    ts(r("f1", 128, 256), r("f1", 128, 256), -64.0, None, mul)
-    tt(r("f2", 0, 128), r("f1", 0, 128), r("f1", 128, 256), add)
-    tt(r("mix"), r("f2", 0, 128), r("blkf"), sub)
-    ts(r("f2", 128, 256), r("r16", 0, 128), 936.0, None, add)
-    tt(r("f1", 0, 128), r("f2", 128, 256), r("blkf"), mul)
-    ts(r("iotas"), r("f1", 0, 128), -1000.0, None, add)
-    ts(f("wu", 1), PRF, 1.0, None, add)
-    ts(r("ly"), r("blkf"), f("wu", 1), None, mul)
-    ts(f("j16"), f("j16"), PRF, None, add)
-    chl()
-    ms(r("big", DUM, VO), 0.0)
-
-    for k in range(16):
-        cp(r("hf", k, 256, 16), r("hok", 16 * k, 16 * k + 16))
-    tt(r("f2"), r("ci"), r("dj"), sub)
-    tt(r("f2"), r("f2"), r("hf"), mul)
-    tt(r("f2"), r("f2"), r("dj"), add)
-    cp(r("loff"), r("f2"))
-
-    def locks(a):
-        for b in (2 * a, 2 * a + 1):
-            act(ind(r("lock"), r("loff", 32 * b, 32 * b + 32)), r("yt", 256 + 512 * b, 768 + 512 * b), ACT.Silu)
-
-    def pre_a():
-        scan(r("mkt"), r("rbig"), r("key"), mx, mn)
-        ts(f("fulls"), tl("mkt"), HELD, 1.0, ALU.is_ge, add)
-        cp(iv("mki"), tl("mkt"))
-        ts(iv("xl"), iv("mki"), 8191, None, band)
-        cp(r("xu"), iv("xl"))
-
-    ts(r("rst"), r("r16"), 0.0, None, ALU.is_gt)
-    ts(r("rbig"), r("r16"), 0.0, 1048576.0, ALU.is_equal, mul)
-    tt(r("f1"), r("ci"), r("kc8"), add)
-    ts(r("f2"), r("hf"), HELD, None, mul)
-    tt(r("key"), r("f1"), r("f2"), add)
-    pre_a()
-    cp(r("sfu"), f("fulls"))
-    tell(0, "lfu", "sfu", "rfu", "qfu")
-    locks(0)
-    locks(1)
-    for oc in range(16):
-        cp(r("big", EA + 256 * oc, EA + 256 * oc + 256), (T.snk[:, :, 16 * oc:16 * oc + 16], [("snk", 0, 256)], 256))
-
-    codes(2)
-    codes(3)
-    iota(r("jt1"), [[16, 256]], EA - VO, 0)
-    iota(r("jt2"), [[16, 256]], EB - VO, 0)
-    iota(r("iw"), [[1, 296]], 0, 0)
-    iota(r("codec"), [[512, 4], [1, 256]], CODE + 512, 0)
-
-    for h in range(8):
-        ts(r("sel_", 16 * h, 2048, 129), r("diag", 0, 16), r("fs", gi + h, gi + h + 1), None, mul)
-    ts(f("home"), f("j16"), float(CODE), None, add)
-    cp(f("cura"), f("home"))
-    cp(r("curu"), f("home"))
-    cp(DG, r("diag"))
-    ms(r("ldw", 0, 8), 100.0)
+    ts(col(1), PGF, 16.0, None, mul)
+    ts(col(2), PRF, 8.0, 4095.0, lt, mul)
+    ts(col(2), col(2), 1.0, None, add)
+    ts(col(3), PRF, 0.0, None, eq_)
+    ts(col(4), PRF, 1.0, None, eq_)
+    ts(col(5), col(4), 512.0, col(3), mul, add)
+    ts(col(7), col(4), 1.0 / 1024 - 1.0, 1.0, mul, add)
+    ts(col(8), col(4), 15.5, -16.0, mul, add)
+    ts(col(9), col(4), -1.0, 1.0, mul, add)
     for t in range(STEPS):
-        ts(iv("aw%d" % t), iv("wk"), t, 1, shr, band)
+        ts(col(10 + t), col(4), 1024.0 * (t + 1.5) - 16.0, 16.0, mul, add)
+    ts(col(14), PRF, 16.0, None, mul)
+    ts(col(15), PRF, 1.0, None, add)
+    for n, c in (("wlu", 2), ("wcode", 3), ("wwin", 5)):
+        ts(r(n), r("qw"), col(1), col(c), eq_, mul)
+    cp(uv("lc"), f("q8"))
+    ts(uv("lr"), f("q8"), 0.0, PRF, mul, add)
+    ts(uv("lperm"), f("q8"), col(14), None, add)
+    ts(f("k1"), f("q8"), col(14), 240.0, sub, add)
+    cp(uv("lrev"), f("k1"))
+    ts(f("k2"), f("q8"), -1.0, 15.0, mul, add)
+    ts(uv("lq"), f("k2"), col(14), None, add)
+    cp(r("coff"), ind(r("csk"), uv("lperm")))
+    cp(r("ci"), r("coff"))
+    ts(r("rst"), r("r16"), 0.0, None, gt)
+    ts(r("rstb"), r("r16"), 0.0, None, gt)
+    for oc in range(16):
+        cp(r("ea", 256 * oc, 256 * oc + 256), (T.snk[:, :, 16 * oc:16 * oc + 16], [("snk", 0, 256)], 256))
+    ts(f("gi", 8), f("q8", 8), PGF, None, eq_)
+    ts(r("wy", 0, 8), f("gi", 8), col(15), None, mul)
+    cp(r("gib", 0, 8), f("gi", 8))
+    ms(f("one"), 1.0)
+    ts(r("diag"), r("r16"), PRF, None, eq_)
+    ts(r("blk"), r("qb"), PGF, None, eq_)
+    ts(r("blkf"), r("qb"), PGF, None, eq_)
+    ts(r("blkh"), r("qb"), PGF, 65536.0, eq_, mul)
+    tt(r("idf"), r("blkf"), r("diag", 0, 128), mul)
+    cp(r("id_"), r("idf"))
+    ts(r("nid_"), r("idf"), -1.0, None, mul)
+    ts(r("f1", 0, 128), r("r16", 0, 128), PRF, -1.0, gt, add)
+    tt(r("f1", 0, 128), r("f1", 0, 128), r("blkf"), mul)
+    ts(r("f1", 128, 256), r("idf"), -64.0, None, mul)
+    tt(r("mix"), r("f1", 0, 128), r("f1", 128, 256), add)
+    ts(r("f1", 128, 256), r("r16", 0, 128), 936.0, None, add)
+    tt(r("f1", 0, 128), r("f1", 128, 256), r("blkf"), mul)
+    ts(r("iotas"), r("f1", 0, 128), -1000.0, None, add)
+    ts(f("j16"), f("q8"), 16.0, PRF, mul, add)
+    ts(f("sent"), f("j16"), float(NV), None, add)
+    ts(f("home"), f("j16"), 1.0, None, add)
+    for t in range(STEPS):
+        ts(f("own%d" % t), f("home"), 512.0 * (t + 1), None, add)
+    ts(f("k1"), f("q8"), PRF, 1.0, gt, add)
+    op("v", lambda: g.vector.tensor_reduce(out=f("k3", 1)[0], in_=f("k1")[0], axis=AxisListType.X, op=mul), [f("k3", 1)], [f("k1")], 0.09)
+    ts(r("blkw"), r("blkf"), f("k3", 1), None, mul)
+    ts(f("k3", 1, 1), f("k3", 1), 2.0, None, mul)
+    ts(r("thd"), r("diag"), -1.0e9, 1.0e9, mul, add)
+    ts(r("thd"), r("thd"), f("k3", 1, 1), None, mx)
+    ts(r("ti"), r("ci"), 7, None, shr)
+    ts(r("tj"), r("ci"), 127, None, band)
+    ts(r("chl", 0, 512, 2), r("ti"), 128.0, 256.0, mul, add)
+    cp(r("chl", 1, 512, 2), r("tj"))
+    act(r("big", DUM, VO), r("zero", 0, 256), ACT.Copy)
+    for n in ("xab", "xw", "ldw"):
+        act(r(n), r("zero", 0, T[n].shape[-1]), ACT.Copy)
+    ms(r("rst4"), 1.0)
+    ms(r("rst4", 0, 64, 4), 0.0)
+    ms(r("tla", 64, 80), 0)
+    ms(r("tlb", 64, 80), 0)
 
-    def constants3():
-        ts(r("jt1"), r("jt1"), PRF, None, add)
-        ts(r("jt2"), r("jt2"), PRF, None, add)
-        ts(r("f2"), r("diag"), 1000000.0, -1.0, mul, add)
-        for t in range(STEPS):
-            tt(r("codec", 256 * t, 256 * t + 256), r("codec", 256 * t, 256 * t + 256), r("f2"), mn)
+    cp(r("cr"), ind(r("csk"), uv("lrev")))
+    cp(r("hr"), ind(r("hok"), uv("lrev")))
+    ts(r("un"), r("hr"), -1.0, 1.0, mul, add)
+    scan(P2, r("rst"), r("un"), mul, add)
+    cp(f("u"), r("b6", 15, 256, 16))
+    ts(f("fulls"), f("u"), 0.0, 1.0, eq_, add)
+    ts(r("f2"), r("hr"), 99.0, None, mul)
+    tt(r("f2"), P2, r("f2"), mx)
+    cp(r("qk"), ind(r("f2"), uv("lq")))
+    tt(r("qk"), r("qk"), r("q16"), sub)
+    ms(hd("hr"), 0.0)
+    ms(hd("un"), 1.0)
+    tt(r("f2"), r("un"), r("cr"), mul)
+    for n in range(4):
+        scan(P2, r("hr"), r("f2"), mul, add)
+        cp(r("tla", n, 64, 4), r("b6", 15, 256, 16))
+        if n < 3:
+            tt(r("f2", 1, 256), r("b6", 0, 255), r("un", 1, 256), mul)
+            cp(hd("f2"), hd("cr"))
+    cp(uv("xu"), r("tla", 0, 64, 4))
+    cp(f("cura"), f("home"))
+    ts(iv("nw"), iv("wk"), -256.0, 3840.0, mul, add)
+    for t in range(STEPS):
+        ts(iv("sl%d" % t), iv("nw"), t, 256, shr, band)
+    tt(f("c2"), f("home"), iv("sl0"), add)
+    cp(uv("cua"), f("c2"))
+    ms(f("thr"), 0.0)
 
-    V = r("big", VO, EB)
-    VD = r("big", DUM, EB)
-    esrc = [EA, EA, EB, EA]
+    V = r("big", VO, VO + NV)
+    VF = r("big", VO, BIGW)
+    VD = r("big", DUM, VO + NV)
+    FD = r("big", FO - 256, BIGW)
+    LK = r("lock", 0, NV)
 
-    def sums(bk, lw, src, base, a):
+    def mat(w, m):
+        return r(w, 15 - m, 143 - m)
+
+    def sums(bk, w, src, base, a, first=True):
         for m in range(16):
-            mm(r(bk, 64 * a, 64 * a + 64), r(lw, 128 * m, 128 * m + 128), r(src, base + 1024 * a + m, base + 1024 * a + 1024, 16), m == 0, m == 15)
+            mm(r(bk, 64 * a, 64 * a + 64), mat(w, m), r(src, base + 1024 * a + m, base + 1024 * a + 1024, 16), first and m == 0, m == 15)
 
-    def dist(a):
-        sums("b0", "ld_", "absd", 0, a)
+    def pick(out, w, src, n):
+        for m in range(16):
+            mm(out, mat(w, m), r(src, m, n, 16), m == 0, m == 15)
 
-    def halves(a):
-        sums("b1", "lu_", "diff", 0, a)
+    def halves(a, t):
+        if a < NVC[t]:
+            mm(r("b1", 64 * a, 64 * a + 64), r("idf"), r("ue", 64 * a, 64 * a + 64), True, False)
+        sums("b1", "wlu", "diff", 0, a, a >= NVC[t])
 
-    def chain(out):
-        ts(r("ti"), r("ui"), 12, None, shr)
-        ts(r("tj"), r("ui"), 4095, None, band)
-        tt(r("ti"), r("ti"), r("tj"), mul)
+    def steps_of(out, head):
+        act(r("am"), r("b1", 0, 256), ACT.Identity, bias=8388608.0, scale=1.0 / 4096)
+        act(r("an"), r("am"), ACT.Identity, bias=8388608.0 * 4096, scale=-4096.0)
+        act(r("aa"), r("am"), ACT.Identity, bias=-8388608.0)
+        tt(P0, r("b1", 0, 256), r("an"), add)
+        tt(r("ti"), P0, r("aa"), mul)
         ts(r("tj"), r("ti"), 3, 511, shr, band)
         ts(iv("h0"), hd("ti"), 3, 8191, shr, band)
-        ts(r("hf"), r("tj"), 8193.0, None, add)
-        ts(hd("hf"), iv("h0"), 8192.0, None, add)
-        scan(out, r("rst"), r("hf"), mul, add)
+        ts(r(out), r("tj"), 1.0, None, add)
+        if isinstance(head, tuple):
+            tt(hd(out), iv("h0"), head, add)
+        else:
+            ts(hd(out), iv("h0"), head, None, add)
 
-    def judge_v(a, t):
-        d = r("diff", 1024 * a, 1024 * a + 1024)
-        tt(d, ind(V, r("coff", 64 * a, 64 * a + 64)), r("big", esrc[t] + 1024 * a, esrc[t] + 1024 * a + 1024), sub)
-        act(r("absd", 1024 * a, 1024 * a + 1024), d, ACT.Abs)
+    def judge(a, t):
+        win = V if t < 2 else VF
+        c = 1024 * a
+        if a < NVC[t]:
+            tt(r("diff", c, c + 1024), ind(win, r("coff", 64 * a, 64 * a + 64)), r("ea", c, c + 1024), sub)
+            act(r("absd", c, c + 1024), r("diff", c, c + 1024), ACT.Abs)
+        else:
+            act(r("diff", c, c + 1024), ind(win, r("coff", 64 * a, 64 * a + 64)), ACT.Copy)
+            for h, bk in ((0, "b2"), (1, "b3")):
+                d = c + 512 * h
+                mm(r(bk), r("id_"), r("diff", d, d + 512), True, False)
+                mm(r(bk), r("nid_"), r("ea", d, d + 512), False, True)
+                act(r("absd", d, d + 512), r(bk), ACT.Abs)
 
-    def judge_s(a, t):
-        act(r("diff", 1024 * a, 1024 * a + 1024), ind(V, r("coff", 64 * a, 64 * a + 64)), ACT.Copy)
-        for h, bk in ((0, "b2"), (1, "b3")):
-            c = 1024 * a + 512 * h
-            mm(r(bk), r("id_"), r("diff", c, c + 512), True, False)
-            mm(r(bk), r("nid_"), r("big", esrc[t] + c, esrc[t] + c + 512), False, True)
-            act(r("absd", c, c + 512), r(bk), ACT.Abs)
-
-    def pre_b():
-        tt(r("cg"), ind(r("lock", 0, NV), r("xu")), r("diag"), mul)
-        scan(r("cs2"), r("rst"), r("cg"), mul, add)
-        cp(iv("cint"), tl("cs2"))
-        ts(iv("o"), iv("cint"), 511, None, band)
-        cp(r("ou"), iv("o"))
-        act(r("ldg"), ind(r("ldw"), r("ou")), ACT.Copy)
-        ts(iv("ep"), iv("cint"), 9, None, shr)
-
-    def pre_c():
+    def far(h, t):
+        bk = ("b0", "b7")[h]
         for m in range(16):
-            mm(r("b5", 256, 272), r("sel_", 128 * m, 128 * m + 128), r("ldg", m, 256, 16), m == 0, m == 15)
-        tt(f("val"), iv("ep"), r("b5", 256, 272), ALU.is_ge)
-        tt(f("byc"), f("val"), iv("o"), mul)
-        ts(f("p8"), f("byc"), 8192.0, None, mul)
-        tt(f("p"), f("p8"), iv("xl"), add)
+            mm(r(bk, m, 128, 16), r("absd", 2048 * h + m, 2048 * h + 2048, 16), r("gib", 0, 8), True, True)
+        ts(r("yb", 128 * h, 128 * h + 128), r(bk, 0, 128), 320.0, None, gt)
+        if t in FTHR:
+            act(r("zb", 128 * h, 128 * h + 128), r(bk, 0, 128), ACT.Relu, bias=-FTHR[t])
+        mm(r("b0", 256 + 8 * h, 264 + 8 * h), r("yb", 128 * h, 128 * h + 128), r("gib", 0, 8), True, t not in FTHR)
+        if t in FTHR:
+            mm(r("b0", 256 + 8 * h, 264 + 8 * h), r("zb", 128 * h, 128 * h + 128), r("gib", 0, 8), False, True)
 
-    def lanes(t):
-        cur, curn = ("cura", "curb") if t % 2 == 0 else ("curb", "cura")
-        cu, cun = ("curu", "curv") if t % 2 == 0 else ("curv", "curu")
-        last = t == STEPS - 1
-        ts(f("decm"), f("dec"), -8388609.0, 8388608.0, mul, add)
-        tt(hd("xp"), f("p"), f("decm"), mn)
-        scan(r("pxx"), r("rst"), r("xp"), mul, add)
-        tt(r("pd"), r("pxx"), DG, mul)
-        mm(r("b4", 0, 256), r("blkf"), r("pd"), True, True)
-        act(r("pw", CODE, CODE + 256), r("b4", 0, 256), ACT.Copy)
-        if not last:
-            act(r("b4", 0, 256), r("pw", CODE, CODE + 256), ACT.Relu, scale=-float(t + 1))
-        act(r("cv"), ind(r("iw"), r(cu)), ACT.Identity, bias=float(512 * (t + 1)))
-        tt(r("cg"), ind(r("pw"), r(cu)), r("diag"), mul)
-        scan(r("cs2"), r("rst"), r("cg"), mul, add)
-        cp(iv("pint"), tl("cs2"))
-        ts(iv("by"), iv("pint"), 13, None, shr)
-        ts(iv("xx"), iv("pint"), 8191, None, band)
-        ts(f("fr"), iv("by"), 0.0, None, ALU.is_equal)
-        tt(f("k1"), iv("xx"), f("sent"), sub)
-        tt(f("cl"), f("fr"), iv("aw%d" % t), mul)
-        tt(f("k1"), f("k1"), f("cl"), mul)
-        tt(hd("xk"), f("k1"), f("sent"), add)
-        scan(r("kx"), r("rst"), r("xk"), mul, add)
-        if not last:
-            tt(r("ldw", CODE, CODE + 256), r("ldw", CODE, CODE + 256), r("b4", 0, 256), mx)
-        tt(r("kd"), r("kx"), DG, mul)
-        mm(r("b4", 256, 512), r("blkf"), r("kd"), True, True)
-        ts(f("isb"), iv("by"), 0.0, None, ALU.is_gt)
-        tt(f("d1"), iv("by"), f(cur), sub)
-        tt(f("mv"), f("isb"), iv("aw%d" % t), mul)
-        ts(f("gone"), iv("by"), 0.0, None, ALU.is_lt)
-        tt(f("d1"), f("d1"), f("mv"), mul)
-        tt(f("c1"), f(cur), f("d1"), add)
-        tt(f("d2"), f("home"), f("c1"), sub)
-        tt(f("d2"), f("d2"), f("gone"), mul)
-        tt(f(curn), f("c1"), f("d2"), add)
-        cp(r(cun), f(curn))
-        tt(T2, r("kx"), r("b4", 256, 512), ALU.is_equal)
-        cp(r("ku"), r("b4", 256, 512))
-        tt(r("eqd"), T2, r("tri"), mul)
-        mm(r("b5", 0, 256), r("blk"), r("eqd"), True, False)
-        at = 0
-        for oc in range(15):
-            n = 240 - 16 * oc
-            ts(r("eq", at, at + n), r("ku", 256 - n, 256), r("kx", 16 * oc, 16 * oc + 1), None, ALU.is_equal)
-            mm(r("b5", 256 - n, 256), r("blk"), r("eq", at, at + n), False, oc == 14)
-            at += n
-        tt(f("k2"), f("sent"), hd("xk"), sub)
-        tt(r("cg"), r("b5", 0, 256), r("diag"), mul)
-        scan(r("cs2"), r("rst"), r("cg"), mul, add)
-        ts(f("lose"), tl("cs2"), 0.0, None, ALU.is_gt)
-        tt(f("k2"), f("k2"), f("lose"), mul)
-        tt(f("offl"), hd("xk"), f("k2"), add)
-        cp(r("offu"), f("offl"))
-        cp(ind(r("lock"), r("offu")), r("cv"))
-        tt(r("clm"), ind(r("lock", 0, NV), r("xu")), r("codec", 256 * t, 256 * t + 256), ALU.is_equal)
-        scan(r("cs2"), r("rst"), r("clm"), mul, add)
-        tt(hd("xm"), tl("mkt"), tl("cs2"), mul)
-        scan(T1, r("rst"), r("xm"), mul, add)
-        tt(T2, r("keyi"), T1, ALU.is_equal)
-        if not last:
-            ts(T1, T2, HELD, None, mul)
-            tt(r("key"), r("keyi"), T1, add)
-            pre_a()
+    def holders(t):
+        if t == 0:
+            act(r("lg", 0, 256), ind(LK, uv("xu")), ACT.Relu, bias=col(8), scale=col(7))
+            pick(r("b4", 0, 16), "wwin", "lg", 256)
+            ts(f("byc"), r("b4", 0, 16), HM, None, mul)
+        else:
+            ts(iv("oi"), iv("hi"), 511, None, band)
+            cp(uv("ou"), iv("oi"))
+            act(r("ldg"), ind(r("ldw"), uv("ou")), ACT.Copy)
+            pick(r("b4", 32, 48), "wcode", "ldg", 256)
+            ts(iv("hs"), iv("hi"), 9, None, shr)
+            tt(f("vs"), r("b4", 32, 48), iv("hs"), ALU.is_le)
+            ts(f("byc"), iv("oi"), HM, None, mul)
+            tt(f("byc"), f("byc"), f("vs"), mul)
+        tt(f("p"), f("byc"), r("tla", 0, 64, 4), add)
 
     def decide(t):
-        if t == 0:
-            tt(f("l1"), f("nb"), f("fulls"), mul)
-            tt(f("l2"), f("l1"), r("lfu"), mul)
-            tt(f("x"), f("l2"), r("lsf0"), mul)
-        else:
-            tt(f("x"), r("sf%d" % t), r("lsf%d" % t), mul)
-        ts(r("rdy"), f("x"), 4.0, None, ALU.is_equal)
+        tt(f("x"), r("sf%d" % t), r("lsf%d" % t), mul)
+        ts(r("rdy"), f("x"), 4.0, None, eq_)
         scan(r("rs"), f("one"), r("rdy"), mul, add)
         mm(r("b2", 0, 16), r("mix"), r("rdy"), True, False)
         mm(r("b2", 0, 16), r("blk"), r("rs"), False, True)
-        ts(hd("xab"), f("x"), 0.0, None, ALU.is_equal)
+        ts(hd("xab"), f("x"), 0.0, LOW + NEW, eq_, mul)
         for oc in range(16):
-            ts(r("oh", 128 * oc, 128 * oc + 128), r("iotas"), r("b2", oc, oc + 1), None, ALU.is_equal)
+            ts(r("oh", 128 * oc, 128 * oc + 128), r("iotas"), r("b2", oc, oc + 1), None, eq_)
             mm(r("b3", 0, 32), r("oh", 128 * oc, 128 * oc + 128), r("chl", 32 * oc, 32 * oc + 32), oc == 0, oc == 15)
-        ts(hd("xcm"), r("b2", 0, 16), -48.0, None, ALU.is_lt)
-        tt(f("dec"), hd("xab"), hd("xcm"), add)
-        ts(f("thr"), f("dec"), 1000000.0, 320.0, mul, add)
-        ts(hd("xun"), f("dec"), -1.0, 1.0, mul, add)
+        ts(f("cm"), r("b2", 0, 16), -48.0, LOWER + NEW, lt, mul)
         tt(f("l1"), r("b3", 0, 32, 2), f("j16"), mx)
         tt(f("l2"), r("b3", 1, 32, 2), f("l1"), add)
-        cp(r("listu"), f("l2"))
-        cp(r("snd%d" % t), ind(VD, r("listu")))
+        cp(uv("listu"), f("l2"))
+        cp(r("snd%d" % t), ind(VD, uv("listu")))
         tell(t, "lnd%d" % t, "snd%d" % t, "rdd%d" % t, "qdd%d" % t)
+        tt(f("dec"), hd("xab"), f("cm"), add)
+        ts(f("dec"), f("dec"), 0.0, GONE, gt, mul)
 
-    def ysum(c):
-        bk = "b%d" % (c % 2)
-        mm(r(bk), r("ly"), r("big", VO + 512 * c, VO + 512 * c + 512), True, True)
-        act(r("yt", 256 + 512 * c, 768 + 512 * c), r(bk), ACT.Copy)
+    def keys(t):
+        lk = "lkc%d" % t
+        scan(P0, r("rst"), r("xab"), mul, add)
+        tt(P1, P0, r("ka"), add)
+        tt(r("s1"), P1, r(("ci", "st", "st", "cf")[t]), mx)
+        tt(hd(lk), hd(lk), f("cm"), add)
+        scan(P2, r("rst"), r(lk), mul, add)
+        tt(RES, P2, r("s1"), mx)
+        if t == STEPS - 1:
+            ts(r("cf"), RES, NV - 1, None, band)
+            return
+        ts(r("cf"), RES, NV - 1 + FB, None, band)
+        cp(r("coff"), r("cf"))
+        if t < 2:
+            ts(P1, RES, NEW, float(FB), ge, mul)
+            tt(r("st"), P1, r("cf"), add)
 
-    nc = 64 * NVC
+    def flags(t):
+        mm(r("b2", 0, 256), r("id_"), r("lnd%d" % t), True, False)
+        mm(r("b2", 0, 256), r("nid_"), r("snd%d" % t), False, True)
+        act(r("fa"), r("b2", 0, 256), ACT.Abs)
+        mm(r("b3", 0, 256), r("blk"), r("fa"), True, True)
+        act(r("fb"), r("b3", 0, 256), ACT.Sign, bias=-320.5)
+        act(r("fv"), r("fb"), ACT.Identity, bias=FLAG[t] / 2, scale=FLAG[t] / 2)
+        cp(ind(FD, uv("listu")), r("fv"))
+
+    def lanes(t):
+        cur, curn = ("cura", "curb") if t % 2 == 0 else ("curb", "cura")
+        cu, cun = ("cua", "cub") if t % 2 == 0 else ("cub", "cua")
+        last = t == STEPS - 1
+        act(r("cv"), ind(r("iw"), uv(cu)), ACT.Identity, bias=col(10 + t), scale=col(9))
+        mm(r("b5", 0, 256), r("zero", 0, 128), r("zero", 0, 256), True, False)
+        tt(f("pm"), f("p"), f("dec"), mx)
+        tt(r("pd"), ind(f("pm"), uv("lc")), r("diag"), mul)
+        mm(r("b4", 0, 256), r("blkf"), r("pd"), True, True)
+        act(r("pw", 1, 257), r("b4", 0, 256), ACT.Copy)
+        act(r("pw", 257, 513), r("b4", 0, 256), ACT.Identity, bias=512 * HM, scale=1.0 / 512)
+        if not last:
+            act(r("b4", 256, 512), r("b4", 0, 256), ACT.Relu, bias=-1.0, scale=(t + 2) / GONE)
+            tt(r("ldw", 1, 257), r("b4", 256, 512), r("ldw", 1, 257), mx)
+        ts(r("tlb", 0, 64), RES4, NV - 1 + int(NEW), None, band)
+        ts(r("tla", 0, 64), r("tla", 0, 64), NEW / 2, None, add)
+        tt(r("tlb", 0, 64), r("tlb", 0, 64), r("tla", 0, 64), mx)
+        ts(r("tlb", 0, 64), r("tlb", 0, 64), NV - 1, None, band)
+        cp(uv("xu"), r("tlb", 0, 64, 4))
+        if not last:
+            cp(uv("xv"), r("tlb", 1, 64, 4))
+            tt(r("td"), r("tlb", 1, 65), r("tlb", 0, 64), sub)
+        tt(f("u1"), f("u"), f("dec"), mx)
+        ts(f("u1"), f("u1"), 16.0, None, mn)
+        tt(r("cg"), ind(r("pw"), uv(cu)), r("diag"), mul)
+        cp(r("ku"), ind(r("pw"), uv(cu)))
+        scan(r("cs2"), r("rst"), r("cg"), mul, add)
+        PL = tl("cs2")
+        for oc in range(16):
+            n = 256 - 16 * oc
+            ts((T.eq[:, oc, 0:n], [("eq", 272 * oc, 272 * oc + n)], n), r("ku", 16 * oc, 256), r("cs2", 16 * oc + 15, 16 * oc + 16), None, eq_)
+            if oc < 15:
+                mm(r("b5", 16 * oc + 16, 256), r("blkh"), (T.eq[:, oc, 16:n], [("eq", 272 * oc, 272 * oc + n)], n - 16), False, False)
+        mm(r("b5", 0, 256), r("blkw"), (T.eq[:, :, 0:16], [("eq", 0, 272 * 16)], 256), False, True)
+        tt(f("k1"), PL, f("sent"), mn)
+        tt(f("k2"), f("sent"), f("k1"), sub)
+        tt(r("lq"), r("b5", 0, 256), r("thd"), ge)
+        scan(r("ls"), r("rstb"), r("lq"), mul, add)
+        tt(f("k2"), f("k2"), tl("ls"), mul)
+        tt(f("k3"), f("k1"), f("k2"), add)
+        cp(uv("offu"), f("k3"))
+        act(ind(r("lock"), uv("offu")), r("cv"), ACT.Silu)
+        n = 16 if last else 32
+        act(r("lg", 0, 16 * n), ind(LK, uv("xu", n)), ACT.Relu, bias=col(8), scale=col(7))
+        pick(r("b4", 0, n), "wwin", "lg", 16 * n)
+        tt(r("xw", 0, 64, 4), r("b4", 0, 16), f("own%d" % t), eq_)
+        tt(f("u"), f("u1"), r("xw", 0, 64, 4), sub)
+        if not last:
+            ts(f("fulls"), f("u"), 0.0, 1.0, eq_, add)
+            scan(r("wx"), r("rst4"), r("xw"), mul, add)
+            tt(r("td"), r("td"), r("wx"), mul)
+            tt(r("tla", 0, 64), r("tlb", 0, 64), r("td"), add)
+            cp(f("h1"), r("b4", 0, 16))
+            tt(f("h2"), r("b4", 16, 32), f("h1"), sub)
+            tt(f("h2"), f("h2"), r("xw", 0, 64, 4), mul)
+            tt(iv("hi"), f("h2"), f("h1"), add)
+        ts(iv("pi"), PL, 1024 * HM, None, mn)
+        ts(iv("by"), iv("pi"), 14, 511, shr, band)
+        ts(f("gm"), PL, 1024 * HM, None, ge)
+        tt(f("d2"), f("home"), f(cur), sub)
+        tt(f("d2"), f("d2"), f("gm"), mul)
+        tt(f("c1"), f(cur), f("d2"), add)
+        ts(f("z"), iv("by"), 0.0, None, eq_)
+        tt(f("c1"), f("c1"), f("z"), mul)
+        tt(f(curn), f("c1"), iv("by"), mx)
+        if not last:
+            tt(f("c2"), f(curn), iv("sl%d" % (t + 1)), add)
+            cp(uv(cun), f("c2"))
+
+    for a in range(4):
+        sums("b1", "wlu", "ea", 0, a)
+    act(r("ue"), r("b1", 0, 256), ACT.Copy)
+    steps_of("f1", -LOW)
+    scan(r("ka"), r("rst"), r("f1"), mul, add)
     for t in range(STEPS):
         last = t == STEPS - 1
-        if t == 0:
-            for a in range(4):
-                sums("b4", "lu_", "big", EA, a)
-            for a in range(4):
-                judge_v(a, t)
-                dist(a)
-                if a < 2:
-                    halves(a)
-            halves(2)
-            halves(3)
-            ms(f("thr"), 320.0)
-        else:
-            chl()
-            for a in range(NVC, 4):
-                judge_s(a, t)
-            for a in range(NVC):
-                judge_v(a, t)
-                dist(a)
-            for a in range(NVC, 4):
-                dist(a)
-            for a in range(4):
-                halves(a)
-        scan(r("mx"), r("rst"), r("b0", 0, 256), mul, mx)
-        tt(f("nb"), f("thr"), tl("mx"), ALU.is_ge)
-        if t == 0:
-            cp(r("sf0"), f("nb"))
-            locks(2)
-            locks(3)
-        else:
-            tt(r("sf%d" % t), f("nb"), f("fulls"), mul)
+        for a in list(range(NVC[t], 4)) + list(range(NVC[t])):
+            judge(a, t)
+        for h in range(2):
+            far(h, t)
+        tt(f("nb"), r("b0", 256, 272), f("thr"), ALU.is_le)
+        tt(r("sf%d" % t), f("nb"), f("fulls"), mul)
         tell(t, "lsf%d" % t, "sf%d" % t, "rsf%d" % t, "qsf%d" % t)
-        if t in (1, 2):
-            e0, e1 = (EA, EB) if t == 1 else (EB, EA)
-            lo, hi = (EA, EB) if t == 1 else (VO, EB + 4096)
-            tt(r("f1"), r("jt%d" % t), r("ci"), sub)
-            tt(T1, r("f1"), UNDX, mul)
-            tt(r("f1"), T1, r("ci"), add)
-            ts(r("eidx"), r("f1"), float(VO - lo), None, add)
-            for a in range(4):
-                act(r("big", e1 + 1024 * a, e1 + 1024 * a + 1024), ind(r("big", lo, hi), r("eidx", 64 * a, 64 * a + 64)), ACT.Copy)
-        if t > 0:
-            pre_b()
-        kg = r("skg%d" % t)
-        if t == 0:
-            cp(r("ue"), r("b4", 0, 256))
-            tt(r("ui"), r("b1", 0, 256), r("ue"), add)
-        else:
-            tt(r("ui", 0, nc), r("b1", 0, nc), r("ue", 0, nc), add)
-            cp(r("ui", nc, 256), r("b1", nc, 256))
-        chain(kg)
+        for a in range(4):
+            halves(a, t)
+        steps_of("skg%d" % t, f("cls") if t else -LOWER)
         tell(t, "lkc%d" % t, "skg%d" % t, "rkc%d" % t, "qkc%d" % t)
-        if t == 0:
-            cp(r("ui"), r("ue"))
-            chain(r("ka"))
-            constants3()
-        else:
-            tt(r("f2"), r("ka"), kg, sub)
-            tt(T1, r("f2"), UNDX, mul)
-            tt(r("ka"), T1, kg, add)
-            pre_c()
-        if last:
-            for c in range(4):
-                ysum(c)
+        if t:
+            scan(P2, r("rst"), r("skg%d" % t), mul, add)
+            tt(r("ka"), P2, r("ka"), mx)
+        holders(t)
         decide(t)
-        if t in (1, 2):
-            for a in range(NVC):
-                sums("b1", "lu_", "big", e1, a)
-            act(r("ue", 0, nc), r("b1", 0, nc), ACT.Copy)
-        if last:
-            for c in range(4, 11):
-                ysum(c)
-        scan(UNDX, r("rst"), r("xun"), mul, add)
-        tt(r("m1"), r("key"), UNDX, mul)
-        scan(T1, r("rst"), r("xab"), mul, add)
-        tt(T1, r("ka"), T1, mul)
-        tt(r("s1"), r("m1"), T1, add)
-        scan(T2, r("rst"), r("xcm"), mul, add)
-        tt(T2, r("lkc%d" % t), T2, mul)
-        tt(r("keyi"), r("s1"), T2, add)
-        ts(r("ci"), r("keyi"), 8191, None, band)
-        if not last:
-            cp(r("coff"), r("ci"))
-            cp(ind(VD, r("listu")), r("lnd%d" % t))
         if t == 0:
-            pre_b()
-            pre_c()
+            noflags(4, 8)
+        keys(t)
+        cp(ind(VD, uv("listu")), r("lnd%d" % t))
+        if t in FLAG:
+            flags(t)
+        if not last:
+            ts(f("cls"), f("dec"), (32768.0 * (t + 1) - LOW + LOWER) / GONE, -LOWER, mul, add)
+        if t == 0:
+            cp(f("thr"), f("dec"))
+            cp(f("ev1"), f("dec"))
+        else:
+            if not last:
+                ts(f("thr"), f("ev1"), 100.0, None, mn)
+                tt(f("thr"), f("thr"), f("dec"), mx)
+            tt(f("ev1"), f("ev1"), f("dec"), add)
+        if last:
+            cp(r("yco"), ind(r("cf"), uv("lperm")))
+            dma("y", ext(T.yc[:]), r("yco"), "oyc", 2.5)
+            ts(f("iso"), f("ev1"), 0.0, None, eq_)
+            tt(r("f1"), ind(f("iso"), uv("lr")), r("qk"), mul)
+            tt(r("f1"), r("f1"), r("q16"), add)
+            for i in range(64):
+                mm(r("b0", 8 * i, 8 * i + 8), r("big", VO + i, VO + NV, 64), r("wy", 0, 8), True, True)
+            for b in range(8):
+                act(r("yt", 64 * b, 64 * b + 64), r("b0", b, 512, 8), ACT.Copy)
+                dma("ys"[b % 2], ext(T.ys[b]), r("yt", 64 * b, 64 * b + 64), "oys%d" % b, 2.5)
         lanes(t)
-    for c in range(11, 16):
-        ysum(c)
-    mm(r("b2", 0, 256), r("ly"), r("lnd3"), True, True)
-    act(r("yd"), r("b2", 0, 256), ACT.Copy)
-    cp(ind(r("yt"), r("listu")), r("yd"))
-    dma("y", ext(T.ys[:]), (T.yt[0:128:16, 256:256 + NV], [("yt", 256, 256 + NV)], 0), "oys", 4.0)
-    ts(f("yl"), f("cura"), -float(CODE), None, add)
-    dma("y", ext(T.yl[:]), f("yl"), "oyl", 2.0)
-    for k in range(16):
-        cp(r("yco", 16 * k, 16 * k + 16), r("ci", k, 256, 16))
-    dma("y", ext(T.yc[:]), r("yco"), "oyc", 2.0)
-    ts(r("f1"), r("keyi"), HELD, None, ALU.is_ge)
-    for k in range(16):
-        tt(r("yho", 16 * k, 16 * k + 16), (T.b7[:, k:256:16], T2[1], 16), r("f1", k, 256, 16), add)
-    dma("y", ext(T.yh[:]), r("yho"), "oyh", 2.0)
+    ts(f("yl"), f("cura"), -1.0, None, add)
+    dma("y", ext(T.yl[:]), f("yl"), "oyl", 2.5)
+    tt(r("yho"), ind(f("u"), uv("lr")), r("f1"), lt)
+    dma("y", ext(T.yh[:]), r("yho"), "oyh", 2.5)
     issue()

@@ -8,17 +8,22 @@ FB = 16384
 DUM, VO = 0, 256
 FO = VO + FB
 BIGW = FO + NV
-LW = NV + 512
+LW = NV + 4096
 NEW = 131072.0
 LOW, LOWER = 1048576.0, 2097152.0
 HM = 16384.0
 GONE = 8589934592.0
 FLAG = {1: 768.0, 2: 2048.0}
 FTHR = {2: 6000.0, 3: 20000.0}
-NVC = (4, 2, 2, 2)
-WAKE, CY = 0.04, 0.00095
-FIX = 0.03
-INORDER = ("y",)
+NVC = (4, 3, 3, 3)
+WAKE = 0.15
+CY = 0.00083
+FIX = 0.0
+ORDER = []
+ROUNDS = 6
+FLY, FLYB = 1.3, 0.002
+WAYS = ("RRRRRRrr", "sRRRRRrr", "sRRRRRrr", "sRRRRRrr")
+ANEW = 8388608.0
 URGE = {"rsf": 4.0}
 
 SCRATCH = {
@@ -28,47 +33,58 @@ SCRATCH = {
     "diff": ("sbuf", [128, 4096], "bfloat16"),
     "absd": ("sbuf", [128, 4096], "bfloat16"),
     "lock": ("sbuf", [128, LW], "float32"),
-    "zero": ("sbuf", [128, 2048], "bfloat16"),
-    "oh": ("sbuf", [128, 2048], "bfloat16"),
+    "ehi": ("sbuf", [128, 768], "bfloat16"),
+    "elo": ("sbuf", [128, 768], "bfloat16"),
+    "pt": ("sbuf", [128, 128], "float32"),
+    "pf": ("sbuf", [128, 128], "float32"),
+    "po": ("sbuf", [128, 128], "float32"),
     "eq": ("sbuf", [128, 16, 272], "bfloat16"),
     "res": ("sbuf", [128, 16, 16], "int32"),
-    "codes": ("sbuf", [128, 512], "float32"),
-    "yt": ("sbuf", [128, 512], "float32"),
+    "oh": ("sbuf", [128, 2048], "bfloat16"),
     "chl": ("sbuf", [128, 512], "bfloat16"),
+    "kc": ("sbuf", [128, 32], "bfloat16"),
+    "alt": ("sbuf", [128, 32], "float32"),
+    "l32": ("sbuf", [128, 32], "float32"),
     "ldw": ("sbuf", [128, 272], "bfloat16"),
-    "tla": ("sbuf", [128, 80], "int32"),
+    "tla": ("sbuf", [128, 64], "float32"),
     "tlb": ("sbuf", [128, 80], "int32"),
 }
+for _n in ("codes", "yt"):
+    SCRATCH[_n] = ("sbuf", [128, 512], "float32")
 for _n in ("csk", "hok", "ci", "cf", "st", "ti", "tj"):
     SCRATCH[_n] = ("sbuf", [128, 256], "int32")
-for _n in ("r16", "dj", "rst", "diag", "thd", "ka", "ue", "mx", "cg", "cs2", "s1", "f1", "f2", "cr", "hr", "un", "qk", "q16", "xab", "pd",
-           "am", "aa", "an", "cv", "fb", "yco", "yho"):
+for _n in ("r16", "dj", "rst", "diag", "thd", "ka", "cg", "cs2", "s1", "f1", "f2", "f3", "cr", "hr", "un", "qk", "q16", "pd",
+           "am", "aa", "cv"):
     SCRATCH[_n] = ("sbuf", [128, 256], "float32")
 for _n in ("iw", "pw"):
     SCRATCH[_n] = ("sbuf", [128, 520], "float32")
 for _n in ("qb", "blkf", "idf"):
     SCRATCH[_n] = ("sbuf", [128, 128], "float32")
-for _n in ("blk", "blkw", "blkh", "mix", "iotas", "id_", "nid_"):
-    SCRATCH[_n] = ("sbuf", [128, 128], "bfloat16")
+MATS = ["blk", "nblk", "blkw", "blkh", "mix", "id_", "nid_", "idn", "blk2", "iotas", "idm", "idc", "none"]
+SCRATCH["mats"] = ("sbuf", [128, 128 * len(MATS)], "bfloat16")
 SCRATCH["qw"] = ("sbuf", [128, 144], "float32")
-for _n in ("wlu", "wcode", "wwin"):
+for _n in ("wcode", "wwin"):
     SCRATCH[_n] = ("sbuf", [128, 144], "bfloat16")
-SCRATCH["lg"] = ("sbuf", [128, 512], "bfloat16")
-for _n in ("ldg", "fa", "fv", "yb", "zb", "lq", "ls", "rstb"):
+for _n in ("lg", "lgo", "ldg"):
+    SCRATCH[_n] = ("sbuf", [128, 512], "bfloat16")
+for _n in ("fa", "fv", "yb", "zb", "lq", "ls", "rstb"):
     SCRATCH[_n] = ("sbuf", [128, 256], "bfloat16")
-for _n in ("xw", "wx", "td", "rst4"):
+for _n in ("xw", "wx", "td", "rst4", "sm", "lf", "own", "slf"):
     SCRATCH[_n] = ("sbuf", [128, 64], "float32")
+for _n in ("sa", "sb"):
+    SCRATCH[_n] = ("sbuf", [128, 72], "float32")
 for _n in ("coff", "loff", "ku"):
     SCRATCH[_n] = ("sbuf", [128, 256], "uint16")
-FS = ["prf", "col", "gi", "q8", "sent", "home", "j16", "one", "thr", "fulls", "nb", "x", "cm", "dec", "cls", "vs", "byc", "p", "pm", "ev1", "ev2",
-      "u", "u1", "z", "c1", "c2", "d2", "gm", "cura", "curb", "k1", "k2", "k3", "l1", "l2", "yl", "own0", "own1", "own2", "own3", "iso", "h1", "h2"]
-IS = ["oi", "hi", "hs", "pi", "by", "sl0", "sl1", "sl2", "sl3", "nw", "h0", "pr", "pg", "wk"]
-US = ["xu", "xv", "ou", "cua", "cub", "offu", "listu", "lc", "lr", "lperm", "lrev", "lq"]
+FS = ["prf", "col", "clm", "gi", "q8", "sent", "home", "one", "cm", "dec", "cls", "vs", "vs2", "hold", "hold2", "nhold", "a32", "a33", "na",
+      "w", "w1", "nd", "k1", "k2", "k3", "l1", "l2", "yl", "iso"]
+IS = ["oi", "oi2", "hi", "hi2", "pi", "by", "sl0", "sl1", "sl2", "sl3", "nw", "h0", "pr", "pg", "wk"]
+US = ["xu", "xv", "ou", "ou2", "cua", "cub", "offu", "listu", "lc", "lr", "lrev", "lperm", "lq"]
 SCRATCH["fs"] = ("sbuf", [128, 16 * len(FS)], "float32")
 SCRATCH["is_"] = ("sbuf", [128, 16 * len(IS)], "int32")
 SCRATCH["us"] = ("sbuf", [128, 16 * len(US)], "uint16")
-for _n in ("rdy", "rs", "wy", "gib"):
+for _n in ("rdy", "rs", "ab", "w1b", "winb"):
     SCRATCH[_n] = ("sbuf", [128, 16], "bfloat16")
+SCRATCH["gib"] = ("sbuf", [128, 56], "bfloat16")
 for _t in range(STEPS):
     SCRATCH["sf%d" % _t] = ("sbuf", [128, 16], "bfloat16")
     SCRATCH["lsf%d" % _t] = ("sbuf", [128, 16], "bfloat16")
@@ -139,8 +155,8 @@ def emitter(g, T):
         rid, pid, _s = topo.addr(dst)
         n = len(topo.engines(core, dst))
         call = lambda: g.remote_dma(out[0], in_[0], T.sem[rsem], T.sem[lsem], pid, rid, topo.mask(core, dst))
-        prog.append(("g", "send", call, in_[1], [], 0.6, 2.0, (lsem, n)))
-        prog.append(("net", "land", None, in_[1], out[1], 0.0, 2.8, (rsem, n)))
+        prog.append(("g", "send", call, in_[1], [], 0.4, 1.8, (lsem, n)))
+        prog.append(("net", "land", None, in_[1], out[1], 0.0, FLY + in_[2] * FLYB, (rsem, n)))
 
     def order():
         m = len(prog)
@@ -154,7 +170,9 @@ def emitter(g, T):
                     for k, lo, hi, w, q2 in seen.get(n, ()):
                         if k != i and ((lo < b and hi > a and (w or isw)) or (bk and (q2 != q or q == "p"))):
                             pred[k] = 1
-            if q in INORDER or kind == "dma":
+            if kind == "land":
+                pred[i - 1] = 0
+            if kind == "dma":
                 if q in lastq:
                     pred.setdefault(lastq[q], 0)
                 lastq[q] = i
@@ -172,42 +190,58 @@ def emitter(g, T):
                 return prog[i][5]
             return prog[i][6] + (0.0 if prog[i][0] == prog[k][0] == "p" else WAKE)
 
+        fore = [[(k, lag(i, k, d)) for k, d in succ[i]] for i in range(m)]
+        back = [[] for _ in range(m)]
+        for i in range(m):
+            for k, l in fore[i]:
+                back[k].append((i, l + prog[k][5] - prog[i][5]))
+
+        def place(nxt, first, key):
+            left = [0] * m
+            for i in range(m):
+                for k, l in nxt[i]:
+                    left[k] += 1
+            when, busy, ready = list(first), {}, sorted((key[i], i) for i in range(m) if left[i] == 0)
+            while ready:
+                i = ready.pop(0)[1]
+                t, occ, line = when[i], prog[i][5], busy.setdefault(prog[i][0], [])
+                if occ:
+                    lo, hi = 0, len(line)
+                    while lo < hi:
+                        mid = (lo + hi) // 2
+                        lo, hi = (mid + 1, hi) if line[mid][1] <= t else (lo, mid)
+                    while lo < len(line) and line[lo][0] < t + occ - 1e-9:
+                        t = max(t, line[lo][1])
+                        lo += 1
+                    line.insert(lo, (t, t + occ))
+                when[i] = t
+                new = []
+                for k, l in nxt[i]:
+                    when[k] = max(when[k], t + l)
+                    left[k] -= 1
+                    if left[k] == 0:
+                        new.append((key[k], k))
+                if new:
+                    ready = sorted(ready + new)
+            return when
+
         way = [0.0] * m
         for i in range(m - 1, -1, -1):
-            way[i] = max([way[k] + lag(i, k, d) for k, d in succ[i]] + [prog[i][6]])
-            if prog[i][1] == "land":
-                way[i] += URGE.get(prog[i][7][0][:3], 0.0)
-        when, free, ready, out = [0.0] * m, {}, {}, []
-        for i in range(m):
-            if npred[i] == 0:
-                ready.setdefault(prog[i][0], []).append(i)
-        while len(out) < m:
-            best = None
-            for q in ready:
-                if not ready[q]:
-                    continue
-                if q == "net":
-                    i = min(ready[q], key=lambda i: when[i])
-                    t = when[i]
-                else:
-                    t = max(free.get(q, 0.0), min(when[i] for i in ready[q]))
-                    i = max((i for i in ready[q] if when[i] <= t + 0.001), key=lambda i: way[i])
-                if best is None or t < best[0]:
-                    best = (t, q, i)
-            t, q, i = best
-            ready[q].remove(i)
-            out.append(i)
-            if q != "net":
-                free[q] = t + prog[i][5]
-            for k, d in succ[i]:
-                when[k] = max(when[k], t + lag(i, k, d))
-                npred[k] -= 1
-                if npred[k] == 0:
-                    ready.setdefault(prog[k][0], []).append(k)
-        return out
+            way[i] = max([way[k] + l for k, l in fore[i]] + [prog[i][6]])
+        key, best = [-w for w in way], None
+        for _ in range(ROUNDS):
+            start = place(fore, [0.0] * m, key)
+            end = max(start[i] + prog[i][6] for i in range(m))
+            if best is None or end < best[0]:
+                best = (end, start)
+            late = place(back, [prog[i][6] - prog[i][5] for i in range(m)], [-(start[i] + prog[i][5]) for i in range(m)])
+            key = [-(late[i] + prog[i][5]) for i in range(m)]
+        return sorted(range(m), key=lambda i: (best[1][i], i))
 
     def issue():
-        for i in order():
+        if not ORDER:
+            ORDER.extend(order())
+        for i in ORDER:
             q, kind, call, rd, wr, occ, lat, x = prog[i]
             if kind == "land":
                 final[x[0]] = x[1]
@@ -237,6 +271,8 @@ def rank_program(g, core, T, topo):
     op, dma, send, issue = emitter(g, T)
 
     def r(n, a=None, b=None, st=None):
+        if n in MATS:
+            return r("mats", 128 * MATS.index(n), 128 * MATS.index(n) + 128)
         a = 0 if a is None else a
         b = T[n].shape[-1] if b is None else b
         return (T[n][:, a:b] if st is None else T[n][:, a:b:st], [(n, a, b)], -((a - b) // (st or 1)))
@@ -301,59 +337,83 @@ def rank_program(g, core, T, topo):
         kw = {k: s[0] if isinstance(s, tuple) else s for k, s in (("bias", bias), ("scale", scale)) if s is not None}
         op("s", lambda: g.scalar.activation(out=out[0], in_=a[0], func=fn, **kw), [out], ins, cs)
 
+    def lin(out, a, scale=None, bias=None):
+        act(out, a, ACT.Identity, bias=bias, scale=scale)
+
     def mm(out, l, x, start, stop):
         op("p", lambda: g.tensor.matmul(out[0], l[0], x[0], start, stop), [out], [l, x], max(64, x[2]) * CY * (1 if kind(x)[2] else 4))
 
-    def iota(out, pat, base, cm):
-        op("g", lambda: g.iota(out[0], pat, base, cm, allow_small_or_imprecise_dtypes=True), [out], [], 0.13 + 2 * CY * out[2])
+    def iota(out, pat, base, cm=0, after=()):
+        op("g", lambda: g.iota(out[0], pat, base, cm, allow_small_or_imprecise_dtypes=True), [out], list(after), 0.13 + 2 * CY * out[2])
+
+    def keep(out, a, pat, cmp, fill, cm=0):
+        op("g", lambda: g.affine_select(out[0], a[0], pat, cmp, fill, 0, cm), [out], [a], 0.17 + 2 * CY * out[2])
 
     def tell(t, out, in_, rsem, lsem):
         send(topo, core, T.cores[rank ^ (1 + t)], r(out), r(in_), rsem, lsem)
 
     add, sub, mul, mx, mn = ALU.add, ALU.subtract, ALU.mult, ALU.max, ALU.min
-    band, shr, eq_, ge, gt, lt = ALU.bitwise_and, ALU.arith_shift_right, ALU.is_equal, ALU.is_ge, ALU.is_gt, ALU.is_lt
+    band, shr, eq_, ge, gt, lt, le = ALU.bitwise_and, ALU.arith_shift_right, ALU.is_equal, ALU.is_ge, ALU.is_gt, ALU.is_lt, ALU.is_le
     RES, RES4 = (T.res[:], [("res", 0, 256)], 256), (T.res[:, :, 0:4], [("res", 0, 256)], 64)
     P0, P1 = r("b6", 0, 256), r("b6", 256, 512)
-    P2 = P0
 
     def col(i):
         return f("col", 1, i)
 
-    dma("s", r("csk"), ext(T.cs[:]), "dcs", 2.5)
-    dma("y", r("hok"), ext(T.hold[:]), "dho", 3.0)
-    dma("s", iv("wk"), ext(T.wake[:]), "dwk", 3.0)
-    dma("y", (T.snk[:], [("snk", 0, 256)], 256), ext(T.snap[:]), "dsn", 8.0)
-    dma("s", r("big", VO, VO + 4096), ext(T.x[:, 0:4096]), "dx0", 14.0)
-    dma("y", r("big", VO + 4096, VO + NV), ext(T.x[:, 4096:8192]), "dx1", 17.0)
+    dma("s", r("csk"), ext(T.cs[:]), "dcs", 1.8)
+    dma("y", r("hok"), ext(T.hold[:]), "dho", 2.3)
+    dma("s", iv("wk"), ext(T.wake[:]), "dwk", 2.5)
+    dma("y", (T.snk[:], [("snk", 0, 256)], 256), ext(T.snap[:]), "dsn", 6.5)
+    dma("s", r("big", VO, VO + 4096), ext(T.x[:, 0:4096]), "dx0", 10.5)
+    dma("y", r("big", VO + 4096, VO + NV), ext(T.x[:, 4096:8192]), "dx1", 14.5)
 
     iota(iv("pr", 1), [[0, 1]], 0, 1)
-    iota(r("dj"), [[0, 8], [16, 32]], NV, 0)
-    iota(r("codes"), [[0, 2], [1, 256]], 17, 0)
-    iota(r("lock", 6656, NV), [[0, 1536]], 0, 0)
-    iota(f("q8"), [[1, 16]], 0, 0)
-    iota(r("qw"), [[1, 144]], -15, 0)
-    iota(r("r16"), [[0, 16], [1, 16]], 0, 0)
-    iota(r("qb"), [[1, 8], [0, 16]], 0, 0)
-    iota(r("iw", 1, 513), [[0, 2], [1, 256]], 1, 0)
-    iota(r("q16"), [[-1, 16], [0, 16]], 16, 0)
+    iota(r("dj"), [[0, 8], [128, 32]], NV, 1)
+    iota(r("codes"), [[0, 2], [1, 256]], 17)
+    iota(r("lock", 6656, NV), [[0, 1536]], 0)
+    iota(f("q8"), [[1, 16]], 0)
+    iota(f("one"), [[0, 16]], 1)
+    iota(f("sent"), [[128, 16]], NV, 1)
+    iota(f("clm", 4), [[1024, 4]], 1520)
+    iota(r("lf", 0, 16), [[1, 16]], 0)
+    iota(r("lf", 16, 32), [[-1, 16]], 15)
+    iota(r("own"), [[512, 4], [16, 16]], 513)
+    iota(r("qw"), [[1, 144]], -15)
+    iota(r("r16"), [[0, 16], [1, 16]], 0)
+    iota(r("qb"), [[1, 8], [0, 16]], 0)
+    iota(r("iw", 1, 513), [[0, 2], [1, 256]], 1)
+    iota(r("q16"), [[1, 16], [0, 16]], int(ANEW) + 1)
+    iota(r("alt"), [[0, 16], [1, 2]], 0)
+    iota(r("kc"), [[16, 16], [0, 2]], 0)
+    keep(r("kc"), r("kc"), [[0, 16], [1, 2]], eq_, 0.0)
+    iota(r("iotas"), [[0, 8], [1, 16]], -64)
+    iota(r("rst"), [[0, 256]], 1)
+    keep(r("rst"), r("rst"), [[0, 16], [1, 16]], gt, 0.0)
+    iota(r("rstb"), [[0, 256]], 1)
+    keep(r("rstb"), r("rstb"), [[0, 16], [1, 16]], gt, 0.0)
+    iota(r("pf"), [[0, 128]], 1)
+    keep(r("pf"), r("pf"), [[0, 16], [1, 8]], gt, 0.0)
+    iota(r("pt"), [[0, 128]], 0)
+    iota(f("a32"), [[8, 16]], 7)
+    iota(r("rst4"), [[0, 64]], 1)
+    keep(r("rst4"), r("rst4"), [[0, 16], [1, 4]], gt, 0.0)
+    iota(r("sm"), [[0, 64]], 1)
+    keep(r("sm"), r("sm"), [[0, 16], [1, 4]], gt, 0.0)
+    iota(r("tlb", 64, 80), [[0, 16]], 0)
+    for n in ("xw", "ldw", "none"):
+        iota(r(n), [[0, r(n)[2]]], 0)
+    iota(r("big", DUM, VO), [[0, 256]], 0)
 
-    def noflags(a, b):
+    def noflags(a, b, after=()):
         for c in range(a, b):
             lo = FO - 256 + 1056 * c
-            iota(r("big", lo, lo + 1056), [[0, 1056]], 0, 0)
+            iota(r("big", lo, lo + 1056), [[0, 1056]], 0, 0, after)
 
-    noflags(0, 4)
+    noflags(0, 3)
 
-    ms(r("zero"), 0.0)
-    ms(r("lock", 0, 2560), 0.0)
-    for a in (2560, 4608):
-        act(r("lock", a, a + 2048), r("zero"), ACT.Copy)
-    ts(iv("pg", 1), iv("pr", 1), 4, None, shr)
-    ts(iv("h0", 1), iv("pr", 1), 15, None, band)
-    cp(f("prf", 1), iv("h0", 1))
-    cp(col(0), iv("pg", 1))
-    PRF, PGF = f("prf", 1), col(0)
-    ts(r("dj"), r("dj"), PRF, None, add)
+    ms(r("lock", 0, 2304), 0.0)
+    for a in (2304, 4480):
+        act(r("lock", a, a + 2176), r("lock", 0, 2176), ACT.Copy)
     ts(r("f1"), r("hok"), -100000.0, 100000.0, mul, add)
     tt(r("f1"), r("f1"), r("csk"), add)
     tt(r("f1"), r("f1"), r("dj"), mn)
@@ -361,102 +421,102 @@ def rank_program(g, core, T, topo):
     for b in range(8):
         act(ind(r("lock"), r("loff", 32 * b, 32 * b + 32)), r("codes"), ACT.Silu)
 
-    ts(col(1), PGF, 16.0, None, mul)
-    ts(col(2), PRF, 8.0, 4095.0, lt, mul)
-    ts(col(2), col(2), 1.0, None, add)
-    ts(col(3), PRF, 0.0, None, eq_)
+    ts(iv("pg", 1, 0), iv("pr", 1), 15, None, band)
+    ts(iv("pg", 1, 1), iv("pr", 1), 4, None, shr)
+    ts(iv("pg", 1, 2), iv("pr", 1), 112, None, band)
+    cp(f("prf", 3), iv("pg", 3))
+    PRF, PGF, G16 = (f("prf", 1, i) for i in range(3))
+    ts(col(2), PRF, 8.0, None, lt)
+    ts(col(6), PRF, 8.0, None, ge)
+    ts(col(3), PRF, 0.0, 512.0, eq_, mul)
     ts(col(4), PRF, 1.0, None, eq_)
-    ts(col(5), col(4), 512.0, col(3), mul, add)
+    ts(col(0), col(3), 1.0 / 512, None, mul)
+    ts(col(5), col(4), 512.0, col(0), mul, add)
     ts(col(7), col(4), 1.0 / 1024 - 1.0, 1.0, mul, add)
     ts(col(8), col(4), 15.5, -16.0, mul, add)
     ts(col(9), col(4), -1.0, 1.0, mul, add)
-    for t in range(STEPS):
-        ts(col(10 + t), col(4), 1024.0 * (t + 1.5) - 16.0, 16.0, mul, add)
+    ts(f("clm", 4), f("clm", 4), col(4), 16.0, mul, add)
     ts(col(14), PRF, 16.0, None, mul)
     ts(col(15), PRF, 1.0, None, add)
-    for n, c in (("wlu", 2), ("wcode", 3), ("wwin", 5)):
-        ts(r(n), r("qw"), col(1), col(c), eq_, mul)
-    cp(uv("lc"), f("q8"))
+    for n, c in (("wcode", 3), ("wwin", 5)):
+        ts(r(n), r("qw"), G16, col(c), eq_, mul)
+    ts(uv("lperm", 32), r("lf", 0, 32), col(14), None, add)
+    cp(uv("lc"), f("a32"))
     ts(uv("lr"), f("q8"), 0.0, PRF, mul, add)
-    ts(uv("lperm"), f("q8"), col(14), None, add)
-    ts(f("k1"), f("q8"), col(14), 240.0, sub, add)
-    cp(uv("lrev"), f("k1"))
-    ts(f("k2"), f("q8"), -1.0, 15.0, mul, add)
-    ts(uv("lq"), f("k2"), col(14), None, add)
+    ts(uv("lrev"), f("q8"), 240.0, col(14), add, sub)
     cp(r("coff"), ind(r("csk"), uv("lperm")))
     cp(r("ci"), r("coff"))
-    ts(r("rst"), r("r16"), 0.0, None, gt)
-    ts(r("rstb"), r("r16"), 0.0, None, gt)
     for oc in range(16):
         cp(r("ea", 256 * oc, 256 * oc + 256), (T.snk[:, :, 16 * oc:16 * oc + 16], [("snk", 0, 256)], 256))
-    ts(f("gi", 8), f("q8", 8), PGF, None, eq_)
-    ts(r("wy", 0, 8), f("gi", 8), col(15), None, mul)
-    cp(r("gib", 0, 8), f("gi", 8))
-    ms(f("one"), 1.0)
+    ts(r("gib", 0, 8), f("q8", 8), PGF, None, eq_)
+    ts(r("gib", 8, 16), f("q8", 8), PGF, -32.0, eq_, mul)
+    ts(r("gib", 16, 24), f("q8", 8), PGF, col(15), eq_, mul)
+    ts(r("gib", 24, 32), f("q8", 8), PGF, -1.0, eq_, mul)
+    ts(r("gib", 32, 40), f("q8", 8), PGF, col(2), eq_, mul)
+    ts(r("gib", 40, 48), f("q8", 8), PGF, col(6), eq_, mul)
+    ts(r("gib", 48, 56), f("q8", 8), PGF, -8192.0, eq_, mul)
     ts(r("diag"), r("r16"), PRF, None, eq_)
     ts(r("blk"), r("qb"), PGF, None, eq_)
+    ts(r("nblk"), r("qb"), PGF, -1.0, eq_, mul)
     ts(r("blkf"), r("qb"), PGF, None, eq_)
-    ts(r("blkh"), r("qb"), PGF, 65536.0, eq_, mul)
-    tt(r("idf"), r("blkf"), r("diag", 0, 128), mul)
-    cp(r("id_"), r("idf"))
-    ts(r("nid_"), r("idf"), -1.0, None, mul)
-    ts(r("f1", 0, 128), r("r16", 0, 128), PRF, -1.0, gt, add)
-    tt(r("f1", 0, 128), r("f1", 0, 128), r("blkf"), mul)
-    ts(r("f1", 128, 256), r("idf"), -64.0, None, mul)
-    tt(r("mix"), r("f1", 0, 128), r("f1", 128, 256), add)
-    ts(r("f1", 128, 256), r("r16", 0, 128), 936.0, None, add)
-    tt(r("f1", 0, 128), r("f1", 128, 256), r("blkf"), mul)
-    ts(r("iotas"), r("f1", 0, 128), -1000.0, None, add)
-    ts(f("j16"), f("q8"), 16.0, PRF, mul, add)
-    ts(f("sent"), f("j16"), float(NV), None, add)
-    ts(f("home"), f("j16"), 1.0, None, add)
-    for t in range(STEPS):
-        ts(f("own%d" % t), f("home"), 512.0 * (t + 1), None, add)
+    lin(r("blkh"), r("blkf"), 65536.0)
+    keep(r("idf"), r("blkf"), [[-1, 128]], eq_, 0.0, 1)
+    keep(r("id_"), r("blk"), [[-1, 128]], eq_, 0.0, 1)
+    keep(r("nid_"), r("nblk"), [[-1, 128]], eq_, 0.0, 1)
+    keep(r("mix"), r("nblk"), [[-1, 128]], ge, 0.0, 1)
+    keep(r("mix"), r("mix"), [[-1, 128]], ALU.not_equal, -65.0, 1)
+    ts(r("idn"), r("id_"), LOW + NEW, None, mul)
+    ts(r("blk2"), r("blk"), 2.0, None, mul)
+    if "s" in WAYS[1]:
+        ts(col(10), iv("pr", 1), 32.0 * WAYS[1].count("s"), None, ge)
+        ts(col(11), col(10), -1.0, None, add)
+        ts(r("idm"), r("id_"), col(10), None, mul)
+        ts(r("idc"), r("id_"), col(11), None, mul)
+    tt(r("iotas"), r("iotas"), r("blk"), mul)
+    ts(r("oh", 0, 128), r("blk"), -0.5, 0.5, mul, add)
+    tt(r("iotas"), r("iotas"), r("oh", 0, 128), add)
+    ts(f("home"), f("q8"), 16.0, col(15), mul, add)
+    ts(r("own"), r("own"), PRF, None, add)
     ts(f("k1"), f("q8"), PRF, 1.0, gt, add)
-    op("v", lambda: g.vector.tensor_reduce(out=f("k3", 1)[0], in_=f("k1")[0], axis=AxisListType.X, op=mul), [f("k3", 1)], [f("k1")], 0.09)
-    ts(r("blkw"), r("blkf"), f("k3", 1), None, mul)
-    ts(f("k3", 1, 1), f("k3", 1), 2.0, None, mul)
-    ts(r("thd"), r("diag"), -1.0e9, 1.0e9, mul, add)
+    op("v", lambda: g.vector.tensor_reduce(out=f("k3", 1)[0], in_=f("k1")[0], axis=AxisListType.X, op=mul), [f("k3", 1)], [f("k1")], 0.1)
+    lin(r("blkw"), r("blkf"), f("k3", 1))
+    lin(f("k3", 1, 1), f("k3", 1), 2.0)
+    lin(r("thd"), r("diag"), -1.0e9, 1.0e9)
     ts(r("thd"), r("thd"), f("k3", 1, 1), None, mx)
-    ts(r("ti"), r("ci"), 7, None, shr)
+    ts(r("ti"), r("ci"), NV - 128, None, band)
     ts(r("tj"), r("ci"), 127, None, band)
-    ts(r("chl", 0, 512, 2), r("ti"), 128.0, 256.0, mul, add)
-    cp(r("chl", 1, 512, 2), r("tj"))
-    act(r("big", DUM, VO), r("zero", 0, 256), ACT.Copy)
-    for n in ("xab", "xw", "ldw"):
-        act(r(n), r("zero", 0, T[n].shape[-1]), ACT.Copy)
-    ms(r("rst4"), 1.0)
-    ms(r("rst4", 0, 64, 4), 0.0)
-    ms(r("tla", 64, 80), 0)
-    ms(r("tlb", 64, 80), 0)
+    ts(r("chl", 0, 512, 2), r("ti"), 256.0, None, add)
+    lin(r("f3"), r("r16"), -16.0)
+    tt(r("chl", 1, 512, 2), r("tj"), r("f3"), add)
 
     cp(r("cr"), ind(r("csk"), uv("lrev")))
     cp(r("hr"), ind(r("hok"), uv("lrev")))
     ts(r("un"), r("hr"), -1.0, 1.0, mul, add)
-    scan(P2, r("rst"), r("un"), mul, add)
-    cp(f("u"), r("b6", 15, 256, 16))
-    ts(f("fulls"), f("u"), 0.0, 1.0, eq_, add)
-    ts(r("f2"), r("hr"), 99.0, None, mul)
-    tt(r("f2"), P2, r("f2"), mx)
-    cp(r("qk"), ind(r("f2"), uv("lq")))
+    ts(r("s1"), r("hr"), -18.0, 17.0, mul, add)
+    scan(r("cs2"), r("rst"), r("un"), mul, add)
+    ts(f("w"), tl("cs2"), -1.0, 17.0, mul, add)
+    ts(r("w1b"), tl("cs2"), -1.0, 17.0, mul, add)
+    lin(r("cg"), r("cs2"), -1.0, 17.0)
+    tt(r("pd"), r("s1"), r("cg"), mn)
+    act(r("qk"), ind(r("pd"), uv("lq")), ACT.Copy)
     tt(r("qk"), r("qk"), r("q16"), sub)
     ms(hd("hr"), 0.0)
     ms(hd("un"), 1.0)
     tt(r("f2"), r("un"), r("cr"), mul)
     for n in range(4):
-        scan(P2, r("hr"), r("f2"), mul, add)
+        scan(P0, r("hr"), r("f2"), mul, add)
         cp(r("tla", n, 64, 4), r("b6", 15, 256, 16))
         if n < 3:
             tt(r("f2", 1, 256), r("b6", 0, 255), r("un", 1, 256), mul)
             cp(hd("f2"), hd("cr"))
     cp(uv("xu"), r("tla", 0, 64, 4))
-    cp(f("cura"), f("home"))
+    act(r("sa", 2, 66, 4), f("home"), ACT.Copy)
     ts(iv("nw"), iv("wk"), -256.0, 3840.0, mul, add)
     for t in range(STEPS):
         ts(iv("sl%d" % t), iv("nw"), t, 256, shr, band)
-    tt(f("c2"), f("home"), iv("sl0"), add)
-    cp(uv("cua"), f("c2"))
-    ms(f("thr"), 0.0)
+    cp(r("slf"), iv("sl0", 64))
+    tt(f("k2"), f("home"), iv("sl0"), add)
+    cp(uv("cua"), f("k2"))
 
     V = r("big", VO, VO + NV)
     VF = r("big", VO, BIGW)
@@ -467,25 +527,23 @@ def rank_program(g, core, T, topo):
     def mat(w, m):
         return r(w, 15 - m, 143 - m)
 
-    def sums(bk, w, src, base, a, first=True):
+    def sums(bk, w, src, a, first=True):
         for m in range(16):
-            mm(r(bk, 64 * a, 64 * a + 64), mat(w, m), r(src, base + 1024 * a + m, base + 1024 * a + 1024, 16), first and m == 0, m == 15)
+            mm(r(bk, 64 * a, 64 * a + 64), mat(w, m), r(src, 1024 * a + m, 1024 * a + 1024, 16), first and m == 0, m == 15)
 
     def pick(out, w, src, n):
         for m in range(16):
             mm(out, mat(w, m), r(src, m, n, 16), m == 0, m == 15)
 
     def halves(a, t):
-        if a < NVC[t]:
-            mm(r("b1", 64 * a, 64 * a + 64), r("idf"), r("ue", 64 * a, 64 * a + 64), True, False)
-        sums("b1", "wlu", "diff", 0, a, a >= NVC[t])
+        bk, c = ("b0", "b7")[a], 128 * a
+        act(r("aa", c, c + 128), r(bk, 128, 256), ACT.Copy)
+        tt(r("am", c, c + 128), r(bk, 256, 384), r("aa", c, c + 128), mul)
 
     def steps_of(out, head):
-        act(r("am"), r("b1", 0, 256), ACT.Identity, bias=8388608.0, scale=1.0 / 4096)
-        act(r("an"), r("am"), ACT.Identity, bias=8388608.0 * 4096, scale=-4096.0)
-        act(r("aa"), r("am"), ACT.Identity, bias=-8388608.0)
-        tt(P0, r("b1", 0, 256), r("an"), add)
-        tt(r("ti"), P0, r("aa"), mul)
+        for h in range(2):
+            mm(r("b1", 128 * h, 128 * h + 128), r("am", 128 * h, 128 * h + 128), r("idf"), True, True)
+        cp(r("ti"), r("b1", 0, 256))
         ts(r("tj"), r("ti"), 3, 511, shr, band)
         ts(iv("h0"), hd("ti"), 3, 8191, shr, band)
         ts(r(out), r("tj"), 1.0, None, add)
@@ -494,74 +552,117 @@ def rank_program(g, core, T, topo):
         else:
             ts(hd(out), iv("h0"), head, None, add)
 
+    def first_keys():
+        for h in range(2):
+            bk, c = ("b4", "b5")[h], 128 * h
+            for m in range(16):
+                mm(r(bk, m, 384, 16), r("ea", 2048 * h + m, 2048 * h + 2048, 16), r("gib", 24, 48), True, True)
+            cp(r("ehi", 384 * h, 384 * h + 384), r(bk, 0, 384))
+            tt(r("elo", 384 * h, 384 * h + 384), r(bk, 0, 384), r("ehi", 384 * h, 384 * h + 384), sub)
+            cp(r("aa", c, c + 128), r(bk, 128, 256))
+            tt(r("am", c, c + 128), r(bk, 256, 384), r("aa", c, c + 128), mul)
+        steps_of("f1", -LOW)
+        scan(r("ka"), r("rst"), r("f1"), mul, add)
+
     def judge(a, t):
         win = V if t < 2 else VF
-        c = 1024 * a
-        if a < NVC[t]:
-            tt(r("diff", c, c + 1024), ind(win, r("coff", 64 * a, 64 * a + 64)), r("ea", c, c + 1024), sub)
-            act(r("absd", c, c + 1024), r("diff", c, c + 1024), ACT.Abs)
+        d, e, out, cells = (r(n, 512 * a, 512 * a + 512) for n in ("diff", "ea", "absd", "diff"))
+        cells = ind(win, r("coff", 32 * a, 32 * a + 32))
+        way = WAYS[t][a]
+        if way == "s":
+            bk = r("b%d" % (2 + a % 2))
+            act(d, cells, ACT.Copy)
+            mm(bk, r("id_"), d, True, False)
+            mm(bk, r("nid_"), e, False, True)
+            act(out, bk, ACT.Relu, scale=2.0)
+            return
+        tt(d, cells, e, sub)
+        if way == "R":
+            act(out, d, ACT.Relu, scale=2.0)
         else:
-            act(r("diff", c, c + 1024), ind(win, r("coff", 64 * a, 64 * a + 64)), ACT.Copy)
-            for h, bk in ((0, "b2"), (1, "b3")):
-                d = c + 512 * h
-                mm(r(bk), r("id_"), r("diff", d, d + 512), True, False)
-                mm(r(bk), r("nid_"), r("ea", d, d + 512), False, True)
-                act(r("absd", d, d + 512), r(bk), ACT.Abs)
+            ts(out, d, 0.0, 2.0, mx, mul)
 
     def far(h, t):
         bk = ("b0", "b7")[h]
+        plain = "s" in WAYS[t][4 * h:4 * h + 4]
+        for e in ("ehi", "elo"):
+            mm(r(bk, 128, 384), r("idm" if plain else "id_"), r(e, 384 * h + 128, 384 * h + 384), e == "ehi", False)
+            if plain or e == "ehi":
+                mm(r(bk, 0, 128), r("idc" if plain else "none"), r(e, 384 * h, 384 * h + 128), False, False)
         for m in range(16):
-            mm(r(bk, m, 128, 16), r("absd", 2048 * h + m, 2048 * h + 2048, 16), r("gib", 0, 8), True, True)
-        ts(r("yb", 128 * h, 128 * h + 128), r(bk, 0, 128), 320.0, None, gt)
+            mm(r(bk, m, 384, 16), r("diff", 2048 * h + m, 2048 * h + 2048, 16), r("gib", 24, 48), False, False)
+        for m in range(16):
+            mm(r(bk, m, 128, 16), r("absd", 2048 * h + m, 2048 * h + 2048, 16), r("gib", 0, 8), False, m == 15)
+        ts(r("yb", 128 * h, 128 * h + 128), r(bk, 0, 128), -320.0, 0.0, add, mx)
         if t in FTHR:
-            act(r("zb", 128 * h, 128 * h + 128), r(bk, 0, 128), ACT.Relu, bias=-FTHR[t])
-        mm(r("b0", 256 + 8 * h, 264 + 8 * h), r("yb", 128 * h, 128 * h + 128), r("gib", 0, 8), True, t not in FTHR)
-        if t in FTHR:
-            mm(r("b0", 256 + 8 * h, 264 + 8 * h), r("zb", 128 * h, 128 * h + 128), r("gib", 0, 8), False, True)
+            ts(r("zb", 128 * h, 128 * h + 128), r(bk, 0, 128), -FTHR[t], 0.0, add, mx)
+
+    def verdicts(t):
+        out = r("b2", 256, 272)
+        mm(out, r("id_"), r("w1b"), True, False)
+        for h in range(2):
+            mm(r("b2", 256 + 8 * h, 264 + 8 * h), r("yb", 128 * h, 128 * h + 128), r("gib", 8, 16), False, t == 0 and h == 1)
+            if t in FTHR:
+                mm(r("b2", 256 + 8 * h, 264 + 8 * h), r("zb", 128 * h, 128 * h + 128), r("gib", 48, 56), False, False)
+        if t:
+            mm(out, r("id_"), r("winb"), False, True)
+        ts(r("sf%d" % t), out, 0.0, None, mx)
+        tell(t, "lsf%d" % t, "sf%d" % t, "rsf%d" % t, "qsf%d" % t)
+        ts(f("l1"), r("sf%d" % t), -1.0, 34.0, mul, add)
+        ts(f("l2"), r("sf%d" % t), 0.0, 1.0e9, eq_, mul)
+
+    def slot(i):
+        return r("pt", i, 128, 8)
 
     def holders(t):
         if t == 0:
             act(r("lg", 0, 256), ind(LK, uv("xu")), ACT.Relu, bias=col(8), scale=col(7))
             pick(r("b4", 0, 16), "wwin", "lg", 256)
-            ts(f("byc"), r("b4", 0, 16), HM, None, mul)
-        else:
-            ts(iv("oi"), iv("hi"), 511, None, band)
-            cp(uv("ou"), iv("oi"))
-            act(r("ldg"), ind(r("ldw"), uv("ou")), ACT.Copy)
-            pick(r("b4", 32, 48), "wcode", "ldg", 256)
-            ts(iv("hs"), iv("hi"), 9, None, shr)
-            tt(f("vs"), r("b4", 32, 48), iv("hs"), ALU.is_le)
-            ts(f("byc"), iv("oi"), HM, None, mul)
-            tt(f("byc"), f("byc"), f("vs"), mul)
-        tt(f("p"), f("byc"), r("tla", 0, 64, 4), add)
+            ts(slot(3), r("b4", 0, 16), HM, None, mul)
+            cp(slot(4), r("tla", 0, 64, 4))
+            return
+        act(r("lgo"), ind(LK, uv("xu", 32)), ACT.Relu, bias=col(8), scale=col(7))
+        pick(r("b1", 256, 288), "wwin", "lgo", 512)
+        cp(iv("hi", 32), r("b1", 256, 288))
+        ts(iv("oi", 32), iv("hi", 32), 511, None, band)
+        cp(uv("ou", 32), iv("oi", 32))
+        act(r("ldg"), ind(r("ldw"), uv("ou", 32)), ACT.Copy)
+        pick(r("b1", 288, 320), "wcode", "ldg", 512)
+        tt(f("vs", 32), r("b1", 288, 320), iv("hi", 32), le)
+        tt(f("vs", 32), iv("oi", 32), f("vs", 32), mul)
+        lin(f("hold", 32), f("vs", 32), HM)
+        lin(f("nhold"), f("vs"), -HM)
 
     def decide(t):
-        tt(f("x"), r("sf%d" % t), r("lsf%d" % t), mul)
-        ts(r("rdy"), f("x"), 4.0, None, eq_)
+        mm(r("b3", 0, 32), r("id_"), r("kc"), True, False)
+        tt(r("rdy"), r("lsf%d" % t), f("l1"), eq_)
+        tt(r("ab"), r("lsf%d" % t), f("l2"), le)
         scan(r("rs"), f("one"), r("rdy"), mul, add)
+        mm(r("b2", 16, 17), r("blk"), r("rs", 15, 16), True, True)
         mm(r("b2", 0, 16), r("mix"), r("rdy"), True, False)
         mm(r("b2", 0, 16), r("blk"), r("rs"), False, True)
-        ts(hd("xab"), f("x"), 0.0, LOW + NEW, eq_, mul)
+        ts(slot(5), r("ab"), GONE, None, mul)
+        ts(slot(6), r("b2", 0, 16), -48.0, GONE, lt, mul)
         for oc in range(16):
             ts(r("oh", 128 * oc, 128 * oc + 128), r("iotas"), r("b2", oc, oc + 1), None, eq_)
-            mm(r("b3", 0, 32), r("oh", 128 * oc, 128 * oc + 128), r("chl", 32 * oc, 32 * oc + 32), oc == 0, oc == 15)
+            mm(r("b3", 0, 32), r("oh", 128 * oc, 128 * oc + 128), r("chl", 32 * oc, 32 * oc + 32), False, oc == 15)
+        ts(col(1), r("b2", 16, 17), PRF, PRF, le, mul)
         ts(f("cm"), r("b2", 0, 16), -48.0, LOWER + NEW, lt, mul)
-        tt(f("l1"), r("b3", 0, 32, 2), f("j16"), mx)
-        tt(f("l2"), r("b3", 1, 32, 2), f("l1"), add)
-        cp(uv("listu"), f("l2"))
-        cp(r("snd%d" % t), ind(VD, uv("listu")))
+        scan(r("l32"), r("alt"), r("b3", 0, 32), mul, add)
+        ts(uv("listu"), r("l32", 1, 32, 2), col(1), None, add)
+        act(r("snd%d" % t), ind(VD, uv("listu")), ACT.Copy)
         tell(t, "lnd%d" % t, "snd%d" % t, "rdd%d" % t, "qdd%d" % t)
-        tt(f("dec"), hd("xab"), f("cm"), add)
-        ts(f("dec"), f("dec"), 0.0, GONE, gt, mul)
+        tt(f("dec"), slot(5), slot(6), mx)
 
     def keys(t):
         lk = "lkc%d" % t
-        scan(P0, r("rst"), r("xab"), mul, add)
-        tt(P1, P0, r("ka"), add)
-        tt(r("s1"), P1, r(("ci", "st", "st", "cf")[t]), mx)
+        mm(r("b7", 0, 256), r("idf"), r("ka"), True, False)
+        for k in range(16):
+            mm(r("b7", k, 256, 16), r("idn"), r("ab"), False, k == 15)
+        tt(r("s1"), r("b7", 0, 256), r(("ci", "st", "st", "cf")[t]), mx)
         tt(hd(lk), hd(lk), f("cm"), add)
-        scan(P2, r("rst"), r(lk), mul, add)
-        tt(RES, P2, r("s1"), mx)
+        scan(P0, r("rst"), r(lk), mul, add)
+        tt(RES, P0, r("s1"), mx)
         if t == STEPS - 1:
             ts(r("cf"), RES, NV - 1, None, band)
             return
@@ -572,38 +673,48 @@ def rank_program(g, core, T, topo):
             tt(r("st"), P1, r("cf"), add)
 
     def flags(t):
-        mm(r("b2", 0, 256), r("id_"), r("lnd%d" % t), True, False)
-        mm(r("b2", 0, 256), r("nid_"), r("snd%d" % t), False, True)
-        act(r("fa"), r("b2", 0, 256), ACT.Abs)
-        mm(r("b3", 0, 256), r("blk"), r("fa"), True, True)
-        act(r("fb"), r("b3", 0, 256), ACT.Sign, bias=-320.5)
-        act(r("fv"), r("fb"), ACT.Identity, bias=FLAG[t] / 2, scale=FLAG[t] / 2)
+        new, old = r("lnd%d" % t), r("snd%d" % t)
+        tt(r("fa"), new, old, mx)
+        mm(r("b3", 0, 256), r("nblk"), old, True, False)
+        mm(r("b3", 0, 256), r("nblk"), new, False, False)
+        mm(r("b3", 0, 256), r("blk2"), r("fa"), False, True)
+        ts(r("fv"), r("b3", 0, 256), 320.0, FLAG[t], gt, mul)
         cp(ind(FD, uv("listu")), r("fv"))
 
     def lanes(t):
-        cur, curn = ("cura", "curb") if t % 2 == 0 else ("curb", "cura")
+        cur, curn = ("sa", "sb") if t % 2 == 0 else ("sb", "sa")
         cu, cun = ("cua", "cub") if t % 2 == 0 else ("cub", "cua")
         last = t == STEPS - 1
-        act(r("cv"), ind(r("iw"), uv(cu)), ACT.Identity, bias=col(10 + t), scale=col(9))
-        mm(r("b5", 0, 256), r("zero", 0, 128), r("zero", 0, 256), True, False)
-        tt(f("pm"), f("p"), f("dec"), mx)
-        tt(r("pd"), ind(f("pm"), uv("lc")), r("diag"), mul)
+        act(r("cv"), ind(r("iw"), uv(cu)), ACT.Identity, bias=f("clm", 1, t), scale=col(9))
+        mm(r("b5", 0, 256), r("none"), r("rstb"), True, False)
+        tt(r(cur, 1, 65, 4), f("home"), r(cur, 2, 66, 4), sub)
+        act(r(cur, 4, 68, 4), r("slf", 16 * ((t + 1) % STEPS), 16 * ((t + 1) % STEPS) + 16), ACT.Copy)
+        scan(r("po"), r("pf"), r("pt"), mul, add)
+        tt(r("pd"), ind(r("po"), uv("lc")), r("diag"), mul)
         mm(r("b4", 0, 256), r("blkf"), r("pd"), True, True)
         act(r("pw", 1, 257), r("b4", 0, 256), ACT.Copy)
-        act(r("pw", 257, 513), r("b4", 0, 256), ACT.Identity, bias=512 * HM, scale=1.0 / 512)
+        lin(r("pw", 257, 513), r("b4", 0, 256), 1.0 / 512, 512 * HM)
         if not last:
             act(r("b4", 256, 512), r("b4", 0, 256), ACT.Relu, bias=-1.0, scale=(t + 2) / GONE)
             tt(r("ldw", 1, 257), r("b4", 256, 512), r("ldw", 1, 257), mx)
-        ts(r("tlb", 0, 64), RES4, NV - 1 + int(NEW), None, band)
-        ts(r("tla", 0, 64), r("tla", 0, 64), NEW / 2, None, add)
-        tt(r("tlb", 0, 64), r("tlb", 0, 64), r("tla", 0, 64), mx)
-        ts(r("tlb", 0, 64), r("tlb", 0, 64), NV - 1, None, band)
-        cp(uv("xu"), r("tlb", 0, 64, 4))
-        if not last:
+            lin(r("tla"), r("tla"), None, NEW / 2)
+            ts(r("tlb", 0, 64), RES4, NV - 1 + int(NEW), None, band)
+            tt(r("tlb", 0, 64), r("tlb", 0, 64), r("tla"), mx)
+            ts(r("tlb", 0, 64), r("tlb", 0, 64), NV - 1, None, band)
+            cp(uv("xu"), r("tlb", 0, 64, 4))
             cp(uv("xv"), r("tlb", 1, 64, 4))
             tt(r("td"), r("tlb", 1, 65), r("tlb", 0, 64), sub)
-        tt(f("u1"), f("u"), f("dec"), mx)
-        ts(f("u1"), f("u1"), 16.0, None, mn)
+            tt(slot(1), r("tlb", 1, 65, 4), r("tlb", 0, 64, 4), sub)
+            cp(slot(4), r("tlb", 0, 64, 4))
+            holders(t + 1)
+        else:
+            cp(uv("xu"), r("tla", 0, 64, 4))
+        ts(f("nd"), f("dec"), 0.0, GONE, eq_, mul)
+        ts(f("nd"), f("nd"), ANEW + 1, None, mx)
+        tt(f("w1"), f("w"), f("dec"), mx)
+        tt(f("w1"), f("w1"), f("nd"), mn)
+        if not last:
+            cp(r("w1b"), f("w1"))
         tt(r("cg"), ind(r("pw"), uv(cu)), r("diag"), mul)
         cp(r("ku"), ind(r("pw"), uv(cu)))
         scan(r("cs2"), r("rst"), r("cg"), mul, add)
@@ -615,93 +726,79 @@ def rank_program(g, core, T, topo):
                 mm(r("b5", 16 * oc + 16, 256), r("blkh"), (T.eq[:, oc, 16:n], [("eq", 272 * oc, 272 * oc + n)], n - 16), False, False)
         mm(r("b5", 0, 256), r("blkw"), (T.eq[:, :, 0:16], [("eq", 0, 272 * 16)], 256), False, True)
         tt(f("k1"), PL, f("sent"), mn)
-        tt(f("k2"), f("sent"), f("k1"), sub)
         tt(r("lq"), r("b5", 0, 256), r("thd"), ge)
         scan(r("ls"), r("rstb"), r("lq"), mul, add)
-        tt(f("k2"), f("k2"), tl("ls"), mul)
-        tt(f("k3"), f("k1"), f("k2"), add)
+        tt(f("k2"), f("sent"), tl("ls"), mul)
+        tt(f("k3"), f("k1"), f("k2"), mx)
         cp(uv("offu"), f("k3"))
         act(ind(r("lock"), uv("offu")), r("cv"), ACT.Silu)
         n = 16 if last else 32
         act(r("lg", 0, 16 * n), ind(LK, uv("xu", n)), ACT.Relu, bias=col(8), scale=col(7))
         pick(r("b4", 0, n), "wwin", "lg", 16 * n)
-        tt(r("xw", 0, 64, 4), r("b4", 0, 16), f("own%d" % t), eq_)
-        tt(f("u"), f("u1"), r("xw", 0, 64, 4), sub)
         if not last:
-            ts(f("fulls"), f("u"), 0.0, 1.0, eq_, add)
+            tt(r("winb"), r("b4", 0, 16), r("own", 16 * t, 16 * t + 16), eq_)
+            ts(f("a32", 32), r("b4", 0, 32), -512.0 * (t + 1), HM, add, mul)
+            ts(f("na"), r("b4", 0, 16), -512.0 * (t + 1), -HM, add, mul)
+            tt(r("pf", 3, 128, 8), r("b4", 0, 16), r("own", 16 * t, 16 * t + 16), eq_)
+            tt(slot(0), f("a32", 16, 16), f("hold", 16, 16), mx)
+            tt(slot(3), f("a32"), f("hold"), mx)
+            tt(slot(2), f("na"), f("nhold"), mn)
+        tt(r("xw", 0, 64, 4), r("b4", 0, 16), r("own", 16 * t, 16 * t + 16), eq_)
+        tt(f("w"), f("w1"), r("xw", 0, 64, 4), add)
+        if not last:
             scan(r("wx"), r("rst4"), r("xw"), mul, add)
             tt(r("td"), r("td"), r("wx"), mul)
-            tt(r("tla", 0, 64), r("tlb", 0, 64), r("td"), add)
-            cp(f("h1"), r("b4", 0, 16))
-            tt(f("h2"), r("b4", 16, 32), f("h1"), sub)
-            tt(f("h2"), f("h2"), r("xw", 0, 64, 4), mul)
-            tt(iv("hi"), f("h2"), f("h1"), add)
+            tt(r("tla"), r("tlb", 0, 64), r("td"), add)
         ts(iv("pi"), PL, 1024 * HM, None, mn)
         ts(iv("by"), iv("pi"), 14, 511, shr, band)
-        ts(f("gm"), PL, 1024 * HM, None, ge)
-        tt(f("d2"), f("home"), f(cur), sub)
-        tt(f("d2"), f("d2"), f("gm"), mul)
-        tt(f("c1"), f(cur), f("d2"), add)
-        ts(f("z"), iv("by"), 0.0, None, eq_)
-        tt(f("c1"), f("c1"), f("z"), mul)
-        tt(f(curn), f("c1"), iv("by"), mx)
+        cp(r(cur, 3, 67, 4), iv("by"))
+        ts(r("sm", 1, 64, 4), PL, 1024 * HM, None, ge)
+        act(r("sm", 2, 64, 4), r(cur, 3, 67, 4), ACT.Relu, bias=1.0, scale=-1.0)
+        scan(r(curn, 0, 64), r("sm"), r(cur, 1, 65), mul, add)
         if not last:
-            tt(f("c2"), f(curn), iv("sl%d" % (t + 1)), add)
-            cp(uv(cun), f("c2"))
+            cp(uv(cun), r(curn, 3, 64, 4))
 
-    for a in range(4):
-        sums("b1", "wlu", "ea", 0, a)
-    act(r("ue"), r("b1", 0, 256), ACT.Copy)
-    steps_of("f1", -LOW)
-    scan(r("ka"), r("rst"), r("f1"), mul, add)
     for t in range(STEPS):
         last = t == STEPS - 1
-        for a in list(range(NVC[t], 4)) + list(range(NVC[t])):
+        for a in range(8):
             judge(a, t)
+        if t == 0:
+            first_keys()
         for h in range(2):
             far(h, t)
-        tt(f("nb"), r("b0", 256, 272), f("thr"), ALU.is_le)
-        tt(r("sf%d" % t), f("nb"), f("fulls"), mul)
-        tell(t, "lsf%d" % t, "sf%d" % t, "rsf%d" % t, "qsf%d" % t)
-        for a in range(4):
+        verdicts(t)
+        for a in range(2):
             halves(a, t)
         steps_of("skg%d" % t, f("cls") if t else -LOWER)
         tell(t, "lkc%d" % t, "skg%d" % t, "rkc%d" % t, "qkc%d" % t)
         if t:
-            scan(P2, r("rst"), r("skg%d" % t), mul, add)
-            tt(r("ka"), P2, r("ka"), mx)
-        holders(t)
+            scan(P0, r("rst"), r("skg%d" % t), mul, add)
+            tt(r("ka"), P0, r("ka"), mx)
+        if t == 0:
+            holders(0)
         decide(t)
         if t == 0:
-            noflags(4, 8)
+            noflags(3, 8, [r("lnd0")])
         keys(t)
         cp(ind(VD, uv("listu")), r("lnd%d" % t))
         if t in FLAG:
             flags(t)
         if not last:
-            ts(f("cls"), f("dec"), (32768.0 * (t + 1) - LOW + LOWER) / GONE, -LOWER, mul, add)
-        if t == 0:
-            cp(f("thr"), f("dec"))
-            cp(f("ev1"), f("dec"))
-        else:
-            if not last:
-                ts(f("thr"), f("ev1"), 100.0, None, mn)
-                tt(f("thr"), f("thr"), f("dec"), mx)
-            tt(f("ev1"), f("ev1"), f("dec"), add)
+            lin(f("cls"), f("dec"), (32768.0 * (t + 1) - LOW + LOWER) / GONE, -LOWER)
         if last:
-            cp(r("yco"), ind(r("cf"), uv("lperm")))
-            dma("y", ext(T.yc[:]), r("yco"), "oyc", 2.5)
-            ts(f("iso"), f("ev1"), 0.0, None, eq_)
-            tt(r("f1"), ind(f("iso"), uv("lr")), r("qk"), mul)
-            tt(r("f1"), r("f1"), r("q16"), add)
+            cp(r("cr"), ind(r("cf"), uv("lperm")))
+            dma("y", ext(T.yc[:]), r("cr"), "oyc", 2.0)
             for i in range(64):
-                mm(r("b0", 8 * i, 8 * i + 8), r("big", VO + i, VO + NV, 64), r("wy", 0, 8), True, True)
+                mm(r("b0", 8 * i, 8 * i + 8), r("big", VO + i, VO + NV, 64), r("gib", 16, 24), True, True)
             for b in range(8):
                 act(r("yt", 64 * b, 64 * b + 64), r("b0", b, 512, 8), ACT.Copy)
-                dma("ys"[b % 2], ext(T.ys[b]), r("yt", 64 * b, 64 * b + 64), "oys%d" % b, 2.5)
+                dma("ys"[b % 2], ext(T.ys[b]), r("yt", 64 * b, 64 * b + 64), "oys%d" % b, 2.0)
         lanes(t)
-    ts(f("yl"), f("cura"), -1.0, None, add)
-    dma("y", ext(T.yl[:]), f("yl"), "oyl", 2.5)
-    tt(r("yho"), ind(f("u"), uv("lr")), r("f1"), lt)
-    dma("y", ext(T.yh[:]), r("yho"), "oyh", 2.5)
+    ts(f("iso"), f("w1"), ANEW, None, lt)
+    tt(r("f1"), ind(f("iso"), uv("lr")), r("qk"), mul)
+    tt(r("f1"), r("f1"), r("q16"), add)
+    ts(f("yl"), r("sa", 2, 66, 4), -1.0, None, add)
+    dma("y", ext(T.yl[:]), f("yl"), "oyl", 2.0)
+    tt(r("hr"), ind(f("w"), uv("lr")), r("f1"), gt)
+    dma("y", ext(T.yh[:]), r("hr"), "oyh", 2.0)
     issue()

@@ -8,74 +8,77 @@ FB = 16384
 DUM, VO = 0, 256
 FO = VO + FB
 BIGW = FO + NV
-LW = NV + 4096
+LW = NV + 512
 NEW = 131072.0
 LOW, LOWER = 1048576.0, 2097152.0
 HM = 16384.0
 GONE = 8589934592.0
+ANEW = 8388608.0
 FLAG = {1: 768.0, 2: 2048.0}
 FTHR = {2: 6000.0, 3: 20000.0}
-NVC = (4, 3, 3, 3)
+NS = 2
+CUTS = (512, 512, 512, 512, 1024, 768, 256)
+PARTS = [(0, 2048), (2048, 3840), (3840, 4096)]
+LA = 8
+NF = 3
+KEYP = ()
+KU = 0
+YV = (0, 1, 2)
+LINV = 128
+SAME = 0
 WAKE = 0.15
-CY = 0.00083
-FIX = 0.0
+CY = 0.00095
+AFIX, FLY, FLYB = 80 * CY, 1.3, 0.0005
+ROUNDS = 30
+TRIES = 2500
+SHAKE, PUSH, MARK = 0.1, 2.5, 0.5
 ORDER = []
-ROUNDS = 6
-FLY, FLYB = 1.3, 0.002
-WAYS = ("RRRRRRrr", "sRRRRRrr", "sRRRRRrr", "sRRRRRrr")
-ANEW = 8388608.0
-URGE = {"rsf": 4.0}
 
 SCRATCH = {
     "big": ("sbuf", [128, BIGW], "bfloat16"),
-    "snk": ("sbuf", [128, 16, 256], "bfloat16"),
     "ea": ("sbuf", [128, 4096], "bfloat16"),
     "diff": ("sbuf", [128, 4096], "bfloat16"),
     "absd": ("sbuf", [128, 4096], "bfloat16"),
     "lock": ("sbuf", [128, LW], "float32"),
-    "ehi": ("sbuf", [128, 768], "bfloat16"),
-    "elo": ("sbuf", [128, 768], "bfloat16"),
-    "pt": ("sbuf", [128, 128], "float32"),
-    "pf": ("sbuf", [128, 128], "float32"),
-    "po": ("sbuf", [128, 128], "float32"),
     "eq": ("sbuf", [128, 16, 272], "bfloat16"),
+    "ab3": ("sbuf", [128, 16, 16], "int32"),
     "res": ("sbuf", [128, 16, 16], "int32"),
     "oh": ("sbuf", [128, 2048], "bfloat16"),
-    "chl": ("sbuf", [128, 512], "bfloat16"),
     "kc": ("sbuf", [128, 32], "bfloat16"),
     "alt": ("sbuf", [128, 32], "float32"),
     "l32": ("sbuf", [128, 32], "float32"),
     "ldw": ("sbuf", [128, 272], "bfloat16"),
     "tla": ("sbuf", [128, 64], "float32"),
     "tlb": ("sbuf", [128, 80], "int32"),
+    "qw": ("sbuf", [128, 144], "float32"),
+    "gib": ("sbuf", [128, 80], "bfloat16"),
 }
 for _n in ("codes", "yt"):
     SCRATCH[_n] = ("sbuf", [128, 512], "float32")
 for _n in ("csk", "hok", "ci", "cf", "st", "ti", "tj"):
     SCRATCH[_n] = ("sbuf", [128, 256], "int32")
 for _n in ("r16", "dj", "rst", "diag", "thd", "ka", "cg", "cs2", "s1", "f1", "f2", "f3", "cr", "hr", "un", "qk", "q16", "pd",
-           "am", "aa", "cv"):
+           "am", "aa", "cv", "xab"):
     SCRATCH[_n] = ("sbuf", [128, 256], "float32")
 for _n in ("iw", "pw"):
     SCRATCH[_n] = ("sbuf", [128, 520], "float32")
-for _n in ("qb", "blkf", "idf"):
+for _n in ("qb", "blkf", "idf", "turn", "pt", "pf", "po"):
     SCRATCH[_n] = ("sbuf", [128, 128], "float32")
-MATS = ["blk", "nblk", "blkw", "blkh", "mix", "id_", "nid_", "idn", "blk2", "iotas", "idm", "idc", "none"]
-SCRATCH["mats"] = ("sbuf", [128, 128 * len(MATS)], "bfloat16")
-SCRATCH["qw"] = ("sbuf", [128, 144], "float32")
-for _n in ("wcode", "wwin"):
-    SCRATCH[_n] = ("sbuf", [128, 144], "bfloat16")
-for _n in ("lg", "lgo", "ldg"):
+for _n in ("blk", "nblk", "blkw", "blkh", "mix", "id_", "nid_", "iotas", "idm", "idn", "none"):
+    SCRATCH[_n] = ("sbuf", [128, 128], "bfloat16")
+SCRATCH["wwin"] = ("sbuf", [128, 144], "bfloat16")
+SCRATCH["lg"] = ("sbuf", [128, 1024], "bfloat16")
+for _n in ("lgo", "ehi", "elo", "chl"):
     SCRATCH[_n] = ("sbuf", [128, 512], "bfloat16")
-for _n in ("fa", "fv", "yb", "zb", "lq", "ls", "rstb"):
+for _n in ("yb", "zb"):
+    SCRATCH[_n] = ("sbuf", [128, 384], "bfloat16")
+for _n in ("fa", "fv", "lq", "ls", "rstb"):
     SCRATCH[_n] = ("sbuf", [128, 256], "bfloat16")
-for _n in ("xw", "wx", "td", "rst4", "sm", "lf", "own", "slf"):
-    SCRATCH[_n] = ("sbuf", [128, 64], "float32")
-for _n in ("sa", "sb"):
-    SCRATCH[_n] = ("sbuf", [128, 72], "float32")
+QUADS = ["xw", "wx", "td", "rst4", "sm", "lf", "own", "sa", "sb"]
+SCRATCH["quads"] = ("sbuf", [128, 72 * len(QUADS)], "float32")
 for _n in ("coff", "loff", "ku"):
     SCRATCH[_n] = ("sbuf", [128, 256], "uint16")
-FS = ["prf", "col", "clm", "gi", "q8", "sent", "home", "one", "cm", "dec", "cls", "vs", "vs2", "hold", "hold2", "nhold", "a32", "a33", "na",
+FS = ["prf", "col", "clm", "q8", "sent", "home", "one", "cm", "dec", "cls", "vs", "vs2", "hold", "hold2", "nhold", "a32", "a33", "na",
       "w", "w1", "nd", "k1", "k2", "k3", "l1", "l2", "yl", "iso"]
 IS = ["oi", "oi2", "hi", "hi2", "pi", "by", "sl0", "sl1", "sl2", "sl3", "nw", "h0", "pr", "pg", "wk"]
 US = ["xu", "xv", "ou", "ou2", "cua", "cub", "offu", "listu", "lc", "lr", "lrev", "lperm", "lq"]
@@ -84,7 +87,6 @@ SCRATCH["is_"] = ("sbuf", [128, 16 * len(IS)], "int32")
 SCRATCH["us"] = ("sbuf", [128, 16 * len(US)], "uint16")
 for _n in ("rdy", "rs", "ab", "w1b", "winb"):
     SCRATCH[_n] = ("sbuf", [128, 16], "bfloat16")
-SCRATCH["gib"] = ("sbuf", [128, 56], "bfloat16")
 for _t in range(STEPS):
     SCRATCH["sf%d" % _t] = ("sbuf", [128, 16], "bfloat16")
     SCRATCH["lsf%d" % _t] = ("sbuf", [128, 16], "bfloat16")
@@ -95,7 +97,7 @@ for _t in range(STEPS):
 for _b in range(8):
     SCRATCH["b%d" % _b] = ("psum", [128, 512], "float32")
 
-SEMAPHORES = ["c" + q for q in "vspgy"] + ["dcs", "dho", "dwk", "dsn", "dx0", "dx1", "oyc", "oyh", "oyl"] + ["oys%d" % _g for _g in range(8)]
+SEMAPHORES = ["c" + q for q in "vspgy"] + ["dcs", "dho", "dwk", "dsn", "ds2", "dx0", "dx1", "oyc", "oyh", "oyl"] + ["oys%d" % _g for _g in range(8)]
 for _t in range(STEPS):
     SEMAPHORES += [k + str(_t) for k in ("rsf", "rkc", "rdd", "qsf", "qkc", "qdd")]
 
@@ -109,14 +111,21 @@ def emitter(g, T):
     def isbank(n):
         return n[0] == "b" and n[1:].isdigit()
 
-    def before(q, rd, wr):
+    def meet(x, y):
+        return x[0] < y[1] and y[0] < x[1] and not (x[2] == y[2] > 1 and (x[0] - y[0]) % x[2])
+
+    def covers(x, y):
+        return x[0] <= y[0] and y[1] <= x[1] and (x[2] == 1 or (x[2] == y[2] and (x[0] - y[0]) % x[2] == 0))
+
+    def before(q, kind, rd, wr):
         evs = []
         for isw, regs in ((False, rd), (True, wr)):
-            for n, a, b in regs:
+            for n, x in regs:
                 if isbank(n):
                     evs += [e for q2, e in bank.get(n, {}).items() if q2 != q]
-                for lo, hi, w, q2, asyn, e in hist.get(n, ()):
-                    if lo < b and hi > a and (w or isw) and not (q2 == q == "p"):
+                for y, w, q2, asyn, e in hist.get(n, ()):
+                    inline = q2 == q and not asyn and kind == "op" and (q == "p" or (isw and SAME))
+                    if meet(x, y) and (w or isw) and not inline:
                         evs.append(e)
         todo = {}
         for s, v, ck in evs:
@@ -135,11 +144,11 @@ def emitter(g, T):
         ck[sem] = val
         e = (sem, val, ck)
         final[sem] = val
-        for n, a, b in wr:
-            hist[n] = [x for x in hist.get(n, ()) if not (a <= x[0] and x[1] <= b)] + [(a, b, True, q, asyn, e)]
-        for n, a, b in rd:
-            hist[n] = [x for x in hist.get(n, ()) if not (not x[2] and x[3] == q and not asyn and a <= x[0] and x[1] <= b)] + [(a, b, False, q, asyn, e)]
-        for n, a, b in rd + wr:
+        for n, x in wr:
+            hist[n] = [h for h in hist.get(n, ()) if not covers(x, h[0])] + [(x, True, q, asyn, e)]
+        for n, x in rd:
+            hist[n] = [h for h in hist.get(n, ()) if not (not h[1] and h[2] == q and not asyn and covers(x, h[0]))] + [(x, False, q, asyn, e)]
+        for n, x in rd + wr:
             if isbank(n):
                 bank.setdefault(n, {})[q] = e
 
@@ -151,59 +160,52 @@ def emitter(g, T):
         call = lambda: eng[q].dma_start(out=out[0], in_=in_[0]).then_inc(T.sem[sem], 16)
         prog.append((q, "dma", call, in_[1], out[1], 0.1, lat, sem))
 
-    def send(topo, core, dst, out, in_, rsem, lsem):
+    def send(topo, core, dst, out, in_, name, size):
         rid, pid, _s = topo.addr(dst)
         n = len(topo.engines(core, dst))
-        call = lambda: g.remote_dma(out[0], in_[0], T.sem[rsem], T.sem[lsem], pid, rid, topo.mask(core, dst))
-        prog.append(("g", "send", call, in_[1], [], 0.4, 1.8, (lsem, n)))
-        prog.append(("net", "land", None, in_[1], out[1], 0.0, FLY + in_[2] * FLYB, (rsem, n)))
+        call = lambda: g.remote_dma(out[0], in_[0], T.sem["r" + name], T.sem["q" + name], pid, rid, topo.mask(core, dst))
+        fly = FLY + size * FLYB + (1.5 if name == "sf0" else 0.0)
+        prog.append(("g", "send", call, in_[1], [], 0.4, 0.4 + fly, ("q" + name, n)))
+        prog.append(("net", "land", None, in_[1], out[1], 0.0, fly, ("r" + name, n)))
 
     def order():
         m = len(prog)
-        succ, npred, seen = [[] for _ in range(m)], [0] * m, {}
-        lastq = {}
-        for i, (q, kind, call, rd, wr, occ, lat, x) in enumerate(prog):
+        fore, back, seen, lastq, tags, was = [[] for _ in range(m)], [[] for _ in range(m)], {}, {}, [], []
+        for i, (q, kind, call, rd, wr, occ, lat, _x) in enumerate(prog):
             pred = {}
             for isw, regs in ((False, rd), (True, wr)):
-                for n, a, b in regs:
-                    bk = isbank(n)
-                    for k, lo, hi, w, q2 in seen.get(n, ()):
-                        if k != i and ((lo < b and hi > a and (w or isw)) or (bk and (q2 != q or q == "p"))):
-                            pred[k] = 1
+                for n, x in regs:
+                    for k, y, w, q2 in seen.get(n, ()):
+                        if k != i and ((meet(x, y) and (w or isw)) or (isbank(n) and (q2 != q or q == "p"))):
+                            inline = q2 == q and kind == prog[k][1] == "op" and (q == "p" or (isw and SAME))
+                            pred[k] = max(pred.get(k, 0.0), prog[k][5] if inline else prog[k][6] + WAKE)
             if kind == "land":
-                pred[i - 1] = 0
+                pred[i - 1] = prog[i - 1][5]
             if kind == "dma":
                 if q in lastq:
-                    pred.setdefault(lastq[q], 0)
+                    pred.setdefault(lastq[q], prog[lastq[q]][5])
                 lastq[q] = i
-            for n, a, b in wr:
-                keep = [e for e in seen.get(n, ()) if not (a <= e[1] and e[2] <= b) or isbank(n)]
-                seen[n] = (keep[-60:] if isbank(n) else keep) + [(i, a, b, True, q)]
-            for n, a, b in rd:
-                seen.setdefault(n, []).append((i, a, b, False, q))
-            npred[i] = len(pred)
-            for k, data in pred.items():
-                succ[k].append((i, data))
-
-        def lag(i, k, data):
-            if not data:
-                return prog[i][5]
-            return prog[i][6] + (0.0 if prog[i][0] == prog[k][0] == "p" else WAKE)
-
-        fore = [[(k, lag(i, k, d)) for k, d in succ[i]] for i in range(m)]
-        back = [[] for _ in range(m)]
-        for i in range(m):
-            for k, l in fore[i]:
-                back[k].append((i, l + prog[k][5] - prog[i][5]))
+            for n, x in wr:
+                left = [e for e in seen.get(n, ()) if not covers(x, e[1]) or isbank(n)]
+                seen[n] = (left[-60:] if isbank(n) else left) + [(i, x, True, q)]
+            for n, x in rd:
+                seen.setdefault(n, []).append((i, x, False, q))
+            for k in [k for k in pred if prog[k][0] == "p" and any(j > k and prog[j][0] == "p" and k in was[j] for j in pred)]:
+                del pred[k]
+            was.append(pred)
+            for k, l in pred.items():
+                fore[k].append((i, l))
+                back[i].append((k, l + occ - prog[k][5]))
+            tags.append((q, wr[0][0], wr[0][1][0] if wr[0][0] in ("fs", "us", "is_", "quads") else 0) if wr else q)
 
         def place(nxt, first, key):
             left = [0] * m
             for i in range(m):
                 for k, l in nxt[i]:
                     left[k] += 1
-            when, busy, ready = list(first), {}, sorted((key[i], i) for i in range(m) if left[i] == 0)
+            when, busy, ready = list(first), {}, sorted((-key[i], -i) for i in range(m) if left[i] == 0)
             while ready:
-                i = ready.pop(0)[1]
+                i = -ready.pop()[1]
                 t, occ, line = when[i], prog[i][5], busy.setdefault(prog[i][0], [])
                 if occ:
                     lo, hi = 0, len(line)
@@ -215,28 +217,45 @@ def emitter(g, T):
                         lo += 1
                     line.insert(lo, (t, t + occ))
                 when[i] = t
-                new = []
                 for k, l in nxt[i]:
-                    when[k] = max(when[k], t + l)
+                    if t + l > when[k]:
+                        when[k] = t + l
                     left[k] -= 1
                     if left[k] == 0:
-                        new.append((key[k], k))
-                if new:
-                    ready = sorted(ready + new)
+                        ready.append((-key[k], -k))
+                        ready.sort()
             return when
+
+        seed = [1]
+
+        def draw():
+            seed[0] = seed[0] * 48271 % 2147483647
+            return seed[0] / 2147483647
+
+        def turn(start, shake):
+            late = place(back, [prog[i][6] - prog[i][5] for i in range(m)], [shake * draw() - start[i] - prog[i][5] for i in range(m)])
+            return place(fore, [0.0] * m, [shake * draw() - late[i] - prog[i][5] for i in range(m)])
+
+        marks = [i for i in range(m) if prog[i][1] == "send"]
+
+        def worth(start):
+            return max(start[i] + prog[i][6] for i in range(m)) + MARK * sum(start[i] for i in marks) / len(marks)
 
         way = [0.0] * m
         for i in range(m - 1, -1, -1):
             way[i] = max([way[k] + l for k, l in fore[i]] + [prog[i][6]])
-        key, best = [-w for w in way], None
-        for _ in range(ROUNDS):
-            start = place(fore, [0.0] * m, key)
-            end = max(start[i] + prog[i][6] for i in range(m))
-            if best is None or end < best[0]:
-                best = (end, start)
-            late = place(back, [prog[i][6] - prog[i][5] for i in range(m)], [-(start[i] + prog[i][5]) for i in range(m)])
-            key = [-(late[i] + prog[i][5]) for i in range(m)]
-        return sorted(range(m), key=lambda i: (best[1][i], i))
+        start = best = place(fore, [0.0] * m, [-w for w in way])
+        for n in range(ROUNDS):
+            start = turn(start if worth(start) < worth(best) + 0.7 else best, SHAKE)
+            best = min(best, start, key=worth)
+        for n in range(TRIES):
+            i, by, span = int(draw() * m), PUSH * (draw() - 0.5), 6.0 * draw() if n % 3 else 1000.0
+            start = place(fore, [0.0] * m, [best[k] + (by if tags[k] == tags[i] and abs(best[k] - best[i]) <= span else 0.0) for k in range(m)])
+            if n % 4 == 0:
+                start = turn(start, 0.0)
+            if worth(start) <= worth(best) + 0.02:
+                best = start
+        return sorted(range(m), key=lambda i: (best[i], i))
 
     def issue():
         if not ORDER:
@@ -245,10 +264,9 @@ def emitter(g, T):
             q, kind, call, rd, wr, occ, lat, x = prog[i]
             if kind == "land":
                 final[x[0]] = x[1]
-                nm, a, b = wr[0]
-                hist[nm] = [(a, b, True, "net", True, (x[0], x[1], {x[0]: x[1]}))]
+                hist.setdefault(wr[0][0], []).append((wr[0][1], True, "net", True, (x[0], x[1], {x[0]: x[1]})))
                 continue
-            before(q, rd, wr)
+            before(q, kind, rd, wr)
             if kind == "op":
                 cnt[q] += 1
                 call().then_inc(T.sem["c" + q], 1)
@@ -271,11 +289,17 @@ def rank_program(g, core, T, topo):
     op, dma, send, issue = emitter(g, T)
 
     def r(n, a=None, b=None, st=None):
-        if n in MATS:
-            return r("mats", 128 * MATS.index(n), 128 * MATS.index(n) + 128)
+        if n in QUADS:
+            return r("quads", 72 * QUADS.index(n) + (a or 0), 72 * QUADS.index(n) + (64 if b is None else b), st)
         a = 0 if a is None else a
         b = T[n].shape[-1] if b is None else b
-        return (T[n][:, a:b] if st is None else T[n][:, a:b:st], [(n, a, b)], -((a - b) // (st or 1)))
+        return (T[n][:, a:b] if st is None else T[n][:, a:b:st], [(n, (a, b, st or 1))], -((a - b) // (st or 1)))
+
+    def rows(k, n, a, b, st=1):
+        return (T[n][0:k, a:b:st],) + r(n, a, b, st)[1:]
+
+    def deep(ap, n, a, b, k):
+        return (ap, [(n, (a, b, 1))], k)
 
     def small(buf, names):
         return lambda n, k=16, at=0: r(buf, 16 * names.index(n) + at, 16 * names.index(n) + at + k)
@@ -305,8 +329,8 @@ def rank_program(g, core, T, topo):
         if ka[0]:
             return 0.05 + n * 1.56 * CY
         if b is not None:
-            return FIX + max(64, n * (1 if ka[1] or kind(b)[1] else 2)) * CY
-        return FIX + max(64, n * (0.5 if ko[2] and ka[2] else 1)) * CY
+            return max(64, n * (1 if ka[1] or kind(b)[1] else 2)) * CY
+        return max(64, n * (0.5 if ko[2] and ka[2] else 1)) * CY
 
     def tt(out, a, b, o):
         op("v", lambda: g.vector.tensor_tensor(out=out[0], in0=a[0], in1=b[0], op=o), [out], [a, b], cost(out, a, b))
@@ -326,22 +350,25 @@ def rank_program(g, core, T, topo):
     def scan(out, d0, d1, o0, o1):
         half = kind(out)[2] and kind(d0)[2] and kind(d1)[2]
         op("v", lambda: g.vector.tensor_tensor_scan(out=out[0], data0=d0[0], data1=d1[0], initial=0.0, op0=o0, op1=o1), [out], [d0, d1],
-           FIX + max(64, d1[2] * (0.5 if half else 1)) * CY)
+           max(64, d1[2] * (0.5 if half else 1)) * CY)
 
     def ms(out, v):
         op("v", lambda: g.vector.memset(out[0], v), [out], [], cost(out, out))
 
     def act(out, a, fn, bias=None, scale=None):
-        cs = cost(out, a) if kind(out)[0] or kind(a)[0] else FIX + max(64, a[2]) * CY
+        cs = cost(out, a) + 0.015 if kind(out)[0] or kind(a)[0] else AFIX + max(64, a[2]) * CY
         ins = [a] + [s for s in (bias, scale) if isinstance(s, tuple)]
         kw = {k: s[0] if isinstance(s, tuple) else s for k, s in (("bias", bias), ("scale", scale)) if s is not None}
         op("s", lambda: g.scalar.activation(out=out[0], in_=a[0], func=fn, **kw), [out], ins, cs)
 
     def lin(out, a, scale=None, bias=None):
-        act(out, a, ACT.Identity, bias=bias, scale=scale)
+        if a[2] <= LINV:
+            ts(out, a, 1.0 if scale is None else scale, 0.0 if bias is None else bias, ALU.mult, ALU.add)
+        else:
+            act(out, a, ACT.Identity, bias=bias, scale=scale)
 
     def mm(out, l, x, start, stop):
-        op("p", lambda: g.tensor.matmul(out[0], l[0], x[0], start, stop), [out], [l, x], max(64, x[2]) * CY * (1 if kind(x)[2] else 4))
+        op("p", lambda: g.tensor.matmul(out[0], l[0], x[0], start, stop), [out], [l, x], max(min(64, l[2]), x[2]) * CY * (1 if kind(x)[2] else 4))
 
     def iota(out, pat, base, cm=0, after=()):
         op("g", lambda: g.iota(out[0], pat, base, cm, allow_small_or_imprecise_dtypes=True), [out], list(after), 0.13 + 2 * CY * out[2])
@@ -349,12 +376,12 @@ def rank_program(g, core, T, topo):
     def keep(out, a, pat, cmp, fill, cm=0):
         op("g", lambda: g.affine_select(out[0], a[0], pat, cmp, fill, 0, cm), [out], [a], 0.17 + 2 * CY * out[2])
 
-    def tell(t, out, in_, rsem, lsem):
-        send(topo, core, T.cores[rank ^ (1 + t)], r(out), r(in_), rsem, lsem)
+    def tell(t, out, in_, name):
+        send(topo, core, T.cores[rank ^ (1 + t)], r(out), r(in_), name, r(in_)[2] * (2 if kind(r(in_))[2] else 4))
 
     add, sub, mul, mx, mn = ALU.add, ALU.subtract, ALU.mult, ALU.max, ALU.min
     band, shr, eq_, ge, gt, lt, le = ALU.bitwise_and, ALU.arith_shift_right, ALU.is_equal, ALU.is_ge, ALU.is_gt, ALU.is_lt, ALU.is_le
-    RES, RES4 = (T.res[:], [("res", 0, 256)], 256), (T.res[:, :, 0:4], [("res", 0, 256)], 64)
+    RES, RES4 = deep(T.res[:], "res", 0, 256, 256), deep(T.res[:, :, 0:4], "res", 0, 256, 64)
     P0, P1 = r("b6", 0, 256), r("b6", 256, 512)
 
     def col(i):
@@ -363,23 +390,24 @@ def rank_program(g, core, T, topo):
     dma("s", r("csk"), ext(T.cs[:]), "dcs", 1.8)
     dma("y", r("hok"), ext(T.hold[:]), "dho", 2.3)
     dma("s", iv("wk"), ext(T.wake[:]), "dwk", 2.5)
-    dma("y", (T.snk[:], [("snk", 0, 256)], 256), ext(T.snap[:]), "dsn", 6.5)
-    dma("s", r("big", VO, VO + 4096), ext(T.x[:, 0:4096]), "dx0", 10.5)
-    dma("y", r("big", VO + 4096, VO + NV), ext(T.x[:, 4096:8192]), "dx1", 14.5)
+    dma("y", r("ea", 0, 2048), ext(T.snap[:, 0:2048]), "dsn", 5.3)
+    dma("s", r("big", VO, VO + 4096), ext(T.x[:, 0:4096]), "dx0", 9.6)
+    dma("y", r("big", VO + 4096, VO + NV), ext(T.x[:, 4096:8192]), "dx1", 13.9)
+    dma("y", r("ea", 2048, 4096), ext(T.snap[:, 2048:4096]), "ds2", 16.1)
 
     iota(iv("pr", 1), [[0, 1]], 0, 1)
-    iota(r("dj"), [[0, 8], [128, 32]], NV, 1)
+    iota(r("dj"), [[0, 8], [16, 32]], NV)
     iota(r("codes"), [[0, 2], [1, 256]], 17)
     iota(r("lock", 6656, NV), [[0, 1536]], 0)
     iota(f("q8"), [[1, 16]], 0)
     iota(f("one"), [[0, 16]], 1)
-    iota(f("sent"), [[128, 16]], NV, 1)
     iota(f("clm", 4), [[1024, 4]], 1520)
     iota(r("lf", 0, 16), [[1, 16]], 0)
     iota(r("lf", 16, 32), [[-1, 16]], 15)
     iota(r("own"), [[512, 4], [16, 16]], 513)
     iota(r("qw"), [[1, 144]], -15)
     iota(r("r16"), [[0, 16], [1, 16]], 0)
+    iota(r("f3"), [[0, 16], [-16, 16]], 0)
     iota(r("qb"), [[1, 8], [0, 16]], 0)
     iota(r("iw", 1, 513), [[0, 2], [1, 256]], 1)
     iota(r("q16"), [[1, 16], [0, 16]], int(ANEW) + 1)
@@ -387,112 +415,106 @@ def rank_program(g, core, T, topo):
     iota(r("kc"), [[16, 16], [0, 2]], 0)
     keep(r("kc"), r("kc"), [[0, 16], [1, 2]], eq_, 0.0)
     iota(r("iotas"), [[0, 8], [1, 16]], -64)
-    iota(r("rst"), [[0, 256]], 1)
-    keep(r("rst"), r("rst"), [[0, 16], [1, 16]], gt, 0.0)
-    iota(r("rstb"), [[0, 256]], 1)
-    keep(r("rstb"), r("rstb"), [[0, 16], [1, 16]], gt, 0.0)
-    iota(r("pf"), [[0, 128]], 1)
-    keep(r("pf"), r("pf"), [[0, 16], [1, 8]], gt, 0.0)
-    iota(r("pt"), [[0, 128]], 0)
+    for n, k in (("rst", 16), ("rstb", 16), ("pf", 8), ("rst4", 4), ("sm", 4)):
+        iota(r(n), [[0, r(n)[2]]], 1)
+        keep(r(n), r(n), [[0, 16], [1, k]], gt, 0.0)
     iota(f("a32"), [[8, 16]], 7)
-    iota(r("rst4"), [[0, 64]], 1)
-    keep(r("rst4"), r("rst4"), [[0, 16], [1, 4]], gt, 0.0)
-    iota(r("sm"), [[0, 64]], 1)
-    keep(r("sm"), r("sm"), [[0, 16], [1, 4]], gt, 0.0)
-    iota(r("tlb", 64, 80), [[0, 16]], 0)
-    for n in ("xw", "ldw", "none"):
-        iota(r(n), [[0, r(n)[2]]], 0)
-    iota(r("big", DUM, VO), [[0, 256]], 0)
+    iota(r("turn"), [[0, 128]], 1)
+    keep(r("turn"), r("turn"), [[-1, 16], [-16, 8]], eq_, 0.0, 1)
+    for x in (r("tlb", 64, 80), r("pt"), r("xw"), r("ldw"), r("none"), r("xab"), r("big", DUM, VO)):
+        iota(x, [[0, x[2]]], 0)
 
     def noflags(a, b, after=()):
         for c in range(a, b):
-            lo = FO - 256 + 1056 * c
-            iota(r("big", lo, lo + 1056), [[0, 1056]], 0, 0, after)
+            iota(r("big", FO + 1024 * c, FO + 1024 * c + 1024), [[0, 1024]], 0, 0, after)
 
-    noflags(0, 3)
+    noflags(0, NF)
 
-    ms(r("lock", 0, 2304), 0.0)
-    for a in (2304, 4480):
-        act(r("lock", a, a + 2176), r("lock", 0, 2176), ACT.Copy)
+    ms(r("lock", 0, 768), 0.0)
+    ms(r("lock", 768, 2560), 0.0)
+    for a, n in ((2560, 768), (3328, 768), (4096, 2560)):
+        act(r("lock", a, a + n), r("lock", 0, n), ACT.Copy)
+    ts(iv("pg", 1, 0), iv("pr", 1), 15, None, band)
+    cp(f("prf", 1), iv("pg", 1))
+    ts(r("dj"), r("dj"), f("prf", 1), None, add)
     ts(r("f1"), r("hok"), -100000.0, 100000.0, mul, add)
     tt(r("f1"), r("f1"), r("csk"), add)
     tt(r("f1"), r("f1"), r("dj"), mn)
     cp(r("loff"), r("f1"))
-    for b in range(8):
-        act(ind(r("lock"), r("loff", 32 * b, 32 * b + 32)), r("codes"), ACT.Silu)
 
-    ts(iv("pg", 1, 0), iv("pr", 1), 15, None, band)
+    def locks(a, b, after=()):
+        for c in range(a, b):
+            codes = r("codes")
+            op("s", lambda c=c: g.scalar.activation(out=ind(r("lock"), r("loff", 32 * c, 32 * c + 32))[0], in_=codes[0], func=ACT.Silu),
+               [ind(r("lock"), r("loff", 32 * c, 32 * c + 32))], [codes] + list(after), 0.065 + 512 * 3.8 * CY)
+
+    locks(0, LA)
+
     ts(iv("pg", 1, 1), iv("pr", 1), 4, None, shr)
     ts(iv("pg", 1, 2), iv("pr", 1), 112, None, band)
-    cp(f("prf", 3), iv("pg", 3))
+    cp(f("prf", 2, 1), iv("pg", 2, 1))
     PRF, PGF, G16 = (f("prf", 1, i) for i in range(3))
     ts(col(2), PRF, 8.0, None, lt)
     ts(col(6), PRF, 8.0, None, ge)
-    ts(col(3), PRF, 0.0, 512.0, eq_, mul)
+    ts(col(3), PRF, 0.0, None, eq_)
     ts(col(4), PRF, 1.0, None, eq_)
-    ts(col(0), col(3), 1.0 / 512, None, mul)
-    ts(col(5), col(4), 512.0, col(0), mul, add)
+    ts(col(5), col(4), 512.0, col(3), mul, add)
     ts(col(7), col(4), 1.0 / 1024 - 1.0, 1.0, mul, add)
     ts(col(8), col(4), 15.5, -16.0, mul, add)
     ts(col(9), col(4), -1.0, 1.0, mul, add)
     ts(f("clm", 4), f("clm", 4), col(4), 16.0, mul, add)
     ts(col(14), PRF, 16.0, None, mul)
     ts(col(15), PRF, 1.0, None, add)
-    for n, c in (("wcode", 3), ("wwin", 5)):
-        ts(r(n), r("qw"), G16, col(c), eq_, mul)
+    ts(r("wwin"), r("qw"), G16, col(5), eq_, mul)
     ts(uv("lperm", 32), r("lf", 0, 32), col(14), None, add)
     cp(uv("lc"), f("a32"))
     ts(uv("lr"), f("q8"), 0.0, PRF, mul, add)
     ts(uv("lrev"), f("q8"), 240.0, col(14), add, sub)
-    cp(r("coff"), ind(r("csk"), uv("lperm")))
-    cp(r("ci"), r("coff"))
-    for oc in range(16):
-        cp(r("ea", 256 * oc, 256 * oc + 256), (T.snk[:, :, 16 * oc:16 * oc + 16], [("snk", 0, 256)], 256))
-    ts(r("gib", 0, 8), f("q8", 8), PGF, None, eq_)
-    ts(r("gib", 8, 16), f("q8", 8), PGF, -32.0, eq_, mul)
-    ts(r("gib", 16, 24), f("q8", 8), PGF, col(15), eq_, mul)
-    ts(r("gib", 24, 32), f("q8", 8), PGF, -1.0, eq_, mul)
-    ts(r("gib", 32, 40), f("q8", 8), PGF, col(2), eq_, mul)
-    ts(r("gib", 40, 48), f("q8", 8), PGF, col(6), eq_, mul)
-    ts(r("gib", 48, 56), f("q8", 8), PGF, -8192.0, eq_, mul)
+    cp(r("coff"), r("csk"))
+    cp(r("ci"), ind(r("csk"), uv("lperm")))
+    BANK, HALF, WEIGH, OVER, FLAGD = r("gib", 0, 8), r("gib", 8, 24), r("gib", 24, 32), (32, 48), (48, 64)
+    ts(BANK, f("q8", 8), PGF, None, eq_)
+    ts(r("gib", 8, 16), f("q8", 8), PGF, col(2), eq_, mul)
+    ts(r("gib", 16, 24), f("q8", 8), PGF, col(6), eq_, mul)
+    ts(WEIGH, f("q8", 8), PGF, col(15), eq_, mul)
+    ts(r("gib", *OVER), f("q8"), PRF, -32.0, eq_, mul)
+    ts(r("gib", *FLAGD), f("q8"), PRF, -8192.0, eq_, mul)
     ts(r("diag"), r("r16"), PRF, None, eq_)
     ts(r("blk"), r("qb"), PGF, None, eq_)
     ts(r("nblk"), r("qb"), PGF, -1.0, eq_, mul)
     ts(r("blkf"), r("qb"), PGF, None, eq_)
-    lin(r("blkh"), r("blkf"), 65536.0)
-    keep(r("idf"), r("blkf"), [[-1, 128]], eq_, 0.0, 1)
+    ts(r("blkh"), r("qb"), PGF, 65536.0, eq_, mul)
     keep(r("id_"), r("blk"), [[-1, 128]], eq_, 0.0, 1)
+    if KEYP:
+        keep(r("idf"), r("blkf"), [[-1, 128]], eq_, 0.0, 1)
+        ts(r("idn"), r("id_"), LOW + NEW, None, mul)
     keep(r("nid_"), r("nblk"), [[-1, 128]], eq_, 0.0, 1)
     keep(r("mix"), r("nblk"), [[-1, 128]], ge, 0.0, 1)
     keep(r("mix"), r("mix"), [[-1, 128]], ALU.not_equal, -65.0, 1)
-    ts(r("idn"), r("id_"), LOW + NEW, None, mul)
-    ts(r("blk2"), r("blk"), 2.0, None, mul)
-    if "s" in WAYS[1]:
-        ts(col(10), iv("pr", 1), 32.0 * WAYS[1].count("s"), None, ge)
-        ts(col(11), col(10), -1.0, None, add)
+    if NS:
+        ts(col(10), iv("pr", 1), 32.0 * NS, None, ge)
         ts(r("idm"), r("id_"), col(10), None, mul)
-        ts(r("idc"), r("id_"), col(11), None, mul)
     tt(r("iotas"), r("iotas"), r("blk"), mul)
     ts(r("oh", 0, 128), r("blk"), -0.5, 0.5, mul, add)
     tt(r("iotas"), r("iotas"), r("oh", 0, 128), add)
     ts(f("home"), f("q8"), 16.0, col(15), mul, add)
     ts(r("own"), r("own"), PRF, None, add)
+    ts(f("sent"), f("home"), NV - 1.0, None, add)
     ts(f("k1"), f("q8"), PRF, 1.0, gt, add)
-    op("v", lambda: g.vector.tensor_reduce(out=f("k3", 1)[0], in_=f("k1")[0], axis=AxisListType.X, op=mul), [f("k3", 1)], [f("k1")], 0.1)
-    lin(r("blkw"), r("blkf"), f("k3", 1))
-    lin(f("k3", 1, 1), f("k3", 1), 2.0)
+    op("v", lambda: g.vector.tensor_reduce(out=f("k3", 1)[0], in_=f("k1")[0], axis=AxisListType.X, op=mul), [f("k3", 1)], [f("k1")], 0.06)
+    ts(r("blkw"), r("blkf"), f("k3", 1), None, mul)
+    ts(f("k3", 1, 1), f("k3", 1), 2.0, None, mul)
     lin(r("thd"), r("diag"), -1.0e9, 1.0e9)
     ts(r("thd"), r("thd"), f("k3", 1, 1), None, mx)
     ts(r("ti"), r("ci"), NV - 128, None, band)
     ts(r("tj"), r("ci"), 127, None, band)
     ts(r("chl", 0, 512, 2), r("ti"), 256.0, None, add)
-    lin(r("f3"), r("r16"), -16.0)
     tt(r("chl", 1, 512, 2), r("tj"), r("f3"), add)
 
     cp(r("cr"), ind(r("csk"), uv("lrev")))
     cp(r("hr"), ind(r("hok"), uv("lrev")))
     ts(r("un"), r("hr"), -1.0, 1.0, mul, add)
-    ts(r("s1"), r("hr"), -18.0, 17.0, mul, add)
+    lin(r("s1"), r("hr"), -18.0, 17.0)
     scan(r("cs2"), r("rst"), r("un"), mul, add)
     ts(f("w"), tl("cs2"), -1.0, 17.0, mul, add)
     ts(r("w1b"), tl("cs2"), -1.0, 17.0, mul, add)
@@ -510,11 +532,10 @@ def rank_program(g, core, T, topo):
             tt(r("f2", 1, 256), r("b6", 0, 255), r("un", 1, 256), mul)
             cp(hd("f2"), hd("cr"))
     cp(uv("xu"), r("tla", 0, 64, 4))
-    act(r("sa", 2, 66, 4), f("home"), ACT.Copy)
+    cp(r("sa", 2, 66, 4), f("home"))
     ts(iv("nw"), iv("wk"), -256.0, 3840.0, mul, add)
     for t in range(STEPS):
         ts(iv("sl%d" % t), iv("nw"), t, 256, shr, band)
-    cp(r("slf"), iv("sl0", 64))
     tt(f("k2"), f("home"), iv("sl0"), add)
     cp(uv("cua"), f("k2"))
 
@@ -524,28 +545,17 @@ def rank_program(g, core, T, topo):
     FD = r("big", FO - 256, BIGW)
     LK = r("lock", 0, NV)
 
-    def mat(w, m):
-        return r(w, 15 - m, 143 - m)
-
-    def sums(bk, w, src, a, first=True):
-        for m in range(16):
-            mm(r(bk, 64 * a, 64 * a + 64), mat(w, m), r(src, 1024 * a + m, 1024 * a + 1024, 16), first and m == 0, m == 15)
-
     def pick(out, w, src, n):
         for m in range(16):
-            mm(out, mat(w, m), r(src, m, n, 16), m == 0, m == 15)
-
-    def halves(a, t):
-        bk, c = ("b0", "b7")[a], 128 * a
-        act(r("aa", c, c + 128), r(bk, 128, 256), ACT.Copy)
-        tt(r("am", c, c + 128), r(bk, 256, 384), r("aa", c, c + 128), mul)
+            mm(out, r(w, 15 - m, 143 - m), r(src, m, n, 16), m == 0, m == 15)
 
     def steps_of(out, head):
         for h in range(2):
-            mm(r("b1", 128 * h, 128 * h + 128), r("am", 128 * h, 128 * h + 128), r("idf"), True, True)
-        cp(r("ti"), r("b1", 0, 256))
-        ts(r("tj"), r("ti"), 3, 511, shr, band)
-        ts(iv("h0"), hd("ti"), 3, 8191, shr, band)
+            mm(r("b1", 128 * h, 128 * h + 128), r("am", 128 * h, 128 * h + 128), r("turn"), True, True)
+        for h in range(2):
+            cp(deep(T.ab3[:, :, 8 * h:8 * h + 8], "ab3", 0, 256, 128), r("b1", 128 * h, 128 * h + 128))
+        ts(r("tj"), deep(T.ab3[:], "ab3", 0, 256, 256), 3, 511, shr, band)
+        ts(iv("h0"), deep(T.ab3[:, :, 0], "ab3", 0, 256, 16), 3, 8191, shr, band)
         ts(r(out), r("tj"), 1.0, None, add)
         if isinstance(head, tuple):
             tt(hd(out), iv("h0"), head, add)
@@ -556,82 +566,91 @@ def rank_program(g, core, T, topo):
         for h in range(2):
             bk, c = ("b4", "b5")[h], 128 * h
             for m in range(16):
-                mm(r(bk, m, 384, 16), r("ea", 2048 * h + m, 2048 * h + 2048, 16), r("gib", 24, 48), True, True)
-            cp(r("ehi", 384 * h, 384 * h + 384), r(bk, 0, 384))
-            tt(r("elo", 384 * h, 384 * h + 384), r(bk, 0, 384), r("ehi", 384 * h, 384 * h + 384), sub)
-            cp(r("aa", c, c + 128), r(bk, 128, 256))
-            tt(r("am", c, c + 128), r(bk, 256, 384), r("aa", c, c + 128), mul)
+                mm(r(bk, m, 256, 16), r("ea", 2048 * h + m, 2048 * h + 2048, 16), HALF, True, True)
+            cp(r("ehi", 2 * c, 2 * c + 256), r(bk, 0, 256))
+            tt(r("elo", 2 * c, 2 * c + 256), r(bk, 0, 256), r("ehi", 2 * c, 2 * c + 256), sub)
+            cp(r("aa", c, c + 128), r(bk, 0, 128))
+            tt(r("am", c, c + 128), r(bk, 128, 256), r("aa", c, c + 128), mul)
         steps_of("f1", -LOW)
         scan(r("ka"), r("rst"), r("f1"), mul, add)
 
     def judge(a, t):
-        win = V if t < 2 else VF
-        d, e, out, cells = (r(n, 512 * a, 512 * a + 512) for n in ("diff", "ea", "absd", "diff"))
-        cells = ind(win, r("coff", 32 * a, 32 * a + 32))
-        way = WAYS[t][a]
-        if way == "s":
+        lo, hi = sum(CUTS[:a]), sum(CUTS[:a + 1])
+        d, e, out = (r(n, lo, hi) for n in ("diff", "ea", "absd"))
+        cells = ind(V if t < 2 else VF, r("coff", lo // 16, hi // 16))
+        if t and a < NS:
             bk = r("b%d" % (2 + a % 2))
             act(d, cells, ACT.Copy)
             mm(bk, r("id_"), d, True, False)
             mm(bk, r("nid_"), e, False, True)
-            act(out, bk, ACT.Relu, scale=2.0)
-            return
-        tt(d, cells, e, sub)
-        if way == "R":
-            act(out, d, ACT.Relu, scale=2.0)
+            act(out, bk, ACT.Abs)
         else:
-            ts(out, d, 0.0, 2.0, mx, mul)
+            tt(d, cells, e, sub)
+            act(out, d, ACT.Abs)
 
     def far(h, t):
-        bk = ("b0", "b7")[h]
-        plain = "s" in WAYS[t][4 * h:4 * h + 4]
-        for e in ("ehi", "elo"):
-            mm(r(bk, 128, 384), r("idm" if plain else "id_"), r(e, 384 * h + 128, 384 * h + 384), e == "ehi", False)
-            if plain or e == "ehi":
-                mm(r(bk, 0, 128), r("idc" if plain else "none"), r(e, 384 * h, 384 * h + 128), False, False)
+        c, (lo, hi) = 128 * h, PARTS[h]
+        n, bk = (hi - lo) // 16, ("b0", "b0", "b3")[h]
         for m in range(16):
-            mm(r(bk, m, 384, 16), r("diff", 2048 * h + m, 2048 * h + 2048, 16), r("gib", 24, 48), False, False)
-        for m in range(16):
-            mm(r(bk, m, 128, 16), r("absd", 2048 * h + m, 2048 * h + 2048, 16), r("gib", 0, 8), False, m == 15)
-        ts(r("yb", 128 * h, 128 * h + 128), r(bk, 0, 128), -320.0, 0.0, add, mx)
-        if t in FTHR:
-            ts(r("zb", 128 * h, 128 * h + 128), r(bk, 0, 128), -FTHR[t], 0.0, add, mx)
+            mm(rows(n, bk, c + m, c + 128, 16), r("absd", lo + m, hi, 16), BANK, True, True)
+        for y, over in [("yb", 320.0)] + ([("zb", FTHR[t])] if t in FTHR else []):
+            if h in YV or t == 0:
+                ts(rows(n, y, c, c + 128), rows(n, bk, c, c + 128), -over, 0.0, add, mx)
+            else:
+                act(rows(n, y, c, c + 128), rows(n, bk, c, c + 128), ACT.Relu, bias=-over)
+
+    def half_sums(t):
+        for h in range(2):
+            c = 256 * h
+            for e in ("ehi", "elo"):
+                mm(r("b7", c, c + 256), r("idm" if t and NS and h == 0 else "id_"), r(e, c, c + 256), e == "ehi", False)
+            for m in range(16):
+                mm(r("b7", c + m, c + 256, 16), r("diff", 2048 * h + m, 2048 * h + 2048, 16), HALF, False, m == 15)
+        for h in range(2):
+            c = 128 * h
+            lin(r("aa", c, c + 128), r("b7", 2 * c, 2 * c + 128))
+            tt(r("am", c, c + 128), r("b7", 2 * c + 128, 2 * c + 256), r("aa", c, c + 128), mul)
 
     def verdicts(t):
         out = r("b2", 256, 272)
         mm(out, r("id_"), r("w1b"), True, False)
-        for h in range(2):
-            mm(r("b2", 256 + 8 * h, 264 + 8 * h), r("yb", 128 * h, 128 * h + 128), r("gib", 8, 16), False, t == 0 and h == 1)
+        for h, (lo, hi) in enumerate(PARTS):
+            n = (hi - lo) // 16
+            mm(out, rows(n, "yb", 128 * h, 128 * h + 128), rows(n, "gib", *OVER), False, t == 0 and h == 2)
             if t in FTHR:
-                mm(r("b2", 256 + 8 * h, 264 + 8 * h), r("zb", 128 * h, 128 * h + 128), r("gib", 48, 56), False, False)
+                mm(out, rows(n, "zb", 128 * h, 128 * h + 128), rows(n, "gib", *FLAGD), False, False)
         if t:
             mm(out, r("id_"), r("winb"), False, True)
         ts(r("sf%d" % t), out, 0.0, None, mx)
-        tell(t, "lsf%d" % t, "sf%d" % t, "rsf%d" % t, "qsf%d" % t)
+        tell(t, "lsf%d" % t, "sf%d" % t, "sf%d" % t)
         ts(f("l1"), r("sf%d" % t), -1.0, 34.0, mul, add)
         ts(f("l2"), r("sf%d" % t), 0.0, 1.0e9, eq_, mul)
 
     def slot(i):
         return r("pt", i, 128, 8)
 
-    def holders(t):
-        if t == 0:
-            act(r("lg", 0, 256), ind(LK, uv("xu")), ACT.Relu, bias=col(8), scale=col(7))
-            pick(r("b4", 0, 16), "wwin", "lg", 256)
-            ts(slot(3), r("b4", 0, 16), HM, None, mul)
-            cp(slot(4), r("tla", 0, 64, 4))
-            return
+    def first_holders():
+        act(r("lg", 0, 256), ind(LK, uv("xu")), ACT.Relu, bias=col(8), scale=col(7))
+        pick(r("b4", 0, 16), "wwin", "lg", 256)
+        ts(slot(3), r("b4", 0, 16), HM, None, mul)
+        cp(slot(4), r("tla", 0, 64, 4))
+
+    def old_holders():
         act(r("lgo"), ind(LK, uv("xu", 32)), ACT.Relu, bias=col(8), scale=col(7))
         pick(r("b1", 256, 288), "wwin", "lgo", 512)
         cp(iv("hi", 32), r("b1", 256, 288))
         ts(iv("oi", 32), iv("hi", 32), 511, None, band)
         cp(uv("ou", 32), iv("oi", 32))
-        act(r("ldg"), ind(r("ldw"), uv("ou", 32)), ACT.Copy)
-        pick(r("b1", 288, 320), "wcode", "ldg", 512)
-        tt(f("vs", 32), r("b1", 288, 320), iv("hi", 32), le)
+        act(r("lg", 512, 1024), ind(r("ldw"), uv("ou", 32)), ACT.Identity, scale=col(4))
+
+    def holders():
+        tt(f("vs", 32), r("b4", 32, 64), iv("hi", 32), le)
         tt(f("vs", 32), iv("oi", 32), f("vs", 32), mul)
-        lin(f("hold", 32), f("vs", 32), HM)
-        lin(f("nhold"), f("vs"), -HM)
+        ts(f("hold", 32), f("vs", 32), HM, None, mul)
+        ts(f("nhold"), f("vs"), -HM, None, mul)
+        tt(slot(0), f("a32", 16, 16), f("hold", 16, 16), mx)
+        tt(slot(3), f("a32"), f("hold"), mx)
+        tt(slot(2), f("na"), f("nhold"), mn)
 
     def decide(t):
         mm(r("b3", 0, 32), r("id_"), r("kc"), True, False)
@@ -651,15 +670,22 @@ def rank_program(g, core, T, topo):
         scan(r("l32"), r("alt"), r("b3", 0, 32), mul, add)
         ts(uv("listu"), r("l32", 1, 32, 2), col(1), None, add)
         act(r("snd%d" % t), ind(VD, uv("listu")), ACT.Copy)
-        tell(t, "lnd%d" % t, "snd%d" % t, "rdd%d" % t, "qdd%d" % t)
+        tell(t, "lnd%d" % t, "snd%d" % t, "dd%d" % t)
         tt(f("dec"), slot(5), slot(6), mx)
 
     def keys(t):
         lk = "lkc%d" % t
-        mm(r("b7", 0, 256), r("idf"), r("ka"), True, False)
-        for k in range(16):
-            mm(r("b7", k, 256, 16), r("idn"), r("ab"), False, k == 15)
-        tt(r("s1"), r("b7", 0, 256), r(("ci", "st", "st", "cf")[t]), mx)
+        if t in KEYP:
+            kept = r("b0", 0, 256)
+            mm(kept, r("idf"), r("ka"), True, False)
+            for k in range(16):
+                mm(r("b0", k, 256, 16), r("idn"), r("ab"), False, k == 15)
+        else:
+            kept = P1
+            ts(hd("xab"), r("ab"), LOW + NEW, None, mul)
+            scan(P0, r("rst"), r("xab"), mul, add)
+            tt(P1, P0, r("ka"), add)
+        tt(r("s1"), kept, r(("ci", "st", "st", "cf")[t]), mx)
         tt(hd(lk), hd(lk), f("cm"), add)
         scan(P0, r("rst"), r(lk), mul, add)
         tt(RES, P0, r("s1"), mx)
@@ -667,17 +693,16 @@ def rank_program(g, core, T, topo):
             ts(r("cf"), RES, NV - 1, None, band)
             return
         ts(r("cf"), RES, NV - 1 + FB, None, band)
-        cp(r("coff"), r("cf"))
+        cp(r("coff"), ind(r("cf"), uv("lperm")))
         if t < 2:
             ts(P1, RES, NEW, float(FB), ge, mul)
             tt(r("st"), P1, r("cf"), add)
 
     def flags(t):
-        new, old = r("lnd%d" % t), r("snd%d" % t)
-        tt(r("fa"), new, old, mx)
-        mm(r("b3", 0, 256), r("nblk"), old, True, False)
-        mm(r("b3", 0, 256), r("nblk"), new, False, False)
-        mm(r("b3", 0, 256), r("blk2"), r("fa"), False, True)
+        mm(r("b2", 0, 256), r("nid_"), r("snd%d" % t), True, False)
+        mm(r("b2", 0, 256), r("id_"), r("lnd%d" % t), False, True)
+        act(r("fa"), r("b2", 0, 256), ACT.Abs)
+        mm(r("b3", 0, 256), r("blk"), r("fa"), True, True)
         ts(r("fv"), r("b3", 0, 256), 320.0, FLAG[t], gt, mul)
         cp(ind(FD, uv("listu")), r("fv"))
 
@@ -688,7 +713,7 @@ def rank_program(g, core, T, topo):
         act(r("cv"), ind(r("iw"), uv(cu)), ACT.Identity, bias=f("clm", 1, t), scale=col(9))
         mm(r("b5", 0, 256), r("none"), r("rstb"), True, False)
         tt(r(cur, 1, 65, 4), f("home"), r(cur, 2, 66, 4), sub)
-        act(r(cur, 4, 68, 4), r("slf", 16 * ((t + 1) % STEPS), 16 * ((t + 1) % STEPS) + 16), ACT.Copy)
+        cp(r(cur, 4, 68, 4), iv("sl%d" % ((t + 1) % STEPS)))
         scan(r("po"), r("pf"), r("pt"), mul, add)
         tt(r("pd"), ind(r("po"), uv("lc")), r("diag"), mul)
         mm(r("b4", 0, 256), r("blkf"), r("pd"), True, True)
@@ -697,7 +722,7 @@ def rank_program(g, core, T, topo):
         if not last:
             act(r("b4", 256, 512), r("b4", 0, 256), ACT.Relu, bias=-1.0, scale=(t + 2) / GONE)
             tt(r("ldw", 1, 257), r("b4", 256, 512), r("ldw", 1, 257), mx)
-            lin(r("tla"), r("tla"), None, NEW / 2)
+            ts(r("tla"), r("tla"), NEW / 2, None, add)
             ts(r("tlb", 0, 64), RES4, NV - 1 + int(NEW), None, band)
             tt(r("tlb", 0, 64), r("tlb", 0, 64), r("tla"), mx)
             ts(r("tlb", 0, 64), r("tlb", 0, 64), NV - 1, None, band)
@@ -706,7 +731,7 @@ def rank_program(g, core, T, topo):
             tt(r("td"), r("tlb", 1, 65), r("tlb", 0, 64), sub)
             tt(slot(1), r("tlb", 1, 65, 4), r("tlb", 0, 64, 4), sub)
             cp(slot(4), r("tlb", 0, 64, 4))
-            holders(t + 1)
+            old_holders()
         else:
             cp(uv("xu"), r("tla", 0, 64, 4))
         ts(f("nd"), f("dec"), 0.0, GONE, eq_, mul)
@@ -716,15 +741,19 @@ def rank_program(g, core, T, topo):
         if not last:
             cp(r("w1b"), f("w1"))
         tt(r("cg"), ind(r("pw"), uv(cu)), r("diag"), mul)
-        cp(r("ku"), ind(r("pw"), uv(cu)))
+        if KU:
+            act(r("f2"), ind(r("pw"), uv(cu)), ACT.Copy)
+            cp(r("ku"), r("f2"))
+        else:
+            cp(r("ku"), ind(r("pw"), uv(cu)))
         scan(r("cs2"), r("rst"), r("cg"), mul, add)
         PL = tl("cs2")
         for oc in range(16):
-            n = 256 - 16 * oc
-            ts((T.eq[:, oc, 0:n], [("eq", 272 * oc, 272 * oc + n)], n), r("ku", 16 * oc, 256), r("cs2", 16 * oc + 15, 16 * oc + 16), None, eq_)
+            n, at = 256 - 16 * oc, 272 * oc
+            ts(deep(T.eq[:, oc, 0:n], "eq", at, at + n, n), r("ku", 16 * oc, 256), r("cs2", 16 * oc + 15, 16 * oc + 16), None, eq_)
             if oc < 15:
-                mm(r("b5", 16 * oc + 16, 256), r("blkh"), (T.eq[:, oc, 16:n], [("eq", 272 * oc, 272 * oc + n)], n - 16), False, False)
-        mm(r("b5", 0, 256), r("blkw"), (T.eq[:, :, 0:16], [("eq", 0, 272 * 16)], 256), False, True)
+                mm(r("b5", 16 * oc + 16, 256), r("blkh"), deep(T.eq[:, oc, 16:n], "eq", at, at + n, n - 16), False, False)
+        mm(r("b5", 0, 256), r("blkw"), deep(T.eq[:, :, 0:16], "eq", 0, 272 * 16, 256), False, True)
         tt(f("k1"), PL, f("sent"), mn)
         tt(r("lq"), r("b5", 0, 256), r("thd"), ge)
         scan(r("ls"), r("rstb"), r("lq"), mul, add)
@@ -734,16 +763,15 @@ def rank_program(g, core, T, topo):
         act(ind(r("lock"), uv("offu")), r("cv"), ACT.Silu)
         n = 16 if last else 32
         act(r("lg", 0, 16 * n), ind(LK, uv("xu", n)), ACT.Relu, bias=col(8), scale=col(7))
-        pick(r("b4", 0, n), "wwin", "lg", 16 * n)
+        pick(r("b4", 0, 16 if last else 64), "wwin", "lg", 256 if last else 1024)
+        mine = r("own", 16 * t, 16 * t + 16)
         if not last:
-            tt(r("winb"), r("b4", 0, 16), r("own", 16 * t, 16 * t + 16), eq_)
+            tt(r("winb"), r("b4", 0, 16), mine, eq_)
             ts(f("a32", 32), r("b4", 0, 32), -512.0 * (t + 1), HM, add, mul)
             ts(f("na"), r("b4", 0, 16), -512.0 * (t + 1), -HM, add, mul)
-            tt(r("pf", 3, 128, 8), r("b4", 0, 16), r("own", 16 * t, 16 * t + 16), eq_)
-            tt(slot(0), f("a32", 16, 16), f("hold", 16, 16), mx)
-            tt(slot(3), f("a32"), f("hold"), mx)
-            tt(slot(2), f("na"), f("nhold"), mn)
-        tt(r("xw", 0, 64, 4), r("b4", 0, 16), r("own", 16 * t, 16 * t + 16), eq_)
+            tt(r("pf", 3, 128, 8), r("b4", 0, 16), mine, eq_)
+            holders()
+        tt(r("xw", 0, 64, 4), r("b4", 0, 16), mine, eq_)
         tt(f("w"), f("w1"), r("xw", 0, 64, 4), add)
         if not last:
             scan(r("wx"), r("rst4"), r("xw"), mul, add)
@@ -753,46 +781,46 @@ def rank_program(g, core, T, topo):
         ts(iv("by"), iv("pi"), 14, 511, shr, band)
         cp(r(cur, 3, 67, 4), iv("by"))
         ts(r("sm", 1, 64, 4), PL, 1024 * HM, None, ge)
-        act(r("sm", 2, 64, 4), r(cur, 3, 67, 4), ACT.Relu, bias=1.0, scale=-1.0)
+        ts(r("sm", 2, 64, 4), iv("by"), 0.0, None, eq_)
         scan(r(curn, 0, 64), r("sm"), r(cur, 1, 65), mul, add)
         if not last:
             cp(uv(cun), r(curn, 3, 64, 4))
 
     for t in range(STEPS):
         last = t == STEPS - 1
-        for a in range(8):
+        for a in range(len(CUTS)):
             judge(a, t)
         if t == 0:
+            locks(LA, 8, [r("absd", 3840, 4096)])
             first_keys()
-        for h in range(2):
+        for h in range(len(PARTS)):
             far(h, t)
         verdicts(t)
-        for a in range(2):
-            halves(a, t)
+        half_sums(t)
         steps_of("skg%d" % t, f("cls") if t else -LOWER)
-        tell(t, "lkc%d" % t, "skg%d" % t, "rkc%d" % t, "qkc%d" % t)
+        tell(t, "lkc%d" % t, "skg%d" % t, "kc%d" % t)
         if t:
             scan(P0, r("rst"), r("skg%d" % t), mul, add)
             tt(r("ka"), P0, r("ka"), mx)
-        if t == 0:
-            holders(0)
+        else:
+            first_holders()
         decide(t)
         if t == 0:
-            noflags(3, 8, [r("lnd0")])
+            noflags(NF, 8, [r("lnd0")])
         keys(t)
         cp(ind(VD, uv("listu")), r("lnd%d" % t))
         if t in FLAG:
             flags(t)
         if not last:
-            lin(f("cls"), f("dec"), (32768.0 * (t + 1) - LOW + LOWER) / GONE, -LOWER)
-        if last:
+            ts(f("cls"), f("dec"), (32768.0 * (t + 1) - LOW + LOWER) / GONE, -LOWER, mul, add)
+        else:
             cp(r("cr"), ind(r("cf"), uv("lperm")))
             dma("y", ext(T.yc[:]), r("cr"), "oyc", 2.0)
             for i in range(64):
-                mm(r("b0", 8 * i, 8 * i + 8), r("big", VO + i, VO + NV, 64), r("gib", 16, 24), True, True)
+                mm(r("b0", 8 * i, 8 * i + 8), r("big", VO + i, VO + NV, 64), WEIGH, True, True)
             for b in range(8):
                 act(r("yt", 64 * b, 64 * b + 64), r("b0", b, 512, 8), ACT.Copy)
-                dma("ys"[b % 2], ext(T.ys[b]), r("yt", 64 * b, 64 * b + 64), "oys%d" % b, 2.0)
+                dma("ys"[b % 2], ext(T.ys[b]), r("yt", 64 * b, 64 * b + 64), "oys%d" % b, 4.6 - 0.35 * b)
         lanes(t)
     ts(f("iso"), f("w1"), ANEW, None, lt)
     tt(r("f1"), ind(f("iso"), uv("lr")), r("qk"), mul)

@@ -16,22 +16,18 @@ GONE = 8589934592.0
 ANEW = 8388608.0
 FLAG = {1: 768.0, 2: 2048.0}
 FTHR = {2: 6000.0, 3: 20000.0}
-NS = 2
+NS = 3
 CUTS = (512, 512, 512, 512, 1024, 768, 256)
 PARTS = [(0, 2048), (2048, 3840), (3840, 4096)]
-LA = 8
-NF = 3
-KEYP = ()
-KU = 0
-YV = (0, 1, 2)
-LINV = 128
-SAME = 0
 WAKE = 0.15
 CY = 0.00095
 AFIX, FLY, FLYB = 80 * CY, 1.3, 0.0005
 ROUNDS = 30
-TRIES = 2500
+TRIES = 6000
 SHAKE, PUSH, MARK = 0.1, 2.5, 0.5
+HEAT = 0.5
+SEED = 2
+AIMED = 4
 ORDER = []
 
 SCRATCH = {
@@ -43,10 +39,8 @@ SCRATCH = {
     "eq": ("sbuf", [128, 16, 272], "bfloat16"),
     "ab3": ("sbuf", [128, 16, 16], "int32"),
     "res": ("sbuf", [128, 16, 16], "int32"),
-    "oh": ("sbuf", [128, 2048], "bfloat16"),
-    "kc": ("sbuf", [128, 32], "bfloat16"),
-    "alt": ("sbuf", [128, 32], "float32"),
-    "l32": ("sbuf", [128, 32], "float32"),
+    "ct": ("sbuf", [128, 560], "float32"),
+    "slw": ("sbuf", [128, 512], "float32"),
     "ldw": ("sbuf", [128, 272], "bfloat16"),
     "tla": ("sbuf", [128, 64], "float32"),
     "tlb": ("sbuf", [128, 80], "int32"),
@@ -55,21 +49,21 @@ SCRATCH = {
 }
 for _n in ("codes", "yt"):
     SCRATCH[_n] = ("sbuf", [128, 512], "float32")
-for _n in ("csk", "hok", "ci", "cf", "st", "ti", "tj"):
+for _n in ("csk", "hok", "ci", "cf", "st", "tj"):
     SCRATCH[_n] = ("sbuf", [128, 256], "int32")
-for _n in ("r16", "dj", "rst", "diag", "thd", "ka", "cg", "cs2", "s1", "f1", "f2", "f3", "cr", "hr", "un", "qk", "q16", "pd",
+for _n in ("r16", "dj", "rst", "diag", "thd", "ka", "cg", "cs2", "s1", "f1", "f2", "pos", "cr", "hr", "un", "qk", "q16", "pd",
            "am", "aa", "cv", "xab"):
     SCRATCH[_n] = ("sbuf", [128, 256], "float32")
 for _n in ("iw", "pw"):
     SCRATCH[_n] = ("sbuf", [128, 520], "float32")
-for _n in ("qb", "blkf", "idf", "turn", "pt", "pf", "po"):
+for _n in ("qb", "blkf", "turn", "pt", "pf", "po"):
     SCRATCH[_n] = ("sbuf", [128, 128], "float32")
-for _n in ("blk", "nblk", "blkw", "blkh", "mix", "id_", "nid_", "iotas", "idm", "idn", "none"):
+for _n in ("blk", "nblk", "blkw", "blkh", "mix", "id_", "nid_"):
     SCRATCH[_n] = ("sbuf", [128, 128], "bfloat16")
 SCRATCH["wwin"] = ("sbuf", [128, 144], "bfloat16")
 SCRATCH["lg"] = ("sbuf", [128, 1024], "bfloat16")
-for _n in ("lgo", "ehi", "elo", "chl"):
-    SCRATCH[_n] = ("sbuf", [128, 512], "bfloat16")
+SCRATCH["es"] = ("sbuf", [128, 768], "float32")
+SCRATCH["lgo"] = ("sbuf", [128, 512], "bfloat16")
 for _n in ("yb", "zb"):
     SCRATCH[_n] = ("sbuf", [128, 384], "bfloat16")
 for _n in ("fa", "fv", "lq", "ls", "rstb"):
@@ -79,9 +73,9 @@ SCRATCH["quads"] = ("sbuf", [128, 72 * len(QUADS)], "float32")
 for _n in ("coff", "loff", "ku"):
     SCRATCH[_n] = ("sbuf", [128, 256], "uint16")
 FS = ["prf", "col", "clm", "q8", "sent", "home", "one", "cm", "dec", "cls", "vs", "vs2", "hold", "hold2", "nhold", "a32", "a33", "na",
-      "w", "w1", "nd", "k1", "k2", "k3", "l1", "l2", "yl", "iso"]
+      "w", "w1", "nd", "k1", "k2", "k3", "l1", "l2", "m1", "m2", "spare", "dbig", "yl", "iso"]
 IS = ["oi", "oi2", "hi", "hi2", "pi", "by", "sl0", "sl1", "sl2", "sl3", "nw", "h0", "pr", "pg", "wk"]
-US = ["xu", "xv", "ou", "ou2", "cua", "cub", "offu", "listu", "lc", "lr", "lrev", "lperm", "lq"]
+US = ["xu", "xv", "ou", "ou2", "cua", "cub", "offu", "listu", "slot", "os", "lc", "lr", "lrev", "lperm", "lq", "ldup", "ldup2"]
 SCRATCH["fs"] = ("sbuf", [128, 16 * len(FS)], "float32")
 SCRATCH["is_"] = ("sbuf", [128, 16 * len(IS)], "int32")
 SCRATCH["us"] = ("sbuf", [128, 16 * len(US)], "uint16")
@@ -124,7 +118,7 @@ def emitter(g, T):
                 if isbank(n):
                     evs += [e for q2, e in bank.get(n, {}).items() if q2 != q]
                 for y, w, q2, asyn, e in hist.get(n, ()):
-                    inline = q2 == q and not asyn and kind == "op" and (q == "p" or (isw and SAME))
+                    inline = q2 == q == "p"
                     if meet(x, y) and (w or isw) and not inline:
                         evs.append(e)
         todo = {}
@@ -177,7 +171,7 @@ def emitter(g, T):
                 for n, x in regs:
                     for k, y, w, q2 in seen.get(n, ()):
                         if k != i and ((meet(x, y) and (w or isw)) or (isbank(n) and (q2 != q or q == "p"))):
-                            inline = q2 == q and kind == prog[k][1] == "op" and (q == "p" or (isw and SAME))
+                            inline = q2 == q == "p"
                             pred[k] = max(pred.get(k, 0.0), prog[k][5] if inline else prog[k][6] + WAKE)
             if kind == "land":
                 pred[i - 1] = prog[i - 1][5]
@@ -226,7 +220,7 @@ def emitter(g, T):
                         ready.sort()
             return when
 
-        seed = [1]
+        seed = [SEED]
 
         def draw():
             seed[0] = seed[0] * 48271 % 2147483647
@@ -248,13 +242,44 @@ def emitter(g, T):
         for n in range(ROUNDS):
             start = turn(start if worth(start) < worth(best) + 0.7 else best, SHAKE)
             best = min(best, start, key=worth)
+        def holdups(start):
+            ahead, last = {}, {}
+            for i in sorted(range(m), key=lambda i: start[i]):
+                if prog[i][5]:
+                    ahead[i], last[prog[i][0]] = last.get(prog[i][0]), i
+            i, pairs = max(range(m), key=lambda i: start[i] + prog[i][6]), []
+            while i is not None:
+                k = next((k for k, l in back[i] if abs(start[k] + l - prog[i][5] + prog[k][5] - start[i]) < 1e-6), None)
+                if k is None:
+                    k = ahead.get(i)
+                    if k is not None:
+                        pairs.append((i, k))
+                i = k
+            return pairs
+
+        held = [None, None]
+        now, had = best, worth(best)
+        least = had
         for n in range(TRIES):
             i, by, span = int(draw() * m), PUSH * (draw() - 0.5), 6.0 * draw() if n % 3 else 1000.0
-            start = place(fore, [0.0] * m, [best[k] + (by if tags[k] == tags[i] and abs(best[k] - best[i]) <= span else 0.0) for k in range(m)])
+            key = [now[k] + (by if tags[k] == tags[i] and abs(now[k] - now[i]) <= span else 0.0) for k in range(m)]
+            if n % 5 < AIMED:
+                if held[0] is not now:
+                    held[:] = [now, holdups(now)]
+                i, k = held[1][int(draw() * len(held[1]))]
+                key = list(now)
+                if draw() < 0.5:
+                    key[i] = now[k] - 0.001 - draw() ** 2
+                else:
+                    key[k] = now[i] + 0.001 + draw() ** 2
+            start = place(fore, [0.0] * m, key)
             if n % 4 == 0:
                 start = turn(start, 0.0)
-            if worth(start) <= worth(best) + 0.02:
-                best = start
+            w = worth(start)
+            if w <= had + 0.02 + HEAT * (1 - n / TRIES) ** 2 * draw():
+                now, had = start, w
+                if w < least:
+                    best, least = start, w
         return sorted(range(m), key=lambda i: (best[i], i))
 
     def issue():
@@ -362,10 +387,7 @@ def rank_program(g, core, T, topo):
         op("s", lambda: g.scalar.activation(out=out[0], in_=a[0], func=fn, **kw), [out], ins, cs)
 
     def lin(out, a, scale=None, bias=None):
-        if a[2] <= LINV:
-            ts(out, a, 1.0 if scale is None else scale, 0.0 if bias is None else bias, ALU.mult, ALU.add)
-        else:
-            act(out, a, ACT.Identity, bias=bias, scale=scale)
+        act(out, a, ACT.Identity, bias=bias, scale=scale)
 
     def mm(out, l, x, start, stop):
         op("p", lambda: g.tensor.matmul(out[0], l[0], x[0], start, stop), [out], [l, x], max(min(64, l[2]), x[2]) * CY * (1 if kind(x)[2] else 4))
@@ -390,10 +412,12 @@ def rank_program(g, core, T, topo):
     dma("s", r("csk"), ext(T.cs[:]), "dcs", 1.8)
     dma("y", r("hok"), ext(T.hold[:]), "dho", 2.3)
     dma("s", iv("wk"), ext(T.wake[:]), "dwk", 2.5)
-    dma("y", r("ea", 0, 2048), ext(T.snap[:, 0:2048]), "dsn", 5.3)
-    dma("s", r("big", VO, VO + 4096), ext(T.x[:, 0:4096]), "dx0", 9.6)
-    dma("y", r("big", VO + 4096, VO + NV), ext(T.x[:, 4096:8192]), "dx1", 13.9)
-    dma("y", r("ea", 2048, 4096), ext(T.snap[:, 2048:4096]), "ds2", 16.1)
+    at = 3.0
+    for q, n, src, a, b, sem in (("y", "ea", T.snap, 0, 2048, "dsn"), ("s", "big", T.x, 0, 4096, "dx0"),
+                                 ("y", "big", T.x, 4096, NV, "dx1"), ("y", "ea", T.snap, 2048, 4096, "ds2")):
+        at += 0.25 + (b - a) / 1000.0
+        off = VO if n == "big" else 0
+        dma(q, r(n, off + a, off + b), ext(src[:, a:b]), sem, at)
 
     iota(iv("pr", 1), [[0, 1]], 0, 1)
     iota(r("dj"), [[0, 8], [16, 32]], NV)
@@ -407,28 +431,25 @@ def rank_program(g, core, T, topo):
     iota(r("own"), [[512, 4], [16, 16]], 513)
     iota(r("qw"), [[1, 144]], -15)
     iota(r("r16"), [[0, 16], [1, 16]], 0)
-    iota(r("f3"), [[0, 16], [-16, 16]], 0)
+    iota(r("lf", 32, 64), [[1, 16], [0, 2]], 0)
     iota(r("qb"), [[1, 8], [0, 16]], 0)
     iota(r("iw", 1, 513), [[0, 2], [1, 256]], 1)
     iota(r("q16"), [[1, 16], [0, 16]], int(ANEW) + 1)
-    iota(r("alt"), [[0, 16], [1, 2]], 0)
-    iota(r("kc"), [[16, 16], [0, 2]], 0)
-    keep(r("kc"), r("kc"), [[0, 16], [1, 2]], eq_, 0.0)
-    iota(r("iotas"), [[0, 8], [1, 16]], -64)
+    iota(r("pos"), [[32, 16], [1, 16]], 32)
     for n, k in (("rst", 16), ("rstb", 16), ("pf", 8), ("rst4", 4), ("sm", 4)):
         iota(r(n), [[0, r(n)[2]]], 1)
         keep(r(n), r(n), [[0, 16], [1, k]], gt, 0.0)
     iota(f("a32"), [[8, 16]], 7)
     iota(r("turn"), [[0, 128]], 1)
     keep(r("turn"), r("turn"), [[-1, 16], [-16, 8]], eq_, 0.0, 1)
-    for x in (r("tlb", 64, 80), r("pt"), r("xw"), r("ldw"), r("none"), r("xab"), r("big", DUM, VO)):
+    for x in (r("tlb", 64, 80), r("pt"), r("xw"), r("ldw"), r("xab"), r("big", DUM, VO)):
         iota(x, [[0, x[2]]], 0)
 
     def noflags(a, b, after=()):
         for c in range(a, b):
             iota(r("big", FO + 1024 * c, FO + 1024 * c + 1024), [[0, 1024]], 0, 0, after)
 
-    noflags(0, NF)
+    noflags(0, 3)
 
     ms(r("lock", 0, 768), 0.0)
     ms(r("lock", 768, 2560), 0.0)
@@ -441,19 +462,14 @@ def rank_program(g, core, T, topo):
     tt(r("f1"), r("f1"), r("csk"), add)
     tt(r("f1"), r("f1"), r("dj"), mn)
     cp(r("loff"), r("f1"))
-
-    def locks(a, b, after=()):
-        for c in range(a, b):
-            codes = r("codes")
-            op("s", lambda c=c: g.scalar.activation(out=ind(r("lock"), r("loff", 32 * c, 32 * c + 32))[0], in_=codes[0], func=ACT.Silu),
-               [ind(r("lock"), r("loff", 32 * c, 32 * c + 32))], [codes] + list(after), 0.065 + 512 * 3.8 * CY)
-
-    locks(0, LA)
+    for c in range(8):
+        act(ind(r("lock"), r("loff", 32 * c, 32 * c + 32)), r("codes"), ACT.Silu)
 
     ts(iv("pg", 1, 1), iv("pr", 1), 4, None, shr)
     ts(iv("pg", 1, 2), iv("pr", 1), 112, None, band)
-    cp(f("prf", 2, 1), iv("pg", 2, 1))
-    PRF, PGF, G16 = (f("prf", 1, i) for i in range(3))
+    ts(iv("pg", 1, 3), iv("pr", 1), 16, None, band)
+    cp(f("prf", 3, 1), iv("pg", 3, 1))
+    PRF, PGF, G16, ODD = (f("prf", 1, i) for i in range(4))
     ts(col(2), PRF, 8.0, None, lt)
     ts(col(6), PRF, 8.0, None, ge)
     ts(col(3), PRF, 0.0, None, eq_)
@@ -466,7 +482,7 @@ def rank_program(g, core, T, topo):
     ts(col(14), PRF, 16.0, None, mul)
     ts(col(15), PRF, 1.0, None, add)
     ts(r("wwin"), r("qw"), G16, col(5), eq_, mul)
-    ts(uv("lperm", 32), r("lf", 0, 32), col(14), None, add)
+    ts(uv("lperm", 64), r("lf"), col(14), None, add)
     cp(uv("lc"), f("a32"))
     ts(uv("lr"), f("q8"), 0.0, PRF, mul, add)
     ts(uv("lrev"), f("q8"), 240.0, col(14), add, sub)
@@ -485,18 +501,10 @@ def rank_program(g, core, T, topo):
     ts(r("blkf"), r("qb"), PGF, None, eq_)
     ts(r("blkh"), r("qb"), PGF, 65536.0, eq_, mul)
     keep(r("id_"), r("blk"), [[-1, 128]], eq_, 0.0, 1)
-    if KEYP:
-        keep(r("idf"), r("blkf"), [[-1, 128]], eq_, 0.0, 1)
-        ts(r("idn"), r("id_"), LOW + NEW, None, mul)
     keep(r("nid_"), r("nblk"), [[-1, 128]], eq_, 0.0, 1)
     keep(r("mix"), r("nblk"), [[-1, 128]], ge, 0.0, 1)
-    keep(r("mix"), r("mix"), [[-1, 128]], ALU.not_equal, -65.0, 1)
-    if NS:
-        ts(col(10), iv("pr", 1), 32.0 * NS, None, ge)
-        ts(r("idm"), r("id_"), col(10), None, mul)
-    tt(r("iotas"), r("iotas"), r("blk"), mul)
-    ts(r("oh", 0, 128), r("blk"), -0.5, 0.5, mul, add)
-    tt(r("iotas"), r("iotas"), r("oh", 0, 128), add)
+    keep(r("mix"), r("mix"), [[-1, 128]], ALU.not_equal, -1024.0, 1)
+    ts(col(10), iv("pr", 1), 32.0 * NS, None, ge)
     ts(f("home"), f("q8"), 16.0, col(15), mul, add)
     ts(r("own"), r("own"), PRF, None, add)
     ts(f("sent"), f("home"), NV - 1.0, None, add)
@@ -506,10 +514,12 @@ def rank_program(g, core, T, topo):
     ts(f("k3", 1, 1), f("k3", 1), 2.0, None, mul)
     lin(r("thd"), r("diag"), -1.0e9, 1.0e9)
     ts(r("thd"), r("thd"), f("k3", 1, 1), None, mx)
-    ts(r("ti"), r("ci"), NV - 128, None, band)
-    ts(r("tj"), r("ci"), 127, None, band)
-    ts(r("chl", 0, 512, 2), r("ti"), 256.0, None, add)
-    tt(r("chl", 1, 512, 2), r("tj"), r("f3"), add)
+    ts(r("yt"), ind(r("csk"), uv("ldup", 32)), 256.0, None, add)
+    op("v", lambda: g.vector.transpose(out=r("ct", 32, 544)[0], in_=r("yt")[0]), [r("ct", 32, 544)], [r("yt")], 512 * CY)
+    ts(r("ct", 544, 560), f("home"), -1.0, None, add)
+    ts(f("spare"), f("home"), -768.0, None, add)
+    ts(f("dbig"), r("diag", 0, 16), 1000.0, None, mul)
+    lin(r("pos"), r("pos"), None, ODD)
 
     cp(r("cr"), ind(r("csk"), uv("lrev")))
     cp(r("hr"), ind(r("hok"), uv("lrev")))
@@ -567,10 +577,9 @@ def rank_program(g, core, T, topo):
             bk, c = ("b4", "b5")[h], 128 * h
             for m in range(16):
                 mm(r(bk, m, 256, 16), r("ea", 2048 * h + m, 2048 * h + 2048, 16), HALF, True, True)
-            cp(r("ehi", 2 * c, 2 * c + 256), r(bk, 0, 256))
-            tt(r("elo", 2 * c, 2 * c + 256), r(bk, 0, 256), r("ehi", 2 * c, 2 * c + 256), sub)
-            cp(r("aa", c, c + 128), r(bk, 0, 128))
-            tt(r("am", c, c + 128), r(bk, 128, 256), r("aa", c, c + 128), mul)
+            cp(r("es", 2 * c, 2 * c + 256), r(bk, 0, 256))
+            tt(r("am", c, c + 128), r(bk, 128, 256), r("es", 2 * c, 2 * c + 128), mul)
+        ts(r("es", 512, 768), r("es", 0, 256), col(10), None, mul)
         steps_of("f1", -LOW)
         scan(r("ka"), r("rst"), r("f1"), mul, add)
 
@@ -581,8 +590,8 @@ def rank_program(g, core, T, topo):
         if t and a < NS:
             bk = r("b%d" % (2 + a % 2))
             act(d, cells, ACT.Copy)
-            mm(bk, r("id_"), d, True, False)
-            mm(bk, r("nid_"), e, False, True)
+            mm(bk, r("nid_"), e, True, False)
+            mm(bk, r("id_"), d, False, True)
             act(out, bk, ACT.Abs)
         else:
             tt(d, cells, e, sub)
@@ -594,22 +603,19 @@ def rank_program(g, core, T, topo):
         for m in range(16):
             mm(rows(n, bk, c + m, c + 128, 16), r("absd", lo + m, hi, 16), BANK, True, True)
         for y, over in [("yb", 320.0)] + ([("zb", FTHR[t])] if t in FTHR else []):
-            if h in YV or t == 0:
-                ts(rows(n, y, c, c + 128), rows(n, bk, c, c + 128), -over, 0.0, add, mx)
-            else:
-                act(rows(n, y, c, c + 128), rows(n, bk, c, c + 128), ACT.Relu, bias=-over)
+            ts(rows(n, y, c, c + 128), rows(n, bk, c, c + 128), -over, 0.0, add, mx)
 
     def half_sums(t):
         for h in range(2):
             c = 256 * h
-            for e in ("ehi", "elo"):
-                mm(r("b7", c, c + 256), r("idm" if t and NS and h == 0 else "id_"), r(e, c, c + 256), e == "ehi", False)
             for m in range(16):
-                mm(r("b7", c + m, c + 256, 16), r("diff", 2048 * h + m, 2048 * h + 2048, 16), HALF, False, m == 15)
+                mm(r("b7", c + m, c + 256, 16), r("diff", 2048 * h + m, 2048 * h + 2048, 16), HALF, True, True)
         for h in range(2):
             c = 128 * h
-            lin(r("aa", c, c + 128), r("b7", 2 * c, 2 * c + 128))
-            tt(r("am", c, c + 128), r("b7", 2 * c + 128, 2 * c + 256), r("aa", c, c + 128), mul)
+            at = 512 if t and h == 0 else 2 * c
+            tt(r("aa", c, c + 128), r("b7", 2 * c, 2 * c + 128), r("es", at, at + 128), add)
+            tt(r("b6", c, c + 128), r("b7", 2 * c + 128, 2 * c + 256), r("es", at + 128, at + 256), add)
+            tt(r("am", c, c + 128), r("b6", c, c + 128), r("aa", c, c + 128), mul)
 
     def verdicts(t):
         out = r("b2", 256, 272)
@@ -641,7 +647,7 @@ def rank_program(g, core, T, topo):
         cp(iv("hi", 32), r("b1", 256, 288))
         ts(iv("oi", 32), iv("hi", 32), 511, None, band)
         cp(uv("ou", 32), iv("oi", 32))
-        act(r("lg", 512, 1024), ind(r("ldw"), uv("ou", 32)), ACT.Identity, scale=col(4))
+        ts(r("lg", 512, 1024), ind(r("ldw"), uv("ou", 32)), col(4), None, mul)
 
     def holders():
         tt(f("vs", 32), r("b4", 32, 64), iv("hi", 32), le)
@@ -653,39 +659,31 @@ def rank_program(g, core, T, topo):
         tt(slot(2), f("na"), f("nhold"), mn)
 
     def decide(t):
-        mm(r("b3", 0, 32), r("id_"), r("kc"), True, False)
+        ts(r("slw", 0, 16), f("q8"), 544.0, None, add)
         tt(r("rdy"), r("lsf%d" % t), f("l1"), eq_)
         tt(r("ab"), r("lsf%d" % t), f("l2"), le)
         scan(r("rs"), f("one"), r("rdy"), mul, add)
-        mm(r("b2", 16, 17), r("blk"), r("rs", 15, 16), True, True)
         mm(r("b2", 0, 16), r("mix"), r("rdy"), True, False)
         mm(r("b2", 0, 16), r("blk"), r("rs"), False, True)
         ts(slot(5), r("ab"), GONE, None, mul)
-        ts(slot(6), r("b2", 0, 16), -48.0, GONE, lt, mul)
-        for oc in range(16):
-            ts(r("oh", 128 * oc, 128 * oc + 128), r("iotas"), r("b2", oc, oc + 1), None, eq_)
-            mm(r("b3", 0, 32), r("oh", 128 * oc, 128 * oc + 128), r("chl", 32 * oc, 32 * oc + 32), False, oc == 15)
-        ts(col(1), r("b2", 16, 17), PRF, PRF, le, mul)
-        ts(f("cm"), r("b2", 0, 16), -48.0, LOWER + NEW, lt, mul)
-        scan(r("l32"), r("alt"), r("b3", 0, 32), mul, add)
-        ts(uv("listu"), r("l32", 1, 32, 2), col(1), None, add)
+        ts(slot(6), r("b2", 0, 16), -1007.0, GONE, lt, mul)
+        tt(f("m1"), r("b2", 0, 16), f("spare"), mn)
+        ts(uv("slot"), f("m1"), 1023.0, None, add)
+        act(ind(r("slw"), uv("slot")), r("pos"), ACT.Silu)
+        ts(f("cm"), r("b2", 0, 16), -1007.0, LOWER + NEW, lt, mul)
+        scan(f("m2"), f("dbig"), r("slw", 0, 16), add, mn)
+        cp(uv("os", 1), f("m2", 1, 15))
+        cp(uv("listu"), ind(r("ct"), uv("os", 1)))
         act(r("snd%d" % t), ind(VD, uv("listu")), ACT.Copy)
         tell(t, "lnd%d" % t, "snd%d" % t, "dd%d" % t)
         tt(f("dec"), slot(5), slot(6), mx)
 
     def keys(t):
         lk = "lkc%d" % t
-        if t in KEYP:
-            kept = r("b0", 0, 256)
-            mm(kept, r("idf"), r("ka"), True, False)
-            for k in range(16):
-                mm(r("b0", k, 256, 16), r("idn"), r("ab"), False, k == 15)
-        else:
-            kept = P1
-            ts(hd("xab"), r("ab"), LOW + NEW, None, mul)
-            scan(P0, r("rst"), r("xab"), mul, add)
-            tt(P1, P0, r("ka"), add)
-        tt(r("s1"), kept, r(("ci", "st", "st", "cf")[t]), mx)
+        ts(hd("xab"), r("ab"), LOW + NEW, None, mul)
+        scan(P0, r("rst"), r("xab"), mul, add)
+        tt(P1, P0, r("ka"), add)
+        tt(r("s1"), P1, r(("ci", "st", "st", "cf")[t]), mx)
         tt(hd(lk), hd(lk), f("cm"), add)
         scan(P0, r("rst"), r(lk), mul, add)
         tt(RES, P0, r("s1"), mx)
@@ -711,7 +709,6 @@ def rank_program(g, core, T, topo):
         cu, cun = ("cua", "cub") if t % 2 == 0 else ("cub", "cua")
         last = t == STEPS - 1
         act(r("cv"), ind(r("iw"), uv(cu)), ACT.Identity, bias=f("clm", 1, t), scale=col(9))
-        mm(r("b5", 0, 256), r("none"), r("rstb"), True, False)
         tt(r(cur, 1, 65, 4), f("home"), r(cur, 2, 66, 4), sub)
         cp(r(cur, 4, 68, 4), iv("sl%d" % ((t + 1) % STEPS)))
         scan(r("po"), r("pf"), r("pt"), mul, add)
@@ -741,19 +738,17 @@ def rank_program(g, core, T, topo):
         if not last:
             cp(r("w1b"), f("w1"))
         tt(r("cg"), ind(r("pw"), uv(cu)), r("diag"), mul)
-        if KU:
-            act(r("f2"), ind(r("pw"), uv(cu)), ACT.Copy)
-            cp(r("ku"), r("f2"))
-        else:
-            cp(r("ku"), ind(r("pw"), uv(cu)))
+        cp(r("ku"), ind(r("pw"), uv(cu)))
         scan(r("cs2"), r("rst"), r("cg"), mul, add)
         PL = tl("cs2")
         for oc in range(16):
             n, at = 256 - 16 * oc, 272 * oc
             ts(deep(T.eq[:, oc, 0:n], "eq", at, at + n, n), r("ku", 16 * oc, 256), r("cs2", 16 * oc + 15, 16 * oc + 16), None, eq_)
             if oc < 15:
-                mm(r("b5", 16 * oc + 16, 256), r("blkh"), deep(T.eq[:, oc, 16:n], "eq", at, at + n, n - 16), False, False)
-        mm(r("b5", 0, 256), r("blkw"), deep(T.eq[:, :, 0:16], "eq", 0, 272 * 16, 256), False, True)
+                mm(r("b5", 16 * oc + 16, 256), r("blkh"), deep(T.eq[:, oc, 16:n], "eq", at, at + n, n - 16), oc == 0, False)
+            if oc == 0:
+                mm(r("b5", 0, 16), r("blkw"), deep(T.eq[:, 0, 0:16], "eq", 0, 16, 16), False, False)
+        mm(r("b5", 16, 256), r("blkw"), deep(T.eq[:, 1:16, 0:16], "eq", 272, 272 * 16, 240), False, True)
         tt(f("k1"), PL, f("sent"), mn)
         tt(r("lq"), r("b5", 0, 256), r("thd"), ge)
         scan(r("ls"), r("rstb"), r("lq"), mul, add)
@@ -791,7 +786,6 @@ def rank_program(g, core, T, topo):
         for a in range(len(CUTS)):
             judge(a, t)
         if t == 0:
-            locks(LA, 8, [r("absd", 3840, 4096)])
             first_keys()
         for h in range(len(PARTS)):
             far(h, t)
@@ -806,7 +800,7 @@ def rank_program(g, core, T, topo):
             first_holders()
         decide(t)
         if t == 0:
-            noflags(NF, 8, [r("lnd0")])
+            noflags(3, 8, [r("lnd0")])
         keys(t)
         cp(ind(VD, uv("listu")), r("lnd%d" % t))
         if t in FLAG:
@@ -817,9 +811,10 @@ def rank_program(g, core, T, topo):
             cp(r("cr"), ind(r("cf"), uv("lperm")))
             dma("y", ext(T.yc[:]), r("cr"), "oyc", 2.0)
             for i in range(64):
-                mm(r("b0", 8 * i, 8 * i + 8), r("big", VO + i, VO + NV, 64), WEIGH, True, True)
+                mm(r("b0", i, 512, 64), r("big", VO + i, VO + NV, 64), WEIGH, True, True)
             for b in range(8):
-                act(r("yt", 64 * b, 64 * b + 64), r("b0", b, 512, 8), ACT.Copy)
+                if b % 4 == 0:
+                    act(r("yt", 64 * b, 64 * b + 256), r("b0", 64 * b, 64 * b + 256), ACT.Copy)
                 dma("ys"[b % 2], ext(T.ys[b]), r("yt", 64 * b, 64 * b + 64), "oys%d" % b, 4.6 - 0.35 * b)
         lanes(t)
     ts(f("iso"), f("w1"), ANEW, None, lt)

@@ -9,25 +9,30 @@ DUM, VO = 0, 256
 FO = VO + FB
 BIGW = FO + NV
 LW = NV + 512
-NEW = 131072.0
-LOW, LOWER = 1048576.0, 2097152.0
+U = 32768.0
+BIG, HUGE = 4194304.0, 16777216.0
 HM = 16384.0
 GONE = 8589934592.0
-ANEW = 8388608.0
-FLAG = {1: 768.0, 2: 2048.0}
-FTHR = {2: 6000.0, 3: 20000.0}
-NS = 3
-CUTS = (512, 512, 512, 512, 1024, 768, 256)
+NAP = 8388608.0
+ANEW = 1024.0
+FLAG = {1: 16384.0, 2: 1048576.0}
+CALM = {1: 2097152.0, 2: 2097152.0, 3: 134217728.0}
+FIRST = ((512, "s"), (512, "s"), (512, "v"), (512, "v"), (1024, "r"), (768, "r"), (256, "r"))
+LATER = ((512, "s"), (512, "s"), (512, "s"), (512, "v"), (1024, "v"), (768, "v"), (256, "v"))
+CUTS = (FIRST, LATER, LATER, LATER)
+YB = ("vvv", "vss", "vss", "vss")
+FILL = ((768, 1792, 1792), (768, 768, 768))
 PARTS = [(0, 2048), (2048, 3840), (3840, 4096)]
 WAKE = 0.15
 CY = 0.00095
 AFIX, FLY, FLYB = 80 * CY, 1.3, 0.0005
 ROUNDS = 30
-TRIES = 6000
+TRIES = 10000
 SHAKE, PUSH, MARK = 0.1, 2.5, 0.5
 HEAT = 0.5
 SEED = 2
 AIMED = 4
+DEBUG = []
 ORDER = []
 
 SCRATCH = {
@@ -37,63 +42,65 @@ SCRATCH = {
     "absd": ("sbuf", [128, 4096], "bfloat16"),
     "lock": ("sbuf", [128, LW], "float32"),
     "eq": ("sbuf", [128, 16, 272], "bfloat16"),
-    "ab3": ("sbuf", [128, 16, 16], "int32"),
-    "res": ("sbuf", [128, 16, 16], "int32"),
+    "res": ("sbuf", [128, 16, 17], "int32"),
+    "cf": ("sbuf", [128, 272], "int32"),
     "ct": ("sbuf", [128, 560], "float32"),
     "slw": ("sbuf", [128, 512], "float32"),
+    "won": ("sbuf", [128, 528], "float32"),
     "ldw": ("sbuf", [128, 272], "bfloat16"),
-    "tla": ("sbuf", [128, 64], "float32"),
-    "tlb": ("sbuf", [128, 80], "int32"),
+    "tla": ("sbuf", [128, 16, 4], "float32"),
+    "tlb": ("sbuf", [128, 16, 4], "int32"),
+    "td": ("sbuf", [128, 16, 4], "float32"),
     "qw": ("sbuf", [128, 144], "float32"),
-    "gib": ("sbuf", [128, 80], "bfloat16"),
+    "gib": ("sbuf", [128, 64], "bfloat16"),
 }
 for _n in ("codes", "yt"):
     SCRATCH[_n] = ("sbuf", [128, 512], "float32")
-for _n in ("csk", "hok", "ci", "cf", "st", "tj"):
+for _n in ("csk", "hok", "ai", "tj"):
     SCRATCH[_n] = ("sbuf", [128, 256], "int32")
-for _n in ("r16", "dj", "rst", "diag", "thd", "ka", "cg", "cs2", "s1", "f1", "f2", "pos", "cr", "hr", "un", "qk", "q16", "pd",
-           "am", "aa", "cv", "xab"):
+for _n in ("r16", "dj", "rst", "diag", "thd", "cg", "cs2", "f1", "f2", "pos", "cr", "hr", "un", "qk", "q16", "pd", "am", "aa", "cv"):
     SCRATCH[_n] = ("sbuf", [128, 256], "float32")
-for _n in ("iw", "pw"):
-    SCRATCH[_n] = ("sbuf", [128, 520], "float32")
-for _n in ("qb", "blkf", "turn", "pt", "pf", "po"):
+for _n in ("iw", "pw", "dg1", "ka", "st", "s1", "s2", "zt"):
+    SCRATCH[_n] = ("sbuf", [128, 272], "float32")
+for _n in ("qb", "blkf", "turn"):
     SCRATCH[_n] = ("sbuf", [128, 128], "float32")
 for _n in ("blk", "nblk", "blkw", "blkh", "mix", "id_", "nid_"):
     SCRATCH[_n] = ("sbuf", [128, 128], "bfloat16")
 SCRATCH["wwin"] = ("sbuf", [128, 144], "bfloat16")
-SCRATCH["lg"] = ("sbuf", [128, 1024], "bfloat16")
-SCRATCH["es"] = ("sbuf", [128, 768], "float32")
-SCRATCH["lgo"] = ("sbuf", [128, 512], "bfloat16")
-for _n in ("yb", "zb"):
-    SCRATCH[_n] = ("sbuf", [128, 384], "bfloat16")
-for _n in ("fa", "fv", "lq", "ls", "rstb"):
+SCRATCH["lg"] = ("sbuf", [128, 512], "bfloat16")
+SCRATCH["yb"] = ("sbuf", [128, 384], "bfloat16")
+for _n in ("fa", "fv", "lq", "ls", "rstb", "lh"):
     SCRATCH[_n] = ("sbuf", [128, 256], "bfloat16")
-QUADS = ["xw", "wx", "td", "rst4", "sm", "lf", "own", "sa", "sb"]
+QUADS = ["pt", "pf", "po", "sm", "lf", "own", "sa", "sb"]
 SCRATCH["quads"] = ("sbuf", [128, 72 * len(QUADS)], "float32")
 for _n in ("coff", "loff", "ku"):
     SCRATCH[_n] = ("sbuf", [128, 256], "uint16")
-FS = ["prf", "col", "clm", "q8", "sent", "home", "one", "cm", "dec", "cls", "vs", "vs2", "hold", "hold2", "nhold", "a32", "a33", "na",
+FS = ["prf", "col", "col2", "clm", "q8", "sent", "home", "one", "vs", "a32", "a33", "xw", "pl", "hd",
       "w", "w1", "nd", "k1", "k2", "k3", "l1", "l2", "m1", "m2", "spare", "dbig", "yl", "iso"]
-IS = ["oi", "oi2", "hi", "hi2", "pi", "by", "sl0", "sl1", "sl2", "sl3", "nw", "h0", "pr", "pg", "wk"]
-US = ["xu", "xv", "ou", "ou2", "cua", "cub", "offu", "listu", "slot", "os", "lc", "lr", "lrev", "lperm", "lq", "ldup", "ldup2"]
+IS = ["oi", "oi2", "hi", "pi", "by", "sl0", "sl1", "sl2", "sl3", "nw", "pr", "pg", "wk"]
+US = ["xu", "xv", "ou", "cua", "cub", "offu", "listu", "slot", "os", "lc", "lr", "lrev", "lperm", "lq", "ldup", "ldup2", "lk", "lk2"]
 SCRATCH["fs"] = ("sbuf", [128, 16 * len(FS)], "float32")
 SCRATCH["is_"] = ("sbuf", [128, 16 * len(IS)], "int32")
 SCRATCH["us"] = ("sbuf", [128, 16 * len(US)], "uint16")
-for _n in ("rdy", "rs", "ab", "w1b", "winb"):
+for _n in ("rdy", "rs", "w1b"):
     SCRATCH[_n] = ("sbuf", [128, 16], "bfloat16")
+for _n in ("cla", "clb"):
+    SCRATCH[_n] = ("sbuf", [128, 32], "bfloat16")
 for _t in range(STEPS):
     SCRATCH["sf%d" % _t] = ("sbuf", [128, 16], "bfloat16")
     SCRATCH["lsf%d" % _t] = ("sbuf", [128, 16], "bfloat16")
-    SCRATCH["skg%d" % _t] = ("sbuf", [128, 256], "float32")
-    SCRATCH["lkc%d" % _t] = ("sbuf", [128, 256], "float32")
+    SCRATCH["fu%d" % _t] = ("sbuf", [128, 16], "bfloat16")
+    SCRATCH["lfu%d" % _t] = ("sbuf", [128, 16], "bfloat16")
+    SCRATCH["skg%d" % _t] = ("sbuf", [128, 272], "float32")
+    SCRATCH["lkc%d" % _t] = ("sbuf", [128, 272], "float32")
     SCRATCH["snd%d" % _t] = ("sbuf", [128, 256], "bfloat16")
     SCRATCH["lnd%d" % _t] = ("sbuf", [128, 256], "bfloat16")
 for _b in range(8):
-    SCRATCH["b%d" % _b] = ("psum", [128, 512], "float32")
+    SCRATCH["b%d" % _b] = ("psum", [128, 16, 32] if _b == 1 else [128, 512], "float32")
 
 SEMAPHORES = ["c" + q for q in "vspgy"] + ["dcs", "dho", "dwk", "dsn", "ds2", "dx0", "dx1", "oyc", "oyh", "oyl"] + ["oys%d" % _g for _g in range(8)]
 for _t in range(STEPS):
-    SEMAPHORES += [k + str(_t) for k in ("rsf", "rkc", "rdd", "qsf", "qkc", "qdd")]
+    SEMAPHORES += [k + str(_t) for k in ("rsf", "rkc", "rdd", "qsf", "qkc", "qdd") + (("rfu", "qfu") if _t else ())]
 
 
 def emitter(g, T):
@@ -149,6 +156,15 @@ def emitter(g, T):
     def op(q, call, outs, ins, cost):
         rd = [x for o in ins for x in o[1]] + [x for o in outs for x in o[1][1:]]
         prog.append((q, "op", call, rd, [o[1][0] for o in outs], cost, cost, None))
+
+    def block(n):
+        part = prog[-n:]
+        del prog[-n:]
+        rd, wr, cost = [], [], sum(p[5] for p in part)
+        for p in part:
+            rd += [x for x in p[3] if x not in rd]
+            wr += [x for x in p[4] if x not in wr]
+        prog.append((part[0][0], "block", None, rd, wr, cost, cost, part))
 
     def dma(q, out, in_, sem, lat):
         call = lambda: eng[q].dma_start(out=out[0], in_=in_[0]).then_inc(T.sem[sem], 16)
@@ -280,13 +296,13 @@ def emitter(g, T):
                 now, had = start, w
                 if w < least:
                     best, least = start, w
+        DEBUG.extend([prog, fore, back, best, way])
         return sorted(range(m), key=lambda i: (best[i], i))
 
     def issue():
         if not ORDER:
             ORDER.extend(order())
-        for i in ORDER:
-            q, kind, call, rd, wr, occ, lat, x = prog[i]
+        for q, kind, call, rd, wr, occ, lat, x in [p for i in ORDER for p in (prog[i][7] if prog[i][1] == "block" else [prog[i]])]:
             if kind == "land":
                 final[x[0]] = x[1]
                 hist.setdefault(wr[0][0], []).append((wr[0][1], True, "net", True, (x[0], x[1], {x[0]: x[1]})))
@@ -304,14 +320,14 @@ def emitter(g, T):
             if known["g"].get(s, 0) < final[s]:
                 g.wait_ge(T.sem[s], final[s])
 
-    return op, dma, send, issue
+    return op, block, dma, send, issue
 
 
 def rank_program(g, core, T, topo):
     rank = T.rank_of(core)
     if rank is None:
         return
-    op, dma, send, issue = emitter(g, T)
+    op, block, dma, send, issue = emitter(g, T)
 
     def r(n, a=None, b=None, st=None):
         if n in QUADS:
@@ -395,16 +411,24 @@ def rank_program(g, core, T, topo):
     def iota(out, pat, base, cm=0, after=()):
         op("g", lambda: g.iota(out[0], pat, base, cm, allow_small_or_imprecise_dtypes=True), [out], list(after), 0.13 + 2 * CY * out[2])
 
-    def keep(out, a, pat, cmp, fill, cm=0):
-        op("g", lambda: g.affine_select(out[0], a[0], pat, cmp, fill, 0, cm), [out], [a], 0.17 + 2 * CY * out[2])
+    def keep(out, a, pat, cmp, fill, cm=0, base=0):
+        op("g", lambda: g.affine_select(out[0], a[0], pat, cmp, fill, base, cm), [out], [a], 0.17 + 2 * CY * out[2])
+
+    def four(n, a, b=None):
+        if b is None:
+            return (T[n][:, :, a], [(n, (a, 64, 4))], 16)
+        return deep(T[n][:, :, a:b], n, 0, 64, 16 * (b - a))
+
+    def gate(n):
+        return r(n, 0, 272, 17)
 
     def tell(t, out, in_, name):
         send(topo, core, T.cores[rank ^ (1 + t)], r(out), r(in_), name, r(in_)[2] * (2 if kind(r(in_))[2] else 4))
 
     add, sub, mul, mx, mn = ALU.add, ALU.subtract, ALU.mult, ALU.max, ALU.min
     band, shr, eq_, ge, gt, lt, le = ALU.bitwise_and, ALU.arith_shift_right, ALU.is_equal, ALU.is_ge, ALU.is_gt, ALU.is_lt, ALU.is_le
-    RES, RES4 = deep(T.res[:], "res", 0, 256, 256), deep(T.res[:, :, 0:4], "res", 0, 256, 64)
-    P0, P1 = r("b6", 0, 256), r("b6", 256, 512)
+    RES = deep(T.res[:], "res", 0, 272, 272)
+    P0 = r("b6", 0, 256)
 
     def col(i):
         return f("col", 1, i)
@@ -422,27 +446,31 @@ def rank_program(g, core, T, topo):
     iota(iv("pr", 1), [[0, 1]], 0, 1)
     iota(r("dj"), [[0, 8], [16, 32]], NV)
     iota(r("codes"), [[0, 2], [1, 256]], 17)
-    iota(r("lock", 6656, NV), [[0, 1536]], 0)
+    at = sum(FILL[0] + FILL[1])
+    iota(r("lock", at, NV), [[0, NV - at]], 0)
     iota(f("q8"), [[1, 16]], 0)
     iota(f("one"), [[0, 16]], 1)
     iota(f("clm", 4), [[1024, 4]], 1520)
-    iota(r("lf", 0, 16), [[1, 16]], 0)
-    iota(r("lf", 16, 32), [[-1, 16]], 15)
+    iota(r("lf", 0, 16), [[-1, 16]], 15)
     iota(r("own"), [[512, 4], [16, 16]], 513)
     iota(r("qw"), [[1, 144]], -15)
     iota(r("r16"), [[0, 16], [1, 16]], 0)
-    iota(r("lf", 32, 64), [[1, 16], [0, 2]], 0)
+    iota(r("lf", 16, 48), [[1, 16], [0, 2]], 0)
     iota(r("qb"), [[1, 8], [0, 16]], 0)
-    iota(r("iw", 1, 513), [[0, 2], [1, 256]], 1)
-    iota(r("q16"), [[1, 16], [0, 16]], int(ANEW) + 1)
+    iota(f("a32", 17), [[256, 17]], -16)
+    iota(f("col2", 4), [[-int(U), 4]], 1 - int(U))
     iota(r("pos"), [[32, 16], [1, 16]], 32)
-    for n, k in (("rst", 16), ("rstb", 16), ("pf", 8), ("rst4", 4), ("sm", 4)):
+    for n, k in (("rst", 16), ("rstb", 16), ("pf", 4), ("sm", 4)):
         iota(r(n), [[0, r(n)[2]]], 1)
         keep(r(n), r(n), [[0, 16], [1, k]], gt, 0.0)
-    iota(f("a32"), [[8, 16]], 7)
+    for i, x in ((2, GONE / HM), (3, HM)):
+        keep(r("pf"), r("pf"), [[0, 16], [1, 4]], ALU.not_equal, x, 0, -i)
+    iota(f("vs"), [[4, 16]], 3)
     iota(r("turn"), [[0, 128]], 1)
     keep(r("turn"), r("turn"), [[-1, 16], [-16, 8]], eq_, 0.0, 1)
-    for x in (r("tlb", 64, 80), r("pt"), r("xw"), r("ldw"), r("xab"), r("big", DUM, VO)):
+    iota(r("iw", 1, 257), [[1, 256]], 1)
+    iota(r("q16"), [[32, 16], [0, 16]], 16)
+    for x in (r("sa", 0, 144), r("ldw", 0, 1), r("zt"), r("big", DUM, VO), r("won", 0, 272)):
         iota(x, [[0, x[2]]], 0)
 
     def noflags(a, b, after=()):
@@ -451,17 +479,21 @@ def rank_program(g, core, T, topo):
 
     noflags(0, 3)
 
-    ms(r("lock", 0, 768), 0.0)
-    ms(r("lock", 768, 2560), 0.0)
-    for a, n in ((2560, 768), (3328, 768), (4096, 2560)):
-        act(r("lock", a, a + n), r("lock", 0, n), ACT.Copy)
+    at = 0
+    for n in FILL[0]:
+        ms(r("lock", at, at + n), 0.0)
+        at += n
+    for i, n in enumerate(FILL[1]):
+        act(r("lock", at, at + n), r("lock", 0, n), ACT.Copy if i else ACT.Silu)
+        at += n
     ts(iv("pg", 1, 0), iv("pr", 1), 15, None, band)
     cp(f("prf", 1), iv("pg", 1))
     ts(r("dj"), r("dj"), f("prf", 1), None, add)
-    ts(r("f1"), r("hok"), -100000.0, 100000.0, mul, add)
-    tt(r("f1"), r("f1"), r("csk"), add)
-    tt(r("f1"), r("f1"), r("dj"), mn)
-    cp(r("loff"), r("f1"))
+    for a, b in ((0, 64), (64, 256)):
+        ts(r("f1", a, b), r("hok", a, b), -100000.0, 100000.0, mul, add)
+        tt(r("f1", a, b), r("f1", a, b), r("csk", a, b), add)
+        tt(r("f1", a, b), r("f1", a, b), r("dj", a, b), mn)
+        cp(r("loff", a, b), r("f1", a, b))
     for c in range(8):
         act(ind(r("lock"), r("loff", 32 * c, 32 * c + 32)), r("codes"), ACT.Silu)
 
@@ -482,19 +514,32 @@ def rank_program(g, core, T, topo):
     ts(col(14), PRF, 16.0, None, mul)
     ts(col(15), PRF, 1.0, None, add)
     ts(r("wwin"), r("qw"), G16, col(5), eq_, mul)
-    ts(uv("lperm", 64), r("lf"), col(14), None, add)
-    cp(uv("lc"), f("a32"))
+    ts(uv("lq", 48), r("lf", 0, 48), col(14), None, add)
+    ts(col(10), PRF, 17.0, 1.0, mul, add)
+    ts(uv("lperm"), f("q8"), col(10), None, add)
+    cp(uv("lc"), f("vs"))
     ts(uv("lr"), f("q8"), 0.0, PRF, mul, add)
     ts(uv("lrev"), f("q8"), 240.0, col(14), add, sub)
     cp(r("coff"), r("csk"))
-    cp(r("ci"), ind(r("csk"), uv("lperm")))
-    BANK, HALF, WEIGH, OVER, FLAGD = r("gib", 0, 8), r("gib", 8, 24), r("gib", 24, 32), (32, 48), (48, 64)
+    ts(f("a32", 17), f("a32", 17), col(14), None, add)
+    ts(iv("oi", 17), f("a32", 17), -112.0, 1.0 / 272, add, mul)
+    ts(f("k1", 17), iv("oi", 17), -271.0, None, mul)
+    tt(f("k1", 17), f("k1", 17), f("a32", 17), add)
+    cp(uv("lk", 17), f("k1", 17))
+    cp(r("st"), ind(r("csk"), uv("lk", 17)))
+    ts(col(11), iv("pr", 1), 16.0, None, ge)
+    ts(f("col2", 4), f("col2", 4), col(11), None, mul)
+    for t in FLAG:
+        ts(f("col2", 1, 4 + t), col(2), FLAG[t], None, mul)
+    for n, a, x in (("cla", 0, 16 * U - BIG), ("cla", 16, -HUGE), ("clb", 0, -2 * BIG)):
+        ms(r(n, a, a + 16), x)
+    BANK, HALF, WEIGH, OVER = r("gib", 0, 8), r("gib", 8, 24), r("gib", 24, 32), (32, 48)
     ts(BANK, f("q8", 8), PGF, None, eq_)
+    ts(r("gib", 48, 56), f("q8", 8), PGF, -1.0, eq_, mul)
     ts(r("gib", 8, 16), f("q8", 8), PGF, col(2), eq_, mul)
     ts(r("gib", 16, 24), f("q8", 8), PGF, col(6), eq_, mul)
     ts(WEIGH, f("q8", 8), PGF, col(15), eq_, mul)
     ts(r("gib", *OVER), f("q8"), PRF, -32.0, eq_, mul)
-    ts(r("gib", *FLAGD), f("q8"), PRF, -8192.0, eq_, mul)
     ts(r("diag"), r("r16"), PRF, None, eq_)
     ts(r("blk"), r("qb"), PGF, None, eq_)
     ts(r("nblk"), r("qb"), PGF, -1.0, eq_, mul)
@@ -504,7 +549,6 @@ def rank_program(g, core, T, topo):
     keep(r("nid_"), r("nblk"), [[-1, 128]], eq_, 0.0, 1)
     keep(r("mix"), r("nblk"), [[-1, 128]], ge, 0.0, 1)
     keep(r("mix"), r("mix"), [[-1, 128]], ALU.not_equal, -1024.0, 1)
-    ts(col(10), iv("pr", 1), 32.0 * NS, None, ge)
     ts(f("home"), f("q8"), 16.0, col(15), mul, add)
     ts(r("own"), r("own"), PRF, None, add)
     ts(f("sent"), f("home"), NV - 1.0, None, add)
@@ -524,30 +568,30 @@ def rank_program(g, core, T, topo):
     cp(r("cr"), ind(r("csk"), uv("lrev")))
     cp(r("hr"), ind(r("hok"), uv("lrev")))
     ts(r("un"), r("hr"), -1.0, 1.0, mul, add)
-    lin(r("s1"), r("hr"), -18.0, 17.0)
+    lin(r("cv"), r("hr"), -18.0, 17.0)
     scan(r("cs2"), r("rst"), r("un"), mul, add)
-    ts(f("w"), tl("cs2"), -1.0, 17.0, mul, add)
-    ts(r("w1b"), tl("cs2"), -1.0, 17.0, mul, add)
+    ts(f("w"), tl("cs2"), -1.0, 16.0 - ANEW, mul, add)
+    ts(r("w1b"), tl("cs2"), -1.0, 16.0, mul, add)
     lin(r("cg"), r("cs2"), -1.0, 17.0)
-    tt(r("pd"), r("s1"), r("cg"), mn)
-    act(r("qk"), ind(r("pd"), uv("lq")), ACT.Copy)
+    tt(r("pd"), r("cv"), r("cg"), mn)
+    lin(r("qk"), ind(r("pd"), uv("lq")), 32.0, 16.0 - 32.0 * (ANEW + 1))
     tt(r("qk"), r("qk"), r("q16"), sub)
+    lin(r("dg1", 1, 257), r("diag"), 32.0)
     ms(hd("hr"), 0.0)
     ms(hd("un"), 1.0)
     tt(r("f2"), r("un"), r("cr"), mul)
     for n in range(4):
         scan(P0, r("hr"), r("f2"), mul, add)
-        cp(r("tla", n, 64, 4), r("b6", 15, 256, 16))
+        cp(four("tla", n), r("b6", 15, 256, 16))
         if n < 3:
             tt(r("f2", 1, 256), r("b6", 0, 255), r("un", 1, 256), mul)
             cp(hd("f2"), hd("cr"))
-    cp(uv("xu"), r("tla", 0, 64, 4))
+    cp(uv("xu"), four("tla", 0))
     cp(r("sa", 2, 66, 4), f("home"))
-    ts(iv("nw"), iv("wk"), -256.0, 3840.0, mul, add)
+    ts(iv("nw"), iv("wk"), -NAP, 15 * NAP, mul, add)
     for t in range(STEPS):
-        ts(iv("sl%d" % t), iv("nw"), t, 256, shr, band)
-    tt(f("k2"), f("home"), iv("sl0"), add)
-    cp(uv("cua"), f("k2"))
+        ts(iv("sl%d" % t), iv("nw"), t, int(NAP), shr, band)
+    cp(uv("cua"), f("home"))
 
     V = r("big", VO, VO + NV)
     VF = r("big", VO, BIGW)
@@ -558,220 +602,231 @@ def rank_program(g, core, T, topo):
     def pick(out, w, src, n):
         for m in range(16):
             mm(out, r(w, 15 - m, 143 - m), r(src, m, n, 16), m == 0, m == 15)
+            if m % 8 == 7:
+                block(8)
 
-    def steps_of(out, head):
-        for h in range(2):
-            mm(r("b1", 128 * h, 128 * h + 128), r("am", 128 * h, 128 * h + 128), r("turn"), True, True)
-        for h in range(2):
-            cp(deep(T.ab3[:, :, 8 * h:8 * h + 8], "ab3", 0, 256, 128), r("b1", 128 * h, 128 * h + 128))
-        ts(r("tj"), deep(T.ab3[:], "ab3", 0, 256, 256), 3, 511, shr, band)
-        ts(iv("h0"), deep(T.ab3[:, :, 0], "ab3", 0, 256, 16), 3, 8191, shr, band)
-        ts(r(out), r("tj"), 1.0, None, add)
-        if isinstance(head, tuple):
-            tt(hd(out), iv("h0"), head, add)
-        else:
-            ts(hd(out), iv("h0"), head, None, add)
+    def sums(bk, c0, c1, src, x, lo, hi, kinds, t, src2, x2, size):
+        runs, at = [], 0
+        for n, q in CUTS[t]:
+            if lo <= at < hi:
+                if runs and runs[-1][2] == (q in kinds):
+                    runs[-1][1] += n
+                else:
+                    runs.append([at, at + n, q in kinds])
+            at += n
+        for m in range(16):
+            for a, b, more in runs:
+                out = (T[bk][(a - lo) // 16:(b - lo) // 16, c0 + m:c1:16],) + r(bk, c0 + m, c1, 16)[1:]
+                mm(out, r(src, a + m, b, 16), x, True, not more)
+                if more:
+                    mm(out, r(src2, a + m, b, 16), x2, False, True)
+            if m % size == size - 1:
+                block(size * sum(1 + more for a, b, more in runs))
 
-    def first_keys():
+    def steps_of(out, src, less, t, banks, unit, cls):
         for h in range(2):
-            bk, c = ("b4", "b5")[h], 128 * h
-            for m in range(16):
-                mm(r(bk, m, 256, 16), r("ea", 2048 * h + m, 2048 * h + 2048, 16), HALF, True, True)
-            cp(r("es", 2 * c, 2 * c + 256), r(bk, 0, 256))
-            tt(r("am", c, c + 128), r(bk, 128, 256), r("es", 2 * c, 2 * c + 128), mul)
-        ts(r("es", 512, 768), r("es", 0, 256), col(10), None, mul)
-        steps_of("f1", -LOW)
-        scan(r("ka"), r("rst"), r("f1"), mul, add)
+            bk, c, lo = banks[h], 128 * h, 2048 * h
+            sums(bk, 0, 256, src, HALF, lo, lo + 2048, less, t, "ea", HALF, 4)
+            act(r("aa", c, c + 128), r(bk, 0, 128), ACT.Copy)
+            tt(r("ai", c, c + 128), r(bk, 128, 256), r("aa", c, c + 128), mul)
+            ts(r("tj", c, c + 128), r("ai", c, c + 128), 3, 511, shr, band)
+            if h == 0:
+                ts(rows(16, "tj", 0, 128), rows(16, "ai", 0, 128), 3, NV - 1, shr, band)
+            ts(r("am", c, c + 128), r("tj", c, c + 128), 1 - unit * U if h else f("col2", 1, unit - 1), None, add)
+        mm(deep(T.b1[:, :, 0], "b1", 0, 512, 16), r("id_"), r("cla", 16, 32), True, False)
+        for h in range(2):
+            mm(deep(T.b1[:, :, 1 + 8 * h:9 + 8 * h], "b1", 0, 512, 128), r("am", 128 * h, 128 * h + 128), r("turn"), False, False)
+        mm(deep(T.b1[:, :, 1], "b1", 0, 512, 16), r("id_"), r(cls, 0, 16), False, True)
+        act(r(out), deep(T.b1[:, :, 0:17], "b1", 0, 512, 272), ACT.Copy)
 
     def judge(a, t):
-        lo, hi = sum(CUTS[:a]), sum(CUTS[:a + 1])
+        lo = sum(n for n, q in CUTS[t][:a])
+        hi = lo + CUTS[t][a][0]
         d, e, out = (r(n, lo, hi) for n in ("diff", "ea", "absd"))
         cells = ind(V if t < 2 else VF, r("coff", lo // 16, hi // 16))
-        if t and a < NS:
-            bk = r("b%d" % (2 + a % 2))
+        if CUTS[t][a][1] == "s":
+            bk = r("b%d" % (2 + a % 2), 0, hi - lo)
             act(d, cells, ACT.Copy)
             mm(bk, r("nid_"), e, True, False)
             mm(bk, r("id_"), d, False, True)
             act(out, bk, ACT.Abs)
         else:
             tt(d, cells, e, sub)
-            act(out, d, ACT.Abs)
+            if CUTS[t][a][1] == "r":
+                ts(out, d, 0.0, 2.0, mx, mul)
+            else:
+                act(out, d, ACT.Abs)
 
     def far(h, t):
         c, (lo, hi) = 128 * h, PARTS[h]
         n, bk = (hi - lo) // 16, ("b0", "b0", "b3")[h]
-        for m in range(16):
-            mm(rows(n, bk, c + m, c + 128, 16), r("absd", lo + m, hi, 16), BANK, True, True)
-        for y, over in [("yb", 320.0)] + ([("zb", FTHR[t])] if t in FTHR else []):
-            ts(rows(n, y, c, c + 128), rows(n, bk, c, c + 128), -over, 0.0, add, mx)
-
-    def half_sums(t):
-        for h in range(2):
-            c = 256 * h
-            for m in range(16):
-                mm(r("b7", c + m, c + 256, 16), r("diff", 2048 * h + m, 2048 * h + 2048, 16), HALF, True, True)
-        for h in range(2):
-            c = 128 * h
-            at = 512 if t and h == 0 else 2 * c
-            tt(r("aa", c, c + 128), r("b7", 2 * c, 2 * c + 128), r("es", at, at + 128), add)
-            tt(r("b6", c, c + 128), r("b7", 2 * c + 128, 2 * c + 256), r("es", at + 128, at + 256), add)
-            tt(r("am", c, c + 128), r("b6", c, c + 128), r("aa", c, c + 128), mul)
+        sums(bk, c, c + 128, "absd", BANK, lo, hi, "r", t, "diff", r("gib", 48, 56), 8)
+        if YB[t][h] == "s":
+            act(rows(n, "yb", c, c + 128), rows(n, bk, c, c + 128), ACT.Relu, bias=-320.0)
+        else:
+            ts(rows(n, "yb", c, c + 128), rows(n, bk, c, c + 128), -320.0, 0.0, add, mx)
 
     def verdicts(t):
         out = r("b2", 256, 272)
         mm(out, r("id_"), r("w1b"), True, False)
         for h, (lo, hi) in enumerate(PARTS):
             n = (hi - lo) // 16
-            mm(out, rows(n, "yb", 128 * h, 128 * h + 128), rows(n, "gib", *OVER), False, t == 0 and h == 2)
-            if t in FTHR:
-                mm(out, rows(n, "zb", 128 * h, 128 * h + 128), rows(n, "gib", *FLAGD), False, False)
+            mm(out, rows(n, "yb", 128 * h, 128 * h + 128), rows(n, "gib", *OVER), False, h == len(PARTS) - 1)
         if t:
-            mm(out, r("id_"), r("winb"), False, True)
-        ts(r("sf%d" % t), out, 0.0, None, mx)
+            ts(r("sf%d" % t), out, 0.0, None, lt)
+        else:
+            ts(r("sf0"), out, 1.0, 0.0, add, mx)
+            ts(f("l1"), r("sf0"), -1.0, 34.0, mul, add)
+            ts(f("l2"), r("sf0"), 0.0, 1.0e9, eq_, mul)
         tell(t, "lsf%d" % t, "sf%d" % t, "sf%d" % t)
-        ts(f("l1"), r("sf%d" % t), -1.0, 34.0, mul, add)
-        ts(f("l2"), r("sf%d" % t), 0.0, 1.0e9, eq_, mul)
 
     def slot(i):
-        return r("pt", i, 128, 8)
+        return r("pt", i, 64, 4)
 
     def first_holders():
         act(r("lg", 0, 256), ind(LK, uv("xu")), ACT.Relu, bias=col(8), scale=col(7))
         pick(r("b4", 0, 16), "wwin", "lg", 256)
-        ts(slot(3), r("b4", 0, 16), HM, None, mul)
-        cp(slot(4), r("tla", 0, 64, 4))
+        cp(slot(2), r("b4", 0, 16))
+        cp(slot(3), four("tla", 0))
 
-    def old_holders():
-        act(r("lgo"), ind(LK, uv("xu", 32)), ACT.Relu, bias=col(8), scale=col(7))
-        pick(r("b1", 256, 288), "wwin", "lgo", 512)
-        cp(iv("hi", 32), r("b1", 256, 288))
-        ts(iv("oi", 32), iv("hi", 32), 511, None, band)
-        cp(uv("ou", 32), iv("oi", 32))
-        ts(r("lg", 512, 1024), ind(r("ldw"), uv("ou", 32)), col(4), None, mul)
-
-    def holders():
-        tt(f("vs", 32), r("b4", 32, 64), iv("hi", 32), le)
-        tt(f("vs", 32), iv("oi", 32), f("vs", 32), mul)
-        ts(f("hold", 32), f("vs", 32), HM, None, mul)
-        ts(f("nhold"), f("vs"), -HM, None, mul)
-        tt(slot(0), f("a32", 16, 16), f("hold", 16, 16), mx)
-        tt(slot(3), f("a32"), f("hold"), mx)
-        tt(slot(2), f("na"), f("nhold"), mn)
+    def holders(mine):
+        tt(f("hd"), r("b4", 1, 32, 2), mine, sub)
+        tt(f("hd"), f("hd"), f("xw"), mul)
+        tt(iv("hi"), r("b4", 0, 32, 2), f("hd"), add)
+        ts(iv("oi"), iv("hi"), 511, None, band)
+        cp(uv("ou"), iv("oi"))
+        lin(r("lh"), ind(r("ldw"), uv("ou")), col(4))
+        pick(r("b4", 32, 48), "wwin", "lh", 256)
+        tt(f("vs"), r("b4", 32, 48), iv("hi"), le)
+        tt(slot(2), iv("oi"), f("vs"), mul)
 
     def decide(t):
-        ts(r("slw", 0, 16), f("q8"), 544.0, None, add)
-        tt(r("rdy"), r("lsf%d" % t), f("l1"), eq_)
-        tt(r("ab"), r("lsf%d" % t), f("l2"), le)
+        iota(r("slw", 0, 16), [[1, 16]], 544)
+        if t:
+            tt(r("rdy"), r("lfu%d" % t), r("fu%d" % t), mul)
+        else:
+            tt(r("rdy"), r("lsf0"), f("l1"), eq_)
+        rk = r("b5", 256, 272)
         scan(r("rs"), f("one"), r("rdy"), mul, add)
-        mm(r("b2", 0, 16), r("mix"), r("rdy"), True, False)
-        mm(r("b2", 0, 16), r("blk"), r("rs"), False, True)
-        ts(slot(5), r("ab"), GONE, None, mul)
-        ts(slot(6), r("b2", 0, 16), -1007.0, GONE, lt, mul)
-        tt(f("m1"), r("b2", 0, 16), f("spare"), mn)
+        mm(rk, r("mix"), r("rdy"), True, False)
+        mm(rk, r("blk"), r("rs"), False, True)
+        ts(slot(1), rk, -1007.0, None, lt)
+        tt(f("m1"), rk, f("spare"), mn)
         ts(uv("slot"), f("m1"), 1023.0, None, add)
         act(ind(r("slw"), uv("slot")), r("pos"), ACT.Silu)
-        ts(f("cm"), r("b2", 0, 16), -1007.0, LOWER + NEW, lt, mul)
+        ts(gate("zt"), slot(1), 2 * BIG + 64 * U, None, mul)
         scan(f("m2"), f("dbig"), r("slw", 0, 16), add, mn)
         cp(uv("os", 1), f("m2", 1, 15))
         cp(uv("listu"), ind(r("ct"), uv("os", 1)))
         act(r("snd%d" % t), ind(VD, uv("listu")), ACT.Copy)
         tell(t, "lnd%d" % t, "snd%d" % t, "dd%d" % t)
-        tt(f("dec"), slot(5), slot(6), mx)
+
+    def aborts(t):
+        if t:
+            tt(slot(0), r("lsf%d" % t), r("sf%d" % t), mx)
+        else:
+            tt(slot(0), r("lsf0"), f("l2"), le)
+        tt(f("nd"), slot(0), slot(1), eq_)
 
     def keys(t):
-        lk = "lkc%d" % t
-        ts(hd("xab"), r("ab"), LOW + NEW, None, mul)
-        scan(P0, r("rst"), r("xab"), mul, add)
-        tt(P1, P0, r("ka"), add)
-        tt(r("s1"), P1, r(("ci", "st", "st", "cf")[t]), mx)
-        tt(hd(lk), hd(lk), f("cm"), add)
-        scan(P0, r("rst"), r(lk), mul, add)
-        tt(RES, P0, r("s1"), mx)
+        scan(r("b5", 0, 272), r("lkc%d" % t), r("zt"), add, mx)
+        ts(gate("st"), slot(0), BIG, None, mul)
+        now = "st"
+        for n, steps in enumerate(["ka"] + ["skg%d" % u for u in range(1, t + 1)]):
+            scan(r("s%d" % (1 + n % 2)), r(steps), r(now), add, mx)
+            now = "s%d" % (1 + n % 2)
+        tt(RES, r("b5", 0, 272), r(now), mx)
         if t == STEPS - 1:
             ts(r("cf"), RES, NV - 1, None, band)
             return
         ts(r("cf"), RES, NV - 1 + FB, None, band)
         cp(r("coff"), ind(r("cf"), uv("lperm")))
         if t < 2:
-            ts(P1, RES, NEW, float(FB), ge, mul)
+            P1 = deep(T.b1[:, :, 0:17], "b1", 0, 512, 272)
+            ts(P1, RES, U, float(FB), ge, mul)
             tt(r("st"), P1, r("cf"), add)
+        else:
+            cp(r("st"), r("cf"))
 
     def flags(t):
         mm(r("b2", 0, 256), r("nid_"), r("snd%d" % t), True, False)
         mm(r("b2", 0, 256), r("id_"), r("lnd%d" % t), False, True)
         act(r("fa"), r("b2", 0, 256), ACT.Abs)
         mm(r("b3", 0, 256), r("blk"), r("fa"), True, True)
-        ts(r("fv"), r("b3", 0, 256), 320.0, FLAG[t], gt, mul)
+        ts(r("fv"), r("b3", 0, 256), 320.0, f("col2", 1, 4 + t), gt, mul)
         cp(ind(FD, uv("listu")), r("fv"))
 
     def lanes(t):
         cur, curn = ("sa", "sb") if t % 2 == 0 else ("sb", "sa")
         cu, cun = ("cua", "cub") if t % 2 == 0 else ("cub", "cua")
         last = t == STEPS - 1
-        act(r("cv"), ind(r("iw"), uv(cu)), ACT.Identity, bias=f("clm", 1, t), scale=col(9))
+        if last:
+            act(r("cv"), ind(r("dg1"), uv(cu)), ACT.Copy)
+        else:
+            act(r("cv"), ind(r("iw"), uv(cu)), ACT.Identity, bias=f("clm", 1, t), scale=col(9))
         tt(r(cur, 1, 65, 4), f("home"), r(cur, 2, 66, 4), sub)
-        cp(r(cur, 4, 68, 4), iv("sl%d" % ((t + 1) % STEPS)))
         scan(r("po"), r("pf"), r("pt"), mul, add)
         tt(r("pd"), ind(r("po"), uv("lc")), r("diag"), mul)
         mm(r("b4", 0, 256), r("blkf"), r("pd"), True, True)
         act(r("pw", 1, 257), r("b4", 0, 256), ACT.Copy)
-        lin(r("pw", 257, 513), r("b4", 0, 256), 1.0 / 512, 512 * HM)
+        d = STEPS - 1 - t
         if not last:
-            act(r("b4", 256, 512), r("b4", 0, 256), ACT.Relu, bias=-1.0, scale=(t + 2) / GONE)
-            tt(r("ldw", 1, 257), r("b4", 256, 512), r("ldw", 1, 257), mx)
-            ts(r("tla"), r("tla"), NEW / 2, None, add)
-            ts(r("tlb", 0, 64), RES4, NV - 1 + int(NEW), None, band)
-            tt(r("tlb", 0, 64), r("tlb", 0, 64), r("tla"), mx)
-            ts(r("tlb", 0, 64), r("tlb", 0, 64), NV - 1, None, band)
-            cp(uv("xu"), r("tlb", 0, 64, 4))
-            cp(uv("xv"), r("tlb", 1, 64, 4))
-            tt(r("td"), r("tlb", 1, 65), r("tlb", 0, 64), sub)
-            tt(slot(1), r("tlb", 1, 65, 4), r("tlb", 0, 64, 4), sub)
-            cp(slot(4), r("tlb", 0, 64, 4))
-            old_holders()
-        else:
-            cp(uv("xu"), r("tla", 0, 64, 4))
-        ts(f("nd"), f("dec"), 0.0, GONE, eq_, mul)
-        ts(f("nd"), f("nd"), ANEW + 1, None, mx)
-        tt(f("w1"), f("w"), f("dec"), mx)
-        tt(f("w1"), f("w1"), f("nd"), mn)
+            act(r("b4", 256, 512) if t else r("ldw", 1, 257), r("b4", 0, 256), ACT.Relu, bias=-1.0, scale=(t + 2) / GONE)
+            if t:
+                tt(r("ldw", 1, 257), r("b4", 256, 512), r("ldw", 1, 257), mx)
+            ts(four("tla", 0, d + 1), four("tla", 0, d + 1), U, None, add)
+            tt(four("tlb", 0, d + 1), deep(T.res[:, :, 1:d + 2], "res", 0, 272, 16 * d + 16), four("tla", 0, d + 1), mx)
+            ts(four("tlb", 0, d + 1), four("tlb", 0, d + 1), NV - 1, None, band)
+            cp(uv("xu", 32), four("tlb", 0, 2))
+            tt(four("td", 0, d), four("tlb", 1, d + 1), four("tlb", 0, d), sub)
+        tt(f("w1"), f("w"), f("nd"), mul)
         if not last:
-            cp(r("w1b"), f("w1"))
+            ts(r("w1b"), f("w1"), 0.0, CALM[t + 1], ge, mul)
         tt(r("cg"), ind(r("pw"), uv(cu)), r("diag"), mul)
         cp(r("ku"), ind(r("pw"), uv(cu)))
         scan(r("cs2"), r("rst"), r("cg"), mul, add)
-        PL = tl("cs2")
+        tt(f("pl"), tl("cs2"), iv("sl%d" % t), mx)
+        PL = f("pl")
         for oc in range(16):
             n, at = 256 - 16 * oc, 272 * oc
-            ts(deep(T.eq[:, oc, 0:n], "eq", at, at + n, n), r("ku", 16 * oc, 256), r("cs2", 16 * oc + 15, 16 * oc + 16), None, eq_)
+            ts(deep(T.eq[:, oc, 0:n], "eq", at, at + n, n), r("ku", 16 * oc, 256), f("pl", 1, oc), None, eq_)
             if oc < 15:
                 mm(r("b5", 16 * oc + 16, 256), r("blkh"), deep(T.eq[:, oc, 16:n], "eq", at, at + n, n - 16), oc == 0, False)
             if oc == 0:
                 mm(r("b5", 0, 16), r("blkw"), deep(T.eq[:, 0, 0:16], "eq", 0, 16, 16), False, False)
         mm(r("b5", 16, 256), r("blkw"), deep(T.eq[:, 1:16, 0:16], "eq", 272, 272 * 16, 240), False, True)
-        tt(f("k1"), PL, f("sent"), mn)
+        if last:
+            ts(f("sent"), f("home"), 271.0, None, add)
+            ts(f("k1"), PL, float(NV), 4096.0, ge, mul)
+            tt(f("k1"), f("k1"), r(cur, 2, 66, 4), add)
+            tt(f("k1"), f("k1"), f("sent"), mn)
+        else:
+            tt(f("k1"), PL, f("sent"), mn)
         tt(r("lq"), r("b5", 0, 256), r("thd"), ge)
         scan(r("ls"), r("rstb"), r("lq"), mul, add)
         tt(f("k2"), f("sent"), tl("ls"), mul)
         tt(f("k3"), f("k1"), f("k2"), mx)
         cp(uv("offu"), f("k3"))
-        act(ind(r("lock"), uv("offu")), r("cv"), ACT.Silu)
-        n = 16 if last else 32
-        act(r("lg", 0, 16 * n), ind(LK, uv("xu", n)), ACT.Relu, bias=col(8), scale=col(7))
-        pick(r("b4", 0, 16 if last else 64), "wwin", "lg", 256 if last else 1024)
-        mine = r("own", 16 * t, 16 * t + 16)
-        if not last:
-            tt(r("winb"), r("b4", 0, 16), mine, eq_)
-            ts(f("a32", 32), r("b4", 0, 32), -512.0 * (t + 1), HM, add, mul)
-            ts(f("na"), r("b4", 0, 16), -512.0 * (t + 1), -HM, add, mul)
-            tt(r("pf", 3, 128, 8), r("b4", 0, 16), mine, eq_)
-            holders()
-        tt(r("xw", 0, 64, 4), r("b4", 0, 16), mine, eq_)
-        tt(f("w"), f("w1"), r("xw", 0, 64, 4), add)
-        if not last:
-            scan(r("wx"), r("rst4"), r("xw"), mul, add)
-            tt(r("td"), r("td"), r("wx"), mul)
-            tt(r("tla"), r("tlb", 0, 64), r("td"), add)
+        if last:
+            act(ind(r("won"), uv("offu")), r("cv"), ACT.Silu)
+            scan(r("cs2"), r("rst"), r("won", 1, 257), mul, add)
+            ts(f("w"), f("w1"), 32.0, None, mul)
+            tt(f("w"), f("w"), tl("cs2"), add)
+        else:
+            act(ind(r("lock"), uv("offu")), r("cv"), ACT.Silu)
+            act(r("lg"), ind(LK, uv("xu", 32)), ACT.Relu, bias=col(8), scale=col(7))
+            pick(r("b4", 0, 32), "wwin", "lg", 512)
+            mine = r("own", 16 * t, 16 * t + 16)
+            tt(f("xw"), r("b4", 0, 32, 2), mine, eq_)
+            tt(f("w"), f("w1"), f("xw"), add)
+            ts(r("fu%d" % (t + 1)), f("w"), 16.0 - ANEW, None, eq_)
+            tell(t + 1, "lfu%d" % (t + 1), "fu%d" % (t + 1), "fu%d" % (t + 1))
+            holders(mine)
+            for n in range(d):
+                tt(four("td", n), four("td", n), f("xw"), mul)
+            if d > 1:
+                tt(four("tla", 0, d), four("tlb", 0, d), four("td", 0, d), add)
+            tt(slot(3), four("tlb", 0), four("td", 0), add)
         ts(iv("pi"), PL, 1024 * HM, None, mn)
         ts(iv("by"), iv("pi"), 14, 511, shr, band)
         cp(r(cur, 3, 67, 4), iv("by"))
@@ -779,26 +834,27 @@ def rank_program(g, core, T, topo):
         ts(r("sm", 2, 64, 4), iv("by"), 0.0, None, eq_)
         scan(r(curn, 0, 64), r("sm"), r(cur, 1, 65), mul, add)
         if not last:
-            cp(uv(cun), r(curn, 3, 64, 4))
+            cp(uv(cun), r(curn, 2, 64, 4))
 
     for t in range(STEPS):
         last = t == STEPS - 1
-        for a in range(len(CUTS)):
+        if t:
+            decide(t)
+        else:
+            steps_of("ka", "ea", "", t, ("b7", "b6"), 1, "cla")
+        for a in range(len(CUTS[t])):
             judge(a, t)
-        if t == 0:
-            first_keys()
         for h in range(len(PARTS)):
             far(h, t)
         verdicts(t)
-        half_sums(t)
-        steps_of("skg%d" % t, f("cls") if t else -LOWER)
-        tell(t, "lkc%d" % t, "skg%d" % t, "kc%d" % t)
-        if t:
-            scan(P0, r("rst"), r("skg%d" % t), mul, add)
-            tt(r("ka"), P0, r("ka"), mx)
-        else:
+        steps_of("skg%d" % t, "diff", "vr", t, ("b7", "b6"), t + 1, "clb")
+        for u in ([0] if t == 0 else []) + ([] if last else [t + 1]):
+            tell(u, "lkc%d" % u, "skg%d" % t, "kc%d" % u)
+        if t == 0:
             first_holders()
-        decide(t)
+        if t == 0:
+            decide(t)
+        aborts(t)
         if t == 0:
             noflags(3, 8, [r("lnd0")])
         keys(t)
@@ -806,18 +862,20 @@ def rank_program(g, core, T, topo):
         if t in FLAG:
             flags(t)
         if not last:
-            ts(f("cls"), f("dec"), (32768.0 * (t + 1) - LOW + LOWER) / GONE, -LOWER, mul, add)
+            ts(r("clb", 0, 16), f("nd"), -BIG - 16 * (t + 2) * U, 16 * (t + 2) * U - BIG, mul, add)
         else:
             cp(r("cr"), ind(r("cf"), uv("lperm")))
             dma("y", ext(T.yc[:]), r("cr"), "oyc", 2.0)
             for i in range(64):
                 mm(r("b0", i, 512, 64), r("big", VO + i, VO + NV, 64), WEIGH, True, True)
+                if i % 4 == 3:
+                    block(4)
             for b in range(8):
                 if b % 4 == 0:
                     act(r("yt", 64 * b, 64 * b + 256), r("b0", 64 * b, 64 * b + 256), ACT.Copy)
                 dma("ys"[b % 2], ext(T.ys[b]), r("yt", 64 * b, 64 * b + 64), "oys%d" % b, 4.6 - 0.35 * b)
         lanes(t)
-    ts(f("iso"), f("w1"), ANEW, None, lt)
+    ts(f("iso"), f("w1"), 0.0, None, lt)
     tt(r("f1"), ind(f("iso"), uv("lr")), r("qk"), mul)
     tt(r("f1"), r("f1"), r("q16"), add)
     ts(f("yl"), r("sa", 2, 66, 4), -1.0, None, add)

@@ -13,24 +13,31 @@ U = 32768.0
 BIG, HUGE = 4194304.0, 16777216.0
 HM = 16384.0
 GONE = 8589934592.0
+FAR = 2.0 ** 40
 NAP = 8388608.0
 ANEW = 1024.0
-FLAG = {1: 16384.0, 2: 1048576.0}
-CALM = {1: 2097152.0, 2: 2097152.0, 3: 134217728.0}
+FLAG = {1: 2.0 ** 15, 2: 2.0 ** 34}
+CALM = {1: 2.0 ** 21, 2: 2.0 ** 21, 3: 2.0 ** 40}
 FIRST = ((512, "s"), (512, "s"), (512, "v"), (512, "v"), (1024, "r"), (768, "r"), (256, "r"))
 LATER = ((512, "s"), (512, "s"), (512, "s"), (512, "v"), (1024, "v"), (768, "v"), (256, "v"))
 CUTS = (FIRST, LATER, LATER, LATER)
-YB = ("vvv", "vss", "vss", "vss")
-FILL = ((768, 1792, 1792), (768, 768, 768))
+AA = ("vvv", "sss", "sss", "sss", "vvv")
+APART = (1, 0, 0, 0)
+EARLY = (0, 0, 1)
+LUMP = 32
+YB = ("vvv", "sss", "sss", "sss")
+FILL = ((768, 1792, 1024), (768, 768, 768, 768))
 PARTS = [(0, 2048), (2048, 3840), (3840, 4096)]
 WAKE = 0.15
 CY = 0.00095
 AFIX, FLY, FLYB = 80 * CY, 1.3, 0.0005
-ROUNDS = 30
-TRIES = 10000
+GOCC, GLAT = 0.8, 2.6
+ROUNDS = 10
+TRIES = 40000
 SHAKE, PUSH, MARK = 0.1, 2.5, 0.5
-HEAT = 0.5
+HEAT = 0.8
 SEED = 2
+TURN = 8
 AIMED = 4
 DEBUG = []
 ORDER = []
@@ -44,7 +51,7 @@ SCRATCH = {
     "eq": ("sbuf", [128, 16, 272], "bfloat16"),
     "res": ("sbuf", [128, 16, 17], "int32"),
     "cf": ("sbuf", [128, 272], "int32"),
-    "ct": ("sbuf", [128, 560], "float32"),
+    "ct": ("sbuf", [128, 512], "float32"),
     "slw": ("sbuf", [128, 512], "float32"),
     "won": ("sbuf", [128, 528], "float32"),
     "ldw": ("sbuf", [128, 272], "bfloat16"),
@@ -58,7 +65,7 @@ for _n in ("codes", "yt"):
     SCRATCH[_n] = ("sbuf", [128, 512], "float32")
 for _n in ("csk", "hok", "ai", "tj"):
     SCRATCH[_n] = ("sbuf", [128, 256], "int32")
-for _n in ("r16", "dj", "rst", "diag", "thd", "cg", "cs2", "f1", "f2", "pos", "cr", "hr", "un", "qk", "q16", "pd", "am", "aa", "cv"):
+for _n in ("r16", "dj", "rst", "diag", "cut", "cg", "cs2", "f1", "f2", "pos", "cr", "hr", "un", "qk", "q16", "pd", "am", "aa", "cv", "cw"):
     SCRATCH[_n] = ("sbuf", [128, 256], "float32")
 for _n in ("iw", "pw", "dg1", "ka", "st", "s1", "s2", "zt"):
     SCRATCH[_n] = ("sbuf", [128, 272], "float32")
@@ -67,30 +74,34 @@ for _n in ("qb", "blkf", "turn"):
 for _n in ("blk", "nblk", "blkw", "blkh", "mix", "id_", "nid_"):
     SCRATCH[_n] = ("sbuf", [128, 128], "bfloat16")
 SCRATCH["wwin"] = ("sbuf", [128, 144], "bfloat16")
+SCRATCH["es"] = ("sbuf", [128, 1024], "float16")
+SCRATCH["idh"] = ("sbuf", [128, 128], "float16")
+SCRATCH["sel"] = ("sbuf", [128, 2048], "bfloat16")
 SCRATCH["lg"] = ("sbuf", [128, 512], "bfloat16")
 SCRATCH["yb"] = ("sbuf", [128, 384], "bfloat16")
-for _n in ("fa", "fv", "lq", "ls", "rstb", "lh"):
+for _n in ("fa", "fv", "thn", "lh"):
     SCRATCH[_n] = ("sbuf", [128, 256], "bfloat16")
-QUADS = ["pt", "pf", "po", "sm", "lf", "own", "sa", "sb"]
+QUADS = ["sm", "lf", "own", "sa", "sb"]
 SCRATCH["quads"] = ("sbuf", [128, 72 * len(QUADS)], "float32")
 for _n in ("coff", "loff", "ku"):
     SCRATCH[_n] = ("sbuf", [128, 256], "uint16")
 FS = ["prf", "col", "col2", "clm", "q8", "sent", "home", "one", "vs", "a32", "a33", "xw", "pl", "hd",
-      "w", "w1", "nd", "k1", "k2", "k3", "l1", "l2", "m1", "m2", "spare", "dbig", "yl", "iso"]
+      "w", "w1", "nd", "k1", "k2", "k3", "l1", "l2", "m1", "m2", "none", "spare", "yl", "iso", "cm", "xn", "j1", "j2", "sen2"]
 IS = ["oi", "oi2", "hi", "pi", "by", "sl0", "sl1", "sl2", "sl3", "nw", "pr", "pg", "wk"]
-US = ["xu", "xv", "ou", "cua", "cub", "offu", "listu", "slot", "os", "lc", "lr", "lrev", "lperm", "lq", "ldup", "ldup2", "lk", "lk2"]
+US = ["xu", "xv", "ou", "cua", "cub", "offu", "listu", "slot", "os", "lc", "lr", "lrev", "lperm", "lq", "ldup", "ldup2", "lk", "lk2", "lct", "offw"]
 SCRATCH["fs"] = ("sbuf", [128, 16 * len(FS)], "float32")
 SCRATCH["is_"] = ("sbuf", [128, 16 * len(IS)], "int32")
 SCRATCH["us"] = ("sbuf", [128, 16 * len(US)], "uint16")
-for _n in ("rdy", "rs", "w1b"):
+SCRATCH["hw"] = ("sbuf", [128, 272], "bfloat16")
+for _n in ("rdy", "rs", "w1b", "ab", "dec", "hb"):
     SCRATCH[_n] = ("sbuf", [128, 16], "bfloat16")
 for _n in ("cla", "clb"):
     SCRATCH[_n] = ("sbuf", [128, 32], "bfloat16")
 for _t in range(STEPS):
     SCRATCH["sf%d" % _t] = ("sbuf", [128, 16], "bfloat16")
     SCRATCH["lsf%d" % _t] = ("sbuf", [128, 16], "bfloat16")
-    SCRATCH["fu%d" % _t] = ("sbuf", [128, 16], "bfloat16")
-    SCRATCH["lfu%d" % _t] = ("sbuf", [128, 16], "bfloat16")
+    SCRATCH["fu%d" % _t] = ("sbuf", [128, 16], "float32")
+    SCRATCH["lfu%d" % _t] = ("sbuf", [128, 16], "float32")
     SCRATCH["skg%d" % _t] = ("sbuf", [128, 272], "float32")
     SCRATCH["lkc%d" % _t] = ("sbuf", [128, 272], "float32")
     SCRATCH["snd%d" % _t] = ("sbuf", [128, 256], "bfloat16")
@@ -100,7 +111,8 @@ for _b in range(8):
 
 SEMAPHORES = ["c" + q for q in "vspgy"] + ["dcs", "dho", "dwk", "dsn", "ds2", "dx0", "dx1", "oyc", "oyh", "oyl"] + ["oys%d" % _g for _g in range(8)]
 for _t in range(STEPS):
-    SEMAPHORES += [k + str(_t) for k in ("rsf", "rkc", "rdd", "qsf", "qkc", "qdd") + (("rfu", "qfu") if _t else ())]
+    SEMAPHORES += [k + str(_t) for k in ("rsf", "rkc", "rdd", "qsf", "qkc", "qdd", "rfu", "qfu")]
+    SEMAPHORES += ["add%d_%d" % (_t, _a) for _a in range(8)]
 
 
 def emitter(g, T):
@@ -167,6 +179,10 @@ def emitter(g, T):
         prog.append((part[0][0], "block", None, rd, wr, cost, cost, part))
 
     def dma(q, out, in_, sem, lat):
+        if q == "g":
+            call = lambda: g.dma_start(out=out[0], in_=in_[0], accum_op=ALU.add).then_inc(T.sem[sem], 16)
+            prog.append((q, "dma", call, in_[1] + out[1], out[1], GOCC, lat, sem))
+            return
         call = lambda: eng[q].dma_start(out=out[0], in_=in_[0]).then_inc(T.sem[sem], 16)
         prog.append((q, "dma", call, in_[1], out[1], 0.1, lat, sem))
 
@@ -174,9 +190,10 @@ def emitter(g, T):
         rid, pid, _s = topo.addr(dst)
         n = len(topo.engines(core, dst))
         call = lambda: g.remote_dma(out[0], in_[0], T.sem["r" + name], T.sem["q" + name], pid, rid, topo.mask(core, dst))
-        fly = FLY + size * FLYB + (1.5 if name == "sf0" else 0.0)
+        fly = FLY + size * FLYB
         prog.append(("g", "send", call, in_[1], [], 0.4, 0.4 + fly, ("q" + name, n)))
-        prog.append(("net", "land", None, in_[1], out[1], 0.0, fly, ("r" + name, n)))
+        loads = [("ea", (0, 4096, 1))] if name == "fu0" else []
+        prog.append(("net", "land", None, in_[1] + loads, out[1], 0.0, fly, ("r" + name, n)))
 
     def order():
         m = len(prog)
@@ -207,6 +224,17 @@ def emitter(g, T):
                 fore[k].append((i, l))
                 back[i].append((k, l + occ - prog[k][5]))
             tags.append((q, wr[0][0], wr[0][1][0] if wr[0][0] in ("fs", "us", "is_", "quads") else 0) if wr else q)
+
+        reach = [0] * m
+        for i in range(m - 1, -1, -1):
+            kept = [(k, l) for k, l in fore[i] if not any(reach[j] >> k & 1 and l2 + WAKE >= l - 1e-9 and (l2 >= l or prog[k][0] != "p") for j, l2 in fore[i])]
+            for k, l in fore[i]:
+                reach[i] |= reach[k] | 1 << k
+            fore[i] = kept
+        back = [[] for _ in range(m)]
+        for k in range(m):
+            for i, l in fore[k]:
+                back[i].append((k, l + prog[i][5] - prog[k][5]))
 
         def place(nxt, first, key):
             left = [0] * m
@@ -273,6 +301,60 @@ def emitter(g, T):
                 i = k
             return pairs
 
+        occs, ques = [p[5] for p in prog], [p[0] for p in prog]
+        needs = [[(k, l - occs[i] + occs[k]) for k, l in back[i]] for i in range(m)]
+        lined = [None, None]
+
+        def again(now, key):
+            if lined[0] is not now:
+                lined[:] = [now, sorted(range(m), key=lambda i: now[i])]
+            line_up = lined[1]
+            edge = min([min(now[i], key[i]) for i in line_up if key[i] != now[i]] + [1e9])
+            when, done, busy, rest = list(now), [False] * m, {q: [(-1.0, 0.0)] for q in eng}, []
+            for n, i in enumerate(line_up):
+                if now[i] >= edge:
+                    rest = sorted(line_up[n:], key=lambda i: -key[i])
+                    break
+                done[i] = True
+                if occs[i] and now[i] > edge - 4.0:
+                    line = busy[ques[i]]
+                    if len(line) == 1:
+                        line[0] = (-1.0, now[i])
+                    line.append((now[i], now[i] + occs[i]))
+                elif occs[i]:
+                    busy[ques[i]][0] = (-1.0, now[i] + occs[i])
+            while rest:
+                i = rest[-1]
+                if done[i]:
+                    rest.pop()
+                    continue
+                t = 0.0
+                for k, l in needs[i]:
+                    if not done[k]:
+                        rest.append(k)
+                        break
+                    if when[k] + l > t:
+                        t = when[k] + l
+                else:
+                    rest.pop()
+                    done[i] = True
+                    occ = occs[i]
+                    if occ:
+                        line = busy[ques[i]]
+                        if line[-1][1] <= t:
+                            line.append((t, t + occ))
+                        else:
+                            lo, top = len(line) - 1, len(line)
+                            while lo and line[lo - 1][1] > t:
+                                lo -= 1
+                            while lo < top and line[lo][0] < t + occ - 1e-9:
+                                if line[lo][1] > t:
+                                    t = line[lo][1]
+                                lo += 1
+                            line.insert(lo, (t, t + occ))
+                    when[i] = t
+            return when
+
         held = [None, None]
         now, had = best, worth(best)
         least = had
@@ -288,15 +370,15 @@ def emitter(g, T):
                     key[i] = now[k] - 0.001 - draw() ** 2
                 else:
                     key[k] = now[i] + 0.001 + draw() ** 2
-            start = place(fore, [0.0] * m, key)
-            if n % 4 == 0:
+            start = again(now, key)
+            if n % TURN == 0:
                 start = turn(start, 0.0)
             w = worth(start)
             if w <= had + 0.02 + HEAT * (1 - n / TRIES) ** 2 * draw():
                 now, had = start, w
                 if w < least:
                     best, least = start, w
-        DEBUG.extend([prog, fore, back, best, way])
+        DEBUG.extend([tags, prog, fore, back, best, way])
         return sorted(range(m), key=lambda i: (best[i], i))
 
     def issue():
@@ -361,7 +443,7 @@ def rank_program(g, core, T, topo):
 
     def kind(o):
         w, _s, d = SCRATCH[o[1][0][0]]
-        return len(o[1]) > 1, w == "psum", d in ("bfloat16", "uint16")
+        return len(o[1]) > 1, w == "psum", d in ("bfloat16", "uint16", "float16")
 
     def cost(out, a, b=None):
         n, ko, ka = a[2], kind(out), kind(a)
@@ -396,8 +478,13 @@ def rank_program(g, core, T, topo):
     def ms(out, v):
         op("v", lambda: g.vector.memset(out[0], v), [out], [], cost(out, out))
 
+    table = []
+
     def act(out, a, fn, bias=None, scale=None):
         cs = cost(out, a) + 0.015 if kind(out)[0] or kind(a)[0] else AFIX + max(64, a[2]) * CY
+        if fn is ACT.Silu and not table:
+            table.append(fn)
+            cs += 1.3
         ins = [a] + [s for s in (bias, scale) if isinstance(s, tuple)]
         kw = {k: s[0] if isinstance(s, tuple) else s for k, s in (("bias", bias), ("scale", scale)) if s is not None}
         op("s", lambda: g.scalar.activation(out=out[0], in_=a[0], func=fn, **kw), [out], ins, cs)
@@ -445,7 +532,7 @@ def rank_program(g, core, T, topo):
 
     iota(iv("pr", 1), [[0, 1]], 0, 1)
     iota(r("dj"), [[0, 8], [16, 32]], NV)
-    iota(r("codes"), [[0, 2], [1, 256]], 17)
+    iota(r("codes", 0, 16 * LUMP), [[0, LUMP // 16], [1, 256]], 17)
     at = sum(FILL[0] + FILL[1])
     iota(r("lock", at, NV), [[0, NV - at]], 0)
     iota(f("q8"), [[1, 16]], 0)
@@ -459,25 +546,22 @@ def rank_program(g, core, T, topo):
     iota(r("qb"), [[1, 8], [0, 16]], 0)
     iota(f("a32", 17), [[256, 17]], -16)
     iota(f("col2", 4), [[-int(U), 4]], 1 - int(U))
-    iota(r("pos"), [[32, 16], [1, 16]], 32)
-    for n, k in (("rst", 16), ("rstb", 16), ("pf", 4), ("sm", 4)):
+    for n, k in (("rst", 16), ("sm", 4)):
         iota(r(n), [[0, r(n)[2]]], 1)
         keep(r(n), r(n), [[0, 16], [1, k]], gt, 0.0)
-    for i, x in ((2, GONE / HM), (3, HM)):
-        keep(r("pf"), r("pf"), [[0, 16], [1, 4]], ALU.not_equal, x, 0, -i)
-    iota(f("vs"), [[4, 16]], 3)
+    keep(r("cut"), r("rst"), [[0, 16], [1, 16]], gt, -2 * FAR)
     iota(r("turn"), [[0, 128]], 1)
     keep(r("turn"), r("turn"), [[-1, 16], [-16, 8]], eq_, 0.0, 1)
     iota(r("iw", 1, 257), [[1, 256]], 1)
     iota(r("q16"), [[32, 16], [0, 16]], 16)
-    for x in (r("sa", 0, 144), r("ldw", 0, 1), r("zt"), r("big", DUM, VO), r("won", 0, 272)):
+    for x in (r("sa", 0, 144), r("ldw", 0, 1), r("zt"), r("big", DUM, VO)):
         iota(x, [[0, x[2]]], 0)
 
     def noflags(a, b, after=()):
         for c in range(a, b):
-            iota(r("big", FO + 1024 * c, FO + 1024 * c + 1024), [[0, 1024]], 0, 0, after)
+            iota(r("big", FO + 512 * c, FO + 512 * c + 512), [[0, 512]], 0, 0, after)
 
-    noflags(0, 3)
+    noflags(0, 16)
 
     at = 0
     for n in FILL[0]:
@@ -494,8 +578,8 @@ def rank_program(g, core, T, topo):
         tt(r("f1", a, b), r("f1", a, b), r("csk", a, b), add)
         tt(r("f1", a, b), r("f1", a, b), r("dj", a, b), mn)
         cp(r("loff", a, b), r("f1", a, b))
-    for c in range(8):
-        act(ind(r("lock"), r("loff", 32 * c, 32 * c + 32)), r("codes"), ACT.Silu)
+    for c in range(0, 256, LUMP):
+        act(ind(r("lock"), r("loff", c, c + LUMP)), r("codes", 0, 16 * LUMP), ACT.Silu)
 
     ts(iv("pg", 1, 1), iv("pr", 1), 4, None, shr)
     ts(iv("pg", 1, 2), iv("pr", 1), 112, None, band)
@@ -517,7 +601,7 @@ def rank_program(g, core, T, topo):
     ts(uv("lq", 48), r("lf", 0, 48), col(14), None, add)
     ts(col(10), PRF, 17.0, 1.0, mul, add)
     ts(uv("lperm"), f("q8"), col(10), None, add)
-    cp(uv("lc"), f("vs"))
+    cp(uv("lc"), f("q8"))
     ts(uv("lr"), f("q8"), 0.0, PRF, mul, add)
     ts(uv("lrev"), f("q8"), 240.0, col(14), add, sub)
     cp(r("coff"), r("csk"))
@@ -530,7 +614,8 @@ def rank_program(g, core, T, topo):
     ts(col(11), iv("pr", 1), 16.0, None, ge)
     ts(f("col2", 4), f("col2", 4), col(11), None, mul)
     for t in FLAG:
-        ts(f("col2", 1, 4 + t), col(2), FLAG[t], None, mul)
+        ts(f("col2", 1, 4 + 2 * t), col(2), FLAG[t], None, mul)
+        ts(f("col2", 1, 5 + 2 * t), col(2), -320.5 * FLAG[t], None, mul)
     for n, a, x in (("cla", 0, 16 * U - BIG), ("cla", 16, -HUGE), ("clb", 0, -2 * BIG)):
         ms(r(n, a, a + 16), x)
     BANK, HALF, WEIGH, OVER = r("gib", 0, 8), r("gib", 8, 24), r("gib", 24, 32), (32, 48)
@@ -544,34 +629,36 @@ def rank_program(g, core, T, topo):
     ts(r("blk"), r("qb"), PGF, None, eq_)
     ts(r("nblk"), r("qb"), PGF, -1.0, eq_, mul)
     ts(r("blkf"), r("qb"), PGF, None, eq_)
-    ts(r("blkh"), r("qb"), PGF, 65536.0, eq_, mul)
+    ts(r("blkh"), r("qb"), PGF, 65536.0 * U, eq_, mul)
     keep(r("id_"), r("blk"), [[-1, 128]], eq_, 0.0, 1)
     keep(r("nid_"), r("nblk"), [[-1, 128]], eq_, 0.0, 1)
     keep(r("mix"), r("nblk"), [[-1, 128]], ge, 0.0, 1)
     keep(r("mix"), r("mix"), [[-1, 128]], ALU.not_equal, -1024.0, 1)
     ts(f("home"), f("q8"), 16.0, col(15), mul, add)
     ts(r("own"), r("own"), PRF, None, add)
-    ts(f("sent"), f("home"), NV - 1.0, None, add)
+    ts(f("sent"), f("home"), NV - 1.0 - HM, None, add)
+    ts(f("sen2"), f("home"), 271.0 - HM, None, add)
     ts(f("k1"), f("q8"), PRF, 1.0, gt, add)
     op("v", lambda: g.vector.tensor_reduce(out=f("k3", 1)[0], in_=f("k1")[0], axis=AxisListType.X, op=mul), [f("k3", 1)], [f("k1")], 0.06)
-    ts(r("blkw"), r("blkf"), f("k3", 1), None, mul)
-    ts(f("k3", 1, 1), f("k3", 1), 2.0, None, mul)
-    lin(r("thd"), r("diag"), -1.0e9, 1.0e9)
-    ts(r("thd"), r("thd"), f("k3", 1, 1), None, mx)
-    ts(r("yt"), ind(r("csk"), uv("ldup", 32)), 256.0, None, add)
-    op("v", lambda: g.vector.transpose(out=r("ct", 32, 544)[0], in_=r("yt")[0]), [r("ct", 32, 544)], [r("yt")], 512 * CY)
-    ts(r("ct", 544, 560), f("home"), -1.0, None, add)
+    ts(r("blkw"), r("blkf"), f("k3", 1), U, mul, mul)
+    ts(f("k3", 1, 1), f("k3", 1), -2.0 * U, FAR, mul, add)
+    ts(r("thn"), r("diag"), f("k3", 1, 1), -FAR, mul, add)
+    cp(r("yt"), ind(r("csk"), uv("ldup", 32)))
+    op("v", lambda: g.vector.transpose(out=r("ct")[0], in_=r("yt")[0]), [r("ct")], [r("yt")], 512 * CY)
+    tt(col(13), PRF, ODD, add)
+    ts(uv("lct"), f("q8"), 32.0, col(13), mul, add)
+    lin(r("pos"), ind(r("ct"), uv("lct")), None, 288.0)
+    ts(f("none"), f("home"), 31.0, None, add)
     ts(f("spare"), f("home"), -768.0, None, add)
-    ts(f("dbig"), r("diag", 0, 16), 1000.0, None, mul)
-    lin(r("pos"), r("pos"), None, ODD)
+    ts(col(12), col(14), 15.0, None, add)
+    ts(uv("os"), f("q8"), 0.0, col(12), mul, add)
 
     cp(r("cr"), ind(r("csk"), uv("lrev")))
     cp(r("hr"), ind(r("hok"), uv("lrev")))
     ts(r("un"), r("hr"), -1.0, 1.0, mul, add)
     lin(r("cv"), r("hr"), -18.0, 17.0)
     scan(r("cs2"), r("rst"), r("un"), mul, add)
-    ts(f("w"), tl("cs2"), -1.0, 16.0 - ANEW, mul, add)
-    ts(r("w1b"), tl("cs2"), -1.0, 16.0, mul, add)
+    ts(r("fu0"), tl("cs2"), -1.0, 16.0 - ANEW, mul, add)
     lin(r("cg"), r("cs2"), -1.0, 17.0)
     tt(r("pd"), r("cv"), r("cg"), mn)
     lin(r("qk"), ind(r("pd"), uv("lq")), 32.0, 16.0 - 32.0 * (ANEW + 1))
@@ -614,20 +701,55 @@ def rank_program(g, core, T, topo):
                 else:
                     runs.append([at, at + n, q in kinds])
             at += n
-        for m in range(16):
+        for second in (True, False):
             for a, b, more in runs:
-                out = (T[bk][(a - lo) // 16:(b - lo) // 16, c0 + m:c1:16],) + r(bk, c0 + m, c1, 16)[1:]
-                mm(out, r(src, a + m, b, 16), x, True, not more)
-                if more:
-                    mm(out, r(src2, a + m, b, 16), x2, False, True)
-            if m % size == size - 1:
-                block(size * sum(1 + more for a, b, more in runs))
+                for m in range(16 if more or not second else 0):
+                    out = (T[bk][(a - lo) // 16:(b - lo) // 16, c0 + m:c1:16],) + r(bk, c0 + m, c1, 16)[1:]
+                    if second:
+                        mm(out, r(src2, a + m, b, 16), x2, m == 0, False)
+                    else:
+                        mm(out, r(src, a + m, b, 16), x, not more, not more or m == 15)
+                    if m % size == size - 1:
+                        block(size)
+
+    def taken(t, h):
+        at, got, sign = 0, [], 0
+        for n, q in CUTS[t]:
+            x = {"s": 0, "d": -1}.get(q, 1)
+            if at // 2048 == h and x != sign:
+                got.append((at % 2048 // 16, x - sign))
+                sign = x
+            at += n
+        return got and (h,) + tuple(got)
+
+    kept = sorted({taken(t, h) for t in range(STEPS) for h in range(2) if taken(t, h)})
+    for i, x in enumerate(kept):
+        for n, (a, by) in enumerate(x[1:]):
+            ts(col(12) if n else f("col2", 1, 10 + i), iv("pr", 1), float(a), float(by), ge, mul)
+            if n:
+                tt(f("col2", 1, 10 + i), f("col2", 1, 10 + i), col(12), add)
+    cp(r("idh"), r("id_"))
+    for m in range(0, 16, 4):
+        keep(r("sel", 128 * m, 128 * m + 512), r("big", FO, FO + 512), [[-1, 4], [-16, 8], [0, 16]], ALU.not_equal, GONE, 1, -m)
 
     def steps_of(out, src, less, t, banks, unit, cls):
         for h in range(2):
             bk, c, lo = banks[h], 128 * h, 2048 * h
-            sums(bk, 0, 256, src, HALF, lo, lo + 2048, less, t, "ea", HALF, 4)
-            act(r("aa", c, c + 128), r(bk, 0, 128), ACT.Copy)
+            more = less and taken(t, h)
+            if more:
+                mm(r(bk, 0, 256), r("idh"), r("es", 256 * kept.index(more), 256 * kept.index(more) + 256), True, False)
+            for m in range(16):
+                mm(r(bk, m, 256, 16), r(src, lo + m, lo + 2048, 16), HALF, not more, not more or m == 15)
+                if m % 8 == 7:
+                    block(8)
+            if not less:
+                for i, x in enumerate(kept):
+                    if x[0] == h:
+                        ts(r("es", 256 * i, 256 * i + 256), r(bk, 0, 256), f("col2", 1, 10 + i), None, mul)
+            if AA[t if less else STEPS][h] == "s":
+                act(r("aa", c, c + 128), r(bk, 0, 128), ACT.Copy)
+            else:
+                cp(r("aa", c, c + 128), r(bk, 0, 128))
             tt(r("ai", c, c + 128), r(bk, 128, 256), r("aa", c, c + 128), mul)
             ts(r("tj", c, c + 128), r("ai", c, c + 128), 3, 511, shr, band)
             if h == 0:
@@ -637,7 +759,10 @@ def rank_program(g, core, T, topo):
         for h in range(2):
             mm(deep(T.b1[:, :, 1 + 8 * h:9 + 8 * h], "b1", 0, 512, 128), r("am", 128 * h, 128 * h + 128), r("turn"), False, False)
         mm(deep(T.b1[:, :, 1], "b1", 0, 512, 16), r("id_"), r(cls, 0, 16), False, True)
-        act(r(out), deep(T.b1[:, :, 0:17], "b1", 0, 512, 272), ACT.Copy)
+        if AA[t if less else STEPS][2] == "s":
+            act(r(out), deep(T.b1[:, :, 0:17], "b1", 0, 512, 272), ACT.Copy)
+        else:
+            cp(r(out), deep(T.b1[:, :, 0:17], "b1", 0, 512, 272))
 
     def judge(a, t):
         lo = sum(n for n, q in CUTS[t][:a])
@@ -650,6 +775,10 @@ def rank_program(g, core, T, topo):
             mm(bk, r("nid_"), e, True, False)
             mm(bk, r("id_"), d, False, True)
             act(out, bk, ACT.Abs)
+        elif CUTS[t][a][1] == "d":
+            act(d, cells, ACT.Copy, scale=-1.0)
+            dma("g", d, e, "add%d_%d" % (t, a), GLAT + (hi - lo) * 0.001)
+            act(out, d, ACT.Abs)
         else:
             tt(d, cells, e, sub)
             if CUTS[t][a][1] == "r":
@@ -668,74 +797,73 @@ def rank_program(g, core, T, topo):
 
     def verdicts(t):
         out = r("b2", 256, 272)
-        mm(out, r("id_"), r("w1b"), True, False)
+        if t:
+            mm(out, r("id_"), r("w1b"), True, False)
         for h, (lo, hi) in enumerate(PARTS):
             n = (hi - lo) // 16
-            mm(out, rows(n, "yb", 128 * h, 128 * h + 128), rows(n, "gib", *OVER), False, h == len(PARTS) - 1)
-        if t:
-            ts(r("sf%d" % t), out, 0.0, None, lt)
-        else:
-            ts(r("sf0"), out, 1.0, 0.0, add, mx)
-            ts(f("l1"), r("sf0"), -1.0, 34.0, mul, add)
-            ts(f("l2"), r("sf0"), 0.0, 1.0e9, eq_, mul)
+            mm(out, rows(n, "yb", 128 * h, 128 * h + 128), rows(n, "gib", *OVER), t == h == 0, h == len(PARTS) - 1)
+        ts(r("sf%d" % t), out, 0.0, None, lt)
         tell(t, "lsf%d" % t, "sf%d" % t, "sf%d" % t)
 
-    def slot(i):
-        return r("pt", i, 64, 4)
+    def counts(t):
+        tell(t, "lfu%d" % t, "fu%d" % t, "fu%d" % t)
+        ts(f("l1"), r("fu%d" % t), -1.0, 2 * (16.0 - ANEW), mul, add)
+
+    def spread(out, src, start):
+        for m in range(16):
+            mm(r(out[0], out[1] + m, out[1] + 256, 16), r("sel", 128 * m, 128 * m + 128), src, start and m == 0, m == 15)
+            if m % 8 == 7:
+                block(8)
 
     def first_holders():
         act(r("lg", 0, 256), ind(LK, uv("xu")), ACT.Relu, bias=col(8), scale=col(7))
         pick(r("b4", 0, 16), "wwin", "lg", 256)
-        cp(slot(2), r("b4", 0, 16))
-        cp(slot(3), four("tla", 0))
+        cp(r("hb"), r("b4", 0, 16))
+        cp(f("xn"), four("tla", 0))
 
-    def holders(mine):
-        tt(f("hd"), r("b4", 1, 32, 2), mine, sub)
-        tt(f("hd"), f("hd"), f("xw"), mul)
-        tt(iv("hi"), r("b4", 0, 32, 2), f("hd"), add)
+    def holders():
         ts(iv("oi"), iv("hi"), 511, None, band)
         cp(uv("ou"), iv("oi"))
         lin(r("lh"), ind(r("ldw"), uv("ou")), col(4))
         pick(r("b4", 32, 48), "wwin", "lh", 256)
         tt(f("vs"), r("b4", 32, 48), iv("hi"), le)
-        tt(slot(2), iv("oi"), f("vs"), mul)
+        tt(r("hb"), iv("oi"), f("vs"), mul)
 
     def decide(t):
-        iota(r("slw", 0, 16), [[1, 16]], 544)
+        keep(r("slw", 0, 16), f("none"), [[0, 16]], eq_, 0.0)
         if t:
-            tt(r("rdy"), r("lfu%d" % t), r("fu%d" % t), mul)
+            tt(r("rdy"), r("lfu%d" % t), f("l1"), eq_)
         else:
-            tt(r("rdy"), r("lsf0"), f("l1"), eq_)
-        rk = r("b5", 256, 272)
+            tt(f("l1"), r("lfu0"), f("l1"), eq_)
+            tt(f("l2"), f("l1"), r("sf0"), gt)
+            tt(r("rdy"), f("l2"), r("lsf0"), gt)
+        rk = r("b7", 272, 288)
         scan(r("rs"), f("one"), r("rdy"), mul, add)
         mm(rk, r("mix"), r("rdy"), True, False)
         mm(rk, r("blk"), r("rs"), False, True)
-        ts(slot(1), rk, -1007.0, None, lt)
+        ts(f("cm"), rk, -1007.0, None, lt)
         tt(f("m1"), rk, f("spare"), mn)
         ts(uv("slot"), f("m1"), 1023.0, None, add)
         act(ind(r("slw"), uv("slot")), r("pos"), ACT.Silu)
-        ts(gate("zt"), slot(1), 2 * BIG + 64 * U, None, mul)
-        scan(f("m2"), f("dbig"), r("slw", 0, 16), add, mn)
-        cp(uv("os", 1), f("m2", 1, 15))
-        cp(uv("listu"), ind(r("ct"), uv("os", 1)))
+        ts(gate("zt"), f("cm"), 2 * BIG + 64 * U, None, mul)
+        ts(uv("listu"), r("slw", 0, 16), -32.0, None, add)
         act(r("snd%d" % t), ind(VD, uv("listu")), ACT.Copy)
         tell(t, "lnd%d" % t, "snd%d" % t, "dd%d" % t)
 
     def aborts(t):
-        if t:
-            tt(slot(0), r("lsf%d" % t), r("sf%d" % t), mx)
-        else:
-            tt(slot(0), r("lsf0"), f("l2"), le)
-        tt(f("nd"), slot(0), slot(1), eq_)
+        a, b = (f("cm"), r("lsf%d" % t)) if t else (r("lsf0"), f("cm"))
+        tt(r("ab"), r("sf%d" % t), a, mx)
+        tt(r("dec"), r("ab"), b, mx)
+        ts(f("nd"), r("dec"), 0.0, None, eq_)
 
     def keys(t):
-        scan(r("b5", 0, 272), r("lkc%d" % t), r("zt"), add, mx)
-        ts(gate("st"), slot(0), BIG, None, mul)
+        scan(r("b7", 0, 272), r("lkc%d" % t), r("zt"), add, mx)
+        ts(gate("st"), r("dec" if t else "ab"), BIG, None, mul)
         now = "st"
         for n, steps in enumerate(["ka"] + ["skg%d" % u for u in range(1, t + 1)]):
             scan(r("s%d" % (1 + n % 2)), r(steps), r(now), add, mx)
             now = "s%d" % (1 + n % 2)
-        tt(RES, r("b5", 0, 272), r(now), mx)
+        tt(RES, r("b7", 0, 272), r(now), mx)
         if t == STEPS - 1:
             ts(r("cf"), RES, NV - 1, None, band)
             return
@@ -753,33 +881,44 @@ def rank_program(g, core, T, topo):
         mm(r("b2", 0, 256), r("id_"), r("lnd%d" % t), False, True)
         act(r("fa"), r("b2", 0, 256), ACT.Abs)
         mm(r("b3", 0, 256), r("blk"), r("fa"), True, True)
-        ts(r("fv"), r("b3", 0, 256), 320.0, f("col2", 1, 4 + t), gt, mul)
+        act(r("fv"), r("b3", 0, 256), ACT.Relu, bias=f("col2", 1, 5 + 2 * t), scale=f("col2", 1, 4 + 2 * t))
         cp(ind(FD, uv("listu")), r("fv"))
 
     def lanes(t):
         cur, curn = ("sa", "sb") if t % 2 == 0 else ("sb", "sa")
         cu, cun = ("cua", "cub") if t % 2 == 0 else ("cub", "cua")
         last = t == STEPS - 1
-        if last:
-            act(r("cv"), ind(r("dg1"), uv(cu)), ACT.Copy)
-        else:
+        early = last or EARLY[t]
+        if early:
+            act(r("cw"), ind(r("dg1"), uv(cu)), ACT.Copy)
+        if not last:
             act(r("cv"), ind(r("iw"), uv(cu)), ACT.Identity, bias=f("clm", 1, t), scale=col(9))
         tt(r(cur, 1, 65, 4), f("home"), r(cur, 2, 66, 4), sub)
-        scan(r("po"), r("pf"), r("pt"), mul, add)
-        tt(r("pd"), ind(r("po"), uv("lc")), r("diag"), mul)
-        mm(r("b4", 0, 256), r("blkf"), r("pd"), True, True)
-        act(r("pw", 1, 257), r("b4", 0, 256), ACT.Copy)
+        if not APART[t]:
+            ts(f("hd"), r("hb"), HM, None, mul)
+            tt(f("xn"), f("xn"), f("hd"), add)
+        tt(r("pd"), ind(f("xn"), uv("lc")), r("diag"), mul)
+        mm(r("b5", 0, 256), r("blkf"), r("pd"), True, False)
+        spread(("b5", 0), r("dec"), False)
+        act(r("pw", 1, 257), r("b5", 0, 256), ACT.Copy)
+        BY = r("b4", 48, 64)
+        if APART[t]:
+            spread(("b4", 256), r("hb"), True)
+            lin(r("hw", 1, 257), r("b4", 256, 512), HM / GONE)
+            lin(r("lh"), ind(r("hw"), uv(cu)), col(3))
+            pick(BY, "wwin", "lh", 256)
         d = STEPS - 1 - t
         if not last:
-            act(r("b4", 256, 512) if t else r("ldw", 1, 257), r("b4", 0, 256), ACT.Relu, bias=-1.0, scale=(t + 2) / GONE)
+            act(r("b4", 256, 512) if t else r("ldw", 1, 257), r("pw", 1, 257), ACT.Relu, bias=-1.0, scale=(t + 2) / GONE)
             if t:
                 tt(r("ldw", 1, 257), r("b4", 256, 512), r("ldw", 1, 257), mx)
             ts(four("tla", 0, d + 1), four("tla", 0, d + 1), U, None, add)
             tt(four("tlb", 0, d + 1), deep(T.res[:, :, 1:d + 2], "res", 0, 272, 16 * d + 16), four("tla", 0, d + 1), mx)
             ts(four("tlb", 0, d + 1), four("tlb", 0, d + 1), NV - 1, None, band)
-            cp(uv("xu", 32), four("tlb", 0, 2))
+            if not early:
+                cp(uv("xu", 32), four("tlb", 0, 2))
             tt(four("td", 0, d), four("tlb", 1, d + 1), four("tlb", 0, d), sub)
-        tt(f("w1"), f("w"), f("nd"), mul)
+        tt(f("w1"), r("fu%d" % t), f("nd"), mul)
         if not last:
             ts(r("w1b"), f("w1"), 0.0, CALM[t + 1], ge, mul)
         tt(r("cg"), ind(r("pw"), uv(cu)), r("diag"), mul)
@@ -787,60 +926,75 @@ def rank_program(g, core, T, topo):
         scan(r("cs2"), r("rst"), r("cg"), mul, add)
         tt(f("pl"), tl("cs2"), iv("sl%d" % t), mx)
         PL = f("pl")
+        mm(r("b5", 0, 256), r("id_"), r("thn"), True, False)
         for oc in range(16):
             n, at = 256 - 16 * oc, 272 * oc
             ts(deep(T.eq[:, oc, 0:n], "eq", at, at + n, n), r("ku", 16 * oc, 256), f("pl", 1, oc), None, eq_)
             if oc < 15:
-                mm(r("b5", 16 * oc + 16, 256), r("blkh"), deep(T.eq[:, oc, 16:n], "eq", at, at + n, n - 16), oc == 0, False)
-            if oc == 0:
-                mm(r("b5", 0, 16), r("blkw"), deep(T.eq[:, 0, 0:16], "eq", 0, 16, 16), False, False)
-        mm(r("b5", 16, 256), r("blkw"), deep(T.eq[:, 1:16, 0:16], "eq", 272, 272 * 16, 240), False, True)
-        if last:
-            ts(f("sent"), f("home"), 271.0, None, add)
-            ts(f("k1"), PL, float(NV), 4096.0, ge, mul)
-            tt(f("k1"), f("k1"), r(cur, 2, 66, 4), add)
-            tt(f("k1"), f("k1"), f("sent"), mn)
+                mm(r("b5", 16 * oc + 16, 256), r("blkh"), deep(T.eq[:, oc, 16:n], "eq", at, at + n, n - 16), False, False)
+        mm(r("b5", 0, 256), r("blkw"), deep(T.eq[:, 0:16, 0:16], "eq", 0, 272 * 16, 256), False, True)
+        if early:
+            ts(f("j1"), PL, float(NV), 4096.0, ge, mul)
+            ts(f("j2"), r(cur, 2, 66, 4), -HM, None, add)
+            tt(f("j1"), f("j1"), f("j2"), add)
+        if not last:
+            ts(f("k1"), PL, -HM, None, add)
+        if APART[t]:
+            for k in ["j1"] * early + ["k1"] * (not last):
+                tt(f(k), BY, f(k), add)
+            ts(f("m2"), PL, float(NV), 1.0 / HM, lt, mul)
+            tt(r(cur, 3, 67, 4), BY, f("m2"), mul)
         else:
-            tt(f("k1"), PL, f("sent"), mn)
-        tt(r("lq"), r("b5", 0, 256), r("thd"), ge)
-        scan(r("ls"), r("rstb"), r("lq"), mul, add)
-        tt(f("k2"), f("sent"), tl("ls"), mul)
-        tt(f("k3"), f("k1"), f("k2"), mx)
-        cp(uv("offu"), f("k3"))
-        if last:
-            act(ind(r("won"), uv("offu")), r("cv"), ACT.Silu)
+            ts(iv("pi"), PL, 2 * NAP, None, mn)
+            ts(iv("by"), iv("pi"), 14, 511, shr, band)
+            cp(r(cur, 3, 67, 4), iv("by"))
+        scan(r("cg"), r("cut"), r("b5", 0, 256), add, mx)
+        if early:
+            tt(f("j2"), f("j1"), tl("cg"), mx)
+            tt(f("j1"), f("j2"), f("sen2"), mn)
+            ts(uv("offw"), f("j1"), HM, None, add)
+            iota(r("won", 0, 272), [[0, 272]], 0)
+            act(ind(r("won"), uv("offw")), r("cw"), ACT.Silu)
             scan(r("cs2"), r("rst"), r("won", 1, 257), mul, add)
-            ts(f("w"), f("w1"), 32.0, None, mul)
-            tt(f("w"), f("w"), tl("cs2"), add)
-        else:
+        if not last:
+            tt(f("k2"), f("k1"), tl("cg"), mx)
+            tt(f("k3"), f("k2"), f("sent"), mn)
+            ts(uv("offu"), f("k3"), HM, None, add)
             act(ind(r("lock"), uv("offu")), r("cv"), ACT.Silu)
-            act(r("lg"), ind(LK, uv("xu", 32)), ACT.Relu, bias=col(8), scale=col(7))
-            pick(r("b4", 0, 32), "wwin", "lg", 512)
             mine = r("own", 16 * t, 16 * t + 16)
-            tt(f("xw"), r("b4", 0, 32, 2), mine, eq_)
-            tt(f("w"), f("w1"), f("xw"), add)
-            ts(r("fu%d" % (t + 1)), f("w"), 16.0 - ANEW, None, eq_)
-            tell(t + 1, "lfu%d" % (t + 1), "fu%d" % (t + 1), "fu%d" % (t + 1))
-            holders(mine)
+            if early:
+                ts(f("xw"), tl("cs2"), 16.0, None, gt)
+            else:
+                act(r("lg"), ind(LK, uv("xu", 32)), ACT.Relu, bias=col(8), scale=col(7))
+                pick(r("b4", 0, 32), "wwin", "lg", 512)
+                tt(f("xw"), r("b4", 0, 32, 2), mine, eq_)
+            tt(r("fu%d" % (t + 1)), f("w1"), f("xw"), add)
+            counts(t + 1)
             for n in range(d):
                 tt(four("td", n), four("td", n), f("xw"), mul)
             if d > 1:
                 tt(four("tla", 0, d), four("tlb", 0, d), four("td", 0, d), add)
-            tt(slot(3), four("tlb", 0), four("td", 0), add)
-        ts(iv("pi"), PL, 1024 * HM, None, mn)
-        ts(iv("by"), iv("pi"), 14, 511, shr, band)
-        cp(r(cur, 3, 67, 4), iv("by"))
-        ts(r("sm", 1, 64, 4), PL, 1024 * HM, None, ge)
-        ts(r("sm", 2, 64, 4), iv("by"), 0.0, None, eq_)
+            tt(f("xn"), four("tlb", 0), four("td", 0), add)
+            if early:
+                cp(uv("xu"), f("xn"))
+                act(r("lg", 0, 256), ind(LK, uv("xu")), ACT.Relu, bias=col(8), scale=col(7))
+                pick(r("b4", 0, 16), "wwin", "lg", 256)
+                cp(iv("hi"), r("b4", 0, 16))
+            else:
+                tt(f("hd"), r("b4", 1, 32, 2), mine, sub)
+                tt(f("hd"), f("hd"), f("xw"), mul)
+                tt(iv("hi"), r("b4", 0, 32, 2), f("hd"), add)
+            holders()
+        ts(r("sm", 1, 64, 4), PL, 2 * NAP, None, ge)
+        ts(r("sm", 2, 64, 4), r(cur, 3, 67, 4), 0.0, None, eq_)
         scan(r(curn, 0, 64), r("sm"), r(cur, 1, 65), mul, add)
         if not last:
             cp(uv(cun), r(curn, 2, 64, 4))
 
     for t in range(STEPS):
         last = t == STEPS - 1
-        if t:
-            decide(t)
-        else:
+        if t == 0:
+            counts(0)
             steps_of("ka", "ea", "", t, ("b7", "b6"), 1, "cla")
         for a in range(len(CUTS[t])):
             judge(a, t)
@@ -852,11 +1006,8 @@ def rank_program(g, core, T, topo):
             tell(u, "lkc%d" % u, "skg%d" % t, "kc%d" % u)
         if t == 0:
             first_holders()
-        if t == 0:
-            decide(t)
+        decide(t)
         aborts(t)
-        if t == 0:
-            noflags(3, 8, [r("lnd0")])
         keys(t)
         cp(ind(VD, uv("listu")), r("lnd%d" % t))
         if t in FLAG:
@@ -878,8 +1029,10 @@ def rank_program(g, core, T, topo):
     ts(f("iso"), f("w1"), 0.0, None, lt)
     tt(r("f1"), ind(f("iso"), uv("lr")), r("qk"), mul)
     tt(r("f1"), r("f1"), r("q16"), add)
+    ts(f("w"), f("w1"), -32.0, None, mul)
+    tt(r("f2"), ind(f("w"), uv("lr")), r("f1"), add)
     ts(f("yl"), r("sa", 2, 66, 4), -1.0, None, add)
     dma("y", ext(T.yl[:]), f("yl"), "oyl", 2.0)
-    tt(r("hr"), ind(f("w"), uv("lr")), r("f1"), gt)
+    tt(r("hr"), ind(r("cs2"), uv("os")), r("f2"), gt)
     dma("y", ext(T.yh[:]), r("hr"), "oyh", 2.0)
     issue()

@@ -8,35 +8,40 @@ FB = 16384
 DUM, VO = 0, 256
 FO = VO + FB
 BIGW = FO + NV
-LW = NV + 512
+LW = NV + 640
 U = 32768.0
-BIG, HUGE = 4194304.0, 16777216.0
+BIG, HUGE = 4194304.0, 12582912.0
 HM = 16384.0
-GONE = 8589934592.0
+GONE = BIG * HM
 FAR = 2.0 ** 40
 NAP = 8388608.0
 ANEW = 1024.0
 FLAG = {1: 2.0 ** 15, 2: 2.0 ** 34}
 CALM = {1: 2.0 ** 21, 2: 2.0 ** 21, 3: 2.0 ** 40}
 FIRST = ((512, "s"), (512, "s"), (512, "v"), (512, "v"), (1024, "r"), (768, "r"), (256, "r"))
-LATER = ((512, "s"), (512, "s"), (512, "s"), (512, "v"), (1024, "v"), (768, "v"), (256, "v"))
+LATER = ((512, "s"), (512, "s"), (512, "s"), (512, "v"), (1024, "r"), (768, "r"), (256, "r"))
 CUTS = (FIRST, LATER, LATER, LATER)
-AA = ("vvv", "sss", "sss", "sss", "vvv")
-APART = (1, 0, 0, 0)
-EARLY = (0, 0, 1)
+AA = ("vvs", "sss", "sss", "sss", "vvs")
+APART = (1, 1, 1, 0)
+EARLY = (0, 1, 1)
+LOADS = (("y", "ea", 0, 2048), ("s", "big", 0, 4096), ("y", "big", 4096, NV), ("y", "ea", 2048, 3072), ("y", "ea", 3072, 4096))
+LOCKV = ()
+ANEWQ = "s"
+BLANK = 16
 LUMP = 32
-YB = ("vvv", "sss", "sss", "sss")
+YB = ("vv", "sv", "sv", "sv")
 FILL = ((768, 1792, 1024), (768, 768, 768, 768))
 PARTS = [(0, 2048), (2048, 3840), (3840, 4096)]
-WAKE = 0.15
-CY = 0.00095
-AFIX, FLY, FLYB = 80 * CY, 1.3, 0.0005
+PRICES = ((0.00086, 1.5, 3.5, 0.18, 1.55, 1.0), (0.00083, 1.08, 1.7, 0.2, 1.6, 1.0), (0.0011, 1.9, 5.0, 0.18, 1.6, 0.6))
+AFIX, FLYB = 0.076, 0.0005
+OTHER = []
 GOCC, GLAT = 0.8, 2.6
 ROUNDS = 10
-TRIES = 40000
+RUNS = 3
+TRIES = 4500
 SHAKE, PUSH, MARK = 0.1, 2.5, 0.5
 HEAT = 0.8
-SEED = 2
+SEED = 6
 TURN = 8
 AIMED = 4
 DEBUG = []
@@ -65,17 +70,19 @@ for _n in ("codes", "yt"):
     SCRATCH[_n] = ("sbuf", [128, 512], "float32")
 for _n in ("csk", "hok", "ai", "tj"):
     SCRATCH[_n] = ("sbuf", [128, 256], "int32")
-for _n in ("r16", "dj", "rst", "diag", "cut", "cg", "cs2", "f1", "f2", "pos", "cr", "hr", "un", "qk", "q16", "pd", "am", "aa", "cv", "cw"):
+for _n in ("r16", "dj", "rst", "diag", "cut", "cg", "cs2", "f1", "f2", "pos", "cr", "hr", "un", "qk", "q16", "pd", "aa", "cv", "cw"):
     SCRATCH[_n] = ("sbuf", [128, 256], "float32")
-for _n in ("iw", "pw", "dg1", "ka", "st", "s1", "s2", "zt"):
+for _n in ("iw", "pw", "dg1", "ka", "st", "s1", "s2", "zt", "sg"):
     SCRATCH[_n] = ("sbuf", [128, 272], "float32")
-for _n in ("qb", "blkf", "turn"):
+for _n in ("qb", "blkf", "turn", "swap"):
     SCRATCH[_n] = ("sbuf", [128, 128], "float32")
 for _n in ("blk", "nblk", "blkw", "blkh", "mix", "id_", "nid_"):
     SCRATCH[_n] = ("sbuf", [128, 128], "bfloat16")
 SCRATCH["wwin"] = ("sbuf", [128, 144], "bfloat16")
-SCRATCH["es"] = ("sbuf", [128, 1024], "float16")
-SCRATCH["idh"] = ("sbuf", [128, 128], "float16")
+SCRATCH["es"] = ("sbuf", [128, 1536], "float16")
+SCRATCH["am"] = ("sbuf", [128, 128], "float32")
+for _n in ("idh", "turh", "amh"):
+    SCRATCH[_n] = ("sbuf", [128, 128], "float16")
 SCRATCH["sel"] = ("sbuf", [128, 2048], "bfloat16")
 SCRATCH["lg"] = ("sbuf", [128, 512], "bfloat16")
 SCRATCH["yb"] = ("sbuf", [128, 384], "bfloat16")
@@ -88,13 +95,13 @@ for _n in ("coff", "loff", "ku"):
 FS = ["prf", "col", "col2", "clm", "q8", "sent", "home", "one", "vs", "a32", "a33", "xw", "pl", "hd",
       "w", "w1", "nd", "k1", "k2", "k3", "l1", "l2", "m1", "m2", "none", "spare", "yl", "iso", "cm", "xn", "j1", "j2", "sen2"]
 IS = ["oi", "oi2", "hi", "pi", "by", "sl0", "sl1", "sl2", "sl3", "nw", "pr", "pg", "wk"]
-US = ["xu", "xv", "ou", "cua", "cub", "offu", "listu", "slot", "os", "lc", "lr", "lrev", "lperm", "lq", "ldup", "ldup2", "lk", "lk2", "lct", "offw"]
+US = ["xu", "xv", "ou", "cua", "cub", "offu", "listu", "slot", "lc", "lr", "lrev", "lperm", "lq", "os", "lk", "lk2", "lct", "offw"]
 SCRATCH["fs"] = ("sbuf", [128, 16 * len(FS)], "float32")
 SCRATCH["is_"] = ("sbuf", [128, 16 * len(IS)], "int32")
 SCRATCH["us"] = ("sbuf", [128, 16 * len(US)], "uint16")
 SCRATCH["hw"] = ("sbuf", [128, 272], "bfloat16")
-for _n in ("rdy", "rs", "w1b", "ab", "dec", "hb"):
-    SCRATCH[_n] = ("sbuf", [128, 16], "bfloat16")
+BS = ["rdy", "rs", "w1b", "ab", "dec", "hb"]
+SCRATCH["bs"] = ("sbuf", [128, 16 * len(BS)], "bfloat16")
 for _n in ("cla", "clb"):
     SCRATCH[_n] = ("sbuf", [128, 32], "bfloat16")
 for _t in range(STEPS):
@@ -109,14 +116,15 @@ for _t in range(STEPS):
 for _b in range(8):
     SCRATCH["b%d" % _b] = ("psum", [128, 16, 32] if _b == 1 else [128, 512], "float32")
 
-SEMAPHORES = ["c" + q for q in "vspgy"] + ["dcs", "dho", "dwk", "dsn", "ds2", "dx0", "dx1", "oyc", "oyh", "oyl"] + ["oys%d" % _g for _g in range(8)]
+SEMAPHORES = ["c" + q for q in "vspgy"] + ["dcs", "dho", "dwk", "in0", "in1", "in2", "in3", "in4", "in5", "oyc", "oyh", "oyl"] + ["oys%d" % _g for _g in range(8)] + ["blank%d" % _g for _g in range(8)]
 for _t in range(STEPS):
     SEMAPHORES += [k + str(_t) for k in ("rsf", "rkc", "rdd", "qsf", "qkc", "qdd", "rfu", "qfu")]
     SEMAPHORES += ["add%d_%d" % (_t, _a) for _a in range(8)]
 
 
-def emitter(g, T):
+def emitter(g, T, price):
     eng = {"v": g.vector, "s": g.scalar, "p": g.tensor, "g": g, "y": g.sync}
+    WAKE, FLY = price[3:5]
     known = {q: {} for q in eng}
     cnt = {q: 0 for q in eng}
     hist, bank, final, prog = {}, {}, {}, []
@@ -223,7 +231,7 @@ def emitter(g, T):
             for k, l in pred.items():
                 fore[k].append((i, l))
                 back[i].append((k, l + occ - prog[k][5]))
-            tags.append((q, wr[0][0], wr[0][1][0] if wr[0][0] in ("fs", "us", "is_", "quads") else 0) if wr else q)
+            tags.append((q, wr[0][0], wr[0][1][0] if wr[0][0] in ("fs", "us", "is_", "quads", "bs") else 0) if wr else q)
 
         reach = [0] * m
         for i in range(m - 1, -1, -1):
@@ -356,28 +364,60 @@ def emitter(g, T):
             return when
 
         held = [None, None]
-        now, had = best, worth(best)
-        least = had
-        for n in range(TRIES):
-            i, by, span = int(draw() * m), PUSH * (draw() - 0.5), 6.0 * draw() if n % 3 else 1000.0
-            key = [now[k] + (by if tags[k] == tags[i] and abs(now[k] - now[i]) <= span else 0.0) for k in range(m)]
-            if n % 5 < AIMED:
-                if held[0] is not now:
-                    held[:] = [now, holdups(now)]
-                i, k = held[1][int(draw() * len(held[1]))]
-                key = list(now)
-                if draw() < 0.5:
-                    key[i] = now[k] - 0.001 - draw() ** 2
+
+        also = []
+        for other, (_c, _g, _s, wake, _f, weight) in OTHER:
+            waits = [[(k, other[k][5] if abs(l - occs[k]) < 1e-9 else other[k][6] + wake) for k, l in needs[i]] for i in range(m)]
+            also.append((waits, [p[5] for p in other], [p[6] for p in other], weight))
+
+        def whole(start):
+            total, line_up = worth(start), sorted(range(m), key=lambda i: start[i])
+            for waits, occ, lat, weight in also:
+                when, free, end = [0.0] * m, {q: 0.0 for q in list(eng) + ["net"]}, 0.0
+                for i in line_up:
+                    t = free[ques[i]] if occ[i] else 0.0
+                    for k, l in waits[i]:
+                        if when[k] + l > t:
+                            t = when[k] + l
+                    when[i] = t
+                    if occ[i]:
+                        free[ques[i]] = t + occ[i]
+                    if t + lat[i] > end:
+                        end = t + lat[i]
+                total += weight * (end + MARK * sum(when[i] for i in marks) / len(marks))
+            return total
+
+        def settle(best, tries, heat):
+            now, had, first = best, whole(best), worth(best)
+            least = had
+            for n in range(tries):
+                if n % 5 < AIMED:
+                    if held[0] is not now:
+                        held[:] = [now, holdups(now)]
+                    i, k = held[1][int(draw() * len(held[1]))]
+                    key = list(now)
+                    if draw() < 0.5:
+                        key[i] = now[k] - 0.001 - draw() ** 2
+                    else:
+                        key[k] = now[i] + 0.001 + draw() ** 2
                 else:
-                    key[k] = now[i] + 0.001 + draw() ** 2
-            start = again(now, key)
-            if n % TURN == 0:
-                start = turn(start, 0.0)
-            w = worth(start)
-            if w <= had + 0.02 + HEAT * (1 - n / TRIES) ** 2 * draw():
-                now, had = start, w
-                if w < least:
-                    best, least = start, w
+                    i, by, span = int(draw() * m), PUSH * (draw() - 0.5), 6.0 * draw() if n % 3 else 1000.0
+                    key = [now[k] + (by if tags[k] == tags[i] and abs(now[k] - now[i]) <= span else 0.0) for k in range(m)]
+                start = again(now, key)
+                if n % TURN == 0:
+                    start = turn(start, 0.0)
+                room = 0.02 + heat * (1 - n / tries) ** 2 * draw()
+                if worth(start) > first + 0.4 + room:
+                    continue
+                w = whole(start)
+                if w <= had + 2 * room:
+                    now, had, first = start, w, worth(start)
+                    if w < least:
+                        best, least = start, w
+            return best
+
+        best = min([settle(best, TRIES, HEAT) for n in range(RUNS)], key=whole)
+        best = settle(best, TRIES, HEAT / 3)
         DEBUG.extend([tags, prog, fore, back, best, way])
         return sorted(range(m), key=lambda i: (best[i], i))
 
@@ -402,16 +442,25 @@ def emitter(g, T):
             if known["g"].get(s, 0) < final[s]:
                 g.wait_ge(T.sem[s], final[s])
 
-    return op, block, dma, send, issue
+    return op, block, dma, send, issue, prog
 
 
 def rank_program(g, core, T, topo):
-    rank = T.rank_of(core)
-    if rank is None:
+    if T.rank_of(core) is None:
         return
-    op, block, dma, send, issue = emitter(g, T)
+    if not ORDER:
+        OTHER[:] = [(written(g, core, T, topo, price)[0], price) for price in PRICES[1:]]
+    written(g, core, T, topo, PRICES[0])[1]()
+
+
+def written(g, core, T, topo, price):
+    rank = T.rank_of(core)
+    CY, GATHER, SCATTER = price[:3]
+    op, block, dma, send, issue, prog = emitter(g, T, price)
 
     def r(n, a=None, b=None, st=None):
+        if n in BS:
+            return r("bs", 16 * BS.index(n), 16 * BS.index(n) + 16)
         if n in QUADS:
             return r("quads", 72 * QUADS.index(n) + (a or 0), 72 * QUADS.index(n) + (64 if b is None else b), st)
         a = 0 if a is None else a
@@ -448,9 +497,9 @@ def rank_program(g, core, T, topo):
     def cost(out, a, b=None):
         n, ko, ka = a[2], kind(out), kind(a)
         if ko[0]:
-            return 0.05 + n * 3.8 * CY
+            return 0.05 + n * SCATTER * CY
         if ka[0]:
-            return 0.05 + n * 1.56 * CY
+            return 0.05 + n * GATHER * CY
         if b is not None:
             return max(64, n * (1 if ka[1] or kind(b)[1] else 2)) * CY
         return max(64, n * (0.5 if ko[2] and ka[2] else 1)) * CY
@@ -524,14 +573,13 @@ def rank_program(g, core, T, topo):
     dma("y", r("hok"), ext(T.hold[:]), "dho", 2.3)
     dma("s", iv("wk"), ext(T.wake[:]), "dwk", 2.5)
     at = 3.0
-    for q, n, src, a, b, sem in (("y", "ea", T.snap, 0, 2048, "dsn"), ("s", "big", T.x, 0, 4096, "dx0"),
-                                 ("y", "big", T.x, 4096, NV, "dx1"), ("y", "ea", T.snap, 2048, 4096, "ds2")):
+    for i, (q, n, a, b) in enumerate(LOADS):
         at += 0.25 + (b - a) / 1000.0
-        off = VO if n == "big" else 0
-        dma(q, r(n, off + a, off + b), ext(src[:, a:b]), sem, at)
+        src, off = (T.x, VO) if n == "big" else (T.snap, 0)
+        dma(q, r(n, off + a, off + b), ext(src[:, a:b]), "in%d" % i, at)
 
     iota(iv("pr", 1), [[0, 1]], 0, 1)
-    iota(r("dj"), [[0, 8], [16, 32]], NV)
+    iota(r("dj"), [[0, 8], [16, 32]], NV, 1)
     iota(r("codes", 0, 16 * LUMP), [[0, LUMP // 16], [1, 256]], 17)
     at = sum(FILL[0] + FILL[1])
     iota(r("lock", at, NV), [[0, NV - at]], 0)
@@ -542,16 +590,20 @@ def rank_program(g, core, T, topo):
     iota(r("own"), [[512, 4], [16, 16]], 513)
     iota(r("qw"), [[1, 144]], -15)
     iota(r("r16"), [[0, 16], [1, 16]], 0)
-    iota(r("lf", 16, 48), [[1, 16], [0, 2]], 0)
+    iota(r("lf", 16, 32), [[0, 16]], 15)
+    iota(r("lf", 32, 48), [[32, 8], [256, 2]], 0)
+    iota(r("lf", 48, 64), [[0, 8], [-32, 2]], 17)
     iota(r("qb"), [[1, 8], [0, 16]], 0)
     iota(f("a32", 17), [[256, 17]], -16)
-    iota(f("col2", 4), [[-int(U), 4]], 1 - int(U))
     for n, k in (("rst", 16), ("sm", 4)):
         iota(r(n), [[0, r(n)[2]]], 1)
         keep(r(n), r(n), [[0, 16], [1, k]], gt, 0.0)
     keep(r("cut"), r("rst"), [[0, 16], [1, 16]], gt, -2 * FAR)
     iota(r("turn"), [[0, 128]], 1)
+    keep(r("swap"), r("turn"), [[-32, 4], [16, 2], [-1, 16]], eq_, 0.0, 1, -16)
     keep(r("turn"), r("turn"), [[-1, 16], [-16, 8]], eq_, 0.0, 1)
+    for n, a, x in (("cla", 0, 17 * U - BIG), ("cla", 16, -HUGE), ("clb", 0, U - 2 * BIG)):
+        iota(r(n, a, a + 16), [[0, 16]], int(x))
     iota(r("iw", 1, 257), [[1, 256]], 1)
     iota(r("q16"), [[32, 16], [0, 16]], 16)
     for x in (r("sa", 0, 144), r("ldw", 0, 1), r("zt"), r("big", DUM, VO)):
@@ -561,7 +613,7 @@ def rank_program(g, core, T, topo):
         for c in range(a, b):
             iota(r("big", FO + 512 * c, FO + 512 * c + 512), [[0, 512]], 0, 0, after)
 
-    noflags(0, 16)
+    noflags(0, BLANK)
 
     at = 0
     for n in FILL[0]:
@@ -572,14 +624,16 @@ def rank_program(g, core, T, topo):
         at += n
     ts(iv("pg", 1, 0), iv("pr", 1), 15, None, band)
     cp(f("prf", 1), iv("pg", 1))
-    ts(r("dj"), r("dj"), f("prf", 1), None, add)
     for a, b in ((0, 64), (64, 256)):
-        ts(r("f1", a, b), r("hok", a, b), -100000.0, 100000.0, mul, add)
-        tt(r("f1", a, b), r("f1", a, b), r("csk", a, b), add)
-        tt(r("f1", a, b), r("f1", a, b), r("dj", a, b), mn)
-        cp(r("loff", a, b), r("f1", a, b))
+        ts(r("b0", a, b), r("hok", a, b), -100000.0, 100000.0, mul, add)
+        tt(r("b0", a, b), r("b0", a, b), r("csk", a, b), add)
+        tt(r("b0", a, b), r("b0", a, b), r("dj", a, b), mn)
+        cp(r("loff", a, b), r("b0", a, b))
     for c in range(0, 256, LUMP):
-        act(ind(r("lock"), r("loff", c, c + LUMP)), r("codes", 0, 16 * LUMP), ACT.Silu)
+        if c // LUMP in LOCKV:
+            cp(ind(r("lock"), r("loff", c, c + LUMP)), r("codes", 0, 16 * LUMP))
+        else:
+            act(ind(r("lock"), r("loff", c, c + LUMP)), r("codes", 0, 16 * LUMP), ACT.Silu)
 
     ts(iv("pg", 1, 1), iv("pr", 1), 4, None, shr)
     ts(iv("pg", 1, 2), iv("pr", 1), 112, None, band)
@@ -598,7 +652,7 @@ def rank_program(g, core, T, topo):
     ts(col(14), PRF, 16.0, None, mul)
     ts(col(15), PRF, 1.0, None, add)
     ts(r("wwin"), r("qw"), G16, col(5), eq_, mul)
-    ts(uv("lq", 48), r("lf", 0, 48), col(14), None, add)
+    ts(uv("lq", 32), r("lf", 0, 32), col(14), None, add)
     ts(col(10), PRF, 17.0, 1.0, mul, add)
     ts(uv("lperm"), f("q8"), col(10), None, add)
     cp(uv("lc"), f("q8"))
@@ -612,15 +666,11 @@ def rank_program(g, core, T, topo):
     cp(uv("lk", 17), f("k1", 17))
     cp(r("st"), ind(r("csk"), uv("lk", 17)))
     ts(col(11), iv("pr", 1), 16.0, None, ge)
-    ts(f("col2", 4), f("col2", 4), col(11), None, mul)
     for t in FLAG:
         ts(f("col2", 1, 4 + 2 * t), col(2), FLAG[t], None, mul)
-        ts(f("col2", 1, 5 + 2 * t), col(2), -320.5 * FLAG[t], None, mul)
-    for n, a, x in (("cla", 0, 16 * U - BIG), ("cla", 16, -HUGE), ("clb", 0, -2 * BIG)):
-        ms(r(n, a, a + 16), x)
-    BANK, HALF, WEIGH, OVER = r("gib", 0, 8), r("gib", 8, 24), r("gib", 24, 32), (32, 48)
+    BANK, HALF, WEIGH, OVER = r("gib", 0, 8), r("gib", 8, 24), r("gib", 48, 56), (32, 48)
     ts(BANK, f("q8", 8), PGF, None, eq_)
-    ts(r("gib", 48, 56), f("q8", 8), PGF, -1.0, eq_, mul)
+    ts(r("gib", 24, 32), f("q8", 8), PGF, -1.0, eq_, mul)
     ts(r("gib", 8, 16), f("q8", 8), PGF, col(2), eq_, mul)
     ts(r("gib", 16, 24), f("q8", 8), PGF, col(6), eq_, mul)
     ts(WEIGH, f("q8", 8), PGF, col(15), eq_, mul)
@@ -643,35 +693,35 @@ def rank_program(g, core, T, topo):
     ts(r("blkw"), r("blkf"), f("k3", 1), U, mul, mul)
     ts(f("k3", 1, 1), f("k3", 1), -2.0 * U, FAR, mul, add)
     ts(r("thn"), r("diag"), f("k3", 1, 1), -FAR, mul, add)
-    cp(r("yt"), ind(r("csk"), uv("ldup", 32)))
-    op("v", lambda: g.vector.transpose(out=r("ct")[0], in_=r("yt")[0]), [r("ct")], [r("yt")], 512 * CY)
-    tt(col(13), PRF, ODD, add)
-    ts(uv("lct"), f("q8"), 32.0, col(13), mul, add)
+    cp(r("cr"), ind(r("csk"), uv("lrev")))
+    op("v", lambda: g.vector.transpose(out=r("ct", 0, 256)[0], in_=r("cr")[0]), [r("ct", 0, 256)], [r("cr")], 256 * CY)
+    mm(r("b0", 256, 512), r("swap"), r("ct", 0, 256), True, True)
+    act(r("ct", 256, 512), r("b0", 256, 512), ACT.Copy)
+    ts(r("lf", 48, 64), r("lf", 48, 64), ODD, PRF, mul, add)
+    tt(r("lf", 48, 64), r("lf", 48, 64), r("lf", 32, 48), add)
+    cp(uv("lct"), r("lf", 48, 64))
     lin(r("pos"), ind(r("ct"), uv("lct")), None, 288.0)
     ts(f("none"), f("home"), 31.0, None, add)
     ts(f("spare"), f("home"), -768.0, None, add)
-    ts(col(12), col(14), 15.0, None, add)
-    ts(uv("os"), f("q8"), 0.0, col(12), mul, add)
 
-    cp(r("cr"), ind(r("csk"), uv("lrev")))
     cp(r("hr"), ind(r("hok"), uv("lrev")))
-    ts(r("un"), r("hr"), -1.0, 1.0, mul, add)
+    ts(r("b5", 0, 256), r("hr"), -1.0, 1.0, mul, add)
     lin(r("cv"), r("hr"), -18.0, 17.0)
-    scan(r("cs2"), r("rst"), r("un"), mul, add)
+    scan(r("cs2"), r("rst"), r("b5", 0, 256), mul, add)
     ts(r("fu0"), tl("cs2"), -1.0, 16.0 - ANEW, mul, add)
-    lin(r("cg"), r("cs2"), -1.0, 17.0)
-    tt(r("pd"), r("cv"), r("cg"), mn)
+    lin(r("b4", 256, 512), r("cs2"), -1.0, 17.0)
+    tt(r("pd"), r("b4", 256, 512), r("cv"), mn)
     lin(r("qk"), ind(r("pd"), uv("lq")), 32.0, 16.0 - 32.0 * (ANEW + 1))
     tt(r("qk"), r("qk"), r("q16"), sub)
     lin(r("dg1", 1, 257), r("diag"), 32.0)
     ms(hd("hr"), 0.0)
-    ms(hd("un"), 1.0)
-    tt(r("f2"), r("un"), r("cr"), mul)
+    ms(hd("b5"), 1.0)
+    tt(r("f2"), r("b5", 0, 256), r("cr"), mul)
     for n in range(4):
-        scan(P0, r("hr"), r("f2"), mul, add)
-        cp(four("tla", n), r("b6", 15, 256, 16))
+        scan(r("un"), r("hr"), r("f2"), mul, add)
+        cp(four("tla", n), tl("un"))
         if n < 3:
-            tt(r("f2", 1, 256), r("b6", 0, 255), r("un", 1, 256), mul)
+            tt(r("f2", 1, 256), r("b5", 1, 256), r("un", 0, 255), mul)
             cp(hd("f2"), hd("cr"))
     cp(uv("xu"), four("tla", 0))
     cp(r("sa", 2, 66, 4), f("home"))
@@ -728,24 +778,35 @@ def rank_program(g, core, T, topo):
             ts(col(12) if n else f("col2", 1, 10 + i), iv("pr", 1), float(a), float(by), ge, mul)
             if n:
                 tt(f("col2", 1, 10 + i), f("col2", 1, 10 + i), col(12), add)
+        if x[0]:
+            ts(r("es", 384 * i + 256, 384 * i + 384), r("blk"), 0.0, None, mul)
     cp(r("idh"), r("id_"))
+    cp(r("turh"), r("turn"))
+
+    def joint(t):
+        return all(q in "qr" for a, (n, q) in enumerate(CUTS[t]) if sum(k for k, _q in CUTS[t][:a]) >= 2048)
+
+    def parts(t):
+        return [(0, 2048), (2048, 4096)] if joint(t) else PARTS
+
     for m in range(0, 16, 4):
-        keep(r("sel", 128 * m, 128 * m + 512), r("big", FO, FO + 512), [[-1, 4], [-16, 8], [0, 16]], ALU.not_equal, GONE, 1, -m)
+        keep(r("sel", 128 * m, 128 * m + 512), r("big", FO, FO + 512), [[-1, 4], [-16, 8], [0, 16]], ALU.not_equal, HM, 1, -m)
 
     def steps_of(out, src, less, t, banks, unit, cls):
         for h in range(2):
             bk, c, lo = banks[h], 128 * h, 2048 * h
             more = less and taken(t, h)
-            if more:
-                mm(r(bk, 0, 256), r("idh"), r("es", 256 * kept.index(more), 256 * kept.index(more) + 256), True, False)
-            for m in range(16):
-                mm(r(bk, m, 256, 16), r(src, lo + m, lo + 2048, 16), HALF, not more, not more or m == 15)
-                if m % 8 == 7:
-                    block(8)
+            if not (less and h and joint(t)):
+                if more:
+                    mm(r(bk, 0, 256), r("idh"), r("es", 384 * kept.index(more), 384 * kept.index(more) + 256), True, False)
+                for m in range(16):
+                    mm(r(bk, m, 256, 16), r(src, lo + m, lo + 2048, 16), HALF, not more, not more or m == 15)
+                    if m % 8 == 7:
+                        block(8)
             if not less:
                 for i, x in enumerate(kept):
                     if x[0] == h:
-                        ts(r("es", 256 * i, 256 * i + 256), r(bk, 0, 256), f("col2", 1, 10 + i), None, mul)
+                        ts(r("es", 384 * i, 384 * i + 256), r(bk, 0, 256), f("col2", 1, 10 + i), None, mul)
             if AA[t if less else STEPS][h] == "s":
                 act(r("aa", c, c + 128), r(bk, 0, 128), ACT.Copy)
             else:
@@ -754,15 +815,15 @@ def rank_program(g, core, T, topo):
             ts(r("tj", c, c + 128), r("ai", c, c + 128), 3, 511, shr, band)
             if h == 0:
                 ts(rows(16, "tj", 0, 128), rows(16, "ai", 0, 128), 3, NV - 1, shr, band)
-            ts(r("am", c, c + 128), r("tj", c, c + 128), 1 - unit * U if h else f("col2", 1, unit - 1), None, add)
+            ts(r("amh" if h else "am"), r("tj", c, c + 128), 1.0 if h else col(11), None, add)
         mm(deep(T.b1[:, :, 0], "b1", 0, 512, 16), r("id_"), r("cla", 16, 32), True, False)
         for h in range(2):
-            mm(deep(T.b1[:, :, 1 + 8 * h:9 + 8 * h], "b1", 0, 512, 128), r("am", 128 * h, 128 * h + 128), r("turn"), False, False)
+            mm(deep(T.b1[:, :, 1 + 8 * h:9 + 8 * h], "b1", 0, 512, 128), r("amh" if h else "am"), r("turh" if h else "turn"), False, False)
         mm(deep(T.b1[:, :, 1], "b1", 0, 512, 16), r("id_"), r(cls, 0, 16), False, True)
         if AA[t if less else STEPS][2] == "s":
-            act(r(out), deep(T.b1[:, :, 0:17], "b1", 0, 512, 272), ACT.Copy)
+            lin(r(out), deep(T.b1[:, :, 0:17], "b1", 0, 512, 272), None, -unit * U)
         else:
-            cp(r(out), deep(T.b1[:, :, 0:17], "b1", 0, 512, 272))
+            ts(r(out), deep(T.b1[:, :, 0:17], "b1", 0, 512, 272), -unit * U, None, add)
 
     def judge(a, t):
         lo = sum(n for n, q in CUTS[t][:a])
@@ -783,26 +844,37 @@ def rank_program(g, core, T, topo):
             tt(d, cells, e, sub)
             if CUTS[t][a][1] == "r":
                 ts(out, d, 0.0, 2.0, mx, mul)
+            elif CUTS[t][a][1] == "q":
+                act(out, d, ACT.Relu, scale=2.0)
             else:
                 act(out, d, ACT.Abs)
 
     def far(h, t):
-        c, (lo, hi) = 128 * h, PARTS[h]
-        n, bk = (hi - lo) // 16, ("b0", "b0", "b3")[h]
-        sums(bk, c, c + 128, "absd", BANK, lo, hi, "r", t, "diff", r("gib", 48, 56), 8)
-        if YB[t][h] == "s":
-            act(rows(n, "yb", c, c + 128), rows(n, bk, c, c + 128), ACT.Relu, bias=-320.0)
+        c, (lo, hi) = 128 * h, parts(t)[h]
+        n, bk, at = (hi - lo) // 16, ("b0", "b0", "b3")[h], c
+        if h and joint(t):
+            bk, at, i = "b6", 256, 384 * kept.index(taken(t, 1))
+            mm(r(bk, 0, 384), r("idh"), r("es", i, i + 384), True, False)
+            for src, a, x in (("diff", 0, r("gib", 8, 32)), ("absd", 256, BANK)):
+                for m in range(16):
+                    mm(r(bk, a + m, 384, 16), r(src, lo + m, hi, 16), x, False, a > 0 and m == 15)
+                    if m % 8 == 7:
+                        block(8)
         else:
-            ts(rows(n, "yb", c, c + 128), rows(n, bk, c, c + 128), -320.0, 0.0, add, mx)
+            sums(bk, c, c + 128, "absd", BANK, lo, hi, "qr", t, "diff", r("gib", 24, 32), 8)
+        if YB[t][h] == "s":
+            act(rows(n, "yb", c, c + 128), rows(n, bk, at, at + 128), ACT.Relu, bias=-320.0)
+        else:
+            ts(rows(n, "yb", c, c + 128), rows(n, bk, at, at + 128), -320.0, 0.0, add, mx)
 
     def verdicts(t):
         out = r("b2", 256, 272)
         if t:
             mm(out, r("id_"), r("w1b"), True, False)
-        for h, (lo, hi) in enumerate(PARTS):
+        for h, (lo, hi) in enumerate(parts(t)):
             n = (hi - lo) // 16
-            mm(out, rows(n, "yb", 128 * h, 128 * h + 128), rows(n, "gib", *OVER), t == h == 0, h == len(PARTS) - 1)
-        ts(r("sf%d" % t), out, 0.0, None, lt)
+            mm(out, rows(n, "yb", 128 * h, 128 * h + 128), rows(n, "gib", *OVER), t == h == 0, h == len(parts(t)) - 1)
+        ts(r("sf%d" % t), out, 0.0, GONE / HM, lt, mul)
         tell(t, "lsf%d" % t, "sf%d" % t, "sf%d" % t)
 
     def counts(t):
@@ -818,7 +890,7 @@ def rank_program(g, core, T, topo):
     def first_holders():
         act(r("lg", 0, 256), ind(LK, uv("xu")), ACT.Relu, bias=col(8), scale=col(7))
         pick(r("b4", 0, 16), "wwin", "lg", 256)
-        cp(r("hb"), r("b4", 0, 16))
+        ts(f("hd"), r("b4", 0, 16), HM, None, mul)
         cp(f("xn"), four("tla", 0))
 
     def holders():
@@ -841,11 +913,11 @@ def rank_program(g, core, T, topo):
         scan(r("rs"), f("one"), r("rdy"), mul, add)
         mm(rk, r("mix"), r("rdy"), True, False)
         mm(rk, r("blk"), r("rs"), False, True)
-        ts(f("cm"), rk, -1007.0, None, lt)
+        ts(f("cm"), rk, -1007.0, GONE / HM, lt, mul)
         tt(f("m1"), rk, f("spare"), mn)
         ts(uv("slot"), f("m1"), 1023.0, None, add)
         act(ind(r("slw"), uv("slot")), r("pos"), ACT.Silu)
-        ts(gate("zt"), f("cm"), 2 * BIG + 64 * U, None, mul)
+        ts(gate("zt"), rk, -1007.0, 2 * BIG + 64 * U, lt, mul)
         ts(uv("listu"), r("slw", 0, 16), -32.0, None, add)
         act(r("snd%d" % t), ind(VD, uv("listu")), ACT.Copy)
         tell(t, "lnd%d" % t, "snd%d" % t, "dd%d" % t)
@@ -854,11 +926,11 @@ def rank_program(g, core, T, topo):
         a, b = (f("cm"), r("lsf%d" % t)) if t else (r("lsf0"), f("cm"))
         tt(r("ab"), r("sf%d" % t), a, mx)
         tt(r("dec"), r("ab"), b, mx)
+        tt(gate("st"), r("ab"), b, mx)
         ts(f("nd"), r("dec"), 0.0, None, eq_)
 
     def keys(t):
         scan(r("b7", 0, 272), r("lkc%d" % t), r("zt"), add, mx)
-        ts(gate("st"), r("dec" if t else "ab"), BIG, None, mul)
         now = "st"
         for n, steps in enumerate(["ka"] + ["skg%d" % u for u in range(1, t + 1)]):
             scan(r("s%d" % (1 + n % 2)), r(steps), r(now), add, mx)
@@ -871,7 +943,11 @@ def rank_program(g, core, T, topo):
         cp(r("coff"), ind(r("cf"), uv("lperm")))
         if t < 2:
             P1 = deep(T.b1[:, :, 0:17], "b1", 0, 512, 272)
-            ts(P1, RES, U, float(FB), ge, mul)
+            if ANEWQ == "s":
+                act(r("sg"), r(now), ACT.Sign, bias=0.5 - U)
+                lin(P1, r("sg"), FB / 2, FB / 2)
+            else:
+                ts(P1, RES, U, float(FB), ge, mul)
             tt(r("st"), P1, r("cf"), add)
         else:
             cp(r("st"), r("cf"))
@@ -881,7 +957,7 @@ def rank_program(g, core, T, topo):
         mm(r("b2", 0, 256), r("id_"), r("lnd%d" % t), False, True)
         act(r("fa"), r("b2", 0, 256), ACT.Abs)
         mm(r("b3", 0, 256), r("blk"), r("fa"), True, True)
-        act(r("fv"), r("b3", 0, 256), ACT.Relu, bias=f("col2", 1, 5 + 2 * t), scale=f("col2", 1, 4 + 2 * t))
+        act(r("fv"), r("b3", 0, 256), ACT.Relu, bias=-320.5 * FLAG[t], scale=f("col2", 1, 4 + 2 * t))
         cp(ind(FD, uv("listu")), r("fv"))
 
     def lanes(t):
@@ -892,40 +968,56 @@ def rank_program(g, core, T, topo):
         if early:
             act(r("cw"), ind(r("dg1"), uv(cu)), ACT.Copy)
         if not last:
-            act(r("cv"), ind(r("iw"), uv(cu)), ACT.Identity, bias=f("clm", 1, t), scale=col(9))
+            act(r("cv"), ind(r("iw"), uv(cu)) if t else r("iw", 1, 257), ACT.Identity, bias=f("clm", 1, t), scale=col(9))
         tt(r(cur, 1, 65, 4), f("home"), r(cur, 2, 66, 4), sub)
         if not APART[t]:
             ts(f("hd"), r("hb"), HM, None, mul)
             tt(f("xn"), f("xn"), f("hd"), add)
         tt(r("pd"), ind(f("xn"), uv("lc")), r("diag"), mul)
-        mm(r("b5", 0, 256), r("blkf"), r("pd"), True, False)
-        spread(("b5", 0), r("dec"), False)
-        act(r("pw", 1, 257), r("b5", 0, 256), ACT.Copy)
-        BY = r("b4", 48, 64)
-        if APART[t]:
+        late = APART[t] == 2
+        mm(r("b5", 0, 256), r("blkf"), r("pd"), True, late or t == 0)
+        if t == 0:
+            cp(r("ku"), r("b5", 0, 256))
+            spread(("b4", 256), r("dec"), True)
+            tt(f("pl"), f("xn"), iv("sl0"), mx)
+            ts(f("m2"), r("dec"), HM, None, mul)
+            tt(f("pl"), f("pl"), f("m2"), mx)
+        elif late:
+            tt(r("hb"), r("hb"), r("ab"), mx)
+            tt(r("hb"), r("hb"), r("lsf%d" % t), mx)
+        else:
+            spread(("b5", 0), r("dec"), False)
+        if t:
+            act(r("pw", 1, 257), r("b5", 0, 256), ACT.Copy)
+        BY = r("b4", 48, 64) if t else f("hd")
+        if t and APART[t]:
             spread(("b4", 256), r("hb"), True)
-            lin(r("hw", 1, 257), r("b4", 256, 512), HM / GONE)
+            act(r("hw", 1, 257), r("b4", 256, 512), ACT.Copy)
             lin(r("lh"), ind(r("hw"), uv(cu)), col(3))
             pick(BY, "wwin", "lh", 256)
         d = STEPS - 1 - t
         if not last:
-            act(r("b4", 256, 512) if t else r("ldw", 1, 257), r("pw", 1, 257), ACT.Relu, bias=-1.0, scale=(t + 2) / GONE)
+            act(r("b4", 256, 512) if t else r("ldw", 1, 257), r("hw" if late else "pw", 1, 257) if t else r("b4", 256, 512), ACT.Relu, bias=-1.0, scale=(t + 2) / GONE)
             if t:
                 tt(r("ldw", 1, 257), r("b4", 256, 512), r("ldw", 1, 257), mx)
             ts(four("tla", 0, d + 1), four("tla", 0, d + 1), U, None, add)
             tt(four("tlb", 0, d + 1), deep(T.res[:, :, 1:d + 2], "res", 0, 272, 16 * d + 16), four("tla", 0, d + 1), mx)
             ts(four("tlb", 0, d + 1), four("tlb", 0, d + 1), NV - 1, None, band)
-            if not early:
+            if t and not early:
                 cp(uv("xu", 32), four("tlb", 0, 2))
             tt(four("td", 0, d), four("tlb", 1, d + 1), four("tlb", 0, d), sub)
         tt(f("w1"), r("fu%d" % t), f("nd"), mul)
         if not last:
             ts(r("w1b"), f("w1"), 0.0, CALM[t + 1], ge, mul)
-        tt(r("cg"), ind(r("pw"), uv(cu)), r("diag"), mul)
-        cp(r("ku"), ind(r("pw"), uv(cu)))
-        scan(r("cs2"), r("rst"), r("cg"), mul, add)
-        tt(f("pl"), tl("cs2"), iv("sl%d" % t), mx)
+        if t:
+            tt(r("cg"), ind(r("pw"), uv(cu)), r("diag"), mul)
+            cp(r("ku"), ind(r("pw"), uv(cu)))
+            scan(r("cs2"), r("rst"), r("cg"), mul, add)
+            tt(f("pl"), tl("cs2"), iv("sl%d" % t), mx)
         PL = f("pl")
+        if late:
+            ts(f("m2"), PL, float(NV), None, lt)
+            tt(PL, BY, PL, add)
         mm(r("b5", 0, 256), r("id_"), r("thn"), True, False)
         for oc in range(16):
             n, at = 256 - 16 * oc, 272 * oc
@@ -939,7 +1031,11 @@ def rank_program(g, core, T, topo):
             tt(f("j1"), f("j1"), f("j2"), add)
         if not last:
             ts(f("k1"), PL, -HM, None, add)
-        if APART[t]:
+        if late:
+            ts(iv("pi"), PL, 2 * NAP, None, mn)
+            ts(iv("by"), iv("pi"), 14, 511, shr, band)
+            tt(r(cur, 3, 67, 4), iv("by"), f("m2"), mul)
+        elif APART[t]:
             for k in ["j1"] * early + ["k1"] * (not last):
                 tt(f(k), BY, f(k), add)
             ts(f("m2"), PL, float(NV), 1.0 / HM, lt, mul)
@@ -962,7 +1058,9 @@ def rank_program(g, core, T, topo):
             ts(uv("offu"), f("k3"), HM, None, add)
             act(ind(r("lock"), uv("offu")), r("cv"), ACT.Silu)
             mine = r("own", 16 * t, 16 * t + 16)
-            if early:
+            if t == 0:
+                ts(f("xw"), f("k2"), NV - HM, None, lt)
+            elif early:
                 ts(f("xw"), tl("cs2"), 16.0, None, gt)
             else:
                 act(r("lg"), ind(LK, uv("xu", 32)), ACT.Relu, bias=col(8), scale=col(7))
@@ -975,7 +1073,7 @@ def rank_program(g, core, T, topo):
             if d > 1:
                 tt(four("tla", 0, d), four("tlb", 0, d), four("td", 0, d), add)
             tt(f("xn"), four("tlb", 0), four("td", 0), add)
-            if early:
+            if early or t == 0:
                 cp(uv("xu"), f("xn"))
                 act(r("lg", 0, 256), ind(LK, uv("xu")), ACT.Relu, bias=col(8), scale=col(7))
                 pick(r("b4", 0, 16), "wwin", "lg", 256)
@@ -998,7 +1096,7 @@ def rank_program(g, core, T, topo):
             steps_of("ka", "ea", "", t, ("b7", "b6"), 1, "cla")
         for a in range(len(CUTS[t])):
             judge(a, t)
-        for h in range(len(PARTS)):
+        for h in range(len(parts(t))):
             far(h, t)
         verdicts(t)
         steps_of("skg%d" % t, "diff", "vr", t, ("b7", "b6"), t + 1, "clb")
@@ -1008,12 +1106,15 @@ def rank_program(g, core, T, topo):
             first_holders()
         decide(t)
         aborts(t)
+        for c in range(512 * BLANK, NV, 1024) if t == 0 else ():
+            src = r("big", FO, FO + 1024)
+            dma("y", r("big", FO + c, FO + c + 1024), (src[0], src[1] + r("lnd0")[1]), "blank%d" % (c // 1024), 2.0 + (c - 512 * BLANK + 1024) / 1000.0)
         keys(t)
         cp(ind(VD, uv("listu")), r("lnd%d" % t))
         if t in FLAG:
             flags(t)
         if not last:
-            ts(r("clb", 0, 16), f("nd"), -BIG - 16 * (t + 2) * U, 16 * (t + 2) * U - BIG, mul, add)
+            ts(r("clb", 0, 16), f("nd"), -BIG - 16 * (t + 2) * U, 17 * (t + 2) * U - BIG, mul, add)
         else:
             cp(r("cr"), ind(r("cf"), uv("lperm")))
             dma("y", ext(T.yc[:]), r("cr"), "oyc", 2.0)
@@ -1035,4 +1136,4 @@ def rank_program(g, core, T, topo):
     dma("y", ext(T.yl[:]), f("yl"), "oyl", 2.0)
     tt(r("hr"), ind(r("cs2"), uv("os")), r("f2"), gt)
     dma("y", ext(T.yh[:]), r("hr"), "oyh", 2.0)
-    issue()
+    return prog, issue

from concourse.mybir import AluOpType, ActivationFunctionType, AxisListType

ALU = AluOpType
ACT = ActivationFunctionType
STEPS = 4
NV = 8192
FB = 16384
DUM, VO = 0, 256
FO = VO + FB
BIGW = FO + NV
LW = NV + 640
U = 32768.0
BIG, HUGE = 4194304.0, 12582912.0
HM = 16384.0
GONE = BIG * HM
FAR = 2.0 ** 40
NAP = 8388608.0
ANEW = 1024.0
FLAG = {1: 2.0 ** 15, 2: 2.0 ** 34}
CALM = {1: 2.0 ** 21, 2: 2.0 ** 21, 3: 2.0 ** 40}
FIRST = ((512, "s"), (512, "s"), (512, "v"), (512, "v"), (1024, "r"), (768, "r"), (256, "r"))
LATER = ((512, "s"), (512, "s"), (512, "s"), (512, "v"), (1024, "r"), (768, "r"), (256, "r"))
CUTS = (FIRST, LATER, LATER, LATER)
AA = ("vvs", "sss", "sss", "sss", "vvs")
APART = (1, 1, 1, 0)
EARLY = (0, 1, 1)
LOADS = (("y", "ea", 0, 2048), ("s", "big", 0, 4096), ("y", "big", 4096, NV), ("y", "ea", 2048, 3072), ("y", "ea", 3072, 4096))
LOCKV = ()
ANEWQ = "s"
BLANK = 16
LUMP = 32
YB = ("vv", "sv", "sv", "sv")
FILL = ((768, 1792, 1024), (768, 768, 768, 768))
PARTS = [(0, 2048), (2048, 3840), (3840, 4096)]
PRICES = ((0.00086, 1.5, 3.5, 0.18, 1.55, 1.0), (0.00083, 1.08, 1.7, 0.2, 1.6, 1.0), (0.0011, 1.9, 5.0, 0.18, 1.6, 0.6))
AFIX, FLYB = 0.076, 0.0005
OTHER = []
GOCC, GLAT = 0.8, 2.6
ROUNDS = 10
RUNS = 3
TRIES = 4500
SHAKE, PUSH, MARK = 0.1, 2.5, 0.5
HEAT = 0.8
SEED = 6
TURN = 8
AIMED = 4
DEBUG = []
ORDER = []

SCRATCH = {
    "big": ("sbuf", [128, BIGW], "bfloat16"),
    "ea": ("sbuf", [128, 4096], "bfloat16"),
    "diff": ("sbuf", [128, 4096], "bfloat16"),
    "absd": ("sbuf", [128, 4096], "bfloat16"),
    "lock": ("sbuf", [128, LW], "float32"),
    "eq": ("sbuf", [128, 16, 272], "bfloat16"),
    "res": ("sbuf", [128, 16, 17], "int32"),
    "cf": ("sbuf", [128, 272], "int32"),
    "ct": ("sbuf", [128, 512], "float32"),
    "slw": ("sbuf", [128, 512], "float32"),
    "won": ("sbuf", [128, 528], "float32"),
    "ldw": ("sbuf", [128, 272], "bfloat16"),
    "tla": ("sbuf", [128, 16, 4], "float32"),
    "tlb": ("sbuf", [128, 16, 4], "int32"),
    "td": ("sbuf", [128, 16, 4], "float32"),
    "qw": ("sbuf", [128, 144], "float32"),
    "gib": ("sbuf", [128, 64], "bfloat16"),
}
for _n in ("codes", "yt"):
    SCRATCH[_n] = ("sbuf", [128, 512], "float32")
for _n in ("csk", "hok", "ai", "tj"):
    SCRATCH[_n] = ("sbuf", [128, 256], "int32")
for _n in ("r16", "dj", "rst", "diag", "cut", "cg", "cs2", "f1", "f2", "pos", "cr", "hr", "un", "qk", "q16", "pd", "aa", "cv", "cw"):
    SCRATCH[_n] = ("sbuf", [128, 256], "float32")
for _n in ("iw", "pw", "dg1", "ka", "st", "s1", "s2", "zt", "sg"):
    SCRATCH[_n] = ("sbuf", [128, 272], "float32")
for _n in ("qb", "blkf", "turn", "swap"):
    SCRATCH[_n] = ("sbuf", [128, 128], "float32")
for _n in ("blk", "nblk", "blkw", "blkh", "mix", "id_", "nid_"):
    SCRATCH[_n] = ("sbuf", [128, 128], "bfloat16")
SCRATCH["wwin"] = ("sbuf", [128, 144], "bfloat16")
SCRATCH["es"] = ("sbuf", [128, 1536], "float16")
SCRATCH["am"] = ("sbuf", [128, 128], "float32")
for _n in ("idh", "turh", "amh"):
    SCRATCH[_n] = ("sbuf", [128, 128], "float16")
SCRATCH["sel"] = ("sbuf", [128, 2048], "bfloat16")
SCRATCH["lg"] = ("sbuf", [128, 512], "bfloat16")
SCRATCH["yb"] = ("sbuf", [128, 384], "bfloat16")
for _n in ("fa", "fv", "thn", "lh"):
    SCRATCH[_n] = ("sbuf", [128, 256], "bfloat16")
QUADS = ["sm", "lf", "own", "sa", "sb"]
SCRATCH["quads"] = ("sbuf", [128, 72 * len(QUADS)], "float32")
for _n in ("coff", "loff", "ku"):
    SCRATCH[_n] = ("sbuf", [128, 256], "uint16")
FS = ["prf", "col", "col2", "clm", "q8", "sent", "home", "one", "vs", "a32", "a33", "xw", "pl", "hd",
      "w", "w1", "nd", "k1", "k2", "k3", "l1", "l2", "m1", "m2", "none", "spare", "yl", "iso", "cm", "xn", "j1", "j2", "sen2"]
IS = ["oi", "oi2", "hi", "pi", "by", "sl0", "sl1", "sl2", "sl3", "nw", "pr", "pg", "wk"]
US = ["xu", "xv", "ou", "cua", "cub", "offu", "listu", "slot", "lc", "lr", "lrev", "lperm", "lq", "os", "lk", "lk2", "lct", "offw"]
SCRATCH["fs"] = ("sbuf", [128, 16 * len(FS)], "float32")
SCRATCH["is_"] = ("sbuf", [128, 16 * len(IS)], "int32")
SCRATCH["us"] = ("sbuf", [128, 16 * len(US)], "uint16")
SCRATCH["hw"] = ("sbuf", [128, 272], "bfloat16")
BS = ["rdy", "rs", "w1b", "ab", "dec", "hb"]
SCRATCH["bs"] = ("sbuf", [128, 16 * len(BS)], "bfloat16")
for _n in ("cla", "clb"):
    SCRATCH[_n] = ("sbuf", [128, 32], "bfloat16")
for _t in range(STEPS):
    SCRATCH["sf%d" % _t] = ("sbuf", [128, 16], "bfloat16")
    SCRATCH["lsf%d" % _t] = ("sbuf", [128, 16], "bfloat16")
    SCRATCH["fu%d" % _t] = ("sbuf", [128, 16], "float32")
    SCRATCH["lfu%d" % _t] = ("sbuf", [128, 16], "float32")
    SCRATCH["skg%d" % _t] = ("sbuf", [128, 272], "float32")
    SCRATCH["lkc%d" % _t] = ("sbuf", [128, 272], "float32")
    SCRATCH["snd%d" % _t] = ("sbuf", [128, 256], "bfloat16")
    SCRATCH["lnd%d" % _t] = ("sbuf", [128, 256], "bfloat16")
for _b in range(8):
    SCRATCH["b%d" % _b] = ("psum", [128, 16, 32] if _b == 1 else [128, 512], "float32")

SEMAPHORES = ["c" + q for q in "vspgy"] + ["dcs", "dho", "dwk", "in0", "in1", "in2", "in3", "in4", "in5", "oyc", "oyh", "oyl"] + ["oys%d" % _g for _g in range(8)] + ["blank%d" % _g for _g in range(8)]
for _t in range(STEPS):
    SEMAPHORES += [k + str(_t) for k in ("rsf", "rkc", "rdd", "qsf", "qkc", "qdd", "rfu", "qfu")]
    SEMAPHORES += ["add%d_%d" % (_t, _a) for _a in range(8)]


def emitter(g, T, price):
    eng = {"v": g.vector, "s": g.scalar, "p": g.tensor, "g": g, "y": g.sync}
    WAKE, FLY = price[3:5]
    known = {q: {} for q in eng}
    cnt = {q: 0 for q in eng}
    hist, bank, final, prog = {}, {}, {}, []

    def isbank(n):
        return n[0] == "b" and n[1:].isdigit()

    def meet(x, y):
        return x[0] < y[1] and y[0] < x[1] and not (x[2] == y[2] > 1 and (x[0] - y[0]) % x[2])

    def covers(x, y):
        return x[0] <= y[0] and y[1] <= x[1] and (x[2] == 1 or (x[2] == y[2] and (x[0] - y[0]) % x[2] == 0))

    def before(q, kind, rd, wr):
        evs = []
        for isw, regs in ((False, rd), (True, wr)):
            for n, x in regs:
                if isbank(n):
                    evs += [e for q2, e in bank.get(n, {}).items() if q2 != q]
                for y, w, q2, asyn, e in hist.get(n, ()):
                    inline = q2 == q == "p"
                    if meet(x, y) and (w or isw) and not inline:
                        evs.append(e)
        todo = {}
        for s, v, ck in evs:
            if known[q].get(s, 0) < v and (s not in todo or todo[s][0] < v):
                todo[s] = (v, ck)
        for s in sorted(todo):
            v = todo[s][0]
            if not any(s2 != s and c2.get(s, 0) >= v for s2, (v2, c2) in todo.items()):
                eng[q].wait_ge(T.sem[s], v)
        for s, (v, ck) in todo.items():
            for s2, v2 in ck.items():
                known[q][s2] = max(known[q].get(s2, 0), v2)

    def after(q, rd, wr, sem, val, asyn):
        ck = dict(known[q])
        ck[sem] = val
        e = (sem, val, ck)
        final[sem] = val
        for n, x in wr:
            hist[n] = [h for h in hist.get(n, ()) if not covers(x, h[0])] + [(x, True, q, asyn, e)]
        for n, x in rd:
            hist[n] = [h for h in hist.get(n, ()) if not (not h[1] and h[2] == q and not asyn and covers(x, h[0]))] + [(x, False, q, asyn, e)]
        for n, x in rd + wr:
            if isbank(n):
                bank.setdefault(n, {})[q] = e

    def op(q, call, outs, ins, cost):
        rd = [x for o in ins for x in o[1]] + [x for o in outs for x in o[1][1:]]
        prog.append((q, "op", call, rd, [o[1][0] for o in outs], cost, cost, None))

    def block(n):
        part = prog[-n:]
        del prog[-n:]
        rd, wr, cost = [], [], sum(p[5] for p in part)
        for p in part:
            rd += [x for x in p[3] if x not in rd]
            wr += [x for x in p[4] if x not in wr]
        prog.append((part[0][0], "block", None, rd, wr, cost, cost, part))

    def dma(q, out, in_, sem, lat):
        if q == "g":
            call = lambda: g.dma_start(out=out[0], in_=in_[0], accum_op=ALU.add).then_inc(T.sem[sem], 16)
            prog.append((q, "dma", call, in_[1] + out[1], out[1], GOCC, lat, sem))
            return
        call = lambda: eng[q].dma_start(out=out[0], in_=in_[0]).then_inc(T.sem[sem], 16)
        prog.append((q, "dma", call, in_[1], out[1], 0.1, lat, sem))

    def send(topo, core, dst, out, in_, name, size):
        rid, pid, _s = topo.addr(dst)
        n = len(topo.engines(core, dst))
        call = lambda: g.remote_dma(out[0], in_[0], T.sem["r" + name], T.sem["q" + name], pid, rid, topo.mask(core, dst))
        fly = FLY + size * FLYB
        prog.append(("g", "send", call, in_[1], [], 0.4, 0.4 + fly, ("q" + name, n)))
        loads = [("ea", (0, 4096, 1))] if name == "fu0" else []
        prog.append(("net", "land", None, in_[1] + loads, out[1], 0.0, fly, ("r" + name, n)))

    def order():
        m = len(prog)
        fore, back, seen, lastq, tags, was = [[] for _ in range(m)], [[] for _ in range(m)], {}, {}, [], []
        for i, (q, kind, call, rd, wr, occ, lat, _x) in enumerate(prog):
            pred = {}
            for isw, regs in ((False, rd), (True, wr)):
                for n, x in regs:
                    for k, y, w, q2 in seen.get(n, ()):
                        if k != i and ((meet(x, y) and (w or isw)) or (isbank(n) and (q2 != q or q == "p"))):
                            inline = q2 == q == "p"
                            pred[k] = max(pred.get(k, 0.0), prog[k][5] if inline else prog[k][6] + WAKE)
            if kind == "land":
                pred[i - 1] = prog[i - 1][5]
            if kind == "dma":
                if q in lastq:
                    pred.setdefault(lastq[q], prog[lastq[q]][5])
                lastq[q] = i
            for n, x in wr:
                left = [e for e in seen.get(n, ()) if not covers(x, e[1]) or isbank(n)]
                seen[n] = (left[-60:] if isbank(n) else left) + [(i, x, True, q)]
            for n, x in rd:
                seen.setdefault(n, []).append((i, x, False, q))
            for k in [k for k in pred if prog[k][0] == "p" and any(j > k and prog[j][0] == "p" and k in was[j] for j in pred)]:
                del pred[k]
            was.append(pred)
            for k, l in pred.items():
                fore[k].append((i, l))
                back[i].append((k, l + occ - prog[k][5]))
            tags.append((q, wr[0][0], wr[0][1][0] if wr[0][0] in ("fs", "us", "is_", "quads", "bs") else 0) if wr else q)

        reach = [0] * m
        for i in range(m - 1, -1, -1):
            kept = [(k, l) for k, l in fore[i] if not any(reach[j] >> k & 1 and l2 + WAKE >= l - 1e-9 and (l2 >= l or prog[k][0] != "p") for j, l2 in fore[i])]
            for k, l in fore[i]:
                reach[i] |= reach[k] | 1 << k
            fore[i] = kept
        back = [[] for _ in range(m)]
        for k in range(m):
            for i, l in fore[k]:
                back[i].append((k, l + prog[i][5] - prog[k][5]))

        def place(nxt, first, key):
            left = [0] * m
            for i in range(m):
                for k, l in nxt[i]:
                    left[k] += 1
            when, busy, ready = list(first), {}, sorted((-key[i], -i) for i in range(m) if left[i] == 0)
            while ready:
                i = -ready.pop()[1]
                t, occ, line = when[i], prog[i][5], busy.setdefault(prog[i][0], [])
                if occ:
                    lo, hi = 0, len(line)
                    while lo < hi:
                        mid = (lo + hi) // 2
                        lo, hi = (mid + 1, hi) if line[mid][1] <= t else (lo, mid)
                    while lo < len(line) and line[lo][0] < t + occ - 1e-9:
                        t = max(t, line[lo][1])
                        lo += 1
                    line.insert(lo, (t, t + occ))
                when[i] = t
                for k, l in nxt[i]:
                    if t + l > when[k]:
                        when[k] = t + l
                    left[k] -= 1
                    if left[k] == 0:
                        ready.append((-key[k], -k))
                        ready.sort()
            return when

        seed = [SEED]

        def draw():
            seed[0] = seed[0] * 48271 % 2147483647
            return seed[0] / 2147483647

        def turn(start, shake):
            late = place(back, [prog[i][6] - prog[i][5] for i in range(m)], [shake * draw() - start[i] - prog[i][5] for i in range(m)])
            return place(fore, [0.0] * m, [shake * draw() - late[i] - prog[i][5] for i in range(m)])

        marks = [i for i in range(m) if prog[i][1] == "send"]

        def worth(start):
            return max(start[i] + prog[i][6] for i in range(m)) + MARK * sum(start[i] for i in marks) / len(marks)

        way = [0.0] * m
        for i in range(m - 1, -1, -1):
            way[i] = max([way[k] + l for k, l in fore[i]] + [prog[i][6]])
        start = best = place(fore, [0.0] * m, [-w for w in way])
        for n in range(ROUNDS):
            start = turn(start if worth(start) < worth(best) + 0.7 else best, SHAKE)
            best = min(best, start, key=worth)
        def holdups(start):
            ahead, last = {}, {}
            for i in sorted(range(m), key=lambda i: start[i]):
                if prog[i][5]:
                    ahead[i], last[prog[i][0]] = last.get(prog[i][0]), i
            i, pairs = max(range(m), key=lambda i: start[i] + prog[i][6]), []
            while i is not None:
                k = next((k for k, l in back[i] if abs(start[k] + l - prog[i][5] + prog[k][5] - start[i]) < 1e-6), None)
                if k is None:
                    k = ahead.get(i)
                    if k is not None:
                        pairs.append((i, k))
                i = k
            return pairs

        occs, ques = [p[5] for p in prog], [p[0] for p in prog]
        needs = [[(k, l - occs[i] + occs[k]) for k, l in back[i]] for i in range(m)]
        lined = [None, None]

        def again(now, key):
            if lined[0] is not now:
                lined[:] = [now, sorted(range(m), key=lambda i: now[i])]
            line_up = lined[1]
            edge = min([min(now[i], key[i]) for i in line_up if key[i] != now[i]] + [1e9])
            when, done, busy, rest = list(now), [False] * m, {q: [(-1.0, 0.0)] for q in eng}, []
            for n, i in enumerate(line_up):
                if now[i] >= edge:
                    rest = sorted(line_up[n:], key=lambda i: -key[i])
                    break
                done[i] = True
                if occs[i] and now[i] > edge - 4.0:
                    line = busy[ques[i]]
                    if len(line) == 1:
                        line[0] = (-1.0, now[i])
                    line.append((now[i], now[i] + occs[i]))
                elif occs[i]:
                    busy[ques[i]][0] = (-1.0, now[i] + occs[i])
            while rest:
                i = rest[-1]
                if done[i]:
                    rest.pop()
                    continue
                t = 0.0
                for k, l in needs[i]:
                    if not done[k]:
                        rest.append(k)
                        break
                    if when[k] + l > t:
                        t = when[k] + l
                else:
                    rest.pop()
                    done[i] = True
                    occ = occs[i]
                    if occ:
                        line = busy[ques[i]]
                        if line[-1][1] <= t:
                            line.append((t, t + occ))
                        else:
                            lo, top = len(line) - 1, len(line)
                            while lo and line[lo - 1][1] > t:
                                lo -= 1
                            while lo < top and line[lo][0] < t + occ - 1e-9:
                                if line[lo][1] > t:
                                    t = line[lo][1]
                                lo += 1
                            line.insert(lo, (t, t + occ))
                    when[i] = t
            return when

        held = [None, None]

        also = []
        for other, (_c, _g, _s, wake, _f, weight) in OTHER:
            waits = [[(k, other[k][5] if abs(l - occs[k]) < 1e-9 else other[k][6] + wake) for k, l in needs[i]] for i in range(m)]
            also.append((waits, [p[5] for p in other], [p[6] for p in other], weight))

        def whole(start):
            total, line_up = worth(start), sorted(range(m), key=lambda i: start[i])
            for waits, occ, lat, weight in also:
                when, free, end = [0.0] * m, {q: 0.0 for q in list(eng) + ["net"]}, 0.0
                for i in line_up:
                    t = free[ques[i]] if occ[i] else 0.0
                    for k, l in waits[i]:
                        if when[k] + l > t:
                            t = when[k] + l
                    when[i] = t
                    if occ[i]:
                        free[ques[i]] = t + occ[i]
                    if t + lat[i] > end:
                        end = t + lat[i]
                total += weight * (end + MARK * sum(when[i] for i in marks) / len(marks))
            return total

        def settle(best, tries, heat):
            now, had, first = best, whole(best), worth(best)
            least = had
            for n in range(tries):
                if n % 5 < AIMED:
                    if held[0] is not now:
                        held[:] = [now, holdups(now)]
                    i, k = held[1][int(draw() * len(held[1]))]
                    key = list(now)
                    if draw() < 0.5:
                        key[i] = now[k] - 0.001 - draw() ** 2
                    else:
                        key[k] = now[i] + 0.001 + draw() ** 2
                else:
                    i, by, span = int(draw() * m), PUSH * (draw() - 0.5), 6.0 * draw() if n % 3 else 1000.0
                    key = [now[k] + (by if tags[k] == tags[i] and abs(now[k] - now[i]) <= span else 0.0) for k in range(m)]
                start = again(now, key)
                if n % TURN == 0:
                    start = turn(start, 0.0)
                room = 0.02 + heat * (1 - n / tries) ** 2 * draw()
                if worth(start) > first + 0.4 + room:
                    continue
                w = whole(start)
                if w <= had + 2 * room:
                    now, had, first = start, w, worth(start)
                    if w < least:
                        best, least = start, w
            return best

        best = min([settle(best, TRIES, HEAT) for n in range(RUNS)], key=whole)
        best = settle(best, TRIES, HEAT / 3)
        DEBUG.extend([tags, prog, fore, back, best, way])
        return sorted(range(m), key=lambda i: (best[i], i))

    def issue():
        if not ORDER:
            ORDER.extend(order())
        for q, kind, call, rd, wr, occ, lat, x in [p for i in ORDER for p in (prog[i][7] if prog[i][1] == "block" else [prog[i]])]:
            if kind == "land":
                final[x[0]] = x[1]
                hist.setdefault(wr[0][0], []).append((wr[0][1], True, "net", True, (x[0], x[1], {x[0]: x[1]})))
                continue
            before(q, kind, rd, wr)
            if kind == "op":
                cnt[q] += 1
                call().then_inc(T.sem["c" + q], 1)
                after(q, rd, wr, "c" + q, cnt[q], False)
            else:
                call()
                s, n = (x, 16) if kind == "dma" else x
                after(q, rd, wr, s, n, True)
        for s in sorted(final):
            if known["g"].get(s, 0) < final[s]:
                g.wait_ge(T.sem[s], final[s])

    return op, block, dma, send, issue, prog


def rank_program(g, core, T, topo):
    if T.rank_of(core) is None:
        return
    if not ORDER:
        OTHER[:] = [(written(g, core, T, topo, price)[0], price) for price in PRICES[1:]]
    written(g, core, T, topo, PRICES[0])[1]()


def written(g, core, T, topo, price):
    rank = T.rank_of(core)
    CY, GATHER, SCATTER = price[:3]
    op, block, dma, send, issue, prog = emitter(g, T, price)

    def r(n, a=None, b=None, st=None):
        if n in BS:
            return r("bs", 16 * BS.index(n), 16 * BS.index(n) + 16)
        if n in QUADS:
            return r("quads", 72 * QUADS.index(n) + (a or 0), 72 * QUADS.index(n) + (64 if b is None else b), st)
        a = 0 if a is None else a
        b = T[n].shape[-1] if b is None else b
        return (T[n][:, a:b] if st is None else T[n][:, a:b:st], [(n, (a, b, st or 1))], -((a - b) // (st or 1)))

    def rows(k, n, a, b, st=1):
        return (T[n][0:k, a:b:st],) + r(n, a, b, st)[1:]

    def deep(ap, n, a, b, k):
        return (ap, [(n, (a, b, 1))], k)

    def small(buf, names):
        return lambda n, k=16, at=0: r(buf, 16 * names.index(n) + at, 16 * names.index(n) + at + k)

    f, iv, uv = small("fs", FS), small("is_", IS), small("us", US)

    def ind(win, off):
        return (win[0].indirect(off[0]), win[1] + off[1], 16 * off[2])

    def hd(n):
        return r(n, 0, 256, 16)

    def tl(n):
        return r(n, 15, 256, 16)

    def ext(t):
        return (t, [], 0)

    def kind(o):
        w, _s, d = SCRATCH[o[1][0][0]]
        return len(o[1]) > 1, w == "psum", d in ("bfloat16", "uint16", "float16")

    def cost(out, a, b=None):
        n, ko, ka = a[2], kind(out), kind(a)
        if ko[0]:
            return 0.05 + n * SCATTER * CY
        if ka[0]:
            return 0.05 + n * GATHER * CY
        if b is not None:
            return max(64, n * (1 if ka[1] or kind(b)[1] else 2)) * CY
        return max(64, n * (0.5 if ko[2] and ka[2] else 1)) * CY

    def tt(out, a, b, o):
        op("v", lambda: g.vector.tensor_tensor(out=out[0], in0=a[0], in1=b[0], op=o), [out], [a, b], cost(out, a, b))

    def ts(out, a, s1, s2, o0, o1=None):
        ins = [a] + [s for s in (s1, s2) if isinstance(s, tuple)]
        x1 = s1[0] if isinstance(s1, tuple) else s1
        x2 = s2[0] if isinstance(s2, tuple) else s2
        if o1 is None:
            op("v", lambda: g.vector.tensor_scalar(out=out[0], in0=a[0], scalar1=x1, scalar2=None, op0=o0), [out], ins, cost(out, a))
        else:
            op("v", lambda: g.vector.tensor_scalar(out=out[0], in0=a[0], scalar1=x1, scalar2=x2, op0=o0, op1=o1), [out], ins, cost(out, a))

    def cp(out, a):
        op("v", lambda: g.vector.tensor_copy(out=out[0], in_=a[0]), [out], [a], cost(out, a))

    def scan(out, d0, d1, o0, o1):
        half = kind(out)[2] and kind(d0)[2] and kind(d1)[2]
        op("v", lambda: g.vector.tensor_tensor_scan(out=out[0], data0=d0[0], data1=d1[0], initial=0.0, op0=o0, op1=o1), [out], [d0, d1],
           max(64, d1[2] * (0.5 if half else 1)) * CY)

    def ms(out, v):
        op("v", lambda: g.vector.memset(out[0], v), [out], [], cost(out, out))

    table = []

    def act(out, a, fn, bias=None, scale=None):
        cs = cost(out, a) + 0.015 if kind(out)[0] or kind(a)[0] else AFIX + max(64, a[2]) * CY
        if fn is ACT.Silu and not table:
            table.append(fn)
            cs += 1.3
        ins = [a] + [s for s in (bias, scale) if isinstance(s, tuple)]
        kw = {k: s[0] if isinstance(s, tuple) else s for k, s in (("bias", bias), ("scale", scale)) if s is not None}
        op("s", lambda: g.scalar.activation(out=out[0], in_=a[0], func=fn, **kw), [out], ins, cs)

    def lin(out, a, scale=None, bias=None):
        act(out, a, ACT.Identity, bias=bias, scale=scale)

    def mm(out, l, x, start, stop):
        op("p", lambda: g.tensor.matmul(out[0], l[0], x[0], start, stop), [out], [l, x], max(min(64, l[2]), x[2]) * CY * (1 if kind(x)[2] else 4))

    def iota(out, pat, base, cm=0, after=()):
        op("g", lambda: g.iota(out[0], pat, base, cm, allow_small_or_imprecise_dtypes=True), [out], list(after), 0.13 + 2 * CY * out[2])

    def keep(out, a, pat, cmp, fill, cm=0, base=0):
        op("g", lambda: g.affine_select(out[0], a[0], pat, cmp, fill, base, cm), [out], [a], 0.17 + 2 * CY * out[2])

    def four(n, a, b=None):
        if b is None:
            return (T[n][:, :, a], [(n, (a, 64, 4))], 16)
        return deep(T[n][:, :, a:b], n, 0, 64, 16 * (b - a))

    def gate(n):
        return r(n, 0, 272, 17)

    def tell(t, out, in_, name):
        send(topo, core, T.cores[rank ^ (1 + t)], r(out), r(in_), name, r(in_)[2] * (2 if kind(r(in_))[2] else 4))

    add, sub, mul, mx, mn = ALU.add, ALU.subtract, ALU.mult, ALU.max, ALU.min
    band, shr, eq_, ge, gt, lt, le = ALU.bitwise_and, ALU.arith_shift_right, ALU.is_equal, ALU.is_ge, ALU.is_gt, ALU.is_lt, ALU.is_le
    RES = deep(T.res[:], "res", 0, 272, 272)
    P0 = r("b6", 0, 256)

    def col(i):
        return f("col", 1, i)

    dma("s", r("csk"), ext(T.cs[:]), "dcs", 1.8)
    dma("y", r("hok"), ext(T.hold[:]), "dho", 2.3)
    dma("s", iv("wk"), ext(T.wake[:]), "dwk", 2.5)
    at = 3.0
    for i, (q, n, a, b) in enumerate(LOADS):
        at += 0.25 + (b - a) / 1000.0
        src, off = (T.x, VO) if n == "big" else (T.snap, 0)
        dma(q, r(n, off + a, off + b), ext(src[:, a:b]), "in%d" % i, at)

    iota(iv("pr", 1), [[0, 1]], 0, 1)
    iota(r("dj"), [[0, 8], [16, 32]], NV, 1)
    iota(r("codes", 0, 16 * LUMP), [[0, LUMP // 16], [1, 256]], 17)
    at = sum(FILL[0] + FILL[1])
    iota(r("lock", at, NV), [[0, NV - at]], 0)
    iota(f("q8"), [[1, 16]], 0)
    iota(f("one"), [[0, 16]], 1)
    iota(f("clm", 4), [[1024, 4]], 1520)
    iota(r("lf", 0, 16), [[-1, 16]], 15)
    iota(r("own"), [[512, 4], [16, 16]], 513)
    iota(r("qw"), [[1, 144]], -15)
    iota(r("r16"), [[0, 16], [1, 16]], 0)
    iota(r("lf", 16, 32), [[0, 16]], 15)
    iota(r("lf", 32, 48), [[32, 8], [256, 2]], 0)
    iota(r("lf", 48, 64), [[0, 8], [-32, 2]], 17)
    iota(r("qb"), [[1, 8], [0, 16]], 0)
    iota(f("a32", 17), [[256, 17]], -16)
    for n, k in (("rst", 16), ("sm", 4)):
        iota(r(n), [[0, r(n)[2]]], 1)
        keep(r(n), r(n), [[0, 16], [1, k]], gt, 0.0)
    keep(r("cut"), r("rst"), [[0, 16], [1, 16]], gt, -2 * FAR)
    iota(r("turn"), [[0, 128]], 1)
    keep(r("swap"), r("turn"), [[-32, 4], [16, 2], [-1, 16]], eq_, 0.0, 1, -16)
    keep(r("turn"), r("turn"), [[-1, 16], [-16, 8]], eq_, 0.0, 1)
    for n, a, x in (("cla", 0, 17 * U - BIG), ("cla", 16, -HUGE), ("clb", 0, U - 2 * BIG)):
        iota(r(n, a, a + 16), [[0, 16]], int(x))
    iota(r("iw", 1, 257), [[1, 256]], 1)
    iota(r("q16"), [[32, 16], [0, 16]], 16)
    for x in (r("sa", 0, 144), r("ldw", 0, 1), r("zt"), r("big", DUM, VO)):
        iota(x, [[0, x[2]]], 0)

    def noflags(a, b, after=()):
        for c in range(a, b):
            iota(r("big", FO + 512 * c, FO + 512 * c + 512), [[0, 512]], 0, 0, after)

    noflags(0, BLANK)

    at = 0
    for n in FILL[0]:
        ms(r("lock", at, at + n), 0.0)
        at += n
    for i, n in enumerate(FILL[1]):
        act(r("lock", at, at + n), r("lock", 0, n), ACT.Copy if i else ACT.Silu)
        at += n
    ts(iv("pg", 1, 0), iv("pr", 1), 15, None, band)
    cp(f("prf", 1), iv("pg", 1))
    for a, b in ((0, 64), (64, 256)):
        ts(r("b0", a, b), r("hok", a, b), -100000.0, 100000.0, mul, add)
        tt(r("b0", a, b), r("b0", a, b), r("csk", a, b), add)
        tt(r("b0", a, b), r("b0", a, b), r("dj", a, b), mn)
        cp(r("loff", a, b), r("b0", a, b))
    for c in range(0, 256, LUMP):
        if c // LUMP in LOCKV:
            cp(ind(r("lock"), r("loff", c, c + LUMP)), r("codes", 0, 16 * LUMP))
        else:
            act(ind(r("lock"), r("loff", c, c + LUMP)), r("codes", 0, 16 * LUMP), ACT.Silu)

    ts(iv("pg", 1, 1), iv("pr", 1), 4, None, shr)
    ts(iv("pg", 1, 2), iv("pr", 1), 112, None, band)
    ts(iv("pg", 1, 3), iv("pr", 1), 16, None, band)
    cp(f("prf", 3, 1), iv("pg", 3, 1))
    PRF, PGF, G16, ODD = (f("prf", 1, i) for i in range(4))
    ts(col(2), PRF, 8.0, None, lt)
    ts(col(6), PRF, 8.0, None, ge)
    ts(col(3), PRF, 0.0, None, eq_)
    ts(col(4), PRF, 1.0, None, eq_)
    ts(col(5), col(4), 512.0, col(3), mul, add)
    ts(col(7), col(4), 1.0 / 1024 - 1.0, 1.0, mul, add)
    ts(col(8), col(4), 15.5, -16.0, mul, add)
    ts(col(9), col(4), -1.0, 1.0, mul, add)
    ts(f("clm", 4), f("clm", 4), col(4), 16.0, mul, add)
    ts(col(14), PRF, 16.0, None, mul)
    ts(col(15), PRF, 1.0, None, add)
    ts(r("wwin"), r("qw"), G16, col(5), eq_, mul)
    ts(uv("lq", 32), r("lf", 0, 32), col(14), None, add)
    ts(col(10), PRF, 17.0, 1.0, mul, add)
    ts(uv("lperm"), f("q8"), col(10), None, add)
    cp(uv("lc"), f("q8"))
    ts(uv("lr"), f("q8"), 0.0, PRF, mul, add)
    ts(uv("lrev"), f("q8"), 240.0, col(14), add, sub)
    cp(r("coff"), r("csk"))
    ts(f("a32", 17), f("a32", 17), col(14), None, add)
    ts(iv("oi", 17), f("a32", 17), -112.0, 1.0 / 272, add, mul)
    ts(f("k1", 17), iv("oi", 17), -271.0, None, mul)
    tt(f("k1", 17), f("k1", 17), f("a32", 17), add)
    cp(uv("lk", 17), f("k1", 17))
    cp(r("st"), ind(r("csk"), uv("lk", 17)))
    ts(col(11), iv("pr", 1), 16.0, None, ge)
    for t in FLAG:
        ts(f("col2", 1, 4 + 2 * t), col(2), FLAG[t], None, mul)
    BANK, HALF, WEIGH, OVER = r("gib", 0, 8), r("gib", 8, 24), r("gib", 48, 56), (32, 48)
    ts(BANK, f("q8", 8), PGF, None, eq_)
    ts(r("gib", 24, 32), f("q8", 8), PGF, -1.0, eq_, mul)
    ts(r("gib", 8, 16), f("q8", 8), PGF, col(2), eq_, mul)
    ts(r("gib", 16, 24), f("q8", 8), PGF, col(6), eq_, mul)
    ts(WEIGH, f("q8", 8), PGF, col(15), eq_, mul)
    ts(r("gib", *OVER), f("q8"), PRF, -32.0, eq_, mul)
    ts(r("diag"), r("r16"), PRF, None, eq_)
    ts(r("blk"), r("qb"), PGF, None, eq_)
    ts(r("nblk"), r("qb"), PGF, -1.0, eq_, mul)
    ts(r("blkf"), r("qb"), PGF, None, eq_)
    ts(r("blkh"), r("qb"), PGF, 65536.0 * U, eq_, mul)
    keep(r("id_"), r("blk"), [[-1, 128]], eq_, 0.0, 1)
    keep(r("nid_"), r("nblk"), [[-1, 128]], eq_, 0.0, 1)
    keep(r("mix"), r("nblk"), [[-1, 128]], ge, 0.0, 1)
    keep(r("mix"), r("mix"), [[-1, 128]], ALU.not_equal, -1024.0, 1)
    ts(f("home"), f("q8"), 16.0, col(15), mul, add)
    ts(r("own"), r("own"), PRF, None, add)
    ts(f("sent"), f("home"), NV - 1.0 - HM, None, add)
    ts(f("sen2"), f("home"), 271.0 - HM, None, add)
    ts(f("k1"), f("q8"), PRF, 1.0, gt, add)
    op("v", lambda: g.vector.tensor_reduce(out=f("k3", 1)[0], in_=f("k1")[0], axis=AxisListType.X, op=mul), [f("k3", 1)], [f("k1")], 0.06)
    ts(r("blkw"), r("blkf"), f("k3", 1), U, mul, mul)
    ts(f("k3", 1, 1), f("k3", 1), -2.0 * U, FAR, mul, add)
    ts(r("thn"), r("diag"), f("k3", 1, 1), -FAR, mul, add)
    cp(r("cr"), ind(r("csk"), uv("lrev")))
    op("v", lambda: g.vector.transpose(out=r("ct", 0, 256)[0], in_=r("cr")[0]), [r("ct", 0, 256)], [r("cr")], 256 * CY)
    mm(r("b0", 256, 512), r("swap"), r("ct", 0, 256), True, True)
    act(r("ct", 256, 512), r("b0", 256, 512), ACT.Copy)
    ts(r("lf", 48, 64), r("lf", 48, 64), ODD, PRF, mul, add)
    tt(r("lf", 48, 64), r("lf", 48, 64), r("lf", 32, 48), add)
    cp(uv("lct"), r("lf", 48, 64))
    lin(r("pos"), ind(r("ct"), uv("lct")), None, 288.0)
    ts(f("none"), f("home"), 31.0, None, add)
    ts(f("spare"), f("home"), -768.0, None, add)

    cp(r("hr"), ind(r("hok"), uv("lrev")))
    ts(r("b5", 0, 256), r("hr"), -1.0, 1.0, mul, add)
    lin(r("cv"), r("hr"), -18.0, 17.0)
    scan(r("cs2"), r("rst"), r("b5", 0, 256), mul, add)
    ts(r("fu0"), tl("cs2"), -1.0, 16.0 - ANEW, mul, add)
    lin(r("b4", 256, 512), r("cs2"), -1.0, 17.0)
    tt(r("pd"), r("b4", 256, 512), r("cv"), mn)
    lin(r("qk"), ind(r("pd"), uv("lq")), 32.0, 16.0 - 32.0 * (ANEW + 1))
    tt(r("qk"), r("qk"), r("q16"), sub)
    lin(r("dg1", 1, 257), r("diag"), 32.0)
    ms(hd("hr"), 0.0)
    ms(hd("b5"), 1.0)
    tt(r("f2"), r("b5", 0, 256), r("cr"), mul)
    for n in range(4):
        scan(r("un"), r("hr"), r("f2"), mul, add)
        cp(four("tla", n), tl("un"))
        if n < 3:
            tt(r("f2", 1, 256), r("b5", 1, 256), r("un", 0, 255), mul)
            cp(hd("f2"), hd("cr"))
    cp(uv("xu"), four("tla", 0))
    cp(r("sa", 2, 66, 4), f("home"))
    ts(iv("nw"), iv("wk"), -NAP, 15 * NAP, mul, add)
    for t in range(STEPS):
        ts(iv("sl%d" % t), iv("nw"), t, int(NAP), shr, band)
    cp(uv("cua"), f("home"))

    V = r("big", VO, VO + NV)
    VF = r("big", VO, BIGW)
    VD = r("big", DUM, VO + NV)
    FD = r("big", FO - 256, BIGW)
    LK = r("lock", 0, NV)

    def pick(out, w, src, n):
        for m in range(16):
            mm(out, r(w, 15 - m, 143 - m), r(src, m, n, 16), m == 0, m == 15)
            if m % 8 == 7:
                block(8)

    def sums(bk, c0, c1, src, x, lo, hi, kinds, t, src2, x2, size):
        runs, at = [], 0
        for n, q in CUTS[t]:
            if lo <= at < hi:
                if runs and runs[-1][2] == (q in kinds):
                    runs[-1][1] += n
                else:
                    runs.append([at, at + n, q in kinds])
            at += n
        for second in (True, False):
            for a, b, more in runs:
                for m in range(16 if more or not second else 0):
                    out = (T[bk][(a - lo) // 16:(b - lo) // 16, c0 + m:c1:16],) + r(bk, c0 + m, c1, 16)[1:]
                    if second:
                        mm(out, r(src2, a + m, b, 16), x2, m == 0, False)
                    else:
                        mm(out, r(src, a + m, b, 16), x, not more, not more or m == 15)
                    if m % size == size - 1:
                        block(size)

    def taken(t, h):
        at, got, sign = 0, [], 0
        for n, q in CUTS[t]:
            x = {"s": 0, "d": -1}.get(q, 1)
            if at // 2048 == h and x != sign:
                got.append((at % 2048 // 16, x - sign))
                sign = x
            at += n
        return got and (h,) + tuple(got)

    kept = sorted({taken(t, h) for t in range(STEPS) for h in range(2) if taken(t, h)})
    for i, x in enumerate(kept):
        for n, (a, by) in enumerate(x[1:]):
            ts(col(12) if n else f("col2", 1, 10 + i), iv("pr", 1), float(a), float(by), ge, mul)
            if n:
                tt(f("col2", 1, 10 + i), f("col2", 1, 10 + i), col(12), add)
        if x[0]:
            ts(r("es", 384 * i + 256, 384 * i + 384), r("blk"), 0.0, None, mul)
    cp(r("idh"), r("id_"))
    cp(r("turh"), r("turn"))

    def joint(t):
        return all(q in "qr" for a, (n, q) in enumerate(CUTS[t]) if sum(k for k, _q in CUTS[t][:a]) >= 2048)

    def parts(t):
        return [(0, 2048), (2048, 4096)] if joint(t) else PARTS

    for m in range(0, 16, 4):
        keep(r("sel", 128 * m, 128 * m + 512), r("big", FO, FO + 512), [[-1, 4], [-16, 8], [0, 16]], ALU.not_equal, HM, 1, -m)

    def steps_of(out, src, less, t, banks, unit, cls):
        for h in range(2):
            bk, c, lo = banks[h], 128 * h, 2048 * h
            more = less and taken(t, h)
            if not (less and h and joint(t)):
                if more:
                    mm(r(bk, 0, 256), r("idh"), r("es", 384 * kept.index(more), 384 * kept.index(more) + 256), True, False)
                for m in range(16):
                    mm(r(bk, m, 256, 16), r(src, lo + m, lo + 2048, 16), HALF, not more, not more or m == 15)
                    if m % 8 == 7:
                        block(8)
            if not less:
                for i, x in enumerate(kept):
                    if x[0] == h:
                        ts(r("es", 384 * i, 384 * i + 256), r(bk, 0, 256), f("col2", 1, 10 + i), None, mul)
            if AA[t if less else STEPS][h] == "s":
                act(r("aa", c, c + 128), r(bk, 0, 128), ACT.Copy)
            else:
                cp(r("aa", c, c + 128), r(bk, 0, 128))
            tt(r("ai", c, c + 128), r(bk, 128, 256), r("aa", c, c + 128), mul)
            ts(r("tj", c, c + 128), r("ai", c, c + 128), 3, 511, shr, band)
            if h == 0:
                ts(rows(16, "tj", 0, 128), rows(16, "ai", 0, 128), 3, NV - 1, shr, band)
            ts(r("amh" if h else "am"), r("tj", c, c + 128), 1.0 if h else col(11), None, add)
        mm(deep(T.b1[:, :, 0], "b1", 0, 512, 16), r("id_"), r("cla", 16, 32), True, False)
        for h in range(2):
            mm(deep(T.b1[:, :, 1 + 8 * h:9 + 8 * h], "b1", 0, 512, 128), r("amh" if h else "am"), r("turh" if h else "turn"), False, False)
        mm(deep(T.b1[:, :, 1], "b1", 0, 512, 16), r("id_"), r(cls, 0, 16), False, True)
        if AA[t if less else STEPS][2] == "s":
            lin(r(out), deep(T.b1[:, :, 0:17], "b1", 0, 512, 272), None, -unit * U)
        else:
            ts(r(out), deep(T.b1[:, :, 0:17], "b1", 0, 512, 272), -unit * U, None, add)

    def judge(a, t):
        lo = sum(n for n, q in CUTS[t][:a])
        hi = lo + CUTS[t][a][0]
        d, e, out = (r(n, lo, hi) for n in ("diff", "ea", "absd"))
        cells = ind(V if t < 2 else VF, r("coff", lo // 16, hi // 16))
        if CUTS[t][a][1] == "s":
            bk = r("b%d" % (2 + a % 2), 0, hi - lo)
            act(d, cells, ACT.Copy)
            mm(bk, r("nid_"), e, True, False)
            mm(bk, r("id_"), d, False, True)
            act(out, bk, ACT.Abs)
        elif CUTS[t][a][1] == "d":
            act(d, cells, ACT.Copy, scale=-1.0)
            dma("g", d, e, "add%d_%d" % (t, a), GLAT + (hi - lo) * 0.001)
            act(out, d, ACT.Abs)
        else:
            tt(d, cells, e, sub)
            if CUTS[t][a][1] == "r":
                ts(out, d, 0.0, 2.0, mx, mul)
            elif CUTS[t][a][1] == "q":
                act(out, d, ACT.Relu, scale=2.0)
            else:
                act(out, d, ACT.Abs)

    def far(h, t):
        c, (lo, hi) = 128 * h, parts(t)[h]
        n, bk, at = (hi - lo) // 16, ("b0", "b0", "b3")[h], c
        if h and joint(t):
            bk, at, i = "b6", 256, 384 * kept.index(taken(t, 1))
            mm(r(bk, 0, 384), r("idh"), r("es", i, i + 384), True, False)
            for src, a, x in (("diff", 0, r("gib", 8, 32)), ("absd", 256, BANK)):
                for m in range(16):
                    mm(r(bk, a + m, 384, 16), r(src, lo + m, hi, 16), x, False, a > 0 and m == 15)
                    if m % 8 == 7:
                        block(8)
        else:
            sums(bk, c, c + 128, "absd", BANK, lo, hi, "qr", t, "diff", r("gib", 24, 32), 8)
        if YB[t][h] == "s":
            act(rows(n, "yb", c, c + 128), rows(n, bk, at, at + 128), ACT.Relu, bias=-320.0)
        else:
            ts(rows(n, "yb", c, c + 128), rows(n, bk, at, at + 128), -320.0, 0.0, add, mx)

    def verdicts(t):
        out = r("b2", 256, 272)
        if t:
            mm(out, r("id_"), r("w1b"), True, False)
        for h, (lo, hi) in enumerate(parts(t)):
            n = (hi - lo) // 16
            mm(out, rows(n, "yb", 128 * h, 128 * h + 128), rows(n, "gib", *OVER), t == h == 0, h == len(parts(t)) - 1)
        ts(r("sf%d" % t), out, 0.0, GONE / HM, lt, mul)
        tell(t, "lsf%d" % t, "sf%d" % t, "sf%d" % t)

    def counts(t):
        tell(t, "lfu%d" % t, "fu%d" % t, "fu%d" % t)
        ts(f("l1"), r("fu%d" % t), -1.0, 2 * (16.0 - ANEW), mul, add)

    def spread(out, src, start):
        for m in range(16):
            mm(r(out[0], out[1] + m, out[1] + 256, 16), r("sel", 128 * m, 128 * m + 128), src, start and m == 0, m == 15)
            if m % 8 == 7:
                block(8)

    def first_holders():
        act(r("lg", 0, 256), ind(LK, uv("xu")), ACT.Relu, bias=col(8), scale=col(7))
        pick(r("b4", 0, 16), "wwin", "lg", 256)
        ts(f("hd"), r("b4", 0, 16), HM, None, mul)
        cp(f("xn"), four("tla", 0))

    def holders():
        ts(iv("oi"), iv("hi"), 511, None, band)
        cp(uv("ou"), iv("oi"))
        lin(r("lh"), ind(r("ldw"), uv("ou")), col(4))
        pick(r("b4", 32, 48), "wwin", "lh", 256)
        tt(f("vs"), r("b4", 32, 48), iv("hi"), le)
        tt(r("hb"), iv("oi"), f("vs"), mul)

    def decide(t):
        keep(r("slw", 0, 16), f("none"), [[0, 16]], eq_, 0.0)
        if t:
            tt(r("rdy"), r("lfu%d" % t), f("l1"), eq_)
        else:
            tt(f("l1"), r("lfu0"), f("l1"), eq_)
            tt(f("l2"), f("l1"), r("sf0"), gt)
            tt(r("rdy"), f("l2"), r("lsf0"), gt)
        rk = r("b7", 272, 288)
        scan(r("rs"), f("one"), r("rdy"), mul, add)
        mm(rk, r("mix"), r("rdy"), True, False)
        mm(rk, r("blk"), r("rs"), False, True)
        ts(f("cm"), rk, -1007.0, GONE / HM, lt, mul)
        tt(f("m1"), rk, f("spare"), mn)
        ts(uv("slot"), f("m1"), 1023.0, None, add)
        act(ind(r("slw"), uv("slot")), r("pos"), ACT.Silu)
        ts(gate("zt"), rk, -1007.0, 2 * BIG + 64 * U, lt, mul)
        ts(uv("listu"), r("slw", 0, 16), -32.0, None, add)
        act(r("snd%d" % t), ind(VD, uv("listu")), ACT.Copy)
        tell(t, "lnd%d" % t, "snd%d" % t, "dd%d" % t)

    def aborts(t):
        a, b = (f("cm"), r("lsf%d" % t)) if t else (r("lsf0"), f("cm"))
        tt(r("ab"), r("sf%d" % t), a, mx)
        tt(r("dec"), r("ab"), b, mx)
        tt(gate("st"), r("ab"), b, mx)
        ts(f("nd"), r("dec"), 0.0, None, eq_)

    def keys(t):
        scan(r("b7", 0, 272), r("lkc%d" % t), r("zt"), add, mx)
        now = "st"
        for n, steps in enumerate(["ka"] + ["skg%d" % u for u in range(1, t + 1)]):
            scan(r("s%d" % (1 + n % 2)), r(steps), r(now), add, mx)
            now = "s%d" % (1 + n % 2)
        tt(RES, r("b7", 0, 272), r(now), mx)
        if t == STEPS - 1:
            ts(r("cf"), RES, NV - 1, None, band)
            return
        ts(r("cf"), RES, NV - 1 + FB, None, band)
        cp(r("coff"), ind(r("cf"), uv("lperm")))
        if t < 2:
            P1 = deep(T.b1[:, :, 0:17], "b1", 0, 512, 272)
            if ANEWQ == "s":
                act(r("sg"), r(now), ACT.Sign, bias=0.5 - U)
                lin(P1, r("sg"), FB / 2, FB / 2)
            else:
                ts(P1, RES, U, float(FB), ge, mul)
            tt(r("st"), P1, r("cf"), add)
        else:
            cp(r("st"), r("cf"))

    def flags(t):
        mm(r("b2", 0, 256), r("nid_"), r("snd%d" % t), True, False)
        mm(r("b2", 0, 256), r("id_"), r("lnd%d" % t), False, True)
        act(r("fa"), r("b2", 0, 256), ACT.Abs)
        mm(r("b3", 0, 256), r("blk"), r("fa"), True, True)
        act(r("fv"), r("b3", 0, 256), ACT.Relu, bias=-320.5 * FLAG[t], scale=f("col2", 1, 4 + 2 * t))
        cp(ind(FD, uv("listu")), r("fv"))

    def lanes(t):
        cur, curn = ("sa", "sb") if t % 2 == 0 else ("sb", "sa")
        cu, cun = ("cua", "cub") if t % 2 == 0 else ("cub", "cua")
        last = t == STEPS - 1
        early = last or EARLY[t]
        if early:
            act(r("cw"), ind(r("dg1"), uv(cu)), ACT.Copy)
        if not last:
            act(r("cv"), ind(r("iw"), uv(cu)) if t else r("iw", 1, 257), ACT.Identity, bias=f("clm", 1, t), scale=col(9))
        tt(r(cur, 1, 65, 4), f("home"), r(cur, 2, 66, 4), sub)
        if not APART[t]:
            ts(f("hd"), r("hb"), HM, None, mul)
            tt(f("xn"), f("xn"), f("hd"), add)
        tt(r("pd"), ind(f("xn"), uv("lc")), r("diag"), mul)
        late = APART[t] == 2
        mm(r("b5", 0, 256), r("blkf"), r("pd"), True, late or t == 0)
        if t == 0:
            cp(r("ku"), r("b5", 0, 256))
            spread(("b4", 256), r("dec"), True)
            tt(f("pl"), f("xn"), iv("sl0"), mx)
            ts(f("m2"), r("dec"), HM, None, mul)
            tt(f("pl"), f("pl"), f("m2"), mx)
        elif late:
            tt(r("hb"), r("hb"), r("ab"), mx)
            tt(r("hb"), r("hb"), r("lsf%d" % t), mx)
        else:
            spread(("b5", 0), r("dec"), False)
        if t:
            act(r("pw", 1, 257), r("b5", 0, 256), ACT.Copy)
        BY = r("b4", 48, 64) if t else f("hd")
        if t and APART[t]:
            spread(("b4", 256), r("hb"), True)
            act(r("hw", 1, 257), r("b4", 256, 512), ACT.Copy)
            lin(r("lh"), ind(r("hw"), uv(cu)), col(3))
            pick(BY, "wwin", "lh", 256)
        d = STEPS - 1 - t
        if not last:
            act(r("b4", 256, 512) if t else r("ldw", 1, 257), r("hw" if late else "pw", 1, 257) if t else r("b4", 256, 512), ACT.Relu, bias=-1.0, scale=(t + 2) / GONE)
            if t:
                tt(r("ldw", 1, 257), r("b4", 256, 512), r("ldw", 1, 257), mx)
            ts(four("tla", 0, d + 1), four("tla", 0, d + 1), U, None, add)
            tt(four("tlb", 0, d + 1), deep(T.res[:, :, 1:d + 2], "res", 0, 272, 16 * d + 16), four("tla", 0, d + 1), mx)
            ts(four("tlb", 0, d + 1), four("tlb", 0, d + 1), NV - 1, None, band)
            if t and not early:
                cp(uv("xu", 32), four("tlb", 0, 2))
            tt(four("td", 0, d), four("tlb", 1, d + 1), four("tlb", 0, d), sub)
        tt(f("w1"), r("fu%d" % t), f("nd"), mul)
        if not last:
            ts(r("w1b"), f("w1"), 0.0, CALM[t + 1], ge, mul)
        if t:
            tt(r("cg"), ind(r("pw"), uv(cu)), r("diag"), mul)
            cp(r("ku"), ind(r("pw"), uv(cu)))
            scan(r("cs2"), r("rst"), r("cg"), mul, add)
            tt(f("pl"), tl("cs2"), iv("sl%d" % t), mx)
        PL = f("pl")
        if late:
            ts(f("m2"), PL, float(NV), None, lt)
            tt(PL, BY, PL, add)
        mm(r("b5", 0, 256), r("id_"), r("thn"), True, False)
        for oc in range(16):
            n, at = 256 - 16 * oc, 272 * oc
            ts(deep(T.eq[:, oc, 0:n], "eq", at, at + n, n), r("ku", 16 * oc, 256), f("pl", 1, oc), None, eq_)
            if oc < 15:
                mm(r("b5", 16 * oc + 16, 256), r("blkh"), deep(T.eq[:, oc, 16:n], "eq", at, at + n, n - 16), False, False)
        mm(r("b5", 0, 256), r("blkw"), deep(T.eq[:, 0:16, 0:16], "eq", 0, 272 * 16, 256), False, True)
        if early:
            ts(f("j1"), PL, float(NV), 4096.0, ge, mul)
            ts(f("j2"), r(cur, 2, 66, 4), -HM, None, add)
            tt(f("j1"), f("j1"), f("j2"), add)
        if not last:
            ts(f("k1"), PL, -HM, None, add)
        if late:
            ts(iv("pi"), PL, 2 * NAP, None, mn)
            ts(iv("by"), iv("pi"), 14, 511, shr, band)
            tt(r(cur, 3, 67, 4), iv("by"), f("m2"), mul)
        elif APART[t]:
            for k in ["j1"] * early + ["k1"] * (not last):
                tt(f(k), BY, f(k), add)
            ts(f("m2"), PL, float(NV), 1.0 / HM, lt, mul)
            tt(r(cur, 3, 67, 4), BY, f("m2"), mul)
        else:
            ts(iv("pi"), PL, 2 * NAP, None, mn)
            ts(iv("by"), iv("pi"), 14, 511, shr, band)
            cp(r(cur, 3, 67, 4), iv("by"))
        scan(r("cg"), r("cut"), r("b5", 0, 256), add, mx)
        if early:
            tt(f("j2"), f("j1"), tl("cg"), mx)
            tt(f("j1"), f("j2"), f("sen2"), mn)
            ts(uv("offw"), f("j1"), HM, None, add)
            iota(r("won", 0, 272), [[0, 272]], 0)
            act(ind(r("won"), uv("offw")), r("cw"), ACT.Silu)
            scan(r("cs2"), r("rst"), r("won", 1, 257), mul, add)
        if not last:
            tt(f("k2"), f("k1"), tl("cg"), mx)
            tt(f("k3"), f("k2"), f("sent"), mn)
            ts(uv("offu"), f("k3"), HM, None, add)
            act(ind(r("lock"), uv("offu")), r("cv"), ACT.Silu)
            mine = r("own", 16 * t, 16 * t + 16)
            if t == 0:
                ts(f("xw"), f("k2"), NV - HM, None, lt)
            elif early:
                ts(f("xw"), tl("cs2"), 16.0, None, gt)
            else:
                act(r("lg"), ind(LK, uv("xu", 32)), ACT.Relu, bias=col(8), scale=col(7))
                pick(r("b4", 0, 32), "wwin", "lg", 512)
                tt(f("xw"), r("b4", 0, 32, 2), mine, eq_)
            tt(r("fu%d" % (t + 1)), f("w1"), f("xw"), add)
            counts(t + 1)
            for n in range(d):
                tt(four("td", n), four("td", n), f("xw"), mul)
            if d > 1:
                tt(four("tla", 0, d), four("tlb", 0, d), four("td", 0, d), add)
            tt(f("xn"), four("tlb", 0), four("td", 0), add)
            if early or t == 0:
                cp(uv("xu"), f("xn"))
                act(r("lg", 0, 256), ind(LK, uv("xu")), ACT.Relu, bias=col(8), scale=col(7))
                pick(r("b4", 0, 16), "wwin", "lg", 256)
                cp(iv("hi"), r("b4", 0, 16))
            else:
                tt(f("hd"), r("b4", 1, 32, 2), mine, sub)
                tt(f("hd"), f("hd"), f("xw"), mul)
                tt(iv("hi"), r("b4", 0, 32, 2), f("hd"), add)
            holders()
        ts(r("sm", 1, 64, 4), PL, 2 * NAP, None, ge)
        ts(r("sm", 2, 64, 4), r(cur, 3, 67, 4), 0.0, None, eq_)
        scan(r(curn, 0, 64), r("sm"), r(cur, 1, 65), mul, add)
        if not last:
            cp(uv(cun), r(curn, 2, 64, 4))

    for t in range(STEPS):
        last = t == STEPS - 1
        if t == 0:
            counts(0)
            steps_of("ka", "ea", "", t, ("b7", "b6"), 1, "cla")
        for a in range(len(CUTS[t])):
            judge(a, t)
        for h in range(len(parts(t))):
            far(h, t)
        verdicts(t)
        steps_of("skg%d" % t, "diff", "vr", t, ("b7", "b6"), t + 1, "clb")
        for u in ([0] if t == 0 else []) + ([] if last else [t + 1]):
            tell(u, "lkc%d" % u, "skg%d" % t, "kc%d" % u)
        if t == 0:
            first_holders()
        decide(t)
        aborts(t)
        for c in range(512 * BLANK, NV, 1024) if t == 0 else ():
            src = r("big", FO, FO + 1024)
            dma("y", r("big", FO + c, FO + c + 1024), (src[0], src[1] + r("lnd0")[1]), "blank%d" % (c // 1024), 2.0 + (c - 512 * BLANK + 1024) / 1000.0)
        keys(t)
        cp(ind(VD, uv("listu")), r("lnd%d" % t))
        if t in FLAG:
            flags(t)
        if not last:
            ts(r("clb", 0, 16), f("nd"), -BIG - 16 * (t + 2) * U, 17 * (t + 2) * U - BIG, mul, add)
        else:
            cp(r("cr"), ind(r("cf"), uv("lperm")))
            dma("y", ext(T.yc[:]), r("cr"), "oyc", 2.0)
            for i in range(64):
                mm(r("b0", i, 512, 64), r("big", VO + i, VO + NV, 64), WEIGH, True, True)
                if i % 4 == 3:
                    block(4)
            for b in range(8):
                if b % 4 == 0:
                    act(r("yt", 64 * b, 64 * b + 256), r("b0", 64 * b, 64 * b + 256), ACT.Copy)
                dma("ys"[b % 2], ext(T.ys[b]), r("yt", 64 * b, 64 * b + 64), "oys%d" % b, 4.6 - 0.35 * b)
        lanes(t)
    ts(f("iso"), f("w1"), 0.0, None, lt)
    tt(r("f1"), ind(f("iso"), uv("lr")), r("qk"), mul)
    tt(r("f1"), r("f1"), r("q16"), add)
    ts(f("w"), f("w1"), -32.0, None, mul)
    tt(r("f2"), ind(f("w"), uv("lr")), r("f1"), add)
    ts(f("yl"), r("sa", 2, 66, 4), -1.0, None, add)
    dma("y", ext(T.yl[:]), f("yl"), "oyl", 2.0)
    tt(r("hr"), ind(r("cs2"), uv("os")), r("f2"), gt)
    dma("y", ext(T.yh[:]), r("hr"), "oyh", 2.0)
    return prog, issue
